import numpy as np, ml_dtypes
CORES = [16,18,20,22]
N = 4
import mx_ref
BF = ml_dtypes.bfloat16
def gcols(t, e):
    v = np.concatenate([t.reshape(8, 16, -1, 4), np.zeros((8, 16, 1, 4), BF)], axis=2)
    return np.ascontiguousarray(np.stack([v[g][:, e[g]] for g in range(8)])).reshape(128, -1)
def tile(rs):
    return np.stack(rs, axis=2).reshape(128, -1).astype(BF)
def pick(q, e):
    c = np.concatenate([q[0].reshape(128, -1, 4), np.zeros((128, 1, 4), np.uint8)], axis=1); s = np.concatenate([q[1], np.ones((16, 1), np.uint8)], axis=1)
    return (np.ascontiguousarray(c[:, e].reshape(128, -1)), np.ascontiguousarray(s[:, e]))
def join(*qs):
    return (np.concatenate([q[0] for q in qs], axis=1), np.concatenate([q[1] for q in qs], axis=1))
def put(q, e, v):
    c, s = q[0].reshape(128, -1, 4).copy(), q[1].copy(); c[:, e] = v[0].reshape(128, -1, 4); s[:, e] = v[1]
    return (c.reshape(128, -1), s)
def pk(c, s):
    return (np.ascontiguousarray(c), mx_ref.live(s))
def emit(q):
    return q[0], q[1]
def packed(v, rng):
    q = [mx_ref.quantize(np.ascontiguousarray(v[r])) for r in range(N)]
    return np.stack([a for a, b in q]), np.stack([mx_ref.plane(b, rng) for a, b in q])
def values_of_codes():
    e, c = np.zeros((128, 128, 4), np.float32), np.zeros((128, 2, 4), np.uint8)
    e[np.arange(128), np.arange(128), 0] = 1
    c[:127, :, 0] = np.arange(256).reshape(2, 128).T[:127]
    return mx_ref.matmul(mx_ref.quantize(e.reshape(128, 512).astype(BF)), (c.reshape(128, 8), np.full((16, 2), 127, np.uint8))).T.reshape(-1).astype(np.float64)
CODE_VALUE, SCALE_VALUE = values_of_codes(), 2.0 ** (np.arange(256) - 127.0)
def decode(q):
    return (CODE_VALUE[q[0]].reshape(16, 8, -1, 4) * SCALE_VALUE[q[1]][:, None, :, None] + 0.0).reshape(128, -1).astype(np.float32)
def f(rng, *shape):
    return mx_ref.flush((rng.standard_normal(shape, dtype=np.float32) * np.exp2(rng.integers(-2, 3, shape[:-1] + (1,)))).astype(BF))
def wide(rng, *shape, cols=0):
    v = rng.standard_normal(shape, dtype=np.float32) * np.exp2(rng.integers(-12, 13, shape)).astype(np.float32)
    if cols: v *= np.repeat(np.exp2(rng.integers(-cols, cols + 1, shape[:-2] + (1, shape[-1] // 4))) * (rng.random(shape[:-2] + (1, shape[-1] // 4)) > 0.0625), 4, axis=-1).astype(np.float32)
    return mx_ref.flush(v.astype(BF))
C, STEP = 384, [1, 2, 3]
def numbers_of(rng):
    return {"x": np.array(f(rng, N, 128, 4 * C)), "u": np.array(f(rng, N, 128, 512)), "v": np.array(f(rng, N, 128, 512))}
def layers(rng):
    return np.array(f(rng, N, 128, 2048)).reshape(N, 8, 16, 4, 8, 16, 4)
def weights(rng, w):
    c, p = packed(np.ascontiguousarray(w).reshape(N, 128, 2048), rng)
    return {"wc": c, "ws": p}
def both(x, u):
    return {"x": x.astype(np.float32).reshape(N, 128, 4 * C).astype(BF), "u": u.astype(np.float32).reshape(N, 128, 512).astype(BF)}
def setup_inputs(rng):
    return {**numbers_of(rng), **weights(rng, layers(rng))}
def setup_inputs_ties(rng):
    d = numbers_of(rng)
    e = rng.permutation(N)
    x = rng.integers(-1, 2, (N, 128, C, 4)) * (rng.random((N, 128, C, 4)) < 0.09375)
    u = rng.integers(-1, 2, (N, 128, 128, 4)) * (rng.random((N, 128, 128, 4)) < 0.09375)
    x[e[0]] = x[e[0]][:, :1].copy()
    x[e[1]] = 0
    u[e[2]] = u[e[2]][:, :1].copy()
    w = np.zeros((N, 128, 512, 4), np.float32)
    for r in range(N):
        a, c = rng.permutation(512)[:128], rng.permutation(512)[:128]
        w[r, a // 4, c, a % 4] = 64
    return {**both(x, u), "v": d["v"], **weights(rng, w.astype(BF))}
def setup_inputs_near(rng):
    d = numbers_of(rng)
    h, o = rng.permutation(8), rng.permutation(N) % 4
    x = d["x"].astype(np.float32).reshape(N, 8, 16, C, 4)
    u = d["u"].astype(np.float32).reshape(N, 8, 16, 128, 4)
    x[:, :, 8:] = 0
    u[:, :, :8] = 0
    x[:, h[:2], :8] = 0
    p = np.exp2(np.arange(4) - 23.0)
    for r in range(N):
        k = 1.0 if o[r] < 2 else 2.0 ** -29
        if o[r] == 3:
            x[r, h[0], 0, :, 0] = rng.choice([1.0, 1.125], C) * 2.0 ** -30
            u[r, h[0], 0, :, 0] = rng.choice([1.125, 1.25], 128) * 2.0 ** -30
        else:
            x[r, h[0], 0, :, 0] = -1.0 if o[r] == 1 else 1.0
            u[r, h[0], 0, :, 0] = k
            x[r, h[1], 0] = ((rng.integers(0, 16, (C, 1)) >> np.arange(4)) & 1) * p
            u[r, h[1], 0] = k
            x[r, h[1], 1] = p
            u[r, h[1], 1] = ((rng.integers(0, 16, (128, 1)) >> np.arange(4)) & 1) * k
            x[r, h[1], 2, :, 0] = 2.0 ** -10
            u[r, h[1], 2, :, 0] = k
        x[r, h[0], 0, rng.integers(C), 0] = 2.0 ** 29
    w = layers(rng)
    w[:, h[:2], :8] = 0
    for g in h[:2]: w[:, :, :, :, g, :8] = 0
    return {**both(x, u), "v": d["v"], **weights(rng, w)}
def setup_inputs_huge(rng):
    d = numbers_of(rng)
    e = rng.permutation(N)
    x = 0.7 + 0.3 * rng.random((N, 8, 16, C, 4))
    u = 0.7 + 0.3 * rng.random((N, 8, 16, 128, 4))
    for i in range(N):
        r = e[i]
        if i == 0:
            x[r] = -0.94 - 0.06 * rng.random((8, 16, C, 4))
            x[r][:, :, rng.permutation(C)[:4]] *= -1.0
            u[r] = 0.94 + 0.06 * rng.random((8, 16, 128, 4))
        elif i % 2 == 1: u[r] *= -1.0
        else:
            x[r] *= rng.choice([-1.0, 1.0], (1, 1, C, 1))
            u[r] *= rng.choice([-1.0, 1.0], (1, 1, 128, 1))
    w = np.zeros((N, 128, 4, 128, 4), np.float32)
    i = np.arange(128)
    for b in range(4): w[:, i, b, i, b] = -1
    return {**both(x * 2.0 ** 30, u * 2.0 ** 30), "v": d["v"], **weights(rng, w.astype(BF))}
def setup_inputs_odd(rng):
    d = numbers_of(rng)
    x = d["x"].astype(np.float32).reshape(N, 8, 16, C, 4)
    u = d["u"].astype(np.float32).reshape(N, 8, 16, 128, 4)
    for a, n in ((x, C), (u, 128)):
        a[:, :, :8] = (2 * rng.integers(0, 8, (N, 8, 8, n, 4)) + 1) * rng.choice([-1.0, 1.0], (N, 8, 8, n, 4)) * 2.0 ** -16
        a[:, :, 0, :, 0] = rng.choice([1.625, 1.75, 1.875, 1.96875], (N, 8, n))
        a[:, :, 8] = 0
        a[:, :, 8, :, 0] = 1
    w = layers(rng)
    w[:, :, :, :, :, :9] = 0
    for g in range(8): w[:, g, 8, 0, g, 0, 0] = 3
    return {**both(x, u), "v": d["v"], **weights(rng, w)}
def setup_inputs_spread(rng):
    d = setup_inputs(rng)
    d["x"] = wide(rng, N, 128, 4 * C, cols=6)
    return d
def check_inputs(d):
    b = []
    for k in ("x", "u", "v"):
        a = np.abs(d[k].astype(np.float32))
        if not (np.isfinite(a).all() and ((a == 0) | (a >= 2.0 ** -30) & (a <= 2.0 ** 30)).all()): b.append("a value of " + k)
    none, least, most = [emit(mx_ref.quantize(np.full((128, 16), k, np.float32).astype(BF)))[1][0, 0] for k in (0.0, 2.0 ** -30, 2.0 ** 30)]
    for r in range(N):
        if ((d["wc"][r] == 0x7F) | (d["wc"][r] == 0xFF)).any(): b.append("wc: a code that is no number")
        s = mx_ref.live(d["ws"][r])
        if ((s != none) & ((s < least) | (s > most))).any(): b.append("ws: a scale out of range")
    return b
def reference(x, u, v, wc, ws):
    lay = [pk(wc[r], ws[r]) for r in range(N)]
    now = [mx_ref.quantize(x[r]) for r in range(N)]
    stat = [mx_ref.quantize(u[r]) for r in range(N)]
    down, along = np.zeros((N, 8, C), np.int64), np.zeros((N, 8, 128), np.int64)
    for h in STEP:
        sent = []
        for r in range(N):
            own = decode(now[r])
            s = mx_ref.matmul(stat[r], now[r]) + np.float32(0.0)
            down[r] = np.argmax(s.reshape(8, 16, C), axis=1) + 16 * np.arange(8)[:, None]
            along[r] = np.argsort(-s, axis=1, kind="stable")[:, :8].T
            a = gcols(decode(stat[r]).astype(BF), down[r]).astype(np.float32)
            z = mx_ref.quantize(((own + a) * np.float32(0.5)).astype(BF))
            now[r] = mx_ref.quantize(tile([mx_ref.matmul(pick(lay[r], np.arange(128 * b, 128 * b + 128)), z) * np.float32(0.03125) + own[:, b::4] for b in range(4)]))
            sent.append(mx_ref.quantize(gcols(decode(now[r]).astype(BF), along[r])))
        stat = [sent[(r - h) % N] for r in range(N)]
    y, op = np.zeros((N, 128, C), np.float32), np.zeros((N, 8, C + 128), np.float32)
    oc, osc = np.zeros((N, 128, 4 * C), np.uint8), np.zeros((N, 16, C), np.uint8)
    uc, usc = np.zeros((N, 128, 512), np.uint8), np.zeros((N, 16, 128), np.uint8)
    for r in range(N):
        y[r] = mx_ref.matmul(mx_ref.quantize(v[r]), now[r])
        op[r, :, :C] = down[r]
        op[r, :, C:] = along[r]
        oc[r], osc[r] = emit(now[r])
        uc[r], usc[r] = emit(stat[r])
    return {"y": y, "op": op, "oc": oc, "osc": osc, "uc": uc, "usc": usc}

@@ -1,0 +1,381 @@
+from concourse.mybir import dt, AluOpType as A, ActivationFunctionType as F
+
+N, C, U, STEP = 4, 384, 128, (1, 2, 3)
+BIG = 1e29
+HW = 388
+PAR = {"down": (0, 1, 1, 1, 1, 1, 1, 2), "z": (6, 3), "x": (19, 5), "zv": (), "xv": (), "dma": (0, 1), "vm": (0, 1), "ea": (1, 3, 4), "eb": (2,),
+       "seq": "M1 M2 E1 M3 M4 O1 M5 H1 E2 E3 B1 M6 H3 E4 Q1 M7 H2 E5 M8 Q3 H5 Q2 H4 E7 O2 H7 Q5 Q7 B2 E6 H6 Q6 Q4"}
+HALF = ((0, 192), (192, 384))
+
+
+def _sb(n, d):
+    return ("sbuf", [128, n], d)
+
+
+CODE, PL, BF, F32, U16, I32 = "float8_e4m3fn_x4", "uint8", "bfloat16", "float32", "uint16", "int32"
+SCRATCH = {
+    "xin": _sb(4 * C, BF), "uin": _sb(512, BF), "vin": _sb(512, BF),
+    "wq": _sb(512, CODE), "wz": _sb(512, PL), "vq": _sb(128, CODE), "vz": _sb(128, PL),
+    "c32": _sb(512, BF), "codd": _sb(512, BF), "eye": _sb(128, BF), "pidx": _sb(1, I32), "pi2": _sb(6, I32), "pf": _sb(8, F32),
+    "ef": _sb(2048, BF), "ee": _sb(2048, BF), "eo": _sb(2048, BF),
+    "efq": _sb(512, CODE), "efz": _sb(512, PL), "eeq": _sb(512, CODE), "eez": _sb(512, PL),
+    "eoq": _sb(512, CODE), "eoz": _sb(512, PL),
+    "cap": _sb(C, F32), "ones": _sb(8, F32), "one": _sb(C, BF), "ssb": _sb(C, F32),
+    "st": _sb(C, F32), "ex": _sb(C, F32), "nr": _sb(C, BF), "tr": _sb(C, BF),
+    "k32": _sb(32, F32), "kd": ("sbuf", [128, 2, 2, 16], F32), "ko": _sb(64, F32),
+    "n32": _sb(32, F32), "nd": ("sbuf", [128, 2, 2, 16], F32), "no": _sb(64, F32),
+    "nop": ("sbuf", [128, 2, 16], F32), "cn": _sb(8, F32), "n0": _sb(1, F32), "it8": _sb(4, F32), "ordk": _sb(4, U16), "ordn": _sb(2, U16),
+    "hist": _sb(9 * HW, F32), "ep": _sb(8, F32), "ob": _sb(8, F32), "sg": _sb(8 * C, BF), "fl": _sb(8 * C, BF), "cu": _sb(8 * C, BF),
+    "junk0": _sb(C, BF), "junk1": _sb(C, BF), "junk2": _sb(C, BF),
+    "zt": _sb(4 * C, BF), "xt": _sb(4 * C, BF), "vt": _sb(512, BF), "yt": _sb(C, F32),
+    "xq0": _sb(C, CODE), "xz0": _sb(C, PL), "uq0": _sb(128, CODE), "uz0": _sb(128, PL),
+    "zq": _sb(C, CODE), "zz": _sb(C, PL), "ok": _sb(48, U16)}
+for _h in (1, 2, 3):
+    SCRATCH.update({
+        "xq%d" % _h: _sb(C, CODE), "xz%d" % _h: _sb(C, PL), "uq%d" % _h: _sb(128, CODE), "uz%d" % _h: _sb(128, PL),
+        "aeq%d" % _h: _sb(C, CODE), "aez%d" % _h: _sb(C, PL), "aoq%d" % _h: _sb(C, CODE), "aoz%d" % _h: _sb(C, PL),
+        "veq%d" % _h: _sb(128, CODE), "vez%d" % _h: _sb(128, PL), "voq%d" % _h: _sb(128, CODE), "voz%d" % _h: _sb(128, PL),
+        "sq%d" % _h: _sb(128, CODE), "sz%d" % _h: _sb(128, PL), "on%d" % _h: _sb(16, U16)})
+for _b in range(8):
+    SCRATCH["p%d" % _b] = ("psum", [128, 512], F32)
+
+SEMAPHORES = (["cv", "cs", "ct", "cp", "sent", "rc1", "rc2", "rc3", "outy", "outs"] + ["d%d" % i for i in range(12)]
+              + ["m%d%d" % (h, i) for h in (1, 2, 3) for i in range(4)])
+
+
+def rank_program(g, core, T, topo):
+    rank = T.rank_of(core)
+    if rank is None:
+        return
+    queues = {"v": g.vector, "s": g.scalar, "t": g.tensor, "p": g, "y": g.sync}
+    count, seen, lastw, readers, nd, njunk = {}, {q: {} for q in queues}, {}, {}, [0], [0]
+
+    def wait(qn, tok):
+        sem, val = tok
+        if seen[qn].get(sem, 0) < val:
+            queues[qn].wait_ge(T.sem[sem], val)
+            seen[qn][sem] = val
+
+    def before(qn, r, w):
+        need = {}
+        own = "c" + qn
+        for k in r:
+            for s, v in lastw.get(k, {}).items():
+                need[s] = max(need.get(s, 0), v)
+        for k in w:
+            for s, v in lastw.get(k, {}).items():
+                if not (qn == "t" and s == own):
+                    need[s] = max(need.get(s, 0), v)
+            for s, v in readers.get(k, {}).items():
+                if s != own:
+                    need[s] = max(need.get(s, 0), v)
+        for s in sorted(need):
+            wait(qn, (s, need[s]))
+
+    def after(tok, r, w):
+        for k in w:
+            lastw[k] = {tok[0]: tok[1]}
+            readers[k] = {}
+        for k in r:
+            readers.setdefault(k, {})[tok[0]] = tok[1]
+
+    def op(qn, f, r, w):
+        before(qn, r, w)
+        sem = "c" + qn
+        count[sem] = count.get(sem, 0) + 1
+        f().then_inc(T.sem[sem], 1)
+        after((sem, count[sem]), r, w)
+
+    def dma(qn, out, in_, r, w, sem=None):
+        before(qn, r, w)
+        if sem is None:
+            sem = "d%d" % nd[0]
+            nd[0] += 1
+        count[sem] = count.get(sem, 0) + 16
+        queues[qn].dma_start(out, in_).then_inc(T.sem[sem], 16)
+        after((sem, count[sem]), r, w)
+
+    v, s, t = g.vector, g.scalar, g.tensor
+    P = [T["p%d" % b] for b in range(8)]
+
+    def mm(bank, lq, lz, a, rq, rz, c, d, keys, start, stop):
+        op("t", lambda: t.matmul_mx(P[bank][:, 0:d - c], T[lq][:, a:a + 128], T[lz][:, a:a + 128], T[rq][:, c:d], T[rz][:, c:d], start, stop),
+           [lq] + keys, ["p%d" % bank])
+
+    def cp(qn, out, in_, r, w, scale=None):
+        if qn == "v":
+            if scale is None:
+                op("v", lambda: v.tensor_copy(out, in_), r, w)
+            else:
+                op("v", lambda: v.tensor_scalar(out, in_, scale, None, A.mult), r, w)
+        else:
+            op("s", lambda: s.activation(out, in_, F.Copy, scale=1.0 if scale is None else scale), r, w)
+
+    def ts(out, in_, s1, s2, o1, o2, r, w):
+        if o2 is None:
+            op("v", lambda: v.tensor_scalar(out, in_, s1, None, o1), r, w)
+        else:
+            op("v", lambda: v.tensor_scalar(out, in_, s1, s2, o1, o2), r, w)
+
+    def quant(q, z, tile, a, b, r, w):
+        op("v", lambda: v.quantize_mx(T[q][:, a:b], T[z][:, a:b], T[tile][:, 4 * a:4 * b]), r, w)
+
+    def pick(dq, dz, sq, sz, off, e, f, c, d, r, w):
+        op("v", lambda: v.tensor_copy(T[dq][:, c:d].bitcast(dt.uint32), T[sq][:].bitcast(dt.uint32).indirect(T[off][:, e:f])), r, [w + "q"])
+        op("s", lambda: s.activation(T[dz][:, c:d], T[sz][:].indirect(T[off][:, e:f]), F.Copy), r, [w + "z"])
+
+    dma("y", T.uin[:], T.u[:], [], ["uin"])
+    dma("s", T.xin[:, 0:512], T.x[:, 0:512], [], ["xin0"])
+    dma("y", T.xin[:, 512:1024], T.x[:, 512:1024], [], ["xin1"])
+    dma("s", T.xin[:, 1024:1536], T.x[:, 1024:1536], [], ["xin2"])
+    dma("y", T.wq[:].bitcast(dt.uint8), T.wc[:], [], ["wq0"])
+    dma("y", T.wz[:], T.ws[:], [], ["wz0"])
+    dma("y", T.vin[:], T.v[:], [], ["vin"])
+
+    op("v", lambda: v.memset(T.c32[:], 32.0), [], ["c32"])
+    op("p", lambda: g.iota(T.pidx[:], [[0, 1]], 0, 1), [], ["pidx"])
+    op("p", lambda: g.affine_select(T.eye[:], T.c32[:, 0:128], [[-1, 128]], A.is_equal, 0.0, 0, 1), ["c32"], ["eye"])
+    op("p", lambda: g.iota(T.it8[:], [[8, 4]], 0, 0, allow_small_or_imprecise_dtypes=True), [], ["it8"])
+    op("v", lambda: v.memset(T.ef[:], 0.0), [], ["ef"])
+    for i, (b, sh) in enumerate(((16, 0), (-1, 5), (15, 1), (1, 0), (6, 0), (8, 3))):
+        if b < 0:
+            ts(T.pi2[:, i:i + 1], T.pidx[:], sh, None, A.arith_shift_right, None, ["pidx"], ["i%d" % i])
+        elif sh:
+            ts(T.pi2[:, i:i + 1], T.pidx[:], b, sh, A.bitwise_and, A.logical_shift_right, ["pidx"], ["i%d" % i])
+        else:
+            ts(T.pi2[:, i:i + 1], T.pidx[:], b, None, A.bitwise_and, None, ["pidx"], ["i%d" % i])
+    for i, (k, m, c) in enumerate(((0, -0.0625, 1.0), (0, 0.0625, 0.0), (1, 32.0, 15.0), (1, 32.0, 31.0), (2, 1.0, 0.0), (3, 32.0, 0.0), (5, 1.0, 0.0))):
+        ts(T.pf[:, i:i + 1], T.pi2[:, k:k + 1], m, c, A.mult, A.add, ["i%d" % k], ["pf%d" % i])
+    for b in range(4):
+        cp("v", T.ef[:, 512 * b + b:512 * (b + 1):4], T.eye[:], ["eye", "ef"], ["efb%d" % b])
+    efk = ["ef"] + ["efb%d" % b for b in range(4)]
+    op("s", lambda: s.activation(T.codd[:], T.c32[:], F.Copy, scale=T.pf[:, 1:2]), ["c32", "pf1"], ["codd"])
+    for b in range(4):
+        op("p", lambda: g.affine_select(T.eo[:, 512 * b:512 * b + 512], T.codd[:], [[-1, 512]], A.is_equal, 0.0, b, 4), ["codd"], ["eo%d" % b])
+    op("s", lambda: s.activation(T.cap[:], T.ef[:, 0:C], F.Copy, scale=0.0, bias=BIG), efk, ["cap"])
+    op("s", lambda: s.activation(T.ee[:], T.ef[:], F.Copy, scale=T.pf[:, 0:1]), efk + ["pf0"], ["ee"])
+    op("s", lambda: s.activation(T.hist[:, 0:HW], T.ef[:, 0:HW], F.Copy, scale=0.0, bias=BIG), efk, ["h0"])
+    op("s", lambda: s.activation(T.one[:], T.ef[:, 0:C], F.Copy, scale=0.0, bias=1.0), efk, ["one"])
+    op("v", lambda: v.quantize_mx(T.efq[:], T.efz[:], T.ef[:]), efk, ["efq"])
+    quant("uq0", "uz0", "uin", 0, 128, ["uin"], ["U0"])
+    for i in range(3):
+        quant("xq0", "xz0", "xin", 128 * i, 128 * i + 128, ["xin%d" % i], ["X00", "X01"] if i == 1 else ["X0%d" % (i // 2)])
+    ts(T.ordk[:], T.it8[:], T.pf[:, 4:5], T.pf[:, 5:6], A.add, A.add, ["it8", "pf4", "pf5"], ["ordk"])
+    ts(T.ordn[:, 0:1], T.pi2[:, 4:5], T.pf[:, 5:6], T.pf[:, 6:7], A.add, A.add, ["i4", "pf5", "pf6"], ["ordn"])
+    op("v", lambda: v.memset(T.ex[:, 0:1], -BIG), [], ["ex0"])
+    op("v", lambda: v.memset(T.k32[:, 24:32], 0.0), [], ["k32z"])
+    op("v", lambda: v.memset(T.n32[:, 8:32], 0.0), [], ["n32z"])
+    op("v", lambda: v.memset(T.ones[:], 1.0), [], ["ones"])
+    op("v", lambda: v.memset(T.ep[:, 0:1], 0.0), [], ["ep0"])
+    op("v", lambda: v.memset(T.hist[:, HW:9 * HW:HW], -BIG), [], ["h%d" % k for k in range(1, 9)])
+    op("v", lambda: v.memset(T.cap[:, 0:C:16], -BIG), ["cap"], ["cap"])
+    SB, S2 = 0, 5
+    BANKS = ((1, 2, 3, 4), (6, 7, 0, 5))
+
+    def hv(k):
+        return T.hist[:, HW * k + C:HW * k + C + 1]
+
+    def sl(name, k):
+        return T[name][:, C * k:C * k + C]
+
+    def counting(dst, src, bias, r, w):
+        j = "junk%d" % (njunk[0] % 3)
+        njunk[0] += 1
+        op("s", lambda: s.activation(T[j][:], src, F.Sign, bias=bias, scale=-1.0, accum_out=dst), r, [j, w])
+
+    def spread(src, keys, db, ob):
+        for i in range(2):
+            op("v", lambda: v.transpose(T[db][:, :, i, :], T[src][:]), keys, [db + str(i)])
+        yield
+        op("v", lambda: v.transpose(T[ob][:], T[db][:]), [db + "0", db + "1"], [ob])
+        yield
+
+    def top8(rd):
+        S = T.ssb[:]
+        todo, ready, done, late = [], set(), set(), []
+
+        def move(G):
+            for a in range(4):
+                o, i = T.n32[32 * G:32 * G + 32, 2 * a:2 * a + 2], T.cn[32 * a:32 * a + 32, 2 * G:2 * G + 2]
+                r, w = ["c%d" % (2 * G), "c%d" % (2 * G + 1)], ["n32%d%d" % (G, a)]
+                if G in PAR["dma"]:
+                    dma("y", o, i, r, w, "m%d%d" % (rd, G))
+                else:
+                    cp("v" if a in PAR["vm"] else "s", o, i, r, w)
+            if G in PAR["dma"]:
+                for a in range(3):
+                    lastw["n32%d%d" % (G, a)] = dict(lastw["n32%d3" % G])
+
+        def flush():
+            for i in [i for i in todo if i in ready]:
+                counting(T.cn[:, i:i + 1], sl("cu", i), T.ob[:, i:i + 1], ["q%d" % i, "ob%d" % (i // 4)], "c%d" % i)
+                todo.remove(i)
+                done.add(i)
+                while late:
+                    move(late.pop())
+                if i == 1 or i % 2 and i - 1 in done or i % 2 == 0 and i + 1 in done:
+                    late.append(i // 2)
+                    if i // 2 in PAR["dma"]:
+                        move(late.pop())
+        for what in PAR["seq"].split():
+            w, k = what[0], int(what[1:])
+            if w == "M":
+                op("v", lambda: v.tensor_tensor_scan(T.hist[:, HW * k + 1:HW * k + 1 + C], S, T.hist[:, HW * (k - 1):HW * (k - 1) + C], -BIG, A.max, A.min),
+                   ["S", "h%d" % (k - 1)], ["h%d" % k])
+                if k == 1:
+                    counting(T.n0[:], T.hist[:, HW + 1:HW + 1 + C], hv(1), ["h1"], "n0")
+            elif w == "E" and k in PAR["ea"] + PAR["eb"]:
+                op("s", lambda: s.activation(sl("sg", k), S, F.Sign, bias=hv(k + 1), scale=-1.0), ["S", "h%d" % (k + 1)], ["s%d" % k])
+                if k in PAR["eb"]:
+                    op("s", lambda: s.activation(sl("fl", k), sl("sg", k), F.Abs), ["s%d" % k], ["f%d" % k])
+                continue
+            elif w == "E":
+                ts(sl("fl", k), S, hv(k + 1), None, A.is_equal, None, ["S", "h%d" % (k + 1)], ["f%d" % k])
+            elif w == "H":
+                if k not in PAR["ea"]:
+                    continue
+                ts(sl("fl", k), sl("sg", k), 0.0, None, A.is_equal, None, ["s%d" % k], ["f%d" % k])
+            elif w == "Q":
+                if k in PAR["eb"]:
+                    op("v", lambda: v.tensor_tensor_scan(sl("cu", k), T.one[:], sl("fl", k), 0.5, A.add, A.subtract), ["f%d" % k, "one"], ["q%d" % k])
+                else:
+                    op("v", lambda: v.tensor_tensor_scan(sl("cu", k), sl("fl", k), sl("fl", k), 0.5, A.add, A.max), ["f%d" % k], ["q%d" % k])
+                todo.append(k)
+                flush()
+            elif w == "O":
+                a, b = (1, 4) if k == 1 else (4, 8)
+                op("v", lambda: v.tensor_tensor(T.ep[:, a:b], T.hist[:, HW * (a + 1) + C:HW * (b + 1):HW], T.hist[:, HW * a + C:HW * b:HW], A.is_equal),
+                   ["h%d" % i for i in range(a, b + 1)], ["ep%d" % k])
+                if k == 1:
+                    ts(T.cn[:, 0:1], T.n0[:], 2.0, -384.0, A.mult, A.add, ["n0"], ["c0"])
+            else:
+                a, b = (0, 4) if k == 1 else (4, 8)
+                op("v", lambda: v.tensor_tensor_scan(T.ob[:, a:b], T.ep[:, a:b], T.ones[:, a:b], T.ob[:, 3:4] if a else 0.0, A.mult, A.add),
+                   (["ob0", "ep2"] if a else ["ep0", "ep1"]) + ["ones"], ["ob%d" % (k - 1)])
+                ready.update(range(a, b))
+                flush()
+            yield
+        while late:
+            move(late.pop())
+        for _ in spread("n32", ["n32z"] + ["n32%d%d" % (G, a) for G in range(4) for a in range(4)], "nd", "no"):
+            yield
+        on = "on%d" % rd
+        ts(T[on][:], T.no[:].indirect(T.ordn[:, 0:1]), 0.5, 192.0, A.mult, A.add, ["no", "ordn"], [on])
+        yield
+
+    for rd in (1, 2, 3):
+        xq, xz, uq, uz = "xq%d" % (rd - 1), "xz%d" % (rd - 1), "uq%d" % (rd - 1), "uz%d" % (rd - 1)
+        nq, nz, on = "xq%d" % rd, "xz%d" % rd, "on%d" % rd
+        uk, xk, nk = ["U%d" % (rd - 1)], ["X%d%d" % (rd - 1, h) for h in (0, 1)], ["X%d%d" % (rd, h) for h in (0, 1)]
+
+        def unpack(bank, h, b):
+            mm(bank, "efq", "efz", 128 * b, xq, xz, HALF[h][0], HALF[h][1], [xk[h]], True, False)
+
+        def ahead():
+            for b in range(4):
+                unpack(BANKS[0][b], 0, b)
+            for b in range(2):
+                unpack(BANKS[1][b], 1, b)
+        if rd > 1:
+            ahead()
+        mm(SB, uq, uz, 0, xq, xz, 0, C, uk + xk, True, True)
+        mm(S2, uq, uz, 0, xq, xz, 0, C, uk + xk, True, True)
+        if rd == 1:
+            ahead()
+        fill = top8(rd)
+        slots = iter(PAR["down"])
+
+        def gap(n=None):
+            n = next(slots, 0) if n is None else n
+            for _ in range(n):
+                next(fill, None)
+        op("v", lambda: v.transpose(T.st[:], P[SB][:, 0:C]), ["p%d" % SB], ["st"])
+        cp("s", T.ssb[:], P[S2][:, 0:C], ["p%d" % S2], ["S"])
+        for b in (2, 3):
+            unpack(BANKS[1][b], 1, b)
+        gap()
+        op("v", lambda: v.tensor_tensor_scan(T.ex[:, 1:C], T.st[:, 0:C - 1], T.cap[:, 1:C], -BIG, A.max, A.min), ["st", "cap"], ["ex"])
+        gap()
+        op("v", lambda: v.tensor_tensor(T.nr[:], T.st[:], T.ex[:], A.is_le), ["st", "ex", "ex0"], ["nr"])
+        gap()
+        if rd == 1:
+            op("v", lambda: v.quantize_mx(T.eeq[:], T.eez[:], T.ee[:]), ["ee"], ["eeq"])
+        op("v", lambda: v.tensor_tensor_scan(T.tr[:], T.nr[:], T.nr[:], 0.0, A.mult, A.add), ["nr"], ["tr"])
+        gap()
+        for i in range(2):
+            ts(T.k32[:, 12 * i:12 * i + 12], T.tr[:, 15 + 16 * i:C:32], -1.0, T.pf[:, 2 + i:3 + i], A.mult, A.add, ["tr", "pf%d" % (2 + i)], ["k32%d" % i])
+        gap()
+        for _ in spread("k32", ["k320", "k321", "k32z"], "kd", "ko"):
+            gap()
+        if rd == 1:
+            op("v", lambda: v.quantize_mx(T.eoq[:], T.eoz[:], T.eo[:]), ["eo%d" % b for b in range(4)], ["eoq"])
+        op("v", lambda: v.tensor_copy(T.ok[:], T.ko[:].indirect(T.ordk[:, 0:3])), ["ko", "ordk"], ["ok"])
+        gap()
+        for h, (c, d) in enumerate(HALF):
+            for i, e in enumerate("eo"):
+                pick("a%sq%d" % (e, rd), "a%sz%d" % (e, rd), uq, uz, "ok", 24 * i + c // 16, 24 * i + d // 16, c, d, uk + ["ok"], "a%s%d" % (e, h))
+                for b in range(4):
+                    mm(BANKS[h][b], "e%sq" % e, "e%sz" % e, 128 * b, "a%sq%d" % (e, rd), "a%sz%d" % (e, rd), c, d, ["a%s%dq" % (e, h), "a%s%dz" % (e, h)], False, e == "o")
+        for h, (c, d) in enumerate(HALF):
+            def take(q, b):
+                cp(q, T.zt[:, 4 * c + b:4 * d:4], P[BANKS[h][b]][:, 0:d - c], ["p%d" % BANKS[h][b]], ["zt%d%d" % (h, b)], 1.0 / 64)
+            for b in range(4):
+                if b not in PAR["zv"]:
+                    take("s", b)
+            gap(PAR["z"][h])
+            for b in PAR["zv"]:
+                take("v", b)
+            for b in range(4):
+                unpack(BANKS[h][b], h, b)
+            quant("zq", "zz", "zt", c, d, ["zt%d%d" % (h, b) for b in range(4)], ["Z%d" % h])
+            for b in range(4):
+                mm(BANKS[h][b], "wq", "wz", 128 * b, "zq", "zz", c, d, ["Z%d" % h, "wq0", "wz0"], False, True)
+        for h, (c, d) in enumerate(HALF):
+            def give(q, b):
+                cp(q, T.xt[:, 4 * c + b:4 * d:4], P[BANKS[h][b]][:, 0:d - c], ["p%d" % BANKS[h][b]], ["xt%d%d" % (h, b)], 1.0 / 32)
+            for b in range(4):
+                if b not in PAR["xv"]:
+                    give("s", b)
+            gap(PAR["x"][h])
+            for b in PAR["xv"]:
+                give("v", b)
+            quant(nq, nz, "xt", c, d, ["xt%d%d" % (h, b) for b in range(4)], [nk[h]])
+        gap(99)
+        for i, e in enumerate("eo"):
+            pick("v%sq%d" % (e, rd), "v%sz%d" % (e, rd), nq, nz, on, 8 * i, 8 * i + 8, 0, 128, nk + [on], "v" + e)
+            for b in range(4):
+                mm(BANKS[0][b], "e%sq" % e, "e%sz" % e, 128 * b, "v%sq%d" % (e, rd), "v%sz%d" % (e, rd), 0, 128, ["v%sq" % e, "v%sz" % e], e == "e", e == "o")
+        for b in range(4):
+            cp("vs"[b % 2], T.vt[:, b:512:4], P[BANKS[0][b]][:, 0:128], ["p%d" % BANKS[0][b]], ["vt%d" % b], 1.0 / 32)
+        quant("sq%d" % rd, "sz%d" % rd, "vt", 0, 128, ["vt%d" % b for b in range(4)], ["out"])
+        dst = T.cores[(rank + STEP[rd - 1]) % N]
+        rid, pid, _ = topo.addr(dst)
+        eng = topo.engines(core, dst)
+        half = len(eng) // 2
+        m1 = sum(1 << e for e in eng[:half])
+        m2 = sum(1 << e for e in eng[half:])
+        before("p", ["out"], [])
+        g.remote_dma(T["uq%d" % rd][:].bitcast(dt.uint8), T["sq%d" % rd][:].bitcast(dt.uint8), T.sem["rc%d" % rd], T.sem["sent"], pid, rid, m1)
+        g.remote_dma(T["uz%d" % rd][:], T["sz%d" % rd][:], T.sem["rc%d" % rd], T.sem["sent"], pid, rid, m2)
+        count["sent"] = count.get("sent", 0) + len(eng)
+        count["rc%d" % rd] = len(eng)
+        lastw["U%d" % rd] = {"rc%d" % rd: len(eng)}
+
+    op("v", lambda: v.quantize_mx(T.vq[:], T.vz[:], T.vin[:]), ["vin"], ["vq"])
+    mm(S2, "vq", "vz", 0, "xq3", "xz3", 0, C, nk, True, True)
+    cp("s", T.yt[:], P[S2][:, 0:C], ["p%d" % S2], ["yt"])
+    ts(T.nop[:], T.nd[:, :, 0, :], 0.5, 192.0, A.mult, A.add, ["nd0"], ["nop"])
+    dma("y", T.oc[:], T.xq3[:].bitcast(dt.uint8), nk, [], "outy")
+    for k in range(4):
+        dma("y", T.osc[4 * k:4 * k + 4, :], T.xz3[32 * k:32 * k + 4, :], nk, [], "outy")
+    for a in range(4):
+        dma("y", T.op[2 * a:2 * a + 2, 0:C], T.kd[32 * a:32 * a + 24, :, 0, :], ["kd0"], [], "outy")
+    dma("s", T.y[:], T.yt[:], ["yt"], [], "outs")
+    for a in range(4):
+        for i in range(2):
+            dma("y" if i else "s", T.op[2 * a + i, C:C + 128], T.nop[32 * a + i:32 * a + 8:2, :, :], ["nop"], [], "outy" if i else "outs")
+    dma("s", T.uc[:], T.uq3[:].bitcast(dt.uint8), ["U3"], [], "outs")
+    for k in range(4):
+        dma("y" if k % 2 else "s", T.usc[4 * k:4 * k + 4, :], T.uz3[32 * k:32 * k + 4, :], ["U3"], [], "outy" if k % 2 else "outs")
+    for sem in sorted(count):
+        wait("p", (sem, count[sem]))

@@ -1,11 +1,10 @@
 from concourse.mybir import dt, AluOpType as A, ActivationFunctionType as F
 
-N, C, U, STEP = 4, 384, 128, (1, 2, 3)
+N, C, STEP = 4, 384, (1, 2, 3)
 BIG = 1e29
 HW = 388
-PAR = {"down": (0, 1, 1, 1, 1, 1, 1, 2), "z": (6, 3), "x": (19, 5), "zv": (), "xv": (), "dma": (0, 1), "vm": (0, 1), "ea": (1, 3, 4), "eb": (2,),
-       "seq": "M1 M2 E1 M3 M4 O1 M5 H1 E2 E3 B1 M6 H3 E4 Q1 M7 H2 E5 M8 Q3 H5 Q2 H4 E7 O2 H7 Q5 Q7 B2 E6 H6 Q6 Q4"}
-HALF = ((0, 192), (192, 384))
+PAR = {"av": (), "dma": (0, 1), "vm": (0, 1), "xv": (), "duv": (), "tv": (0, 1), "vv": (0, 2), "half": ((0, 192), (192, 384)),
+       "lat": 90.0, "fly": 3000.0, "bias": {}}
 
 
 def _sb(n, d):
@@ -16,31 +15,81 @@ CODE, PL, BF, F32, U16, I32 = "float8_e4m3fn_x4", "uint8", "bfloat16", "float32"
 SCRATCH = {
     "xin": _sb(4 * C, BF), "uin": _sb(512, BF), "vin": _sb(512, BF),
     "wq": _sb(512, CODE), "wz": _sb(512, PL), "vq": _sb(128, CODE), "vz": _sb(128, PL),
-    "c32": _sb(512, BF), "codd": _sb(512, BF), "eye": _sb(128, BF), "pidx": _sb(1, I32), "pi2": _sb(6, I32), "pf": _sb(8, F32),
-    "ef": _sb(2048, BF), "ee": _sb(2048, BF), "eo": _sb(2048, BF),
+    "c32": _sb(128, BF), "eye": _sb(128, BF), "pidx": _sb(1, I32), "pi2": _sb(6, I32), "pf": _sb(8, F32),
+    "ef": _sb(520, BF), "ee": _sb(520, BF), "eo": _sb(520, BF),
     "efq": _sb(512, CODE), "efz": _sb(512, PL), "eeq": _sb(512, CODE), "eez": _sb(512, PL),
     "eoq": _sb(512, CODE), "eoz": _sb(512, PL),
-    "cap": _sb(C, F32), "ones": _sb(8, F32), "one": _sb(C, BF), "ssb": _sb(C, F32),
-    "st": _sb(C, F32), "ex": _sb(C, F32), "nr": _sb(C, BF), "tr": _sb(C, BF),
-    "k32": _sb(32, F32), "kd": ("sbuf", [128, 2, 2, 16], F32), "ko": _sb(64, F32),
+    "cap": _sb(C, F32), "st": _sb(C, F32), "ex": _sb(C, F32), "nr": _sb(C, BF), "tr": _sb(1024, BF),
+    "kd": ("sbuf", [128, 2, 2, 16], BF), "ko": _sb(64, BF), "kf": ("sbuf", [128, 2, 2, 16], F32),
     "n32": _sb(32, F32), "nd": ("sbuf", [128, 2, 2, 16], F32), "no": _sb(64, F32),
-    "nop": ("sbuf", [128, 2, 16], F32), "cn": _sb(8, F32), "n0": _sb(1, F32), "it8": _sb(4, F32), "ordk": _sb(4, U16), "ordn": _sb(2, U16),
-    "hist": _sb(9 * HW, F32), "ep": _sb(8, F32), "ob": _sb(8, F32), "sg": _sb(8 * C, BF), "fl": _sb(8 * C, BF), "cu": _sb(8 * C, BF),
-    "junk0": _sb(C, BF), "junk1": _sb(C, BF), "junk2": _sb(C, BF),
+    "cn": _sb(8, F32), "ca": _sb(8, F32), "sg": _sb(8, F32), "b0": _sb(1, F32), "ordn": _sb(2, U16),
+    "hist": _sb(9 * HW, F32), "ab": _sb(8 * C, BF), "al": _sb(8 * HW, BF), "bl": _sb(8 * C, BF), "nop": ("sbuf", [128, 2, 16], F32),
+    "th": _sb(4 * C, BF), "du": _sb(512, BF),
     "zt": _sb(4 * C, BF), "xt": _sb(4 * C, BF), "vt": _sb(512, BF), "yt": _sb(C, F32),
     "xq0": _sb(C, CODE), "xz0": _sb(C, PL), "uq0": _sb(128, CODE), "uz0": _sb(128, PL),
-    "zq": _sb(C, CODE), "zz": _sb(C, PL), "ok": _sb(48, U16)}
+    "zq": _sb(C, CODE), "zz": _sb(C, PL), "ok": _sb(24, U16)}
 for _h in (1, 2, 3):
     SCRATCH.update({
         "xq%d" % _h: _sb(C, CODE), "xz%d" % _h: _sb(C, PL), "uq%d" % _h: _sb(128, CODE), "uz%d" % _h: _sb(128, PL),
-        "aeq%d" % _h: _sb(C, CODE), "aez%d" % _h: _sb(C, PL), "aoq%d" % _h: _sb(C, CODE), "aoz%d" % _h: _sb(C, PL),
         "veq%d" % _h: _sb(128, CODE), "vez%d" % _h: _sb(128, PL), "voq%d" % _h: _sb(128, CODE), "voz%d" % _h: _sb(128, PL),
         "sq%d" % _h: _sb(128, CODE), "sz%d" % _h: _sb(128, PL), "on%d" % _h: _sb(16, U16)})
 for _b in range(8):
     SCRATCH["p%d" % _b] = ("psum", [128, 512], F32)
 
-SEMAPHORES = (["cv", "cs", "ct", "cp", "sent", "rc1", "rc2", "rc3", "outy", "outs"] + ["d%d" % i for i in range(12)]
-              + ["m%d%d" % (h, i) for h in (1, 2, 3) for i in range(4)])
+SEMAPHORES = (["cv", "cs", "ct", "cp", "sent", "rc1", "rc2", "rc3", "outy", "outs"] + ["d%d" % i for i in range(60)])
+CYC = 0.83
+
+
+def lay_out(calls):
+    lat = PAR["lat"]
+    lastw, readers, lastp = {}, {}, {}
+    for i, c in enumerate(calls):
+        hard, soft = set(), set()
+        for k in c["r"]:
+            if k in lastw:
+                hard.add(lastw[k])
+        for k in c["w"]:
+            if k in lastw:
+                (soft if c["q"] == "t" and calls[lastw[k]]["q"] == "t" else hard).add(lastw[k])
+            for j in readers.get(k, ()):
+                (soft if calls[j]["q"] == c["q"] and not calls[j]["late"] else hard).add(j)
+        for k in c["r"] + c["w"]:
+            if k[0] == "p" and k[1:].isdigit():
+                q, ahead, mine = lastp.get(k, (c["q"], [], []))
+                if q != c["q"]:
+                    ahead, mine = mine, []
+                hard.update(ahead)
+                lastp[k] = (c["q"], ahead, mine + [i])
+        for k in c["w"]:
+            lastw[k], readers[k] = i, []
+        for k in c["r"]:
+            readers.setdefault(k, []).append(i)
+        c["hard"], c["soft"], c["next"] = hard, soft - hard, []
+    for i, c in enumerate(calls):
+        for j in c["hard"] | c["soft"]:
+            calls[j]["next"].append(i)
+    for i in range(len(calls) - 1, -1, -1):
+        c = calls[i]
+        c["way"] = c["ns"] + max([0.0] + [calls[j]["way"] + (lat + c["late"] if i in calls[j]["hard"] else 0.0) for j in c["next"]])
+    free, left, order = {}, [len(c["hard"] | c["soft"]) for c in calls], []
+    ready = [i for i in range(len(calls)) if left[i] == 0]
+    for c in calls:
+        c["at"] = 0.0
+    while ready:
+        now = min(max(calls[i]["at"], free.get(calls[i]["q"], 0.0)) for i in ready)
+        can = [i for i in ready if max(calls[i]["at"], free.get(calls[i]["q"], 0.0)) <= now + 1e-6]
+        i = max(can, key=lambda j: (calls[j]["way"] + PAR["bias"].get(calls[j]["tag"], 0.0), -j))
+        c = calls[i]
+        ready.remove(i)
+        order.append(i)
+        free[c["q"]] = now + c["ns"]
+        for j in c["next"]:
+            d = calls[j]
+            d["at"] = max(d["at"], now + c["ns"] + (lat + c["late"] if i in d["hard"] else 0.0))
+            left[j] -= 1
+            if left[j] == 0:
+                ready.append(j)
+    return order
 
 
 def rank_program(g, core, T, topo):
@@ -48,334 +97,266 @@ def rank_program(g, core, T, topo):
     if rank is None:
         return
     queues = {"v": g.vector, "s": g.scalar, "t": g.tensor, "p": g, "y": g.sync}
-    count, seen, lastw, readers, nd, njunk = {}, {q: {} for q in queues}, {}, {}, [0], [0]
-
-    def wait(qn, tok):
-        sem, val = tok
-        if seen[qn].get(sem, 0) < val:
-            queues[qn].wait_ge(T.sem[sem], val)
-            seen[qn][sem] = val
-
-    def before(qn, r, w):
-        need = {}
-        own = "c" + qn
-        for k in r:
-            for s, v in lastw.get(k, {}).items():
-                need[s] = max(need.get(s, 0), v)
-        for k in w:
-            for s, v in lastw.get(k, {}).items():
-                if not (qn == "t" and s == own):
-                    need[s] = max(need.get(s, 0), v)
-            for s, v in readers.get(k, {}).items():
-                if s != own:
-                    need[s] = max(need.get(s, 0), v)
-        for s in sorted(need):
-            wait(qn, (s, need[s]))
-
-    def after(tok, r, w):
-        for k in w:
-            lastw[k] = {tok[0]: tok[1]}
-            readers[k] = {}
-        for k in r:
-            readers.setdefault(k, {})[tok[0]] = tok[1]
-
-    def op(qn, f, r, w):
-        before(qn, r, w)
-        sem = "c" + qn
-        count[sem] = count.get(sem, 0) + 1
-        f().then_inc(T.sem[sem], 1)
-        after((sem, count[sem]), r, w)
-
-    def dma(qn, out, in_, r, w, sem=None):
-        before(qn, r, w)
-        if sem is None:
-            sem = "d%d" % nd[0]
-            nd[0] += 1
-        count[sem] = count.get(sem, 0) + 16
-        queues[qn].dma_start(out, in_).then_inc(T.sem[sem], 16)
-        after((sem, count[sem]), r, w)
-
+    calls = []
     v, s, t = g.vector, g.scalar, g.tensor
     P = [T["p%d" % b] for b in range(8)]
 
-    def mm(bank, lq, lz, a, rq, rz, c, d, keys, start, stop):
-        op("t", lambda: t.matmul_mx(P[bank][:, 0:d - c], T[lq][:, a:a + 128], T[lz][:, a:a + 128], T[rq][:, c:d], T[rz][:, c:d], start, stop),
-           [lq] + keys, ["p%d" % bank])
+    def op(qn, f, r, w, n, tag="", late=0.0, kind="op", sem=None):
+        calls.append({"q": qn, "f": f, "r": list(r), "w": list(w), "ns": n, "tag": tag, "late": late, "kind": kind, "sem": sem})
 
-    def cp(qn, out, in_, r, w, scale=None):
+    def cy(n):
+        return max(64.0, n) * CYC
+
+    def dma(qn, out, in_, r, w, sem=None, tag=""):
+        op(qn, lambda: queues[qn].dma_start(out, in_), r, w, 60.0, tag, 1800.0, "dma", sem)
+
+    def mm(bank, lq, lz, a, rq, rz, c, d, keys, start, stop, tag=""):
+        op("t", lambda: t.matmul_mx(P[bank][:, 0:d - c], T[lq][:, a:a + 128], T[lz][:, a:a + 128], T[rq][:, c:d], T[rz][:, c:d], start, stop),
+           keys, ["p%d" % bank], (d - c + 16) * 0.6, tag)
+
+    def cp(qn, out, in_, r, w, n, scale=None, tag=""):
         if qn == "v":
             if scale is None:
-                op("v", lambda: v.tensor_copy(out, in_), r, w)
+                op("v", lambda: v.tensor_copy(out, in_), r, w, cy(n), tag)
             else:
-                op("v", lambda: v.tensor_scalar(out, in_, scale, None, A.mult), r, w)
+                op("v", lambda: v.tensor_scalar(out, in_, scale, None, A.mult), r, w, cy(n), tag)
         else:
-            op("s", lambda: s.activation(out, in_, F.Copy, scale=1.0 if scale is None else scale), r, w)
+            op("s", lambda: s.activation(out, in_, F.Copy, scale=1.0 if scale is None else scale), r, w, cy(n), tag)
 
-    def ts(out, in_, s1, s2, o1, o2, r, w):
+    def ts(out, in_, s1, s2, o1, o2, r, w, n=1, tag=""):
         if o2 is None:
-            op("v", lambda: v.tensor_scalar(out, in_, s1, None, o1), r, w)
+            op("v", lambda: v.tensor_scalar(out, in_, s1, None, o1), r, w, cy(n), tag)
         else:
-            op("v", lambda: v.tensor_scalar(out, in_, s1, s2, o1, o2), r, w)
+            op("v", lambda: v.tensor_scalar(out, in_, s1, s2, o1, o2), r, w, cy(n), tag)
 
-    def quant(q, z, tile, a, b, r, w):
-        op("v", lambda: v.quantize_mx(T[q][:, a:b], T[z][:, a:b], T[tile][:, 4 * a:4 * b]), r, w)
+    def fill(ap, c, w, n=1):
+        op("v", lambda: v.memset(ap, c), [], w, cy(n))
 
-    def pick(dq, dz, sq, sz, off, e, f, c, d, r, w):
-        op("v", lambda: v.tensor_copy(T[dq][:, c:d].bitcast(dt.uint32), T[sq][:].bitcast(dt.uint32).indirect(T[off][:, e:f])), r, [w + "q"])
-        op("s", lambda: s.activation(T[dz][:, c:d], T[sz][:].indirect(T[off][:, e:f]), F.Copy), r, [w + "z"])
+    def quant(q, z, a, b, src, r, w, tag=""):
+        op("v", lambda: v.quantize_mx(T[q][:, a:b], T[z][:, a:b], src), r, w, 12 + 0.88 * (b - a), tag)
+
+    def scan(out, d0, d1, first, o0, o1, r, w, n, tag=""):
+        op("v", lambda: v.tensor_tensor_scan(out, d0, d1, first, o0, o1), r, w, cy(n), tag)
+
+    def turn(out, in_, r, w, n=1, tag=""):
+        op("v", lambda: v.transpose(out, in_), r, w, cy(n), tag)
+
+    def act(out, in_, f, r, w, n, tag="", **k):
+        op("s", lambda: s.activation(out, in_, f, **k), r, w, cy(n) + (20 if "accum_out" in k else 0), tag)
+
+    def picked(n):
+        return 55 + 1.3 * CYC * n
 
     dma("y", T.uin[:], T.u[:], [], ["uin"])
     dma("s", T.xin[:, 0:512], T.x[:, 0:512], [], ["xin0"])
     dma("y", T.xin[:, 512:1024], T.x[:, 512:1024], [], ["xin1"])
     dma("s", T.xin[:, 1024:1536], T.x[:, 1024:1536], [], ["xin2"])
-    dma("y", T.wq[:].bitcast(dt.uint8), T.wc[:], [], ["wq0"])
-    dma("y", T.wz[:], T.ws[:], [], ["wz0"])
+    dma("y", T.wq[:].bitcast(dt.uint8), T.wc[:], ["xin1"][:0], ["wq"])
+    dma("y", T.wz[:], T.ws[:], [], ["wz"])
     dma("y", T.vin[:], T.v[:], [], ["vin"])
 
-    op("v", lambda: v.memset(T.c32[:], 32.0), [], ["c32"])
-    op("p", lambda: g.iota(T.pidx[:], [[0, 1]], 0, 1), [], ["pidx"])
-    op("p", lambda: g.affine_select(T.eye[:], T.c32[:, 0:128], [[-1, 128]], A.is_equal, 0.0, 0, 1), ["c32"], ["eye"])
-    op("p", lambda: g.iota(T.it8[:], [[8, 4]], 0, 0, allow_small_or_imprecise_dtypes=True), [], ["it8"])
-    op("v", lambda: v.memset(T.ef[:], 0.0), [], ["ef"])
-    for i, (b, sh) in enumerate(((16, 0), (-1, 5), (15, 1), (1, 0), (6, 0), (8, 3))):
-        if b < 0:
-            ts(T.pi2[:, i:i + 1], T.pidx[:], sh, None, A.arith_shift_right, None, ["pidx"], ["i%d" % i])
-        elif sh:
+    fill(T.c32[:], 32.0, ["c32"], 64)
+    op("p", lambda: g.affine_select(T.eye[:], T.c32[:], [[-1, 128]], A.is_equal, 0.0, 0, 1), ["c32"], ["eye"], 385)
+    op("p", lambda: g.iota(T.pidx[:], [[0, 1]], 0, 1), [], ["pidx"], 135)
+    fill(T.ef[:], 0.0, ["ef"], 260)
+    cp("v", T.ef[:, 3:515:4], T.eye[:], ["eye", "ef"], ["ef"], 64)
+    for i, (b, sh) in enumerate(((16, 0), (-16, 0), (1, 0), (6, 0), (8, 3), (-32, 0))):
+        b = b % 128
+        if sh:
             ts(T.pi2[:, i:i + 1], T.pidx[:], b, sh, A.bitwise_and, A.logical_shift_right, ["pidx"], ["i%d" % i])
         else:
             ts(T.pi2[:, i:i + 1], T.pidx[:], b, None, A.bitwise_and, None, ["pidx"], ["i%d" % i])
-    for i, (k, m, c) in enumerate(((0, -0.0625, 1.0), (0, 0.0625, 0.0), (1, 32.0, 15.0), (1, 32.0, 31.0), (2, 1.0, 0.0), (3, 32.0, 0.0), (5, 1.0, 0.0))):
+    for i, (k, m, c) in enumerate(((0, -0.0625, 1.0), (0, 0.0625, 0.0), (1, 1.0, 15.0), (5, 1.0, 15.0), (5, 1.0, 31.0), (2, 32.0, 0.0), (4, 1.0, 0.0))):
         ts(T.pf[:, i:i + 1], T.pi2[:, k:k + 1], m, c, A.mult, A.add, ["i%d" % k], ["pf%d" % i])
-    for b in range(4):
-        cp("v", T.ef[:, 512 * b + b:512 * (b + 1):4], T.eye[:], ["eye", "ef"], ["efb%d" % b])
-    efk = ["ef"] + ["efb%d" % b for b in range(4)]
-    op("s", lambda: s.activation(T.codd[:], T.c32[:], F.Copy, scale=T.pf[:, 1:2]), ["c32", "pf1"], ["codd"])
-    for b in range(4):
-        op("p", lambda: g.affine_select(T.eo[:, 512 * b:512 * b + 512], T.codd[:], [[-1, 512]], A.is_equal, 0.0, b, 4), ["codd"], ["eo%d" % b])
-    op("s", lambda: s.activation(T.cap[:], T.ef[:, 0:C], F.Copy, scale=0.0, bias=BIG), efk, ["cap"])
-    op("s", lambda: s.activation(T.ee[:], T.ef[:], F.Copy, scale=T.pf[:, 0:1]), efk + ["pf0"], ["ee"])
-    op("s", lambda: s.activation(T.hist[:, 0:HW], T.ef[:, 0:HW], F.Copy, scale=0.0, bias=BIG), efk, ["h0"])
-    op("s", lambda: s.activation(T.one[:], T.ef[:, 0:C], F.Copy, scale=0.0, bias=1.0), efk, ["one"])
-    op("v", lambda: v.quantize_mx(T.efq[:], T.efz[:], T.ef[:]), efk, ["efq"])
-    quant("uq0", "uz0", "uin", 0, 128, ["uin"], ["U0"])
+    ts(T.ordn[:, 0:1], T.pi2[:, 3:4], T.pf[:, 5:6], T.pf[:, 6:7], A.add, A.add, ["i3", "pf5", "pf6"], ["ordn"])
+    act(T.ee[:], T.ef[:], F.Copy, ["ef", "pf0"], ["ee"], 520, scale=T.pf[:, 0:1])
+    act(T.eo[:], T.ef[:], F.Copy, ["ef", "pf1"], ["eo"], 520, scale=T.pf[:, 1:2])
+    act(T.cap[:], T.ef[:, 0:C], F.Copy, ["ef"], ["cap"], C, scale=0.0, bias=BIG)
+    act(T.hist[:, 0:HW], T.ef[:, 0:HW], F.Copy, ["ef"], ["h0"], HW, scale=0.0, bias=BIG)
+    for e in "feo":
+        for b in range(4):
+            quant("e%sq" % e, "e%sz" % e, 128 * b, 128 * b + 128, T["e" + e][:, 3 - b:515 - b], ["e" + e], ["e%s%d" % (e, b)])
+    quant("uq0", "uz0", 0, 128, T.uin[:], ["uin"], ["U0"])
     for i in range(3):
-        quant("xq0", "xz0", "xin", 128 * i, 128 * i + 128, ["xin%d" % i], ["X00", "X01"] if i == 1 else ["X0%d" % (i // 2)])
-    ts(T.ordk[:], T.it8[:], T.pf[:, 4:5], T.pf[:, 5:6], A.add, A.add, ["it8", "pf4", "pf5"], ["ordk"])
-    ts(T.ordn[:, 0:1], T.pi2[:, 4:5], T.pf[:, 5:6], T.pf[:, 6:7], A.add, A.add, ["i4", "pf5", "pf6"], ["ordn"])
-    op("v", lambda: v.memset(T.ex[:, 0:1], -BIG), [], ["ex0"])
-    op("v", lambda: v.memset(T.k32[:, 24:32], 0.0), [], ["k32z"])
-    op("v", lambda: v.memset(T.n32[:, 8:32], 0.0), [], ["n32z"])
-    op("v", lambda: v.memset(T.ones[:], 1.0), [], ["ones"])
-    op("v", lambda: v.memset(T.ep[:, 0:1], 0.0), [], ["ep0"])
-    op("v", lambda: v.memset(T.hist[:, HW:9 * HW:HW], -BIG), [], ["h%d" % k for k in range(1, 9)])
-    op("v", lambda: v.memset(T.cap[:, 0:C:16], -BIG), ["cap"], ["cap"])
-    SB, S2 = 0, 5
-    BANKS = ((1, 2, 3, 4), (6, 7, 0, 5))
+        quant("xq0", "xz0", 128 * i, 128 * i + 128, T.xin[:, 512 * i:512 * i + 512], ["xin%d" % i], ["X0%d" % i])
+    fill(T.ex[:, 0:1], -BIG, ["ex0"])
+    fill(T.tr[:, C + 15:1024:16], 0.0, ["trz"])
+    fill(T.n32[:, 8:32], 0.0, ["n32z"])
+    fill(T.sg[:, 7:8], 1.0, ["g7"])
+    fill(T.hist[:, HW:9 * HW:HW], -BIG, ["hz"])
+    fill(T.al[:, 1:8 * HW:HW], 1.0, ["alz"])
+    op("v", lambda: v.memset(T.cap[:, 0:C:16], -BIG), ["cap"], ["cap"], cy(1))
+    HALF = PAR["half"]
+    SV, SS = 0, 1
+    TB, DB, VB = (4, 5, 0, 1), (6, 7, 2, 3), (6, 7, 2, 3)
+    RB = ((4, 5, 6, 7), (2, 3, 4, 5))
 
     def hv(k):
-        return T.hist[:, HW * k + C:HW * k + C + 1]
+        return T.hist[:, HW * (k + 1) + C:HW * (k + 1) + C + 1]
 
     def sl(name, k):
         return T[name][:, C * k:C * k + C]
 
-    def counting(dst, src, bias, r, w):
-        j = "junk%d" % (njunk[0] % 3)
-        njunk[0] += 1
-        op("s", lambda: s.activation(T[j][:], src, F.Sign, bias=bias, scale=-1.0, accum_out=dst), r, [j, w])
-
-    def spread(src, keys, db, ob):
-        for i in range(2):
-            op("v", lambda: v.transpose(T[db][:, :, i, :], T[src][:]), keys, [db + str(i)])
-        yield
-        op("v", lambda: v.transpose(T[ob][:], T[db][:]), [db + "0", db + "1"], [ob])
-        yield
-
-    def top8(rd):
-        S = T.ssb[:]
-        todo, ready, done, late = [], set(), set(), []
-
-        def move(G):
-            for a in range(4):
-                o, i = T.n32[32 * G:32 * G + 32, 2 * a:2 * a + 2], T.cn[32 * a:32 * a + 32, 2 * G:2 * G + 2]
-                r, w = ["c%d" % (2 * G), "c%d" % (2 * G + 1)], ["n32%d%d" % (G, a)]
-                if G in PAR["dma"]:
-                    dma("y", o, i, r, w, "m%d%d" % (rd, G))
-                else:
-                    cp("v" if a in PAR["vm"] else "s", o, i, r, w)
-            if G in PAR["dma"]:
-                for a in range(3):
-                    lastw["n32%d%d" % (G, a)] = dict(lastw["n32%d3" % G])
-
-        def flush():
-            for i in [i for i in todo if i in ready]:
-                counting(T.cn[:, i:i + 1], sl("cu", i), T.ob[:, i:i + 1], ["q%d" % i, "ob%d" % (i // 4)], "c%d" % i)
-                todo.remove(i)
-                done.add(i)
-                while late:
-                    move(late.pop())
-                if i == 1 or i % 2 and i - 1 in done or i % 2 == 0 and i + 1 in done:
-                    late.append(i // 2)
-                    if i // 2 in PAR["dma"]:
-                        move(late.pop())
-        for what in PAR["seq"].split():
-            w, k = what[0], int(what[1:])
-            if w == "M":
-                op("v", lambda: v.tensor_tensor_scan(T.hist[:, HW * k + 1:HW * k + 1 + C], S, T.hist[:, HW * (k - 1):HW * (k - 1) + C], -BIG, A.max, A.min),
-                   ["S", "h%d" % (k - 1)], ["h%d" % k])
-                if k == 1:
-                    counting(T.n0[:], T.hist[:, HW + 1:HW + 1 + C], hv(1), ["h1"], "n0")
-            elif w == "E" and k in PAR["ea"] + PAR["eb"]:
-                op("s", lambda: s.activation(sl("sg", k), S, F.Sign, bias=hv(k + 1), scale=-1.0), ["S", "h%d" % (k + 1)], ["s%d" % k])
-                if k in PAR["eb"]:
-                    op("s", lambda: s.activation(sl("fl", k), sl("sg", k), F.Abs), ["s%d" % k], ["f%d" % k])
-                continue
-            elif w == "E":
-                ts(sl("fl", k), S, hv(k + 1), None, A.is_equal, None, ["S", "h%d" % (k + 1)], ["f%d" % k])
-            elif w == "H":
-                if k not in PAR["ea"]:
-                    continue
-                ts(sl("fl", k), sl("sg", k), 0.0, None, A.is_equal, None, ["s%d" % k], ["f%d" % k])
-            elif w == "Q":
-                if k in PAR["eb"]:
-                    op("v", lambda: v.tensor_tensor_scan(sl("cu", k), T.one[:], sl("fl", k), 0.5, A.add, A.subtract), ["f%d" % k, "one"], ["q%d" % k])
-                else:
-                    op("v", lambda: v.tensor_tensor_scan(sl("cu", k), sl("fl", k), sl("fl", k), 0.5, A.add, A.max), ["f%d" % k], ["q%d" % k])
-                todo.append(k)
-                flush()
-            elif w == "O":
-                a, b = (1, 4) if k == 1 else (4, 8)
-                op("v", lambda: v.tensor_tensor(T.ep[:, a:b], T.hist[:, HW * (a + 1) + C:HW * (b + 1):HW], T.hist[:, HW * a + C:HW * b:HW], A.is_equal),
-                   ["h%d" % i for i in range(a, b + 1)], ["ep%d" % k])
-                if k == 1:
-                    ts(T.cn[:, 0:1], T.n0[:], 2.0, -384.0, A.mult, A.add, ["n0"], ["c0"])
-            else:
-                a, b = (0, 4) if k == 1 else (4, 8)
-                op("v", lambda: v.tensor_tensor_scan(T.ob[:, a:b], T.ep[:, a:b], T.ones[:, a:b], T.ob[:, 3:4] if a else 0.0, A.mult, A.add),
-                   (["ob0", "ep2"] if a else ["ep0", "ep1"]) + ["ones"], ["ob%d" % (k - 1)])
-                ready.update(range(a, b))
-                flush()
-            yield
-        while late:
-            move(late.pop())
-        for _ in spread("n32", ["n32z"] + ["n32%d%d" % (G, a) for G in range(4) for a in range(4)], "nd", "no"):
-            yield
-        on = "on%d" % rd
-        ts(T[on][:], T.no[:].indirect(T.ordn[:, 0:1]), 0.5, 192.0, A.mult, A.add, ["no", "ordn"], [on])
-        yield
-
-    for rd in (1, 2, 3):
+    def one_round(rd):
         xq, xz, uq, uz = "xq%d" % (rd - 1), "xz%d" % (rd - 1), "uq%d" % (rd - 1), "uz%d" % (rd - 1)
         nq, nz, on = "xq%d" % rd, "xz%d" % rd, "on%d" % rd
-        uk, xk, nk = ["U%d" % (rd - 1)], ["X%d%d" % (rd - 1, h) for h in (0, 1)], ["X%d%d" % (rd, h) for h in (0, 1)]
-
-        def unpack(bank, h, b):
-            mm(bank, "efq", "efz", 128 * b, xq, xz, HALF[h][0], HALF[h][1], [xk[h]], True, False)
-
-        def ahead():
+        uk, nk = ["U%d" % (rd - 1)], ["X%d%d" % (rd, h) for h in range(len(HALF))]
+        xk = ["X%d%d" % (rd - 1, h) for h in range(3 if rd == 1 else len(HALF))]
+        def own(banks, behind):
             for b in range(4):
-                unpack(BANKS[0][b], 0, b)
-            for b in range(2):
-                unpack(BANKS[1][b], 1, b)
+                mm(banks[b], "efq", "efz", 128 * b, xq, xz, 0, C, xk + ["ef%d" % b] + behind, True, True, "T")
+                cp("v" if b in PAR["tv"] and rd > 1 else "s", sl("th", b), P[banks[b]][:, 0:C], ["p%d" % banks[b]], ["th%d" % b], C, 1.0 / 64, "T")
         if rd > 1:
-            ahead()
-        mm(SB, uq, uz, 0, xq, xz, 0, C, uk + xk, True, True)
-        mm(S2, uq, uz, 0, xq, xz, 0, C, uk + xk, True, True)
-        if rd == 1:
-            ahead()
-        fill = top8(rd)
-        slots = iter(PAR["down"])
-
-        def gap(n=None):
-            n = next(slots, 0) if n is None else n
-            for _ in range(n):
-                next(fill, None)
-        op("v", lambda: v.transpose(T.st[:], P[SB][:, 0:C]), ["p%d" % SB], ["st"])
-        cp("s", T.ssb[:], P[S2][:, 0:C], ["p%d" % S2], ["S"])
-        for b in (2, 3):
-            unpack(BANKS[1][b], 1, b)
-        gap()
-        op("v", lambda: v.tensor_tensor_scan(T.ex[:, 1:C], T.st[:, 0:C - 1], T.cap[:, 1:C], -BIG, A.max, A.min), ["st", "cap"], ["ex"])
-        gap()
-        op("v", lambda: v.tensor_tensor(T.nr[:], T.st[:], T.ex[:], A.is_le), ["st", "ex", "ex0"], ["nr"])
-        gap()
-        if rd == 1:
-            op("v", lambda: v.quantize_mx(T.eeq[:], T.eez[:], T.ee[:]), ["ee"], ["eeq"])
-        op("v", lambda: v.tensor_tensor_scan(T.tr[:], T.nr[:], T.nr[:], 0.0, A.mult, A.add), ["nr"], ["tr"])
-        gap()
-        for i in range(2):
-            ts(T.k32[:, 12 * i:12 * i + 12], T.tr[:, 15 + 16 * i:C:32], -1.0, T.pf[:, 2 + i:3 + i], A.mult, A.add, ["tr", "pf%d" % (2 + i)], ["k32%d" % i])
-        gap()
-        for _ in spread("k32", ["k320", "k321", "k32z"], "kd", "ko"):
-            gap()
-        if rd == 1:
-            op("v", lambda: v.quantize_mx(T.eoq[:], T.eoz[:], T.eo[:]), ["eo%d" % b for b in range(4)], ["eoq"])
-        op("v", lambda: v.tensor_copy(T.ok[:], T.ko[:].indirect(T.ordk[:, 0:3])), ["ko", "ordk"], ["ok"])
-        gap()
-        for h, (c, d) in enumerate(HALF):
-            for i, e in enumerate("eo"):
-                pick("a%sq%d" % (e, rd), "a%sz%d" % (e, rd), uq, uz, "ok", 24 * i + c // 16, 24 * i + d // 16, c, d, uk + ["ok"], "a%s%d" % (e, h))
-                for b in range(4):
-                    mm(BANKS[h][b], "e%sq" % e, "e%sz" % e, 128 * b, "a%sq%d" % (e, rd), "a%sz%d" % (e, rd), c, d, ["a%s%dq" % (e, h), "a%s%dz" % (e, h)], False, e == "o")
-        for h, (c, d) in enumerate(HALF):
-            def take(q, b):
-                cp(q, T.zt[:, 4 * c + b:4 * d:4], P[BANKS[h][b]][:, 0:d - c], ["p%d" % BANKS[h][b]], ["zt%d%d" % (h, b)], 1.0 / 64)
-            for b in range(4):
-                if b not in PAR["zv"]:
-                    take("s", b)
-            gap(PAR["z"][h])
-            for b in PAR["zv"]:
-                take("v", b)
-            for b in range(4):
-                unpack(BANKS[h][b], h, b)
-            quant("zq", "zz", "zt", c, d, ["zt%d%d" % (h, b) for b in range(4)], ["Z%d" % h])
-            for b in range(4):
-                mm(BANKS[h][b], "wq", "wz", 128 * b, "zq", "zz", c, d, ["Z%d" % h, "wq0", "wz0"], False, True)
-        for h, (c, d) in enumerate(HALF):
-            def give(q, b):
-                cp(q, T.xt[:, 4 * c + b:4 * d:4], P[BANKS[h][b]][:, 0:d - c], ["p%d" % BANKS[h][b]], ["xt%d%d" % (h, b)], 1.0 / 32)
-            for b in range(4):
-                if b not in PAR["xv"]:
-                    give("s", b)
-            gap(PAR["x"][h])
-            for b in PAR["xv"]:
-                give("v", b)
-            quant(nq, nz, "xt", c, d, ["xt%d%d" % (h, b) for b in range(4)], [nk[h]])
-        gap(99)
-        for i, e in enumerate("eo"):
-            pick("v%sq%d" % (e, rd), "v%sz%d" % (e, rd), nq, nz, on, 8 * i, 8 * i + 8, 0, 128, nk + [on], "v" + e)
-            for b in range(4):
-                mm(BANKS[0][b], "e%sq" % e, "e%sz" % e, 128 * b, "v%sq%d" % (e, rd), "v%sz%d" % (e, rd), 0, 128, ["v%sq" % e, "v%sz" % e], e == "e", e == "o")
+            own(TB, ["vt1"])
+        for b in (SV, SS):
+            mm(b, uq, uz, 0, xq, xz, 0, C, uk + xk, True, True, "S")
+            calls[-1]["w"].append("S")
         for b in range(4):
-            cp("vs"[b % 2], T.vt[:, b:512:4], P[BANKS[0][b]][:, 0:128], ["p%d" % BANKS[0][b]], ["vt%d" % b], 1.0 / 32)
-        quant("sq%d" % rd, "sz%d" % rd, "vt", 0, 128, ["vt%d" % b for b in range(4)], ["out"])
+            mm(DB[b], "efq", "efz", 128 * b, uq, uz, 0, 128, uk + ["ef%d" % b], True, True, "D")
+            cp("v" if b in PAR["duv"] else "s", T.du[:, 128 * b:128 * b + 128], P[DB[b]][:, 0:128], ["p%d" % DB[b]], ["du%d" % b], 128, 1.0 / 64, "D")
+        if rd == 1:
+            own((4, 5, 6, 7), ["S"])
+        turn(T.st[:], P[SV][:, 0:C], ["p%d" % SV], ["st"], C, "k")
+        scan(T.ex[:, 1:C], T.st[:, 0:C - 1], T.cap[:, 1:C], -BIG, A.max, A.min, ["st", "cap"], ["ex"], C, "k")
+        op("v", lambda: v.tensor_tensor(T.nr[:], T.st[:], T.ex[:], A.is_le), ["st", "ex", "ex0"], ["nr"], cy(2 * C), "k")
+        scan(T.tr[:, 0:C], T.nr[:], T.nr[:], 0.0, A.mult, A.add, ["nr"], ["tr"], C / 2, "k")
+        for h in range(2):
+            turn(T.kd[:, :, h, :], T.tr[:, 15 + 16 * h:1024:32], ["tr", "trz"], ["kd%d" % h], 1, "k")
+        turn(T.ko[:], T.kd[:], ["kd0", "kd1"], ["ko"], 1, "k")
+        for h in range(2):
+            ts(T.ok[:, h:24:2], T.ko[:, 32 * h:32 * h + 12], -1.0, T.pf[:, 2:3], A.mult, A.add, ["ko", "pf2"], ["ok%d" % h], 1, "k")
+        for k in range(8):
+            scan(T.hist[:, HW * (k + 1) + 1:HW * (k + 1) + 1 + C], P[SV][:, 0:C], T.hist[:, HW * k:HW * k + C], -BIG, A.max, A.min,
+                 ["p%d" % SV, "h%d" % k, "hz"], ["h%d" % (k + 1)], C, "M%d" % k)
+        ts(T.sg[:, 0:1], hv(0), hv(1), -0.5, A.not_equal, A.add, ["h1", "h2"], ["g0"], 1, "g")
+        ts(T.b0[:], hv(0), T.sg[:, 0:1], -1.0, A.mult, A.mult, ["h1", "g0"], ["b0"], 1, "g")
+        for k in range(8):
+            out = sl("bl", k)
+            if k == 0:
+                act(out, T.hist[:, HW:HW + C], F.Sign, ["h1", "g0", "b0"], ["bl0", "c0"], C, "c0",
+                    bias=T.b0[:], scale=T.sg[:, 0:1], accum_out=T.cn[:, 0:1])
+            else:
+                if k < 7:
+                    ts(T.sg[:, k:k + 1], hv(k), hv(k + 1), -0.5, A.is_equal, A.add, ["h%d" % (k + 1), "h%d" % (k + 2)], ["g%d" % k], 1, "g")
+                if k in PAR["av"]:
+                    ts(sl("ab", k), P[SV][:, 0:C], hv(k), None, A.not_equal, None, ["p%d" % SV, "h%d" % (k + 1)], ["a%d" % k], C, "a%d" % k)
+                else:
+                    act(sl("ab", k), P[SS][:, 0:C], F.Abs, ["p%d" % SS, "h%d" % (k + 1)], ["a%d" % k], C, "a%d" % k, bias=hv(k), scale=-1.0)
+                scan(T.al[:, HW * k + 2:HW * k + 2 + C], sl("ab", k), sl("bl", k - 1), 1.0, A.min, A.max, ["a%d" % k, "bl%d" % (k - 1)], ["l%d" % k], C / 2, "l%d" % k)
+                act(out, T.al[:, HW * k + 1:HW * k + 1 + C], F.Sign, ["l%d" % k, "g%d" % k, "alz"], ["bl%d" % k, "c%d" % k], C, "c%d" % k,
+                    scale=T.sg[:, k:k + 1], accum_out=T.cn[:, k:k + 1])
+            if k % 2:
+                G, r = k // 2, ["c%d" % (k - 1), "c%d" % k]
+                whole = G in PAR["dma"] or PAR["vm"]
+                if whole:
+                    e = k + 1 if k < 7 else k
+                    act(T.ca[:, k - 1:e], T.cn[:, k - 1:e], F.Abs, r[:e - k + 1], ["ca%d" % G], 1, "m%d" % G)
+                for a in range(4):
+                    o, w = T.n32[32 * G:32 * G + 32, 2 * a:2 * a + 2], ["n32%d%d" % (G, a)]
+                    if G in PAR["dma"]:
+                        dma("y", o, T.ca[32 * a:32 * a + 32, k - 1:k + 1], ["ca%d" % G], w, None, "m%d" % G)
+                    elif a in PAR["vm"] and k < 7:
+                        cp("v", o, T.ca[32 * a:32 * a + 32, k - 1:k + 1], ["ca%d" % G], w, 1, None, "m%d" % G)
+                    elif a in PAR["vm"]:
+                        op("v", lambda o=o, a=a: v.tensor_tensor(o, T.cn[32 * a:32 * a + 32, 6:8], T.ca[32 * a:32 * a + 32, 6:8], A.max), r + ["ca3", "ca7"], w, cy(1), "m3")
+                    else:
+                        act(o, T.cn[32 * a:32 * a + 32, k - 1:k + 1], F.Abs, r, w, 1, "m%d" % G)
+        for i in range(2):
+            turn(T.nd[:, :, i, :], T.n32[:], ["n32z"] + ["n32%d%d" % (G, a) for G in range(4) for a in range(4)], ["nd%d" % i], 1, "n")
+        turn(T.no[:], T.nd[:], ["nd0", "nd1"], ["no"], 1, "n")
+        op("v", lambda: v.tensor_scalar(T[on][:], T.no[:].indirect(T.ordn[:, 0:1]), -1.0, None, A.add), ["no", "ordn"], [on], picked(16), "n")
+        for h, (c, d) in enumerate(HALF):
+            for b in range(4):
+                op("v", lambda b=b, c=c, d=d: v.tensor_tensor(T.zt[:, 4 * c + b:4 * d:4], T.du[:, 128 * b:128 * b + 128].indirect(T.ok[:, c // 16:d // 16]),
+                                                              T.th[:, C * b + c:C * b + d], A.add),
+                   ["du%d" % b, "th%d" % b, "ok0", "ok1"], ["zt%d%d" % (h, b)], picked(d - c), "z%d" % h)
+            quant("zq", "zz", c, d, T.zt[:, 4 * c:4 * d], ["zt%d%d" % (h, b) for b in range(4)], ["Z%d" % h], "z%d" % h)
+            for b in range(4):
+                bank = RB[h % 2][b]
+                mm(bank, "efq", "efz", 128 * b, xq, xz, c, d, xk + ["ef%d" % b], True, False, "R")
+                mm(bank, "wq", "wz", 128 * b, "zq", "zz", c, d, ["Z%d" % h, "wq", "wz"], False, True, "W")
+                cp("v" if (h, b) in PAR["xv"] else "s", T.xt[:, 4 * c + b:4 * d:4], P[bank][:, 0:d - c], ["p%d" % bank], ["xt%d%d" % (h, b)], d - c, 1.0 / 32, "x%d" % h)
+            quant(nq, nz, c, d, T.xt[:, 4 * c:4 * d], ["xt%d%d" % (h, b) for b in range(4)], [nk[h]], "x%d" % h)
+        for i, e in enumerate("eo"):
+            dq, dz = "v%sq%d" % (e, rd), "v%sz%d" % (e, rd)
+            op("v", lambda dq=dq, i=i: v.tensor_copy(T[dq][:].bitcast(dt.uint32), T[nq][:].bitcast(dt.uint32).indirect(T[on][:, 8 * i:8 * i + 8])),
+               nk + [on], [dq], picked(128), "V")
+            op("s", lambda dz=dz, i=i: s.activation(T[dz][:], T[nz][:].indirect(T[on][:, 8 * i:8 * i + 8]), F.Copy), nk + [on], [dz], picked(128), "V")
+        for i, e in enumerate("eo"):
+            dq, dz = "v%sq%d" % (e, rd), "v%sz%d" % (e, rd)
+            for b in range(4):
+                mm(VB[b], "e%sq" % e, "e%sz" % e, 128 * b, dq, dz, 0, 128, [dq, dz, "e%s%d" % (e, b)], e == "e", e == "o", "V")
+        for b in range(4):
+            cp("v" if b in PAR["vv"] else "s", T.vt[:, b:512:4], P[VB[b]][:, 0:128], ["p%d" % VB[b]], ["vt%d" % b], 128, 1.0 / 32, "V")
+        quant("sq%d" % rd, "sz%d" % rd, 0, 128, T.vt[:], ["vt%d" % b for b in range(4)], ["out%d" % rd], "V")
         dst = T.cores[(rank + STEP[rd - 1]) % N]
         rid, pid, _ = topo.addr(dst)
         eng = topo.engines(core, dst)
         half = len(eng) // 2
         m1 = sum(1 << e for e in eng[:half])
         m2 = sum(1 << e for e in eng[half:])
-        before("p", ["out"], [])
-        g.remote_dma(T["uq%d" % rd][:].bitcast(dt.uint8), T["sq%d" % rd][:].bitcast(dt.uint8), T.sem["rc%d" % rd], T.sem["sent"], pid, rid, m1)
-        g.remote_dma(T["uz%d" % rd][:], T["sz%d" % rd][:], T.sem["rc%d" % rd], T.sem["sent"], pid, rid, m2)
-        count["sent"] = count.get("sent", 0) + len(eng)
-        count["rc%d" % rd] = len(eng)
-        lastw["U%d" % rd] = {"rc%d" % rd: len(eng)}
 
-    op("v", lambda: v.quantize_mx(T.vq[:], T.vz[:], T.vin[:]), ["vin"], ["vq"])
-    mm(S2, "vq", "vz", 0, "xq3", "xz3", 0, C, nk, True, True)
-    cp("s", T.yt[:], P[S2][:, 0:C], ["p%d" % S2], ["yt"])
-    ts(T.nop[:], T.nd[:, :, 0, :], 0.5, 192.0, A.mult, A.add, ["nd0"], ["nop"])
+        def hand_on():
+            g.remote_dma(T["uq%d" % rd][:].bitcast(dt.uint8), T["sq%d" % rd][:].bitcast(dt.uint8), T.sem["rc%d" % rd], T.sem["sent"], pid, rid, m1)
+            g.remote_dma(T["uz%d" % rd][:], T["sz%d" % rd][:], T.sem["rc%d" % rd], T.sem["sent"], pid, rid, m2)
+            return len(eng)
+        op("p", hand_on, ["out%d" % rd], ["U%d" % rd], 500.0, "", PAR["fly"], "far", "rc%d" % rd)
+        return nk
+
+    fill(T.ca[:, 7:8], 0.0, ["ca7"])
+    for rd in (1, 2, 3):
+        nk = one_round(rd)
+
+    quant("vq", "vz", 0, 128, T.vin[:], ["vin"], ["vq"])
+    mm(SS, "vq", "vz", 0, "xq3", "xz3", 0, C, nk + ["vq"], True, True)
+    cp("s", T.yt[:], P[SS][:, 0:C], ["p%d" % SS], ["yt"], C)
+    for h in range(2):
+        ts(T.kf[:, :, h, :], T.kd[:, :, h, :], -1.0, T.pf[:, 3 + h:4 + h], A.mult, A.add, ["kd%d" % h, "pf%d" % (3 + h)], ["kf%d" % h])
+    ts(T.nop[:], T.nd[:, :, 0, :], -1.0, None, A.add, None, ["nd0"], ["nop"])
     dma("y", T.oc[:], T.xq3[:].bitcast(dt.uint8), nk, [], "outy")
     for k in range(4):
         dma("y", T.osc[4 * k:4 * k + 4, :], T.xz3[32 * k:32 * k + 4, :], nk, [], "outy")
     for a in range(4):
-        dma("y", T.op[2 * a:2 * a + 2, 0:C], T.kd[32 * a:32 * a + 24, :, 0, :], ["kd0"], [], "outy")
+        for h in range(2):
+            dma("y", T.op[2 * a + h, 0:C], T.kf[32 * a:32 * a + 12, :, h, :], ["kf%d" % h], [], "outy")
     dma("s", T.y[:], T.yt[:], ["yt"], [], "outs")
     for a in range(4):
         for i in range(2):
-            dma("y" if i else "s", T.op[2 * a + i, C:C + 128], T.nop[32 * a + i:32 * a + 8:2, :, :], ["nop"], [], "outy" if i else "outs")
+            dma("y", T.op[2 * a + i, C:C + 128], T.nop[32 * a + i:32 * a + 8:2, :, :], ["nop"], [], "outy")
     dma("s", T.uc[:], T.uq3[:].bitcast(dt.uint8), ["U3"], [], "outs")
     for k in range(4):
-        dma("y" if k % 2 else "s", T.usc[4 * k:4 * k + 4, :], T.uz3[32 * k:32 * k + 4, :], ["U3"], [], "outy" if k % 2 else "outs")
+        dma("y" if k % 2 == 0 else "s", T.usc[4 * k:4 * k + 4, :], T.uz3[32 * k:32 * k + 4, :], ["U3"], [], "outy" if k % 2 == 0 else "outs")
+
+    count, seen, nd = {}, {q: {} for q in queues}, [0]
+    for i in lay_out(calls):
+        c = calls[i]
+        know = seen[c["q"]]
+        need = [calls[j] for j in sorted(c["hard"])]
+        for d in need:
+            sem, val = d["tok"]
+            if know.get(sem, 0) >= val or any(e is not d and e["know"].get(sem, 0) >= val and (e["tok"][0] != sem or e["tok"][1] > val) for e in need):
+                continue
+            queues[c["q"]].wait_ge(T.sem[sem], val)
+        for d in need:
+            for sem, val in d["know"].items():
+                know[sem] = max(know.get(sem, 0), val)
+        if c["kind"] == "far":
+            n = c["f"]()
+            count["sent"] = count.get("sent", 0) + n
+            count[c["sem"]] = n
+            c["tok"] = (c["sem"], n)
+            c["know"] = {c["sem"]: n}
+            continue
+        sem, n = c["sem"], 16
+        if c["kind"] == "op":
+            sem, n = "c" + c["q"], 1
+        elif sem is None:
+            sem = "d%d" % nd[0]
+            nd[0] += 1
+        count[sem] = count.get(sem, 0) + n
+        c["f"]().then_inc(T.sem[sem], n)
+        c["tok"] = (sem, count[sem])
+        c["know"] = dict(know)
+        c["know"][sem] = count[sem]
     for sem in sorted(count):
-        wait("p", (sem, count[sem]))
+        g.wait_ge(T.sem[sem], count[sem])

@@ -1,10 +1,20 @@
+from concourse.bass import DstId, RemoteDMATransfer
 from concourse.mybir import dt, AluOpType as A, ActivationFunctionType as F
 
 N, C, STEP = 4, 384, (1, 2, 3)
 BIG = 1e29
 HW = 388
-PAR = {"av": (), "dma": (0, 1), "vm": (0, 1), "xv": (), "duv": (), "tv": (0, 1), "vv": (0, 2), "half": ((0, 192), (192, 384)),
-       "lat": 90.0, "fly": 3000.0, "bias": {}}
+PAR = {"av": (), "mv": ("yyyy", "yyyy", "pppp", "vvss"), "xv": (), "zv": (), "duv": (), "tv": (0, 1), "vv": (0, 2), "half": ((0, 192), (192, 384)),
+       "z": ("pp", "pp", "pp"), "down": "mm", "kq": "y", "ttg": 2.0, "g": 1.56, "dl": 1300.0, "ov": 20.0,
+       "lat": 90.0, "fly": 1400.0, "rq": 700.0, "dq": 200.0, "ld": 800.0, "far": "X", "xh": True, "bias": {},
+       "bv": (), "own": None, "tw": 0.0, "tc": 0.6, "xf": 1000.0, "vg": False, "uv": ()}
+PAR.update({'av': (), 'mv': ('pppp', 'ppsp', 'pvpp', 'vvss'), 'xv': ((0, 3), (1, 0), (1, 2)), 'zv': ((1, 0), (1, 1), (1, 2)), 'duv': (), 'tv': (), 'vv': (0, 2), 'half': ((0, 192), (192, 384)), 'z': ('pp', 'pg', 'pg'), 'down': 'mm', 'bias': {'k': 21260.0, 'M6': 54910.0, 'l2': 43530.0, 'M4': 60850.0, 'c7': 37180.0, 'l1': 61590.0, '': 910.0, 'x1': 4610.0, 'Z': -4950.0, 'l4': 45000.0, 'c5': -56700.0, 'V': 60990.0, 'a7': 31440.0, 'l7': 15560.0, 'T': 17360.0, 'a6': -37160.0, 'D': 5520.0, 'l6': 7560.0, 'M0': 21150.0, 'S': 17020.0, 'm3': 102830.0, 'M2': -1480.0, 'n': 21250.0, 'R': -53130.0, 'M5': 17520.0, 'm1': 95530.0, 'M7': 18650.0, 'z0': 71550.0, 'a2': -38570.0, 'c2': -44000.0, 'l3': 29270.0, 'm0': -63490.0, 'l5': 9490.0, 'x0': 33010.0, 'a3': -42060.0, 'a4': -88140.0, 'a1': -68760.0, 'z1': 150.0, 'c3': 72190.0, 'c1': 4150.0, 'W': 11830.0, 'm2': 15760.0, 'c0': -40290.0, 'c6': 109120.0, 'M1': 49170.0, 'a5': -42030.0, 'c4': -14060.0, 'g': 40.0, 'M3': 280.0, 'F': -9590.0}})
+PAR.update({'av': (), 'mv': ('pppp', 'ppsp', 'ppvv', 'vvss'), 'xv': ((0, 2), (1, 0), (1, 2)), 'zv': ((1, 0), (1, 1), (1, 3)), 'duv': (), 'tv': (), 'vv': (0, 1, 2), 'half': ((0, 192), (192, 384)), 'z': ('pp', 'pg', 'pg'), 'down': 'turn', 'kq': 'y', 'ttg': 2.0, 'g': 1.56, 'dl': 1300.0, 'ov': 20.0, 'lat': 90.0, 'fly': 1400.0, 'rq': 300.0, 'dq': 200.0, 'far': 'X', 'xh': True, 'bias': {'k': 11450.0, 'M6': 75670.0, 'l2': 37200.0, 'M4': 56220.0, 'c7': 12470.0, 'l1': 46350.0, '': 1650.0, 'x1': 7070.0, 'Z': -36540.0, 'l4': 57440.0, 'c5': -47760.0, 'V': 44630.0, 'a7': 27300.0, 'l7': 14130.0, 'T': -19010.0, 'a6': -35950.0, 'D': 6610.0, 'l6': 46070.0, 'M0': 12930.0, 'S': 14250.0, 'm3': 54510.0, 'M2': 4250.0, 'n': 11880.0, 'R': -58950.0, 'M5': 9700.0, 'm1': 155810.0, 'M7': 14590.0, 'z0': 80910.0, 'a2': -52710.0, 'c2': -8120.0, 'l3': 83250.0, 'm0': -53990.0, 'l5': 3430.0, 'x0': 89050.0, 'a3': -58770.0, 'a4': -69060.0, 'a1': -103920.0, 'z1': 190.0, 'c3': 39720.0, 'c1': -60340.0, 'W': 22380.0, 'm2': -5820.0, 'c0': -77950.0, 'c6': 97550.0, 'M1': 95260.0, 'a5': -133440.0, 'c4': 23460.0, 'g': 510.0, 'M3': -220.0, 'F': -37140.0}})
+PAR.update({'av': (), 'mv': ('ppsp', 'pppp', 'pspp', 'vvsp'), 'xv': ((0, 2), (1, 2)), 'zv': ((1, 1), (1, 3)), 'duv': (), 'tv': (1, 2), 'vv': (0, 1, 2), 'half': ((0, 192), (192, 384)), 'z': ('pp', 'pg', 'pg'), 'down': 'mm', 'kq': 'y', 'ttg': 2.0, 'g': 1.56, 'dl': 1100.0, 'ov': 8.0, 'lat': 70.0, 'fly': 1100.0, 'rq': 800.0, 'dq': 110.0, 'far': 'W', 'xh': True, 'bias': {'z0': 340.0, 'a3': -980.0, 'T': 3050.0, 'c6': 3220.0, 'W': 2440.0, 'l3': 6000, 'M2': 180.0, 'c7': -1560.0, 'a2': -3610.0, 'c4': 4170.0, 'c0': 3180.0, 'M6': 580.0, 'S': -480.0, 'D': -1680.0, 'M4': 10.0, 'l1': -880.0, 'V': 6000, 'l5': -390.0, 'a6': -1100.0, 'm3': -120.0, 'm0': -2750.0, 'l4': -1030.0, 'M5': 2350.0, 'l2': -370.0, 'F': -2970.0, 'c2': -2140.0, 'x0': -2810.0, '': 490.0, 'a1': 440.0, 'M3': -1240.0, 'l7': 1140.0, 'x1': -4850.0, 'k': 1230.0, 'c3': -940.0, 'a4': -40.0, 'Z': -480.0, 'M1': 2200.0, 'a5': 2400.0, 'z1': 240.0, 'c5': 2590.0, 'g': 150.0, 'a7': -650.0, 'R': -840.0, 'n': -1760.0, 'm1': -4730.0, 'c1': 5160.0, 'M7': 2020.0, 'm2': -3060.0, 'M0': -1950.0, 'l6': -60.0}})
+PAR.update({'av': (), 'mv': ('ssss', 'pppp', 'pppp', 'vvsp'), 'xv': ((0, 2), (1, 2)), 'zv': ((1, 1), (1, 2)), 'duv': (), 'tv': (0, 3), 'vv': (0, 1, 2), 'z': ('pg', 'pg', 'pg'), 'bias': {'z0': -1770.0, 'a3': 4050.0, 'T': 1770.0, 'c6': -420.0, 'W': -1900.0, 'l3': -2010.0, 'M2': -3560.0, 'c7': -3640.0, 'a2': 1940.0, 'c4': -1930.0, 'c0': -60.0, 'M6': 2530.0, 'S': 5890.0, 'D': -1350.0, 'M4': -990.0, 'l1': -420.0, 'V': -2790.0, 'l5': 3220.0, 'a6': -4880.0, 'm3': 5160.0, 'm0': -6000, 'l4': 1880.0, 'M5': -3620.0, 'l2': 2440.0, 'F': 3100.0, 'c2': 3090.0, 'x0': -5960.0, '': -2010.0, 'a1': 790.0, 'M3': -1040.0, 'l7': -2580.0, 'x1': -2960.0, 'k': 1140.0, 'c3': 1420.0, 'a4': 2920.0, 'Z': -1110.0, 'M1': 1130.0, 'a5': 1280.0, 'z1': -2240.0, 'c5': -4160.0, 'g': -40.0, 'a7': -950.0, 'R': 2240.0, 'n': 600.0, 'm1': -5740.0, 'c1': 5230.0, 'M7': -2710.0, 'm2': -2000.0, 'M0': 3220.0, 'l6': -610.0}})
+PAR.update({'av': (), 'mv': ('pspp', 'pppp', 'vsvs', 'vsss'), 'xv': ((1, 0), (1, 1)), 'zv': (), 'duv': (), 'tv': (0, 3), 'vv': (0, 1), 'half': ((0, 192), (192, 384)), 'z': ('gg', 'gg', 'gg'), 'down': 'mm', 'kq': 'y', 'ttg': 1.6, 'g': 1.56, 'dl': 900.0, 'ov': 0.0, 'lat': 180.0, 'fly': 400.0, 'rq': 500.0, 'dq': 120.0, 'ld': 600.0, 'far': 'W', 'xh': True, 'bias': {'x0': -2670.0, 'z0': 3030.0, 'a5': 1760.0, 'k': 3220.0, 'm3': 2710.0, 'l4': 2090.0, 'S': 660.0, 'z1': 240.0, 'M3': 2100.0, 'm2': 1410.0, 'l3': 130.0, 'M6': 1820.0, 'c0': 2780.0, 'D': -2360.0, 'M4': -400.0, 'T0': -3960.0, 'm1': 2470.0, 'M7': 3330.0, 'c4': -240.0, 'l6': -570.0, 'g': -470.0, 'l2': 730.0, 'M5': 1130.0, 'a7': -60.0, 'b3': 1170.0, 'x1': -1440.0, 'F': 1450.0, '': -3420.0, 'n': 2120.0, 'l5': 1470.0, 'a4': -1800.0, 'W': -2120.0, 'a1': 2590.0, 'a2': -2090.0, 'c1': 2770.0, 'a3': 3040.0, 'V': -300.0, 'M1': -2220.0, 'a6': -1070.0, 'c6': 3060.0, 'c3': 3180.0, 'M0': 2770.0, 'c7': 330.0, 'c5': -1860.0, 'T': -2420.0, 'l7': 510.0, 'c2': -5550.0, 'm0': 340.0, 'M2': -770.0, 'R': 1580.0, 'l1': -430.0, 'T1': 3850.0, 'b7': -320.0}, 'bv': (3, 7), 'own': 30.0, 'tw': 85.0, 'tc': 0.67, 'xf': 800.0, 'vg': True, 'uv': ((0, 1), (1, 0), (1, 1))})
+PAR.update({'av': (), 'mv': ('pspp', 'psvv', 'vppp', 'vsvs'), 'xv': ((0, 1), (0, 2), (1, 1), (1, 2)), 'zv': (), 'duv': (), 'tv': (0, 3), 'vv': (0, 1), 'half': ((0, 256), (256, 384)), 'z': ('gg', 'gg', 'gg'), 'down': 'turn', 'kq': 'y', 'ttg': 1.6, 'g': 1.56, 'dl': 1100.0, 'ov': 0.0, 'lat': 190.0, 'fly': 450.0, 'rq': 450.0, 'dq': 140.0, 'ld': 600.0, 'far': 'W', 'xh': True, 'bias': {'k': 1620.0, 'M6': -1200.0, 'a5': 2040.0, 'l1': -1650.0, 'n': 3910.0, 'l5': 3250.0, 'S': -3630.0, 'M3': -2290.0, 'm3': -1640.0, 'l4': 3930.0, 'a3': -2750.0, 'F': -3770.0, 'V': 1830.0, 'g': -350.0, 'c1': 990.0, 'M2': -90.0, 'D': -790.0, 'M4': 5500.0, 'T0': -230.0, 'M7': 1090.0, 'c5': -2910.0, 'l7': 3140.0, 'm2': -3880.0, 'l3': 1300.0, 'M5': 5270.0, '': 3490.0, 'x0': -3640.0, 'W': -2110.0, 'a1': 1270.0, 'a2': 650.0, 'c2': 410.0, 'M1': -2080.0, 'a4': -2700.0, 'c7': -2290.0, 'z0': 770.0, 'c4': 5930.0, 'c6': 1020.0, 'a6': 3410.0, 'T': -2270.0, 'T1': 1450.0, 'R': -2120.0, 'l6': 890.0, 'm1': -3660.0, 'x1': -220.0, 'a7': -70.0, 'm0': -820.0, 'c3': 380.0, 'z1': -120.0, 'l2': -2320.0, 'M0': -160.0, 'c0': 4140.0}, 'bv': (), 'own': 240.0, 'tw': 40.0, 'tc': 0.55, 'xf': 800.0, 'vg': True, 'uv': ((0, 0), (1, 0), (1, 1), (1, 2))})
+PAR.update({'mv': ('vvps', 'psps', 'pspp', 'vsvs'), 'bias': {'k': 1000.0, 'M6': -200.0, 'a5': 2930.0, 'l1': -1750.0, 'n': 2660.0, 'l5': 1330.0, 'S': -1750.0, 'M3': -2460.0, 'm3': -690.0, 'l4': 4160.0, 'a3': -3070.0, 'F': -3810.0, 'V': 2840.0, 'g': -150.0, 'c1': 890.0, 'M2': -2290.0, 'D': 1560.0, 'M4': 6000, 'T0': -80.0, 'M7': 1090.0, 'c5': 110.0, 'l7': 1880.0, 'm2': -3460.0, 'l3': 1370.0, 'M5': 6000, '': 3490.0, 'x0': -3970.0, 'W': -580.0, 'a1': -740.0, 'a2': -2140.0, 'c2': 450.0, 'M1': -1330.0, 'a4': -2700.0, 'c7': -590.0, 'z0': 730.0, 'c4': 4120.0, 'c6': 1010.0, 'a6': 2460.0, 'T': 1110.0, 'T1': 1450.0, 'R': -2120.0, 'l6': 1480.0, 'm1': -1700.0, 'x1': -520.0, 'a7': -70.0, 'm0': -3770.0, 'c3': 960.0, 'z1': -120.0, 'l2': -2320.0, 'M0': -160.0, 'c0': 2230.0}})
 
 
 def _sb(n, d):
@@ -15,32 +25,36 @@ CODE, PL, BF, F32, U16, I32 = "float8_e4m3fn_x4", "uint8", "bfloat16", "float32"
 SCRATCH = {
     "xin": _sb(4 * C, BF), "uin": _sb(512, BF), "vin": _sb(512, BF),
     "wq": _sb(512, CODE), "wz": _sb(512, PL), "vq": _sb(128, CODE), "vz": _sb(128, PL),
-    "c32": _sb(128, BF), "eye": _sb(128, BF), "pidx": _sb(1, I32), "pi2": _sb(6, I32), "pf": _sb(8, F32),
+    "c32": _sb(128, BF), "eye": _sb(128, BF), "pidx": _sb(1, I32), "pi2": _sb(8, I32), "pf": _sb(10, F32),
     "ef": _sb(520, BF), "ee": _sb(520, BF), "eo": _sb(520, BF),
     "efq": _sb(512, CODE), "efz": _sb(512, PL), "eeq": _sb(512, CODE), "eez": _sb(512, PL),
     "eoq": _sb(512, CODE), "eoz": _sb(512, PL),
     "cap": _sb(C, F32), "st": _sb(C, F32), "ex": _sb(C, F32), "nr": _sb(C, BF), "tr": _sb(1024, BF),
-    "kd": ("sbuf", [128, 2, 2, 16], BF), "ko": _sb(64, BF), "kf": ("sbuf", [128, 2, 2, 16], F32),
-    "n32": _sb(32, F32), "nd": ("sbuf", [128, 2, 2, 16], F32), "no": _sb(64, F32),
+    "kd": ("sbuf", [128, 2, 2, 2, 16], BF), "ko": _sb(128, BF), "ct": ("sbuf", [128, 2, 2, 16], BF), "it8": _sb(4, F32), "ordk": _sb(6, U16), "kf": ("sbuf", [128, 2, 2, 16], F32),
+    "n32": _sb(32, F32), "n64": ("sbuf", [128, 2, 32], F32), "npg": ("sbuf", [128, 2, 2, 16], F32), "nd": ("sbuf", [128, 2, 2, 16], F32), "no": _sb(64, F32),
     "cn": _sb(8, F32), "ca": _sb(8, F32), "sg": _sb(8, F32), "b0": _sb(1, F32), "ordn": _sb(2, U16),
-    "hist": _sb(9 * HW, F32), "ab": _sb(8 * C, BF), "al": _sb(8 * HW, BF), "bl": _sb(8 * C, BF), "nop": ("sbuf", [128, 2, 16], F32),
+    "hist": _sb(9 * HW, F32), "ab": _sb(8 * C, BF), "al": _sb(8 * HW, BF), "bl": _sb(8 * C, BF), "bv": _sb(8 * C, BF), "nop": ("sbuf", [128, 2, 16], F32),
     "th": _sb(4 * C, BF), "du": _sb(512, BF),
     "zt": _sb(4 * C, BF), "xt": _sb(4 * C, BF), "vt": _sb(512, BF), "yt": _sb(C, F32),
     "xq0": _sb(C, CODE), "xz0": _sb(C, PL), "uq0": _sb(128, CODE), "uz0": _sb(128, PL),
-    "zq": _sb(C, CODE), "zz": _sb(C, PL), "ok": _sb(24, U16)}
+    "zq": _sb(C, CODE), "zz": _sb(C, PL), "ok": _sb(96, U16)}
 for _h in (1, 2, 3):
     SCRATCH.update({
-        "xq%d" % _h: _sb(C, CODE), "xz%d" % _h: _sb(C, PL), "uq%d" % _h: _sb(128, CODE), "uz%d" % _h: _sb(128, PL),
+        "aq%d" % _h: _sb(C, CODE), "az%d" % _h: _sb(C, PL), "an%d" % _h: _sb(16, U16),
+        "aeq%d" % _h: _sb(C, CODE), "aez%d" % _h: _sb(C, PL), "aoq%d" % _h: _sb(C, CODE), "aoz%d" % _h: _sb(C, PL),
+        "xq%d" % _h: _sb(C, CODE), "xz%d" % _h: _sb(C, PL), "uq%d" % _h: _sb(128, CODE), "uz%d" % _h: _sb(512, PL),
         "veq%d" % _h: _sb(128, CODE), "vez%d" % _h: _sb(128, PL), "voq%d" % _h: _sb(128, CODE), "voz%d" % _h: _sb(128, PL),
-        "sq%d" % _h: _sb(128, CODE), "sz%d" % _h: _sb(128, PL), "on%d" % _h: _sb(16, U16)})
+        "sq%d" % _h: _sb(128, CODE), "sz%d" % _h: _sb(512, PL), "on%d" % _h: _sb(16, U16)})
 for _b in range(8):
     SCRATCH["p%d" % _b] = ("psum", [128, 512], F32)
 
-SEMAPHORES = (["cv", "cs", "ct", "cp", "sent", "rc1", "rc2", "rc3", "outy", "outs"] + ["d%d" % i for i in range(60)])
+SEMAPHORES = (["cv", "cs", "ct", "cp", "sent", "rc1", "rc2", "rc3", "outy", "outs"] + ["d%d" % i for i in range(12)]
+              + ["m%d%d" % (h, i) for h in (1, 2, 3) for i in range(4)] + ["k1", "k2", "k3"]
+              + ["%s%d%d" % (n, h, i) for n in "qz" for h in (1, 2, 3) for i in range(2)])
 CYC = 0.83
 
 
-def lay_out(calls):
+def lay_out(calls, ways_only=False):
     lat = PAR["lat"]
     lastw, readers, lastp = {}, {}, {}
     for i, c in enumerate(calls):
@@ -68,9 +82,21 @@ def lay_out(calls):
     for i, c in enumerate(calls):
         for j in c["hard"] | c["soft"]:
             calls[j]["next"].append(i)
+    for i, c in enumerate(calls):
+        c["gap"] = {}
+        for j in c["next"]:
+            d = calls[j]
+            if i not in d["hard"]:
+                c["gap"][j] = 0.0
+            elif c["q"] == d["q"] and not c["late"] and PAR["own"] is not None:
+                c["gap"][j] = PAR["own"] + (PAR["tw"] if c["q"] == "t" else 0.0)
+            else:
+                c["gap"][j] = lat + c["late"] + (PAR["tw"] if "t" in (c["q"], d["q"]) else 0.0)
     for i in range(len(calls) - 1, -1, -1):
         c = calls[i]
-        c["way"] = c["ns"] + max([0.0] + [calls[j]["way"] + (lat + c["late"] if i in calls[j]["hard"] else 0.0) for j in c["next"]])
+        c["way"] = c["ns"] + max([0.0] + [calls[j]["way"] + c["gap"][j] for j in c["next"]])
+    if ways_only:
+        return []
     free, left, order = {}, [len(c["hard"] | c["soft"]) for c in calls], []
     ready = [i for i in range(len(calls)) if left[i] == 0]
     for c in calls:
@@ -85,7 +111,7 @@ def lay_out(calls):
         free[c["q"]] = now + c["ns"]
         for j in c["next"]:
             d = calls[j]
-            d["at"] = max(d["at"], now + c["ns"] + (lat + c["late"] if i in d["hard"] else 0.0))
+            d["at"] = max(d["at"], now + c["ns"] + c["gap"][j])
             left[j] -= 1
             if left[j] == 0:
                 ready.append(j)
@@ -104,15 +130,21 @@ def rank_program(g, core, T, topo):
     def op(qn, f, r, w, n, tag="", late=0.0, kind="op", sem=None):
         calls.append({"q": qn, "f": f, "r": list(r), "w": list(w), "ns": n, "tag": tag, "late": late, "kind": kind, "sem": sem})
 
+    def plane(z, a, b):
+        if PAR["far"] == "W" and z in ("efz", "wz", "vz"):
+            at = {"efz": 0, "wz": 512, "vz": 1024}[z] + a
+            return T["sz%d" % (1 + at // 384)][:, 128 + at % 384:128 + at % 384 + b - a]
+        return T[z][:, a:b]
+
     def cy(n):
-        return max(64.0, n) * CYC
+        return max(64.0, n) * CYC + PAR["ov"]
 
     def dma(qn, out, in_, r, w, sem=None, tag=""):
-        op(qn, lambda: queues[qn].dma_start(out, in_), r, w, 60.0, tag, 1800.0, "dma", sem)
+        op(qn, lambda: queues[qn].dma_start(out, in_), r, w, PAR["dq"], tag, PAR["dl"] + (0.0 if r else PAR["ld"]), "dma", sem)
 
     def mm(bank, lq, lz, a, rq, rz, c, d, keys, start, stop, tag=""):
-        op("t", lambda: t.matmul_mx(P[bank][:, 0:d - c], T[lq][:, a:a + 128], T[lz][:, a:a + 128], T[rq][:, c:d], T[rz][:, c:d], start, stop),
-           keys, ["p%d" % bank], (d - c + 16) * 0.6, tag)
+        op("t", lambda: t.matmul_mx(P[bank][:, 0:d - c], T[lq][:, a:a + 128], plane(lz, a, a + 128), T[rq][:, c:d], T[rz][:, c:d], start, stop),
+           keys, ["p%d" % bank], (d - c + 16) * PAR["tc"], tag)
 
     def cp(qn, out, in_, r, w, n, scale=None, tag=""):
         if qn == "v":
@@ -133,7 +165,7 @@ def rank_program(g, core, T, topo):
         op("v", lambda: v.memset(ap, c), [], w, cy(n))
 
     def quant(q, z, a, b, src, r, w, tag=""):
-        op("v", lambda: v.quantize_mx(T[q][:, a:b], T[z][:, a:b], src), r, w, 12 + 0.88 * (b - a), tag)
+        op("v", lambda: v.quantize_mx(T[q][:, a:b], plane(z, a, b), src), r, w, 12 + 0.88 * (b - a), tag)
 
     def scan(out, d0, d1, first, o0, o1, r, w, n, tag=""):
         op("v", lambda: v.tensor_tensor_scan(out, d0, d1, first, o0, o1), r, w, cy(n), tag)
@@ -145,14 +177,15 @@ def rank_program(g, core, T, topo):
         op("s", lambda: s.activation(out, in_, f, **k), r, w, cy(n) + (20 if "accum_out" in k else 0), tag)
 
     def picked(n):
-        return 55 + 1.3 * CYC * n
+        return 55 + PAR["g"] * CYC * n
 
     dma("y", T.uin[:], T.u[:], [], ["uin"])
     dma("s", T.xin[:, 0:512], T.x[:, 0:512], [], ["xin0"])
     dma("y", T.xin[:, 512:1024], T.x[:, 512:1024], [], ["xin1"])
     dma("s", T.xin[:, 1024:1536], T.x[:, 1024:1536], [], ["xin2"])
     dma("y", T.wq[:].bitcast(dt.uint8), T.wc[:], ["xin1"][:0], ["wq"])
-    dma("y", T.wz[:], T.ws[:], [], ["wz"])
+    for i in range(2):
+        dma("y", plane("wz", 256 * i, 256 * i + 256), T.ws[:, 256 * i:256 * i + 256], [], ["wz%d" % i])
     dma("y", T.vin[:], T.v[:], [], ["vin"])
 
     fill(T.c32[:], 32.0, ["c32"], 64)
@@ -160,36 +193,46 @@ def rank_program(g, core, T, topo):
     op("p", lambda: g.iota(T.pidx[:], [[0, 1]], 0, 1), [], ["pidx"], 135)
     fill(T.ef[:], 0.0, ["ef"], 260)
     cp("v", T.ef[:, 3:515:4], T.eye[:], ["eye", "ef"], ["ef"], 64)
-    for i, (b, sh) in enumerate(((16, 0), (-16, 0), (1, 0), (6, 0), (8, 3), (-32, 0))):
-        b = b % 128
+    for i, (b, sh) in enumerate(((16, 0), (112, 0), (1, 0), (6, 0), (8, 3), (96, 0), (15, 1))):
         if sh:
             ts(T.pi2[:, i:i + 1], T.pidx[:], b, sh, A.bitwise_and, A.logical_shift_right, ["pidx"], ["i%d" % i])
         else:
             ts(T.pi2[:, i:i + 1], T.pidx[:], b, None, A.bitwise_and, None, ["pidx"], ["i%d" % i])
-    for i, (k, m, c) in enumerate(((0, -0.0625, 1.0), (0, 0.0625, 0.0), (1, 1.0, 15.0), (5, 1.0, 15.0), (5, 1.0, 31.0), (2, 32.0, 0.0), (4, 1.0, 0.0))):
+    for i, (k, m, c) in enumerate(((0, -0.0625, 1.0), (0, 0.0625, 0.0), (5, 1.0, 15.0), (5, 1.0, 31.0), (1, 1.0, 15.0), (2, 32.0, 0.0), (4, 1.0, 0.0),
+                                   (6, 1.0, 0.0), (0, 4.0, 0.0))):
         ts(T.pf[:, i:i + 1], T.pi2[:, k:k + 1], m, c, A.mult, A.add, ["i%d" % k], ["pf%d" % i])
     ts(T.ordn[:, 0:1], T.pi2[:, 3:4], T.pf[:, 5:6], T.pf[:, 6:7], A.add, A.add, ["i3", "pf5", "pf6"], ["ordn"])
-    act(T.ee[:], T.ef[:], F.Copy, ["ef", "pf0"], ["ee"], 520, scale=T.pf[:, 0:1])
-    act(T.eo[:], T.ef[:], F.Copy, ["ef", "pf1"], ["eo"], 520, scale=T.pf[:, 1:2])
+    op("p", lambda: g.iota(T.it8[:], [[64, 2], [8, 2]], 0, 0, allow_small_or_imprecise_dtypes=True), [], ["it8"], 140)
+    ts(T.ordk[:, 0:4], T.it8[:], T.pf[:, 5:6], T.pf[:, 7:8], A.add, A.add, ["it8", "pf5", "pf7"], ["ordk0", "ordk1"])
+    twice = PAR["down"] == "mm" or any("p" in z for z in PAR["z"])
+    if any("g" in z for z in PAR["z"]) and twice:
+        ts(T.ordk[:, 4:6], T.ordk[:, 0:2], T.pf[:, 8:9], None, A.add, None, ["ordk0", "pf8"], ["ordk2"])
+    pairs = not PAR["vg"] or any("p" in z for z in PAR["z"])
+    if pairs:
+        act(T.ee[:], T.ef[:], F.Copy, ["ef", "pf0"], ["ee"], 520, scale=T.pf[:, 0:1])
+        act(T.eo[:], T.ef[:], F.Copy, ["ef", "pf1"], ["eo"], 520, scale=T.pf[:, 1:2])
     act(T.cap[:], T.ef[:, 0:C], F.Copy, ["ef"], ["cap"], C, scale=0.0, bias=BIG)
     act(T.hist[:, 0:HW], T.ef[:, 0:HW], F.Copy, ["ef"], ["h0"], HW, scale=0.0, bias=BIG)
-    for e in "feo":
+    for e in "feo" if pairs else "f":
         for b in range(4):
             quant("e%sq" % e, "e%sz" % e, 128 * b, 128 * b + 128, T["e" + e][:, 3 - b:515 - b], ["e" + e], ["e%s%d" % (e, b)])
     quant("uq0", "uz0", 0, 128, T.uin[:], ["uin"], ["U0"])
     for i in range(3):
         quant("xq0", "xz0", 128 * i, 128 * i + 128, T.xin[:, 512 * i:512 * i + 512], ["xin%d" % i], ["X0%d" % i])
-    fill(T.ex[:, 0:1], -BIG, ["ex0"])
+    fill(T.ex[:, 0:C:128], -BIG, ["exz"])
     fill(T.tr[:, C + 15:1024:16], 0.0, ["trz"])
-    fill(T.n32[:, 8:32], 0.0, ["n32z"])
-    fill(T.sg[:, 7:8], 1.0, ["g7"])
+    fill(T.kd[:], 0.0, ["kdz"])
+    fill(T.n64[:] if PAR["vg"] else T.n32[:], 1.0, ["n32z"] + ["n32%d%d" % (G, a) for G in range(4) for a in range(4)])
     fill(T.hist[:, HW:9 * HW:HW], -BIG, ["hz"])
     fill(T.al[:, 1:8 * HW:HW], 1.0, ["alz"])
     op("v", lambda: v.memset(T.cap[:, 0:C:16], -BIG), ["cap"], ["cap"], cy(1))
     HALF = PAR["half"]
     SV, SS = 0, 1
-    TB, DB, VB = (4, 5, 0, 1), (6, 7, 2, 3), (6, 7, 2, 3)
-    RB = ((4, 5, 6, 7), (2, 3, 4, 5))
+    turnb = [0]
+
+    def banks(n):
+        turnb[0] += n
+        return [2 + (turnb[0] - n + i) % 6 for i in range(n)]
 
     def hv(k):
         return T.hist[:, HW * (k + 1) + C:HW * (k + 1) + C + 1]
@@ -200,31 +243,65 @@ def rank_program(g, core, T, topo):
     def one_round(rd):
         xq, xz, uq, uz = "xq%d" % (rd - 1), "xz%d" % (rd - 1), "uq%d" % (rd - 1), "uz%d" % (rd - 1)
         nq, nz, on = "xq%d" % rd, "xz%d" % rd, "on%d" % rd
-        uk, nk = ["U%d" % (rd - 1)], ["X%d%d" % (rd, h) for h in range(len(HALF))]
+        uk, nk = ["U%d" % (rd - 1), "Uz%d" % (rd - 1)], ["X%d%d" % (rd, h) for h in range(len(HALF))]
         xk = ["X%d%d" % (rd - 1, h) for h in range(3 if rd == 1 else len(HALF))]
-        def own(banks, behind):
-            for b in range(4):
-                mm(banks[b], "efq", "efz", 128 * b, xq, xz, 0, C, xk + ["ef%d" % b] + behind, True, True, "T")
-                cp("v" if b in PAR["tv"] and rd > 1 else "s", sl("th", b), P[banks[b]][:, 0:C], ["p%d" % banks[b]], ["th%d" % b], C, 1.0 / 64, "T")
-        if rd > 1:
-            own(TB, ["vt1"])
+        ZM = PAR["z"][rd - 1]
+        gath = [HALF[h] for h in range(len(HALF)) if ZM[h] == "g"]
+        behind = ["S"] if rd == 1 else ["vt1"] if PAR["far"] != "X" else []
+
+        def own():
+            c, d = gath[0][0], gath[-1][1]
+            for b, bank in enumerate(banks(4)):
+                mm(bank, "efq", "efz", 128 * b, xq, xz, c, d, xk + ["ef%d" % b] + behind, True, True, "T")
+                cp("v" if b in PAR["tv"] and rd > 1 else "s", T.th[:, C * b + c:C * b + d], P[bank][:, 0:d - c], ["p%d" % bank],
+                   ["th%d%d" % (h, b) for h in range(len(HALF))], d - c, 1.0 / 64, "T")
+        if rd > 1 and gath and not PAR["vg"]:
+            own()
         for b in (SV, SS):
             mm(b, uq, uz, 0, xq, xz, 0, C, uk + xk, True, True, "S")
             calls[-1]["w"].append("S")
-        for b in range(4):
-            mm(DB[b], "efq", "efz", 128 * b, uq, uz, 0, 128, uk + ["ef%d" % b], True, True, "D")
-            cp("v" if b in PAR["duv"] else "s", T.du[:, 128 * b:128 * b + 128], P[DB[b]][:, 0:128], ["p%d" % DB[b]], ["du%d" % b], 128, 1.0 / 64, "D")
-        if rd == 1:
-            own((4, 5, 6, 7), ["S"])
-        turn(T.st[:], P[SV][:, 0:C], ["p%d" % SV], ["st"], C, "k")
-        scan(T.ex[:, 1:C], T.st[:, 0:C - 1], T.cap[:, 1:C], -BIG, A.max, A.min, ["st", "cap"], ["ex"], C, "k")
-        op("v", lambda: v.tensor_tensor(T.nr[:], T.st[:], T.ex[:], A.is_le), ["st", "ex", "ex0"], ["nr"], cy(2 * C), "k")
-        scan(T.tr[:, 0:C], T.nr[:], T.nr[:], 0.0, A.mult, A.add, ["nr"], ["tr"], C / 2, "k")
-        for h in range(2):
-            turn(T.kd[:, :, h, :], T.tr[:, 15 + 16 * h:1024:32], ["tr", "trz"], ["kd%d" % h], 1, "k")
-        turn(T.ko[:], T.kd[:], ["kd0", "kd1"], ["ko"], 1, "k")
-        for h in range(2):
-            ts(T.ok[:, h:24:2], T.ko[:, 32 * h:32 * h + 12], -1.0, T.pf[:, 2:3], A.mult, A.add, ["ko", "pf2"], ["ok%d" % h], 1, "k")
+        if PAR["down"] == "mm":
+            SB = banks(3)
+            for j in range(3):
+                mm(SB[j], xq, xz, 128 * j, uq, uz, 0, 128, uk + xk, True, True, "S")
+        if PAR["down"] == "mm":
+            for j in range(3):
+                scan(T.ex[:, 128 * j + 1:128 * j + 128], P[SB[j]][:, 0:127], T.cap[:, 1:128], -BIG, A.max, A.min, ["p%d" % SB[j], "cap"], ["ex%d" % j], 128, "k")
+                op("v", lambda j=j: v.tensor_tensor(T.nr[:, 128 * j:128 * j + 128], P[SB[j]][:, 0:128], T.ex[:, 128 * j:128 * j + 128], A.is_le),
+                   ["p%d" % SB[j], "ex%d" % j, "exz"], ["nr%d" % j], cy(128), "k")
+            scan(T.tr[:, 0:C], T.nr[:], T.nr[:], 0.0, A.mult, A.add, ["nr0", "nr1", "nr2"], ["tr"], C / 2, "k")
+            for i in range(2):
+                turn(T.ct[:, :, i, :], T.tr[:, 15:512:16], ["tr", "trz"], ["ct%d" % i], 1, "k")
+            for a in range(4):
+                for j in range(3):
+                    dma(PAR["kq"][(3 * a + j) % len(PAR["kq"])], T.kd[4 * j + a:128:32], T.ct[32 * a + 8 * j:32 * a + 8 * j + 8], ["ct0", "ct1", "kdz"], ["kd%d%d" % (a, j)], "k%d" % rd, "k")
+            kdk = ["kd%d%d" % (a, j) for a in range(4) for j in range(3)]
+        else:
+            turn(T.st[:], P[SV][:, 0:C], ["p%d" % SV], ["st"], C, "k")
+            scan(T.ex[:, 1:C], T.st[:, 0:C - 1], T.cap[:, 1:C], -BIG, A.max, A.min, ["st", "cap"], ["ex"], C, "k")
+            op("v", lambda: v.tensor_tensor(T.nr[:], T.st[:], T.ex[:], A.is_le), ["st", "ex", "exz"], ["nr"], cy(2 * C), "k")
+            scan(T.tr[:, 0:C], T.nr[:], T.nr[:], 0.0, A.mult, A.add, ["nr"], ["tr"], C / 2, "k")
+            kdk = []
+            for h in range(2):
+                for i in range(2) if twice else (h,):
+                    turn(T.kd[:, h if twice else 0, :, i, :], T.tr[:, 15 + 16 * h:1024:32], ["tr", "trz", "kdz"], ["kd%d%d" % (h, i)], 1, "k")
+                    kdk.append("kd%d%d" % (h, i))
+        if gath:
+            for b, bank in enumerate(banks(4)):
+                mm(bank, "efq", "efz", 128 * b, uq, uz, 0, 128, uk + ["ef%d" % b], True, True, "D")
+                cp("v" if b in PAR["duv"] else "s", T.du[:, 128 * b:128 * b + 128], P[bank][:, 0:128], ["p%d" % bank], ["du%d" % b], 128, 1.0 / 64, "D")
+            if rd == 1:
+                own()
+        if twice:
+            turn(T.ko[:], T.kd[:], kdk, ["ko"], 1, "k")
+        else:
+            turn(T.ko[:, 0:64], T.kd[:, 0], kdk, ["ko"], 1, "k")
+            op("v", lambda: v.tensor_scalar(T.ok[:, 64:96], T.ko[:, 0:64].indirect(T.ordk[:, 0:2]), -1.0, T.pf[:, 4:5], A.mult, A.add),
+               ["ko", "pf4", "ordk0"], ["ok2"], picked(32), "k")
+        for h in range(3 if twice else 0):
+            if (h == 2 and gath) or (h < 2 and len(gath) < len(HALF)):
+                op("v", lambda h=h: v.tensor_scalar(T.ok[:, 32 * h:32 * h + 32], T.ko[:].indirect(T.ordk[:, 2 * h:2 * h + 2]), -1.0, T.pf[:, 2 + h:3 + h], A.mult, A.add),
+                   ["ko", "pf%d" % (2 + h), "ordk%d" % h], ["ok%d" % h], picked(32), "k")
         for k in range(8):
             scan(T.hist[:, HW * (k + 1) + 1:HW * (k + 1) + 1 + C], P[SV][:, 0:C], T.hist[:, HW * k:HW * k + C], -BIG, A.max, A.min,
                  ["p%d" % SV, "h%d" % k, "hz"], ["h%d" % (k + 1)], C, "M%d" % k)
@@ -242,77 +319,142 @@ def rank_program(g, core, T, topo):
                     ts(sl("ab", k), P[SV][:, 0:C], hv(k), None, A.not_equal, None, ["p%d" % SV, "h%d" % (k + 1)], ["a%d" % k], C, "a%d" % k)
                 else:
                     act(sl("ab", k), P[SS][:, 0:C], F.Abs, ["p%d" % SS, "h%d" % (k + 1)], ["a%d" % k], C, "a%d" % k, bias=hv(k), scale=-1.0)
-                scan(T.al[:, HW * k + 2:HW * k + 2 + C], sl("ab", k), sl("bl", k - 1), 1.0, A.min, A.max, ["a%d" % k, "bl%d" % (k - 1)], ["l%d" % k], C / 2, "l%d" % k)
-                act(out, T.al[:, HW * k + 1:HW * k + 1 + C], F.Sign, ["l%d" % k, "g%d" % k, "alz"], ["bl%d" % k, "c%d" % k], C, "c%d" % k,
-                    scale=T.sg[:, k:k + 1], accum_out=T.cn[:, k:k + 1])
+                bar = "bv" if k in PAR["bv"] else "bl"
+                if bar == "bv":
+                    ts(sl("bv", k - 1), T.al[:, HW * (k - 1) + 1:HW * (k - 1) + 1 + C], T.sg[:, k - 1:k], None, A.mult, None,
+                       ["l%d" % (k - 1), "g%d" % (k - 1), "alz"], ["bv%d" % (k - 1)], C / 2, "b%d" % k)
+                scan(T.al[:, HW * k + 2:HW * k + 2 + C], sl("ab", k), sl(bar, k - 1), 1.0, A.min, A.max, ["a%d" % k, bar + str(k - 1)], ["l%d" % k], C / 2, "l%d" % k)
+                if k + 1 in PAR["bv"] or k == 7:
+                    act(out, T.al[:, HW * k + 1:HW * k + 1 + C], F.Sign, ["l%d" % k, "alz"], ["bl%d" % k, "c%d" % k], C, "c%d" % k,
+                        accum_out=T.cn[:, k:k + 1] if k < 7 else T.ca[:, 7:8])
+                else:
+                    act(out, T.al[:, HW * k + 1:HW * k + 1 + C], F.Sign, ["l%d" % k, "g%d" % k, "alz"], ["bl%d" % k, "c%d" % k], C, "c%d" % k,
+                        scale=T.sg[:, k:k + 1], accum_out=T.cn[:, k:k + 1])
             if k % 2:
                 G, r = k // 2, ["c%d" % (k - 1), "c%d" % k]
-                whole = G in PAR["dma"] or PAR["vm"]
-                if whole:
+                plain = k == 7 or PAR["mv"][G] != "ssss"
+                if plain:
                     e = k + 1 if k < 7 else k
                     act(T.ca[:, k - 1:e], T.cn[:, k - 1:e], F.Abs, r[:e - k + 1], ["ca%d" % G], 1, "m%d" % G)
+                    r = ["ca%d" % G] + r[e - k + 1:]
                 for a in range(4):
-                    o, w = T.n32[32 * G:32 * G + 32, 2 * a:2 * a + 2], ["n32%d%d" % (G, a)]
-                    if G in PAR["dma"]:
-                        dma("y", o, T.ca[32 * a:32 * a + 32, k - 1:k + 1], ["ca%d" % G], w, None, "m%d" % G)
-                    elif a in PAR["vm"] and k < 7:
-                        cp("v", o, T.ca[32 * a:32 * a + 32, k - 1:k + 1], ["ca%d" % G], w, 1, None, "m%d" % G)
-                    elif a in PAR["vm"]:
-                        op("v", lambda o=o, a=a: v.tensor_tensor(o, T.cn[32 * a:32 * a + 32, 6:8], T.ca[32 * a:32 * a + 32, 6:8], A.max), r + ["ca3", "ca7"], w, cy(1), "m3")
+                    o = T.n64[32 * G:32 * G + 32, :, 2 * a] if PAR["vg"] else T.n32[32 * G:32 * G + 32, 2 * a:2 * a + 2]
+                    w, q = ["n32%d%d" % (G, a)], PAR["mv"][G][a]
+                    src = T["ca" if plain else "cn"][32 * a:32 * a + 32, k - 1:k + 1]
+                    if q == "y":
+                        dma("y", o, src, r, w, "m%d%d" % (rd, G), "m%d" % G)
+                    elif q == "p":
+                        op("p", lambda o=o, src=src: g.affine_select(o, src, [[0, 2]], A.is_ge, 0.0, 0, 0), r, w, 175.0, "m%d" % G)
+                    elif q == "v":
+                        cp("v", o, src, r, w, 1, None, "m%d" % G)
                     else:
-                        act(o, T.cn[32 * a:32 * a + 32, k - 1:k + 1], F.Abs, r, w, 1, "m%d" % G)
+                        act(o, src, F.Abs, r, w, 1, "m%d" % G)
         for i in range(2):
-            turn(T.nd[:, :, i, :], T.n32[:], ["n32z"] + ["n32%d%d" % (G, a) for G in range(4) for a in range(4)], ["nd%d" % i], 1, "n")
+            turn(T.nd[:, :, i, :], T.n64[:, i, :] if PAR["vg"] else T.n32[:], ["n32z"] + ["n32%d%d" % (G, a) for G in range(4) for a in range(4)], ["nd%d" % i], 1, "n")
         turn(T.no[:], T.nd[:], ["nd0", "nd1"], ["no"], 1, "n")
         op("v", lambda: v.tensor_scalar(T[on][:], T.no[:].indirect(T.ordn[:, 0:1]), -1.0, None, A.add), ["no", "ordn"], [on], picked(16), "n")
         for h, (c, d) in enumerate(HALF):
-            for b in range(4):
-                op("v", lambda b=b, c=c, d=d: v.tensor_tensor(T.zt[:, 4 * c + b:4 * d:4], T.du[:, 128 * b:128 * b + 128].indirect(T.ok[:, c // 16:d // 16]),
-                                                              T.th[:, C * b + c:C * b + d], A.add),
-                   ["du%d" % b, "th%d" % b, "ok0", "ok1"], ["zt%d%d" % (h, b)], picked(d - c), "z%d" % h)
+            if ZM[h] == "g":
+                for b in range(4):
+                    op("v", lambda b=b, c=c, d=d: v.tensor_tensor(T.zt[:, 4 * c + b:4 * d:4], T.du[:, 128 * b:128 * b + 128].indirect(T.ok[:, 64 + c // 16:64 + d // 16]),
+                                                                  T.th[:, C * b + c:C * b + d], A.add),
+                       ["du%d" % b, "th%d%d" % (h, b), "ok2"], ["zt%d%d" % (h, b)], 55 + PAR["ttg"] * CYC * (d - c), "z%d" % h)
+            else:
+                ZB = banks(4)
+                for b in range(4):
+                    mm(ZB[b], "efq", "efz", 128 * b, xq, xz, c, d, xk + ["ef%d" % b] + behind, True, False, "R")
+                for i, e in enumerate("eo"):
+                    dq, dz = "a%sq%d" % (e, rd), "a%sz%d" % (e, rd)
+                    off = T.ok[:, 32 * i + c // 16:32 * i + d // 16]
+                    op("v", lambda dq=dq, off=off, c=c, d=d: v.tensor_copy(T[dq][:, c:d].bitcast(dt.uint32), T[uq][:].bitcast(dt.uint32).indirect(off)),
+                       uk + ["ok%d" % i], [dq + str(h)], picked(d - c), "z%d" % h)
+                    op("s", lambda dz=dz, off=off, c=c, d=d: s.activation(T[dz][:, c:d], T[uz][:, 0:128].indirect(off), F.Copy), uk + ["ok%d" % i], [dz + str(h)], picked(d - c), "z%d" % h)
+                    for b in range(4):
+                        mm(ZB[b], "e%sq" % e, "e%sz" % e, 128 * b, dq, dz, c, d, [dq + str(h), dz + str(h), "e%s%d" % (e, b)], False, e == "o", "Z")
+                for b in range(4):
+                    cp("v" if (h, b) in PAR["zv"] else "s", T.zt[:, 4 * c + b:4 * d:4], P[ZB[b]][:, 0:d - c], ["p%d" % ZB[b]], ["zt%d%d" % (h, b)], d - c, 1.0 / 64, "z%d" % h)
             quant("zq", "zz", c, d, T.zt[:, 4 * c:4 * d], ["zt%d%d" % (h, b) for b in range(4)], ["Z%d" % h], "z%d" % h)
-            for b in range(4):
-                bank = RB[h % 2][b]
+        for h, (c, d) in enumerate(HALF):
+            for b, bank in enumerate(banks(4)):
                 mm(bank, "efq", "efz", 128 * b, xq, xz, c, d, xk + ["ef%d" % b], True, False, "R")
-                mm(bank, "wq", "wz", 128 * b, "zq", "zz", c, d, ["Z%d" % h, "wq", "wz"], False, True, "W")
+                mm(bank, "wq", "wz", 128 * b, "zq", "zz", c, d, ["Z%d" % h, "wq", "wz%d" % (b // 2)], False, True, "W")
                 cp("v" if (h, b) in PAR["xv"] else "s", T.xt[:, 4 * c + b:4 * d:4], P[bank][:, 0:d - c], ["p%d" % bank], ["xt%d%d" % (h, b)], d - c, 1.0 / 32, "x%d" % h)
             quant(nq, nz, c, d, T.xt[:, 4 * c:4 * d], ["xt%d%d" % (h, b) for b in range(4)], [nk[h]], "x%d" % h)
-        for i, e in enumerate("eo"):
-            dq, dz = "v%sq%d" % (e, rd), "v%sz%d" % (e, rd)
-            op("v", lambda dq=dq, i=i: v.tensor_copy(T[dq][:].bitcast(dt.uint32), T[nq][:].bitcast(dt.uint32).indirect(T[on][:, 8 * i:8 * i + 8])),
-               nk + [on], [dq], picked(128), "V")
-            op("s", lambda dz=dz, i=i: s.activation(T[dz][:], T[nz][:].indirect(T[on][:, 8 * i:8 * i + 8]), F.Copy), nk + [on], [dz], picked(128), "V")
-        for i, e in enumerate("eo"):
-            dq, dz = "v%sq%d" % (e, rd), "v%sz%d" % (e, rd)
-            for b in range(4):
-                mm(VB[b], "e%sq" % e, "e%sz" % e, 128 * b, dq, dz, 0, 128, [dq, dz, "e%s%d" % (e, b)], e == "e", e == "o", "V")
-        for b in range(4):
-            cp("v" if b in PAR["vv"] else "s", T.vt[:, b:512:4], P[VB[b]][:, 0:128], ["p%d" % VB[b]], ["vt%d" % b], 128, 1.0 / 32, "V")
-        quant("sq%d" % rd, "sz%d" % rd, 0, 128, T.vt[:], ["vt%d" % b for b in range(4)], ["out%d" % rd], "V")
+        for h, (c, d) in enumerate(HALF if PAR["vg"] else ()):
+            for b, bank in enumerate(banks(4)):
+                mm(bank, "efq", "efz", 128 * b, nq, nz, c, d, [nk[h], "ef%d" % b], True, True, "T%d" % h)
+                cp("v" if (h, b) in PAR["uv"] else "s", T.th[:, C * b + c:C * b + d], P[bank][:, 0:d - c], ["p%d" % bank], ["th%d%d" % (h, b)], d - c, 1.0 / 64, "T%d" % h)
         dst = T.cores[(rank + STEP[rd - 1]) % N]
         rid, pid, _ = topo.addr(dst)
         eng = topo.engines(core, dst)
-        half = len(eng) // 2
-        m1 = sum(1 << e for e in eng[:half])
-        m2 = sum(1 << e for e in eng[half:])
 
-        def hand_on():
-            g.remote_dma(T["uq%d" % rd][:].bitcast(dt.uint8), T["sq%d" % rd][:].bitcast(dt.uint8), T.sem["rc%d" % rd], T.sem["sent"], pid, rid, m1)
-            g.remote_dma(T["uz%d" % rd][:], T["sz%d" % rd][:], T.sem["rc%d" % rd], T.sem["sent"], pid, rid, m2)
-            return len(eng)
-        op("p", hand_on, ["out%d" % rd], ["U%d" % rd], 500.0, "", PAR["fly"], "far", "rc%d" % rd)
-        return nk
-
-    fill(T.ca[:, 7:8], 0.0, ["ca7"])
-    for rd in (1, 2, 3):
-        nk = one_round(rd)
+        def far(out, in_, sem, a, b, r, w, late, tag):
+            def f():
+                g.remote_dma(out, in_, T.sem[sem], T.sem["sent"], pid, rid, sum(1 << e for e in eng[a:b]))
+                return b - a
+            op("p", f, r, w, PAR["rq"], tag, late, "far", sem)
+        ne = len(eng)
+        wq, wz, wn, wk = nq, nz, on, nk + nk + [on]
+        if PAR["far"] == "X":
+            wq, wz, wn, wk = "aq%d" % rd, "az%d" % rd, "an%d" % rd, []
+            for h, (c, d) in enumerate(HALF if PAR["xh"] else ((0, C),)):
+                r = [nk[h]] if PAR["xh"] else nk
+                far(T[wq][:, c:d].bitcast(dt.uint8), T[nq][:, c:d].bitcast(dt.uint8), "q%d%d" % (rd, h), 0, ne, r, ["aq%d" % h], PAR["fly"] + 5.0 * (d - c), "F")
+                far(T[wz][:, c:d], T[nz][:, c:d], "z%d%d" % (rd, h), 0, ne, r, ["az%d" % h], PAR["fly"] + 1.5 * (d - c), "F")
+                wk += ["aq%d" % h, "az%d" % h]
+            far(T[wn][:], T[on][:], "rc%d" % rd, 0, ne, [on], ["an"], PAR["fly"], "F")
+            wk = wk + ["an"]
+        if PAR["vg"]:
+            for b in range(4):
+                src = T.th[:, C * b:C * b + C].indirect(T[on][:, 0:8])
+                r = ["th%d%d" % (h, b) for h in range(len(HALF))] + [on]
+                if b in PAR["vv"]:
+                    op("v", lambda b=b, src=src: v.tensor_scalar(T.vt[:, b:512:4], src, 2.0, None, A.mult), r, ["vt%d" % b], picked(128), "V")
+                else:
+                    op("s", lambda b=b, src=src: s.activation(T.vt[:, b:512:4], src, F.Copy, scale=2.0), r, ["vt%d" % b], picked(128), "V")
+        VB = [] if PAR["vg"] else banks(4)
+        for i, e in enumerate("" if PAR["vg"] else "eo"):
+            dq, dz = "v%sq%d" % (e, rd), "v%sz%d" % (e, rd)
+            op("v", lambda dq=dq, i=i: v.tensor_copy(T[dq][:].bitcast(dt.uint32), T[wq][:].bitcast(dt.uint32).indirect(T[wn][:, 8 * i:8 * i + 8])),
+               [k for k in wk if k[:2] != "az"], [dq], picked(128), "V")
+            op("s", lambda dz=dz, i=i: s.activation(T[dz][:], T[wz][:].indirect(T[wn][:, 8 * i:8 * i + 8]), F.Copy), [k for k in wk if k[:2] != "aq"], [dz], picked(128), "V")
+        for i, e in enumerate("" if PAR["vg"] else "eo"):
+            dq, dz = "v%sq%d" % (e, rd), "v%sz%d" % (e, rd)
+            for b in range(4):
+                mm(VB[b], "e%sq" % e, "e%sz" % e, 128 * b, dq, dz, 0, 128, [dq, dz, "e%s%d" % (e, b)], e == "e", e == "o", "V")
+        for b in range(len(VB)):
+            cp("v" if b in PAR["vv"] else "s", T.vt[:, b:512:4], P[VB[b]][:, 0:128], ["p%d" % VB[b]], ["vt%d" % b], 128, 1.0 / 32, "V")
+        if PAR["far"] == "X":
+            quant("uq%d" % rd, "uz%d" % rd, 0, 128, T.vt[:], ["vt%d" % b for b in range(4)], ["U%d" % rd, "Uz%d" % rd], "V")
+        else:
+            quant("sq%d" % rd, "sz%d" % rd, 0, 128, T.vt[:], ["vt%d" % b for b in range(4)], ["out%d" % rd], "V")
+            if PAR["far"] == "V":
+                far(T["uq%d" % rd][:].bitcast(dt.uint8), T["sq%d" % rd][:].bitcast(dt.uint8), "rc%d" % rd, 0, ne // 2, ["out%d" % rd], ["U%d" % rd], PAR["fly"] + 1000, "F")
+                far(T["uz%d" % rd][:, 0:128], T["sz%d" % rd][:, 0:128], "z%d0" % rd, ne // 2, ne, ["out%d" % rd], ["Uz%d" % rd], PAR["fly"] + 500, "F")
+            else:
+                def both():
+                    to = [DstId(rid=rid, pnc=pid)]
+                    g.remote_dma_fused([
+                        RemoteDMATransfer(dst_ids=to, dma_engine_mask=sum(1 << e for e in eng[:ne // 2]), remote_sem=T.sem["rc%d" % rd],
+                                          src=T["sq%d" % rd][:].bitcast(dt.uint8), dst=T["uq%d" % rd][:].bitcast(dt.uint8)),
+                        RemoteDMATransfer(dst_ids=to, dma_engine_mask=sum(1 << e for e in eng[ne // 2:]), remote_sem=T.sem["rc%d" % rd],
+                                          src=T["sz%d" % rd][:], dst=T["uz%d" % rd][:])], local_sem=T.sem["sent"])
+                    return ne
+                op("p", both, ["out%d" % rd] + (["ef0", "ef1", "ef2"], ["ef3", "wz0"], ["wz1", "vq"])[rd - 1], ["U%d" % rd, "Uz%d" % rd], PAR["rq"], "F", PAR["fly"] + PAR["xf"], "far", "rc%d" % rd)
+        return nk, kdk
 
     quant("vq", "vz", 0, 128, T.vin[:], ["vin"], ["vq"])
+    for rd in (1, 2, 3):
+        nk, kdk = one_round(rd)
+
     mm(SS, "vq", "vz", 0, "xq3", "xz3", 0, C, nk + ["vq"], True, True)
     cp("s", T.yt[:], P[SS][:, 0:C], ["p%d" % SS], ["yt"], C)
     for h in range(2):
-        ts(T.kf[:, :, h, :], T.kd[:, :, h, :], -1.0, T.pf[:, 3 + h:4 + h], A.mult, A.add, ["kd%d" % h, "pf%d" % (3 + h)], ["kf%d" % h])
-    ts(T.nop[:], T.nd[:, :, 0, :], -1.0, None, A.add, None, ["nd0"], ["nop"])
+        ts(T.kf[:, :, h, :], T.kd[:, h, :, 0, :] if twice else T.kd[:, 0, :, h, :], -1.0, T.pf[:, 2 + h:3 + h], A.mult, A.add, kdk + ["pf%d" % (2 + h)], ["kf%d" % h])
+    if PAR["vg"]:
+        ts(T.npg[:], T.nd[:], -1.0, None, A.add, None, ["nd0", "nd1"], ["nop"])
+    else:
+        ts(T.nop[:], T.nd[:, :, 0, :], -1.0, None, A.add, None, ["nd0"], ["nop"])
     dma("y", T.oc[:], T.xq3[:].bitcast(dt.uint8), nk, [], "outy")
     for k in range(4):
         dma("y", T.osc[4 * k:4 * k + 4, :], T.xz3[32 * k:32 * k + 4, :], nk, [], "outy")
@@ -322,10 +464,10 @@ def rank_program(g, core, T, topo):
     dma("s", T.y[:], T.yt[:], ["yt"], [], "outs")
     for a in range(4):
         for i in range(2):
-            dma("y", T.op[2 * a + i, C:C + 128], T.nop[32 * a + i:32 * a + 8:2, :, :], ["nop"], [], "outy")
+            dma("y", T.op[2 * a + i, C:C + 128], T.npg[32 * a:32 * a + 8:2, :, i, :] if PAR["vg"] else T.nop[32 * a + i:32 * a + 8:2, :, :], ["nop"], [], "outy")
     dma("s", T.uc[:], T.uq3[:].bitcast(dt.uint8), ["U3"], [], "outs")
     for k in range(4):
-        dma("y" if k % 2 == 0 else "s", T.usc[4 * k:4 * k + 4, :], T.uz3[32 * k:32 * k + 4, :], ["U3"], [], "outy" if k % 2 == 0 else "outs")
+        dma("y" if k % 2 == 0 else "s", T.usc[4 * k:4 * k + 4, :], T.uz3[32 * k:32 * k + 4, 0:128], ["Uz3"], [], "outy" if k % 2 == 0 else "outs")
 
     count, seen, nd = {}, {q: {} for q in queues}, [0]
     for i in lay_out(calls):

@@ -4,58 +4,46 @@ from concourse.mybir import dt, AluOpType as A, ActivationFunctionType as F
 N, C, STEP = 4, 384, (1, 2, 3)
 BIG = 1e29
 HW = 388
-PAR = {"av": (), "mv": ("yyyy", "yyyy", "pppp", "vvss"), "xv": (), "zv": (), "duv": (), "tv": (0, 1), "vv": (0, 2), "half": ((0, 192), (192, 384)),
-       "z": ("pp", "pp", "pp"), "down": "mm", "kq": "y", "ttg": 2.0, "g": 1.56, "dl": 1300.0, "ov": 20.0,
-       "lat": 90.0, "fly": 1400.0, "rq": 700.0, "dq": 200.0, "ld": 800.0, "far": "X", "xh": True, "bias": {},
-       "bv": (), "own": None, "tw": 0.0, "tc": 0.6, "xf": 1000.0, "vg": False, "uv": ()}
-PAR.update({'av': (), 'mv': ('pppp', 'ppsp', 'pvpp', 'vvss'), 'xv': ((0, 3), (1, 0), (1, 2)), 'zv': ((1, 0), (1, 1), (1, 2)), 'duv': (), 'tv': (), 'vv': (0, 2), 'half': ((0, 192), (192, 384)), 'z': ('pp', 'pg', 'pg'), 'down': 'mm', 'bias': {'k': 21260.0, 'M6': 54910.0, 'l2': 43530.0, 'M4': 60850.0, 'c7': 37180.0, 'l1': 61590.0, '': 910.0, 'x1': 4610.0, 'Z': -4950.0, 'l4': 45000.0, 'c5': -56700.0, 'V': 60990.0, 'a7': 31440.0, 'l7': 15560.0, 'T': 17360.0, 'a6': -37160.0, 'D': 5520.0, 'l6': 7560.0, 'M0': 21150.0, 'S': 17020.0, 'm3': 102830.0, 'M2': -1480.0, 'n': 21250.0, 'R': -53130.0, 'M5': 17520.0, 'm1': 95530.0, 'M7': 18650.0, 'z0': 71550.0, 'a2': -38570.0, 'c2': -44000.0, 'l3': 29270.0, 'm0': -63490.0, 'l5': 9490.0, 'x0': 33010.0, 'a3': -42060.0, 'a4': -88140.0, 'a1': -68760.0, 'z1': 150.0, 'c3': 72190.0, 'c1': 4150.0, 'W': 11830.0, 'm2': 15760.0, 'c0': -40290.0, 'c6': 109120.0, 'M1': 49170.0, 'a5': -42030.0, 'c4': -14060.0, 'g': 40.0, 'M3': 280.0, 'F': -9590.0}})
-PAR.update({'av': (), 'mv': ('pppp', 'ppsp', 'ppvv', 'vvss'), 'xv': ((0, 2), (1, 0), (1, 2)), 'zv': ((1, 0), (1, 1), (1, 3)), 'duv': (), 'tv': (), 'vv': (0, 1, 2), 'half': ((0, 192), (192, 384)), 'z': ('pp', 'pg', 'pg'), 'down': 'turn', 'kq': 'y', 'ttg': 2.0, 'g': 1.56, 'dl': 1300.0, 'ov': 20.0, 'lat': 90.0, 'fly': 1400.0, 'rq': 300.0, 'dq': 200.0, 'far': 'X', 'xh': True, 'bias': {'k': 11450.0, 'M6': 75670.0, 'l2': 37200.0, 'M4': 56220.0, 'c7': 12470.0, 'l1': 46350.0, '': 1650.0, 'x1': 7070.0, 'Z': -36540.0, 'l4': 57440.0, 'c5': -47760.0, 'V': 44630.0, 'a7': 27300.0, 'l7': 14130.0, 'T': -19010.0, 'a6': -35950.0, 'D': 6610.0, 'l6': 46070.0, 'M0': 12930.0, 'S': 14250.0, 'm3': 54510.0, 'M2': 4250.0, 'n': 11880.0, 'R': -58950.0, 'M5': 9700.0, 'm1': 155810.0, 'M7': 14590.0, 'z0': 80910.0, 'a2': -52710.0, 'c2': -8120.0, 'l3': 83250.0, 'm0': -53990.0, 'l5': 3430.0, 'x0': 89050.0, 'a3': -58770.0, 'a4': -69060.0, 'a1': -103920.0, 'z1': 190.0, 'c3': 39720.0, 'c1': -60340.0, 'W': 22380.0, 'm2': -5820.0, 'c0': -77950.0, 'c6': 97550.0, 'M1': 95260.0, 'a5': -133440.0, 'c4': 23460.0, 'g': 510.0, 'M3': -220.0, 'F': -37140.0}})
-PAR.update({'av': (), 'mv': ('ppsp', 'pppp', 'pspp', 'vvsp'), 'xv': ((0, 2), (1, 2)), 'zv': ((1, 1), (1, 3)), 'duv': (), 'tv': (1, 2), 'vv': (0, 1, 2), 'half': ((0, 192), (192, 384)), 'z': ('pp', 'pg', 'pg'), 'down': 'mm', 'kq': 'y', 'ttg': 2.0, 'g': 1.56, 'dl': 1100.0, 'ov': 8.0, 'lat': 70.0, 'fly': 1100.0, 'rq': 800.0, 'dq': 110.0, 'far': 'W', 'xh': True, 'bias': {'z0': 340.0, 'a3': -980.0, 'T': 3050.0, 'c6': 3220.0, 'W': 2440.0, 'l3': 6000, 'M2': 180.0, 'c7': -1560.0, 'a2': -3610.0, 'c4': 4170.0, 'c0': 3180.0, 'M6': 580.0, 'S': -480.0, 'D': -1680.0, 'M4': 10.0, 'l1': -880.0, 'V': 6000, 'l5': -390.0, 'a6': -1100.0, 'm3': -120.0, 'm0': -2750.0, 'l4': -1030.0, 'M5': 2350.0, 'l2': -370.0, 'F': -2970.0, 'c2': -2140.0, 'x0': -2810.0, '': 490.0, 'a1': 440.0, 'M3': -1240.0, 'l7': 1140.0, 'x1': -4850.0, 'k': 1230.0, 'c3': -940.0, 'a4': -40.0, 'Z': -480.0, 'M1': 2200.0, 'a5': 2400.0, 'z1': 240.0, 'c5': 2590.0, 'g': 150.0, 'a7': -650.0, 'R': -840.0, 'n': -1760.0, 'm1': -4730.0, 'c1': 5160.0, 'M7': 2020.0, 'm2': -3060.0, 'M0': -1950.0, 'l6': -60.0}})
-PAR.update({'av': (), 'mv': ('ssss', 'pppp', 'pppp', 'vvsp'), 'xv': ((0, 2), (1, 2)), 'zv': ((1, 1), (1, 2)), 'duv': (), 'tv': (0, 3), 'vv': (0, 1, 2), 'z': ('pg', 'pg', 'pg'), 'bias': {'z0': -1770.0, 'a3': 4050.0, 'T': 1770.0, 'c6': -420.0, 'W': -1900.0, 'l3': -2010.0, 'M2': -3560.0, 'c7': -3640.0, 'a2': 1940.0, 'c4': -1930.0, 'c0': -60.0, 'M6': 2530.0, 'S': 5890.0, 'D': -1350.0, 'M4': -990.0, 'l1': -420.0, 'V': -2790.0, 'l5': 3220.0, 'a6': -4880.0, 'm3': 5160.0, 'm0': -6000, 'l4': 1880.0, 'M5': -3620.0, 'l2': 2440.0, 'F': 3100.0, 'c2': 3090.0, 'x0': -5960.0, '': -2010.0, 'a1': 790.0, 'M3': -1040.0, 'l7': -2580.0, 'x1': -2960.0, 'k': 1140.0, 'c3': 1420.0, 'a4': 2920.0, 'Z': -1110.0, 'M1': 1130.0, 'a5': 1280.0, 'z1': -2240.0, 'c5': -4160.0, 'g': -40.0, 'a7': -950.0, 'R': 2240.0, 'n': 600.0, 'm1': -5740.0, 'c1': 5230.0, 'M7': -2710.0, 'm2': -2000.0, 'M0': 3220.0, 'l6': -610.0}})
-PAR.update({'av': (), 'mv': ('pspp', 'pppp', 'vsvs', 'vsss'), 'xv': ((1, 0), (1, 1)), 'zv': (), 'duv': (), 'tv': (0, 3), 'vv': (0, 1), 'half': ((0, 192), (192, 384)), 'z': ('gg', 'gg', 'gg'), 'down': 'mm', 'kq': 'y', 'ttg': 1.6, 'g': 1.56, 'dl': 900.0, 'ov': 0.0, 'lat': 180.0, 'fly': 400.0, 'rq': 500.0, 'dq': 120.0, 'ld': 600.0, 'far': 'W', 'xh': True, 'bias': {'x0': -2670.0, 'z0': 3030.0, 'a5': 1760.0, 'k': 3220.0, 'm3': 2710.0, 'l4': 2090.0, 'S': 660.0, 'z1': 240.0, 'M3': 2100.0, 'm2': 1410.0, 'l3': 130.0, 'M6': 1820.0, 'c0': 2780.0, 'D': -2360.0, 'M4': -400.0, 'T0': -3960.0, 'm1': 2470.0, 'M7': 3330.0, 'c4': -240.0, 'l6': -570.0, 'g': -470.0, 'l2': 730.0, 'M5': 1130.0, 'a7': -60.0, 'b3': 1170.0, 'x1': -1440.0, 'F': 1450.0, '': -3420.0, 'n': 2120.0, 'l5': 1470.0, 'a4': -1800.0, 'W': -2120.0, 'a1': 2590.0, 'a2': -2090.0, 'c1': 2770.0, 'a3': 3040.0, 'V': -300.0, 'M1': -2220.0, 'a6': -1070.0, 'c6': 3060.0, 'c3': 3180.0, 'M0': 2770.0, 'c7': 330.0, 'c5': -1860.0, 'T': -2420.0, 'l7': 510.0, 'c2': -5550.0, 'm0': 340.0, 'M2': -770.0, 'R': 1580.0, 'l1': -430.0, 'T1': 3850.0, 'b7': -320.0}, 'bv': (3, 7), 'own': 30.0, 'tw': 85.0, 'tc': 0.67, 'xf': 800.0, 'vg': True, 'uv': ((0, 1), (1, 0), (1, 1))})
-PAR.update({'av': (), 'mv': ('pspp', 'psvv', 'vppp', 'vsvs'), 'xv': ((0, 1), (0, 2), (1, 1), (1, 2)), 'zv': (), 'duv': (), 'tv': (0, 3), 'vv': (0, 1), 'half': ((0, 256), (256, 384)), 'z': ('gg', 'gg', 'gg'), 'down': 'turn', 'kq': 'y', 'ttg': 1.6, 'g': 1.56, 'dl': 1100.0, 'ov': 0.0, 'lat': 190.0, 'fly': 450.0, 'rq': 450.0, 'dq': 140.0, 'ld': 600.0, 'far': 'W', 'xh': True, 'bias': {'k': 1620.0, 'M6': -1200.0, 'a5': 2040.0, 'l1': -1650.0, 'n': 3910.0, 'l5': 3250.0, 'S': -3630.0, 'M3': -2290.0, 'm3': -1640.0, 'l4': 3930.0, 'a3': -2750.0, 'F': -3770.0, 'V': 1830.0, 'g': -350.0, 'c1': 990.0, 'M2': -90.0, 'D': -790.0, 'M4': 5500.0, 'T0': -230.0, 'M7': 1090.0, 'c5': -2910.0, 'l7': 3140.0, 'm2': -3880.0, 'l3': 1300.0, 'M5': 5270.0, '': 3490.0, 'x0': -3640.0, 'W': -2110.0, 'a1': 1270.0, 'a2': 650.0, 'c2': 410.0, 'M1': -2080.0, 'a4': -2700.0, 'c7': -2290.0, 'z0': 770.0, 'c4': 5930.0, 'c6': 1020.0, 'a6': 3410.0, 'T': -2270.0, 'T1': 1450.0, 'R': -2120.0, 'l6': 890.0, 'm1': -3660.0, 'x1': -220.0, 'a7': -70.0, 'm0': -820.0, 'c3': 380.0, 'z1': -120.0, 'l2': -2320.0, 'M0': -160.0, 'c0': 4140.0}, 'bv': (), 'own': 240.0, 'tw': 40.0, 'tc': 0.55, 'xf': 800.0, 'vg': True, 'uv': ((0, 0), (1, 0), (1, 1), (1, 2))})
-PAR.update({'mv': ('vvps', 'psps', 'pspp', 'vsvs'), 'bias': {'k': 1000.0, 'M6': -200.0, 'a5': 2930.0, 'l1': -1750.0, 'n': 2660.0, 'l5': 1330.0, 'S': -1750.0, 'M3': -2460.0, 'm3': -690.0, 'l4': 4160.0, 'a3': -3070.0, 'F': -3810.0, 'V': 2840.0, 'g': -150.0, 'c1': 890.0, 'M2': -2290.0, 'D': 1560.0, 'M4': 6000, 'T0': -80.0, 'M7': 1090.0, 'c5': 110.0, 'l7': 1880.0, 'm2': -3460.0, 'l3': 1370.0, 'M5': 6000, '': 3490.0, 'x0': -3970.0, 'W': -580.0, 'a1': -740.0, 'a2': -2140.0, 'c2': 450.0, 'M1': -1330.0, 'a4': -2700.0, 'c7': -590.0, 'z0': 730.0, 'c4': 4120.0, 'c6': 1010.0, 'a6': 2460.0, 'T': 1110.0, 'T1': 1450.0, 'R': -2120.0, 'l6': 1480.0, 'm1': -1700.0, 'x1': -520.0, 'a7': -70.0, 'm0': -3770.0, 'c3': 960.0, 'z1': -120.0, 'l2': -2320.0, 'M0': -160.0, 'c0': 2230.0}})
+PAR = {"ttg": 1.6, "g": 1.56, "dl": 1100.0, "ld": 600.0, "dq": 140.0, "rq": 450.0, "fly": 450.0, "xf": 800.0, "first": 1000.0,
+       "lat": 190.0, "own": 240.0, "tw": 40.0, "tc": 0.55, "far": "W", "ahead": 2, "xh": True, "bias": {}}
+for _h in (1, 2, 3):
+    PAR.update({"av%d" % _h: (), "bv%d" % _h: (), "mv%d" % _h: ("vvps", "psps", "pspp", "vsvs"), "xv%d" % _h: ((0, 1), (0, 2), (1, 1), (1, 2)),
+                "uv%d" % _h: ((0, 0), (1, 0), (1, 1), (1, 2)), "wv%d" % _h: ((1, 0), (1, 1)), "vv%d" % _h: (0, 1), "duv%d" % _h: (), "tv%d" % _h: (),
+                "cut%d" % _h: (256,), "down%d" % _h: "turn", "kq%d" % _h: "yyyy", "gb%d" % _h: (4,), "st%d" % _h: ()})
+PAR.update({'xh': False, 'mv2': ('ssss', 'ssss', 'vvvs', 'vsps'), 'xv2': ((1, 0), (1, 3)), 'uv2': (), 'wv2': ((0, 2), (1, 0), (1, 1)), 'vv2': (0, 3), 'gb2': (), 'st2': (3, 5, 7), 'order': {'v': '0t000q01070u0405080r020c030e0k090s0i0j0d0h0n0o0m0l0g0v060w0p0b0a0f0F0x0G0y0N0H0O0z0I0Q0A0P0J0C0B0T0K0D0U0L0S0E0V0R0M0W190X1a0Z0Y1c1b101f1d1e1g111h1j1i1k121l1m1n14131o15161p171q181r1s1t1u1v1E1w1F1x1G1y1M1H1N1z1O1I1A1B1S1U1R1C1J1D1T1P1Y2f2i2h2g1Q1V2j202k1Z2n2l2m1K2o211X2p1L2q2r25262s1W2827292324222a2t2c2b2d2u2e2v2w2x2y2H2z2I2A2P2J2Q2B2R2K2C2S2L2V2E2D2M2F2W2N2G3y2X2T2O2Y3b2Z3c31303e3d323g3f3h3i333j3l3m3k343n3z2U3o3p35363q38373r393A3s3a3t3u3v3w3x', 's': '0100030402070a080e05090d060i0k0f0b0g0r0j0c0p0l0v0m0x0q0s0h0t0n0o0C0w0D0z0E0y0F0u0B0A0G0I0J0H0L0K0R0N0O0M0P0Z0Q15170S0U0W0T0X0V0Y101i1j1k1l1314111b181n1m121d1c161f191e1a1h1g1o1p1q1r1s1C1B1t1v1u1x1w1y1D1z1E1F1A1I1H1G1M1J1T1K1O1N1Z1V1P1Q1U1W211X26201R271L1Y231S22282924252a2c2d2b2f2e2g2h2k2j2i', 't': '000504070201030a060e0g090c080b0d0k0i0h0f0o0j0m0p0l0n0r0q0t0s0u0v0x0w0y0A0E0B0D0C0z0P0H0L0F0N0J0G0I0K0M0R0T0Q0U0S0O0X0V0W0Y0Z1110121315171814161b1e191f1a1d1h1c1l1j1n1g1p1i1k1r1m1o1v1t1q1s1u1w1y1x1z1A1B1E1C1D1F', 'p': '010002050403080706090a0b0c0e0f0g0h0d0j0l0k0n0m0i0p0o', 'y': '0100040205030q070i0o0c0m0b0n0j0k0p0h0g0a060d090e0f0l080s0r'}})
 
 
 def _sb(n, d):
-    return ("sbuf", [128, n], d)
+    return ("sbuf", [128] + (n if isinstance(n, list) else [n]), d)
 
 
 CODE, PL, BF, F32, U16, I32 = "float8_e4m3fn_x4", "uint8", "bfloat16", "float32", "uint16", "int32"
 SCRATCH = {
-    "xin": _sb(4 * C, BF), "uin": _sb(512, BF), "vin": _sb(512, BF),
-    "wq": _sb(512, CODE), "wz": _sb(512, PL), "vq": _sb(128, CODE), "vz": _sb(128, PL),
+    "xin": _sb(4 * C, BF), "uin": _sb(512, BF), "vin": _sb(512, BF), "wq": _sb(512, CODE), "vq": _sb(128, CODE),
     "c32": _sb(128, BF), "eye": _sb(128, BF), "pidx": _sb(1, I32), "pi2": _sb(8, I32), "pf": _sb(10, F32),
-    "ef": _sb(520, BF), "ee": _sb(520, BF), "eo": _sb(520, BF),
-    "efq": _sb(512, CODE), "efz": _sb(512, PL), "eeq": _sb(512, CODE), "eez": _sb(512, PL),
-    "eoq": _sb(512, CODE), "eoz": _sb(512, PL),
-    "cap": _sb(C, F32), "st": _sb(C, F32), "ex": _sb(C, F32), "nr": _sb(C, BF), "tr": _sb(1024, BF),
-    "kd": ("sbuf", [128, 2, 2, 2, 16], BF), "ko": _sb(128, BF), "ct": ("sbuf", [128, 2, 2, 16], BF), "it8": _sb(4, F32), "ordk": _sb(6, U16), "kf": ("sbuf", [128, 2, 2, 16], F32),
-    "n32": _sb(32, F32), "n64": ("sbuf", [128, 2, 32], F32), "npg": ("sbuf", [128, 2, 2, 16], F32), "nd": ("sbuf", [128, 2, 2, 16], F32), "no": _sb(64, F32),
-    "cn": _sb(8, F32), "ca": _sb(8, F32), "sg": _sb(8, F32), "b0": _sb(1, F32), "ordn": _sb(2, U16),
-    "hist": _sb(9 * HW, F32), "ab": _sb(8 * C, BF), "al": _sb(8 * HW, BF), "bl": _sb(8 * C, BF), "bv": _sb(8 * C, BF), "nop": ("sbuf", [128, 2, 16], F32),
-    "th": _sb(4 * C, BF), "du": _sb(512, BF),
+    "ef": _sb(520, BF), "efq": _sb(512, CODE), "cz": _sb(1152, PL),
+    "cap": _sb(C, F32), "st": _sb(C, F32), "ex": _sb(C, F32), "nr": _sb(C, BF), "tr": _sb(1024, BF), "nr4": _sb([4, 128], BF), "tr4": _sb([4, 128], BF),
+    "kd": _sb([2, 2, 16], BF), "kd4": _sb([2, 2, 16], BF), "ko": _sb(64, BF), "ct": _sb(32, BF), "it8": _sb(4, F32), "ordk": _sb(4, U16), "kf": _sb([2, 2, 16], F32),
+    "n64": _sb([2, 32], F32), "nd": _sb([2, 2, 16], F32), "no": _sb(64, F32), "npg": _sb([2, 2, 16], F32),
+    "cn": _sb(8, F32), "ca": _sb(8, F32), "sg": _sb(8, F32), "ep": _sb(8, F32), "eq": _sb(8, F32), "ob": _sb(8, F32), "one": _sb(8, F32), "zero": _sb(C, BF), "b0": _sb(1, F32), "ordn": _sb(2, U16), "on": _sb(16, U16), "ok": _sb(32, U16),
+    "hist": _sb(9 * HW, F32), "ab": _sb(8 * C, BF), "al": _sb(8 * HW, BF), "bl": _sb(8 * C, BF), "bv": _sb(8 * C, BF),
+    "th": _sb(4 * C, BF), "tf": _sb(4 * C, BF), "du": _sb(512, BF),
     "zt": _sb(4 * C, BF), "xt": _sb(4 * C, BF), "vt": _sb(512, BF), "yt": _sb(C, F32),
-    "xq0": _sb(C, CODE), "xz0": _sb(C, PL), "uq0": _sb(128, CODE), "uz0": _sb(128, PL),
-    "zq": _sb(C, CODE), "zz": _sb(C, PL), "ok": _sb(96, U16)}
+    "xq0": _sb(512, CODE), "xz0": _sb(512, PL), "hq": _sb(C, CODE), "hz": _sb(C, PL), "gq": _sb(128, CODE), "gz": _sb(512, PL), "aq": _sb(C, CODE), "az": _sb(C, PL),
+    "zq": _sb(C, CODE), "zz": _sb(C, PL)}
 for _h in (1, 2, 3):
-    SCRATCH.update({
-        "aq%d" % _h: _sb(C, CODE), "az%d" % _h: _sb(C, PL), "an%d" % _h: _sb(16, U16),
-        "aeq%d" % _h: _sb(C, CODE), "aez%d" % _h: _sb(C, PL), "aoq%d" % _h: _sb(C, CODE), "aoz%d" % _h: _sb(C, PL),
-        "xq%d" % _h: _sb(C, CODE), "xz%d" % _h: _sb(C, PL), "uq%d" % _h: _sb(128, CODE), "uz%d" % _h: _sb(512, PL),
-        "veq%d" % _h: _sb(128, CODE), "vez%d" % _h: _sb(128, PL), "voq%d" % _h: _sb(128, CODE), "voz%d" % _h: _sb(128, PL),
-        "sq%d" % _h: _sb(128, CODE), "sz%d" % _h: _sb(512, PL), "on%d" % _h: _sb(16, U16)})
+    SCRATCH.update({"xq%d" % _h: _sb(C, CODE), "xz%d" % _h: _sb(C, PL), "uq%d" % _h: _sb(128, CODE), "uz%d" % _h: _sb(512, PL),
+                    "sq%d" % _h: _sb(128, CODE), "sz%d" % _h: _sb(512, PL)})
 for _b in range(8):
     SCRATCH["p%d" % _b] = ("psum", [128, 512], F32)
 
-SEMAPHORES = (["cv", "cs", "ct", "cp", "sent", "rc1", "rc2", "rc3", "outy", "outs"] + ["d%d" % i for i in range(12)]
-              + ["m%d%d" % (h, i) for h in (1, 2, 3) for i in range(4)] + ["k1", "k2", "k3"]
-              + ["%s%d%d" % (n, h, i) for n in "qz" for h in (1, 2, 3) for i in range(2)])
+SEMAPHORES = (["cv", "cs", "ct", "cp", "sent", "outy", "outs"] + ["d%d" % i for i in range(12)] + ["f%d" % i for i in range(14)]
+              + ["m%d%d%s" % (h, i, q) for h in (1, 2, 3) for i in range(5) for q in "ys"])
 CYC = 0.83
+ABC = "0123456789abcdefghijklmnopqrstuvwxyzABCDEFGHIJKLMNOPQRSTUVWXYZ"
 
 
 def lay_out(calls, ways_only=False):
-    lat = PAR["lat"]
     lastw, readers, lastp = {}, {}, {}
     for i, c in enumerate(calls):
         hard, soft = set(), set()
@@ -86,17 +74,23 @@ def lay_out(calls, ways_only=False):
         c["gap"] = {}
         for j in c["next"]:
             d = calls[j]
-            if i not in d["hard"]:
-                c["gap"][j] = 0.0
-            elif c["q"] == d["q"] and not c["late"] and PAR["own"] is not None:
-                c["gap"][j] = PAR["own"] + (PAR["tw"] if c["q"] == "t" else 0.0)
-            else:
-                c["gap"][j] = lat + c["late"] + (PAR["tw"] if "t" in (c["q"], d["q"]) else 0.0)
+            c["gap"][j] = 0.0 if i not in d["hard"] else (
+                (PAR["own"] if c["q"] == d["q"] and not c["late"] else PAR["lat"] + c["late"]) + (PAR["tw"] if "t" in (c["q"], d["q"]) else 0.0))
     for i in range(len(calls) - 1, -1, -1):
         c = calls[i]
-        c["way"] = c["ns"] + max([0.0] + [calls[j]["way"] + c["gap"][j] for j in c["next"]])
+        c["way"] = c["ns"] + max([c["late"]] + [calls[j]["way"] + c["gap"][j] for j in c["next"]])
     if ways_only:
         return []
+    if PAR.get("order"):
+        seq, done, order = {}, set(), []
+        for q, e in PAR["order"].items():
+            mine = [i for i, c in enumerate(calls) if c["q"] == q]
+            seq[q] = [mine[62 * ABC.index(e[j]) + ABC.index(e[j + 1])] for j in range(len(e) - 2, -1, -2)]
+        while len(order) < len(calls):
+            q = [q for q in seq if seq[q] and calls[seq[q][-1]]["hard"] | calls[seq[q][-1]]["soft"] <= done][0]
+            done.add(seq[q][-1])
+            order.append(seq[q].pop())
+        return order
     free, left, order = {}, [len(c["hard"] | c["soft"]) for c in calls], []
     ready = [i for i in range(len(calls)) if left[i] == 0]
     for c in calls:
@@ -123,21 +117,23 @@ def rank_program(g, core, T, topo):
     if rank is None:
         return
     queues = {"v": g.vector, "s": g.scalar, "t": g.tensor, "p": g, "y": g.sync}
-    calls = []
+    calls, now, nfar = [], [""], [0]
     v, s, t = g.vector, g.scalar, g.tensor
     P = [T["p%d" % b] for b in range(8)]
 
     def op(qn, f, r, w, n, tag="", late=0.0, kind="op", sem=None):
-        calls.append({"q": qn, "f": f, "r": list(r), "w": list(w), "ns": n, "tag": tag, "late": late, "kind": kind, "sem": sem})
+        calls.append({"q": qn, "f": f, "r": list(r), "w": list(w), "ns": n, "tag": tag + now[0], "late": late, "kind": kind, "sem": sem})
 
     def plane(z, a, b):
-        if PAR["far"] == "W" and z in ("efz", "wz", "vz"):
+        if z in ("efz", "wz", "vz"):
             at = {"efz": 0, "wz": 512, "vz": 1024}[z] + a
-            return T["sz%d" % (1 + at // 384)][:, 128 + at % 384:128 + at % 384 + b - a]
+            if PAR["far"] == "W":
+                return T["sz%d" % (1 + at // 384)][:, 128 + at % 384:128 + at % 384 + b - a]
+            return T.cz[:, at:at + b - a]
         return T[z][:, a:b]
 
     def cy(n):
-        return max(64.0, n) * CYC + PAR["ov"]
+        return max(64.0, n) * CYC
 
     def dma(qn, out, in_, r, w, sem=None, tag=""):
         op(qn, lambda: queues[qn].dma_start(out, in_), r, w, PAR["dq"], tag, PAR["dl"] + (0.0 if r else PAR["ld"]), "dma", sem)
@@ -155,14 +151,17 @@ def rank_program(g, core, T, topo):
         else:
             op("s", lambda: s.activation(out, in_, F.Copy, scale=1.0 if scale is None else scale), r, w, cy(n), tag)
 
-    def ts(out, in_, s1, s2, o1, o2, r, w, n=1, tag=""):
+    def ts(out, in_, s1, s2, o1, o2, r, w, n=1, tag="", ns=None):
         if o2 is None:
-            op("v", lambda: v.tensor_scalar(out, in_, s1, None, o1), r, w, cy(n), tag)
+            op("v", lambda: v.tensor_scalar(out, in_, s1, None, o1), r, w, ns or cy(n), tag)
         else:
-            op("v", lambda: v.tensor_scalar(out, in_, s1, s2, o1, o2), r, w, cy(n), tag)
+            op("v", lambda: v.tensor_scalar(out, in_, s1, s2, o1, o2), r, w, ns or cy(n), tag)
 
-    def fill(ap, c, w, n=1):
-        op("v", lambda: v.memset(ap, c), [], w, cy(n))
+    def tt(out, in0, in1, o, r, w, ns, tag):
+        op("v", lambda: v.tensor_tensor(out, in0, in1, o), r, w, ns, tag)
+
+    def fill(ap, c, w, n=1, r=()):
+        op("v", lambda: v.memset(ap, c), r, w, cy(n), "f")
 
     def quant(q, z, a, b, src, r, w, tag=""):
         op("v", lambda: v.quantize_mx(T[q][:, a:b], plane(z, a, b), src), r, w, 12 + 0.88 * (b - a), tag)
@@ -173,60 +172,79 @@ def rank_program(g, core, T, topo):
     def turn(out, in_, r, w, n=1, tag=""):
         op("v", lambda: v.transpose(out, in_), r, w, cy(n), tag)
 
-    def act(out, in_, f, r, w, n, tag="", **k):
-        op("s", lambda: s.activation(out, in_, f, **k), r, w, cy(n) + (20 if "accum_out" in k else 0), tag)
+    def act(out, in_, f, r, w, n, tag="", ns=None, **k):
+        op("s", lambda: s.activation(out, in_, f, **k), r, w, ns or cy(n) + (20 if "accum_out" in k else 0), tag)
 
     def picked(n):
         return 55 + PAR["g"] * CYC * n
 
-    dma("y", T.uin[:], T.u[:], [], ["uin"])
-    dma("s", T.xin[:, 0:512], T.x[:, 0:512], [], ["xin0"])
-    dma("y", T.xin[:, 512:1024], T.x[:, 512:1024], [], ["xin1"])
-    dma("s", T.xin[:, 1024:1536], T.x[:, 1024:1536], [], ["xin2"])
-    dma("y", T.wq[:].bitcast(dt.uint8), T.wc[:], ["xin1"][:0], ["wq"])
+    def far(step, pairs, r, w, late, tag):
+        dst = T.cores[(rank + step) % N]
+        rid, pid, _ = topo.addr(dst)
+        eng = topo.engines(core, dst)
+        sem, k = "f%d" % nfar[0], len(eng) // len(pairs)
+
+        def f():
+            if len(pairs) == 1:
+                g.remote_dma(pairs[0][0], pairs[0][1], T.sem[sem], T.sem["sent"], pid, rid, sum(1 << e for e in eng))
+            else:
+                g.remote_dma_fused([RemoteDMATransfer(dst_ids=[DstId(rid=rid, pnc=pid)], dma_engine_mask=sum(1 << e for e in eng[k * i:k * i + k]),
+                                                      remote_sem=T.sem[sem], src=b, dst=a) for i, (a, b) in enumerate(pairs)], local_sem=T.sem["sent"])
+            return len(eng)
+        op("p", f, r, w, PAR["rq"] + (0.0 if nfar[0] else PAR["first"]), tag, PAR["fly"] + late, "far", sem)
+        nfar[0] += 1
+
+    def u8(ap):
+        return ap.bitcast(dt.uint8)
+
+    dma("y", T.uin[:], T.u[:], [], ["uin"], None, "L")
+    dma("s", T.xin[:, 0:512], T.x[:, 0:512], [], ["xin0"], None, "L")
+    dma("y", T.xin[:, 512:1024], T.x[:, 512:1024], [], ["xin1"], None, "L")
+    dma("s", T.xin[:, 1024:1536], T.x[:, 1024:1536], [], ["xin2"], None, "L")
+    dma("y", u8(T.wq[:]), T.wc[:], [], ["wq"])
     for i in range(2):
         dma("y", plane("wz", 256 * i, 256 * i + 256), T.ws[:, 256 * i:256 * i + 256], [], ["wz%d" % i])
     dma("y", T.vin[:], T.v[:], [], ["vin"])
 
+    by_product = [PAR["down%d" % h] == "mm" for h in (1, 2, 3)]
     fill(T.c32[:], 32.0, ["c32"], 64)
     op("p", lambda: g.affine_select(T.eye[:], T.c32[:], [[-1, 128]], A.is_equal, 0.0, 0, 1), ["c32"], ["eye"], 385)
     op("p", lambda: g.iota(T.pidx[:], [[0, 1]], 0, 1), [], ["pidx"], 135)
+    op("p", lambda: g.iota(T.it8[:], [[8, 4]], 0, 0, allow_small_or_imprecise_dtypes=True), [], ["it8"], 140)
     fill(T.ef[:], 0.0, ["ef"], 260)
     cp("v", T.ef[:, 3:515:4], T.eye[:], ["eye", "ef"], ["ef"], 64)
-    for i, (b, sh) in enumerate(((16, 0), (112, 0), (1, 0), (6, 0), (8, 3), (96, 0), (15, 1))):
+    for i, (b, sh) in enumerate(((96, 0), (112, 0), (1, 0), (6, 0), (8, 0), (15, 1))):
         if sh:
             ts(T.pi2[:, i:i + 1], T.pidx[:], b, sh, A.bitwise_and, A.logical_shift_right, ["pidx"], ["i%d" % i])
         else:
             ts(T.pi2[:, i:i + 1], T.pidx[:], b, None, A.bitwise_and, None, ["pidx"], ["i%d" % i])
-    for i, (k, m, c) in enumerate(((0, -0.0625, 1.0), (0, 0.0625, 0.0), (5, 1.0, 15.0), (5, 1.0, 31.0), (1, 1.0, 15.0), (2, 32.0, 0.0), (4, 1.0, 0.0),
-                                   (6, 1.0, 0.0), (0, 4.0, 0.0))):
-        ts(T.pf[:, i:i + 1], T.pi2[:, k:k + 1], m, c, A.mult, A.add, ["i%d" % k], ["pf%d" % i])
-    ts(T.ordn[:, 0:1], T.pi2[:, 3:4], T.pf[:, 5:6], T.pf[:, 6:7], A.add, A.add, ["i3", "pf5", "pf6"], ["ordn"])
-    op("p", lambda: g.iota(T.it8[:], [[64, 2], [8, 2]], 0, 0, allow_small_or_imprecise_dtypes=True), [], ["it8"], 140)
-    ts(T.ordk[:, 0:4], T.it8[:], T.pf[:, 5:6], T.pf[:, 7:8], A.add, A.add, ["it8", "pf5", "pf7"], ["ordk0", "ordk1"])
-    twice = PAR["down"] == "mm" or any("p" in z for z in PAR["z"])
-    if any("g" in z for z in PAR["z"]) and twice:
-        ts(T.ordk[:, 4:6], T.ordk[:, 0:2], T.pf[:, 8:9], None, A.add, None, ["ordk0", "pf8"], ["ordk2"])
-    pairs = not PAR["vg"] or any("p" in z for z in PAR["z"])
-    if pairs:
-        act(T.ee[:], T.ef[:], F.Copy, ["ef", "pf0"], ["ee"], 520, scale=T.pf[:, 0:1])
-        act(T.eo[:], T.ef[:], F.Copy, ["ef", "pf1"], ["eo"], 520, scale=T.pf[:, 1:2])
+    for i, (k, m, c) in enumerate(((0, 1.0, 15.0), (0, 1.0, 31.0), (1, 1.0, 15.0), (2, 32.0, 0.0), (4, 0.125, 0.0), (5, 1.0, 0.0), (3, 0.5, 0.0))):
+        if i < 6 or any(by_product):
+            ts(T.pf[:, i:i + 1], T.pi2[:, k:k + 1], m, c, A.mult, A.add, ["i%d" % k], ["pf%d" % i])
+    ts(T.ordn[:, 0:1], T.pi2[:, 3:4], T.pf[:, 3:4], T.pf[:, 4:5], A.add, A.add, ["i3", "pf3", "pf4"], ["ordn"])
+    ts(T.ordk[:, 0:2], T.it8[:, 0:2], T.pf[:, 3:4], T.pf[:, 5:6], A.add, A.add, ["it8", "pf3", "pf5"], ["ordk0"])
+    if any(by_product):
+        ts(T.pf[:, 7:8], T.pi2[:, 4:5], T.pf[:, 3:4], T.pf[:, 6:7], A.add, A.add, ["i4", "pf3", "pf6"], ["pf7"])
+        ts(T.ordk[:, 2:4], T.it8[:, 0:4:2], T.pf[:, 7:8], None, A.add, None, ["it8", "pf7"], ["ordk1"])
+        fill(T.tr4[:, :, 96:128], 0.0, ["tr4z"])
+        fill(T.kd4[:], 0.0, ["kd4z"])
     act(T.cap[:], T.ef[:, 0:C], F.Copy, ["ef"], ["cap"], C, scale=0.0, bias=BIG)
     act(T.hist[:, 0:HW], T.ef[:, 0:HW], F.Copy, ["ef"], ["h0"], HW, scale=0.0, bias=BIG)
-    for e in "feo" if pairs else "f":
-        for b in range(4):
-            quant("e%sq" % e, "e%sz" % e, 128 * b, 128 * b + 128, T["e" + e][:, 3 - b:515 - b], ["e" + e], ["e%s%d" % (e, b)])
-    quant("uq0", "uz0", 0, 128, T.uin[:], ["uin"], ["U0"])
+    for b in range(4):
+        quant("efq", "efz", 128 * b, 128 * b + 128, T.ef[:, 3 - b:515 - b], ["ef"], ["ef%d" % b], "E")
+    quant("xq0", "xz0", C, C + 128, T.uin[:], ["uin"], ["U0"], "L")
     for i in range(3):
-        quant("xq0", "xz0", 128 * i, 128 * i + 128, T.xin[:, 512 * i:512 * i + 512], ["xin%d" % i], ["X0%d" % i])
+        quant("xq0", "xz0", 128 * i, 128 * i + 128, T.xin[:, 512 * i:512 * i + 512], ["xin%d" % i], ["X0%d" % i], "L")
+    quant("vq", "vz", 0, 128, T.vin[:], ["vin"], ["vq"])
     fill(T.ex[:, 0:C:128], -BIG, ["exz"])
     fill(T.tr[:, C + 15:1024:16], 0.0, ["trz"])
-    fill(T.kd[:], 0.0, ["kdz"])
-    fill(T.n64[:] if PAR["vg"] else T.n32[:], 1.0, ["n32z"] + ["n32%d%d" % (G, a) for G in range(4) for a in range(4)])
-    fill(T.hist[:, HW:9 * HW:HW], -BIG, ["hz"])
+    fill(T.n64[:], 1.0, ["n%d%d" % (G, a) for G in range(4) for a in range(4)])
+    fill(T.hist[:, HW:9 * HW:HW], -BIG, ["hsz"])
     fill(T.al[:, 1:8 * HW:HW], 1.0, ["alz"])
-    op("v", lambda: v.memset(T.cap[:, 0:C:16], -BIG), ["cap"], ["cap"], cy(1))
-    HALF = PAR["half"]
+    fill(T.cap[:, 0:C:16], -BIG, ["cap"], 1, ["cap"])
+    if any(PAR["st%d" % h] for h in (1, 2, 3)):
+        fill(T.one[:], 1.0, ["one"])
+        act(T.zero[:], T.ef[:, 0:C], F.Copy, ["ef"], ["zero"], C, scale=0.0)
     SV, SS = 0, 1
     turnb = [0]
 
@@ -240,71 +258,76 @@ def rank_program(g, core, T, topo):
     def sl(name, k):
         return T[name][:, C * k:C * k + C]
 
-    def one_round(rd):
-        xq, xz, uq, uz = "xq%d" % (rd - 1), "xz%d" % (rd - 1), "uq%d" % (rd - 1), "uz%d" % (rd - 1)
-        nq, nz, on = "xq%d" % rd, "xz%d" % rd, "on%d" % rd
-        uk, nk = ["U%d" % (rd - 1), "Uz%d" % (rd - 1)], ["X%d%d" % (rd, h) for h in range(len(HALF))]
-        xk = ["X%d%d" % (rd - 1, h) for h in range(3 if rd == 1 else len(HALF))]
-        ZM = PAR["z"][rd - 1]
-        gath = [HALF[h] for h in range(len(HALF)) if ZM[h] == "g"]
-        behind = ["S"] if rd == 1 else ["vt1"] if PAR["far"] != "X" else []
+    def pieces(rd):
+        e = (0,) + PAR["cut%d" % rd] + (C,)
+        return [(e[i], e[i + 1]) for i in range(len(e) - 1)]
 
-        def own():
-            c, d = gath[0][0], gath[-1][1]
-            for b, bank in enumerate(banks(4)):
-                mm(bank, "efq", "efz", 128 * b, xq, xz, c, d, xk + ["ef%d" % b] + behind, True, True, "T")
-                cp("v" if b in PAR["tv"] and rd > 1 else "s", T.th[:, C * b + c:C * b + d], P[bank][:, 0:d - c], ["p%d" % bank],
-                   ["th%d%d" % (h, b) for h in range(len(HALF))], d - c, 1.0 / 64, "T")
-        if rd > 1 and gath and not PAR["vg"]:
-            own()
-        for b in (SV, SS):
-            mm(b, uq, uz, 0, xq, xz, 0, C, uk + xk, True, True, "S")
-            calls[-1]["w"].append("S")
-        if PAR["down"] == "mm":
+    def within(rd, c, d):
+        return [h for h, (a, b) in enumerate(pieces(rd)) if a < d and c < b]
+
+    def unpack(dst, q, z, c, d, r, w, bs, onv, tag):
+        for b in range(4):
+            mm(bs[b], "efq", "efz", 128 * b, q, z, c, d, r + ["ef%d" % b], True, True, tag)
+            cp("v" if onv(b) else "s", T[dst][:, C * b + c:C * b + d], P[bs[b]][:, 0:d - c], ["p%d" % bs[b]], [k + str(b) for k in w], d - c, 1.0 / 64, tag)
+
+    def one_round(rd):
+        now[0] = str(rd)
+        par = {k[:-1]: x for k, x in PAR.items() if k[-1] == str(rd)}
+        xq, xz, nq, nz = "xq%d" % (rd - 1), "xz%d" % (rd - 1), "xq%d" % rd, "xz%d" % rd
+        uq, uz, ua = ("uq%d" % (rd - 1), "uz%d" % (rd - 1), 0) if rd > 1 else (xq, xz, C)
+        HALF = pieces(rd)
+        uk, nk = ["U%d" % (rd - 1), "Uz%d" % (rd - 1)], ["X%d%d" % (rd, h) for h in range(len(HALF))]
+        xk = ["X%d%d" % (rd - 1, h) for h in range(3 if rd == 1 else len(pieces(rd - 1)))]
+        ahead = rd == PAR["ahead"]
+        if ahead:
+            hk = ["h%s%d" % (e, h) for e in "qz" for h in range(len(pieces(rd - 1)) if PAR["xh"] else 1)]
+            for b in (SV, SS):
+                mm(b, "gq", "gz", 0, "hq", "hz", 0, C, ["gq"] + hk, True, True, "B")
+        mine = SV
+        if par["down"] == "mm":
             SB = banks(3)
+            if not ahead:
+                mm(SV, uq, uz, ua, xq, xz, 0, C, uk + xk, True, True, "S")
             for j in range(3):
-                mm(SB[j], xq, xz, 128 * j, uq, uz, 0, 128, uk + xk, True, True, "S")
-        if PAR["down"] == "mm":
+                mm(SB[j], xq, xz, 128 * j, uq, uz, ua, ua + 128, uk + xk, True, True, "S")
+        else:
+            if ahead:
+                mine = banks(1)[0]
+            mm(mine, uq, uz, ua, xq, xz, 0, C, uk + xk, True, True, "S")
+        calls[-1]["w"].append("S")
+        if not ahead:
+            mm(SS, uq, uz, ua, xq, xz, 0, C, uk + xk, True, True, "S")
+        if par["down"] == "mm":
             for j in range(3):
                 scan(T.ex[:, 128 * j + 1:128 * j + 128], P[SB[j]][:, 0:127], T.cap[:, 1:128], -BIG, A.max, A.min, ["p%d" % SB[j], "cap"], ["ex%d" % j], 128, "k")
-                op("v", lambda j=j: v.tensor_tensor(T.nr[:, 128 * j:128 * j + 128], P[SB[j]][:, 0:128], T.ex[:, 128 * j:128 * j + 128], A.is_le),
-                   ["p%d" % SB[j], "ex%d" % j, "exz"], ["nr%d" % j], cy(128), "k")
-            scan(T.tr[:, 0:C], T.nr[:], T.nr[:], 0.0, A.mult, A.add, ["nr0", "nr1", "nr2"], ["tr"], C / 2, "k")
-            for i in range(2):
-                turn(T.ct[:, :, i, :], T.tr[:, 15:512:16], ["tr", "trz"], ["ct%d" % i], 1, "k")
+                tt(T.nr4[:, :, 32 * j:32 * j + 32], P[SB[j]][:, 0:128], T.ex[:, 128 * j:128 * j + 128], A.is_le, ["p%d" % SB[j], "ex%d" % j, "exz"], ["nr%d" % j], cy(128), "k")
+            scan(T.tr4[:, :, 0:96], T.nr4[:, :, 0:96], T.nr4[:, :, 0:96], 0.0, A.mult, A.add, ["nr0", "nr1", "nr2"], ["tr"], C / 2, "k")
+            turn(T.ct[:], T.tr4[:, :, 15:128:16], ["tr", "tr4z"], ["ct"], 1, "k")
             for a in range(4):
-                for j in range(3):
-                    dma(PAR["kq"][(3 * a + j) % len(PAR["kq"])], T.kd[4 * j + a:128:32], T.ct[32 * a + 8 * j:32 * a + 8 * j + 8], ["ct0", "ct1", "kdz"], ["kd%d%d" % (a, j)], "k%d" % rd, "k")
-            kdk = ["kd%d%d" % (a, j) for a in range(4) for j in range(3)]
-        else:
-            turn(T.st[:], P[SV][:, 0:C], ["p%d" % SV], ["st"], C, "k")
-            scan(T.ex[:, 1:C], T.st[:, 0:C - 1], T.cap[:, 1:C], -BIG, A.max, A.min, ["st", "cap"], ["ex"], C, "k")
-            op("v", lambda: v.tensor_tensor(T.nr[:], T.st[:], T.ex[:], A.is_le), ["st", "ex", "exz"], ["nr"], cy(2 * C), "k")
-            scan(T.tr[:, 0:C], T.nr[:], T.nr[:], 0.0, A.mult, A.add, ["nr"], ["tr"], C / 2, "k")
-            kdk = []
+                dma(par["kq"][a], T.kd4[a:128:8], T.ct[32 * a:32 * a + 32, :], ["ct", "kd4z"], ["kd4%d" % a], "m%d4%s" % (rd, par["kq"][a]), "k")
+            kdk = ["kd4%d" % a for a in range(4)]
             for h in range(2):
-                for i in range(2) if twice else (h,):
-                    turn(T.kd[:, h if twice else 0, :, i, :], T.tr[:, 15 + 16 * h:1024:32], ["tr", "trz", "kdz"], ["kd%d%d" % (h, i)], 1, "k")
-                    kdk.append("kd%d%d" % (h, i))
-        if gath:
-            for b, bank in enumerate(banks(4)):
-                mm(bank, "efq", "efz", 128 * b, uq, uz, 0, 128, uk + ["ef%d" % b], True, True, "D")
-                cp("v" if b in PAR["duv"] else "s", T.du[:, 128 * b:128 * b + 128], P[bank][:, 0:128], ["p%d" % bank], ["du%d" % b], 128, 1.0 / 64, "D")
-            if rd == 1:
-                own()
-        if twice:
-            turn(T.ko[:], T.kd[:], kdk, ["ko"], 1, "k")
+                turn(T.ko[:, 32 * h:32 * h + 32], T.kd4[:, :, h, :], kdk, ["ko%d" % h], 1, "k")
+            o = 2
         else:
-            turn(T.ko[:, 0:64], T.kd[:, 0], kdk, ["ko"], 1, "k")
-            op("v", lambda: v.tensor_scalar(T.ok[:, 64:96], T.ko[:, 0:64].indirect(T.ordk[:, 0:2]), -1.0, T.pf[:, 4:5], A.mult, A.add),
-               ["ko", "pf4", "ordk0"], ["ok2"], picked(32), "k")
-        for h in range(3 if twice else 0):
-            if (h == 2 and gath) or (h < 2 and len(gath) < len(HALF)):
-                op("v", lambda h=h: v.tensor_scalar(T.ok[:, 32 * h:32 * h + 32], T.ko[:].indirect(T.ordk[:, 2 * h:2 * h + 2]), -1.0, T.pf[:, 2 + h:3 + h], A.mult, A.add),
-                   ["ko", "pf%d" % (2 + h), "ordk%d" % h], ["ok%d" % h], picked(32), "k")
+            turn(T.st[:], P[mine][:, 0:C], ["p%d" % mine], ["st"], C, "k")
+            scan(T.ex[:, 1:C], T.st[:, 0:C - 1], T.cap[:, 1:C], -BIG, A.max, A.min, ["st", "cap"], ["ex0", "ex1", "ex2", "exw"], C, "k")
+            tt(T.nr[:], T.st[:], T.ex[:], A.is_le, ["st", "ex0", "exz"], ["nr"], cy(2 * C), "k")
+            scan(T.tr[:, 0:C], T.nr[:], T.nr[:], 0.0, A.mult, A.add, ["nr"], ["tr"], C / 2, "k")
+            for h in range(2):
+                turn(T.kd[:, :, h, :], T.tr[:, 15 + 16 * h:1024:32], ["tr", "trz"], ["kd%d" % h], 1, "k")
+            kdk = ["kd0", "kd1"]
+            turn(T.ko[:], T.kd[:], kdk, ["ko0", "ko1"], 1, "k")
+            o = 0
+        ts(T.ok[:], T.ko[:].indirect(T.ordk[:, o:o + 2]), -1.0, T.pf[:, 2:3], A.mult, A.add, ["ko0", "ko1", "pf2", "ordk%d" % (o // 2)], ["ok"], 1, "k", picked(32))
+        for b, bank in enumerate(banks(4)):
+            mm(bank, "efq", "efz", 128 * b, uq, uz, ua, ua + 128, uk + ["ef%d" % b, "S"], True, True, "D")
+            cp("v" if b in par["duv"] else "s", T.du[:, 128 * b:128 * b + 128], P[bank][:, 0:128], ["p%d" % bank], ["du%d" % b], 128, 1.0 / 64, "D")
+        if rd == 1:
+            unpack("th", xq, xz, 0, C, xk + ["S"], ["th0"], banks(4), lambda b: b in par["tv"], "T")
         for k in range(8):
             scan(T.hist[:, HW * (k + 1) + 1:HW * (k + 1) + 1 + C], P[SV][:, 0:C], T.hist[:, HW * k:HW * k + C], -BIG, A.max, A.min,
-                 ["p%d" % SV, "h%d" % k, "hz"], ["h%d" % (k + 1)], C, "M%d" % k)
+                 ["p%d" % SV, "h%d" % k, "hsz"], ["h%d" % (k + 1)], C, "M%d" % k)
         ts(T.sg[:, 0:1], hv(0), hv(1), -0.5, A.not_equal, A.add, ["h1", "h2"], ["g0"], 1, "g")
         ts(T.b0[:], hv(0), T.sg[:, 0:1], -1.0, A.mult, A.mult, ["h1", "g0"], ["b0"], 1, "g")
         for k in range(8):
@@ -313,161 +336,131 @@ def rank_program(g, core, T, topo):
                 act(out, T.hist[:, HW:HW + C], F.Sign, ["h1", "g0", "b0"], ["bl0", "c0"], C, "c0",
                     bias=T.b0[:], scale=T.sg[:, 0:1], accum_out=T.cn[:, 0:1])
             else:
-                if k < 7:
-                    ts(T.sg[:, k:k + 1], hv(k), hv(k + 1), -0.5, A.is_equal, A.add, ["h%d" % (k + 1), "h%d" % (k + 2)], ["g%d" % k], 1, "g")
-                if k in PAR["av"]:
+                if k in par["gb"]:
+                    tt(T.ep[:, k:k + 3], T.hist[:, HW * (k + 1) + C:HW * (k + 4):HW], T.hist[:, HW * (k + 2) + C:HW * (k + 5):HW], A.is_equal,
+                       ["h%d" % i for i in range(k + 1, k + 5)], ["ep%d" % k], cy(1), "g%d" % k)
+                    ts(T.sg[:, k:k + 3], T.ep[:, k:k + 3], -0.5, None, A.add, None, ["ep%d" % k], ["g%d" % i for i in range(k, k + 3)], 1, "g%d" % k)
+                elif k < 7 and k - 1 not in par["gb"] and k - 2 not in par["gb"] and k + 1 not in par["st"]:
+                    ts(T.sg[:, k:k + 1], hv(k), hv(k + 1), -0.5, A.is_equal, A.add, ["h%d" % (k + 1), "h%d" % (k + 2)], ["g%d" % k], 1, "g%d" % k)
+                if k in par["st"]:
+                    j = max([0] + [i for i in par["st"] if i < k])
+                    tt(T.eq[:, j + 1:k + 1], T.hist[:, HW * (j + 1) + C:HW * (k + 1):HW], T.hist[:, HW * (j + 2) + C:HW * (k + 2):HW], A.is_equal,
+                       ["h%d" % i for i in range(j + 1, k + 2)], ["eq%d" % k], cy(1), "o%d" % k)
+                    scan(T.ob[:, j + 1:k + 1], T.eq[:, j + 1:k + 1], T.one[:, j + 1:k + 1], T.ob[:, j:j + 1] if j else 1.0, A.mult, A.add,
+                         ["eq%d" % k, "one", "ob%d" % j], ["ob%d" % k], 1, "o%d" % k)
+                    if k in par["av"]:
+                        ts(sl("ab", k), P[SV][:, 0:C], hv(k), -1.0, A.is_equal, A.mult, ["p%d" % SV, "h%d" % (k + 1)], ["a%d" % k], C, "a%d" % k)
+                    else:
+                        act(sl("bv", k), P[SS][:, 0:C], F.Sign, ["p%d" % SS, "h%d" % (k + 1)], ["bv%d" % k], C, "a%d" % k, bias=hv(k), scale=-1.0)
+                        ts(sl("ab", k), sl("bv", k), 0.0, -1.0, A.is_equal, A.mult, ["bv%d" % k], ["a%d" % k], C / 2, "b%d" % k)
+                elif k in par["av"]:
                     ts(sl("ab", k), P[SV][:, 0:C], hv(k), None, A.not_equal, None, ["p%d" % SV, "h%d" % (k + 1)], ["a%d" % k], C, "a%d" % k)
                 else:
                     act(sl("ab", k), P[SS][:, 0:C], F.Abs, ["p%d" % SS, "h%d" % (k + 1)], ["a%d" % k], C, "a%d" % k, bias=hv(k), scale=-1.0)
-                bar = "bv" if k in PAR["bv"] else "bl"
-                if bar == "bv":
-                    ts(sl("bv", k - 1), T.al[:, HW * (k - 1) + 1:HW * (k - 1) + 1 + C], T.sg[:, k - 1:k], None, A.mult, None,
-                       ["l%d" % (k - 1), "g%d" % (k - 1), "alz"], ["bv%d" % (k - 1)], C / 2, "b%d" % k)
-                scan(T.al[:, HW * k + 2:HW * k + 2 + C], sl("ab", k), sl(bar, k - 1), 1.0, A.min, A.max, ["a%d" % k, bar + str(k - 1)], ["l%d" % k], C / 2, "l%d" % k)
-                if k + 1 in PAR["bv"] or k == 7:
-                    act(out, T.al[:, HW * k + 1:HW * k + 1 + C], F.Sign, ["l%d" % k, "alz"], ["bl%d" % k, "c%d" % k], C, "c%d" % k,
-                        accum_out=T.cn[:, k:k + 1] if k < 7 else T.ca[:, 7:8])
+                alive = T.al[:, HW * k + 1:HW * k + 1 + C]
+                bar = "bv" if k in par["bv"] else "bl"
+                if k in par["st"]:
+                    scan(T.al[:, HW * k + 2:HW * k + 2 + C], sl("ab", k), T.zero[:], T.ob[:, k:k + 1], A.add, A.max, ["a%d" % k, "zero", "ob%d" % k], ["l%d" % k], C / 2, "l%d" % k)
                 else:
-                    act(out, T.al[:, HW * k + 1:HW * k + 1 + C], F.Sign, ["l%d" % k, "g%d" % k, "alz"], ["bl%d" % k, "c%d" % k], C, "c%d" % k,
-                        scale=T.sg[:, k:k + 1], accum_out=T.cn[:, k:k + 1])
+                    if bar == "bv":
+                        ts(sl("bv", k - 1), T.al[:, HW * (k - 1) + 1:HW * (k - 1) + 1 + C], T.sg[:, k - 1:k], None, A.mult, None,
+                           ["l%d" % (k - 1), "g%d" % (k - 1), "alz"], ["bv%d" % (k - 1)], C / 2, "b%d" % k)
+                    scan(T.al[:, HW * k + 2:HW * k + 2 + C], sl("ab", k), sl(bar, k - 1), 1.0, A.min, A.max, ["a%d" % k, bar + str(k - 1)], ["l%d" % k], C / 2, "l%d" % k)
+                if k + 1 in par["bv"] or k + 1 in par["st"] or k == 7:
+                    act(out, alive, F.Sign, ["l%d" % k, "alz"], ["bl%d" % k, "c%d" % k], C, "c%d" % k, accum_out=T.cn[:, k:k + 1] if k < 7 else T.ca[:, 7:8])
+                else:
+                    act(out, alive, F.Sign, ["l%d" % k, "g%d" % k, "alz"], ["bl%d" % k, "c%d" % k], C, "c%d" % k, scale=T.sg[:, k:k + 1], accum_out=T.cn[:, k:k + 1])
             if k % 2:
                 G, r = k // 2, ["c%d" % (k - 1), "c%d" % k]
-                plain = k == 7 or PAR["mv"][G] != "ssss"
+                plain = k == 7 or par["mv"][G] != "ssss"
                 if plain:
                     e = k + 1 if k < 7 else k
                     act(T.ca[:, k - 1:e], T.cn[:, k - 1:e], F.Abs, r[:e - k + 1], ["ca%d" % G], 1, "m%d" % G)
                     r = ["ca%d" % G] + r[e - k + 1:]
                 for a in range(4):
-                    o = T.n64[32 * G:32 * G + 32, :, 2 * a] if PAR["vg"] else T.n32[32 * G:32 * G + 32, 2 * a:2 * a + 2]
-                    w, q = ["n32%d%d" % (G, a)], PAR["mv"][G][a]
+                    o, w, q = T.n64[32 * G:32 * G + 32, :, 2 * a], ["n%d%d" % (G, a)], par["mv"][G][a]
                     src = T["ca" if plain else "cn"][32 * a:32 * a + 32, k - 1:k + 1]
-                    if q == "y":
-                        dma("y", o, src, r, w, "m%d%d" % (rd, G), "m%d" % G)
-                    elif q == "p":
+                    if q == "p":
                         op("p", lambda o=o, src=src: g.affine_select(o, src, [[0, 2]], A.is_ge, 0.0, 0, 0), r, w, 175.0, "m%d" % G)
                     elif q == "v":
                         cp("v", o, src, r, w, 1, None, "m%d" % G)
                     else:
                         act(o, src, F.Abs, r, w, 1, "m%d" % G)
         for i in range(2):
-            turn(T.nd[:, :, i, :], T.n64[:, i, :] if PAR["vg"] else T.n32[:], ["n32z"] + ["n32%d%d" % (G, a) for G in range(4) for a in range(4)], ["nd%d" % i], 1, "n")
+            turn(T.nd[:, :, i, :], T.n64[:, i, :], ["n%d%d" % (G, a) for G in range(4) for a in range(4)], ["nd%d" % i], 1, "n")
         turn(T.no[:], T.nd[:], ["nd0", "nd1"], ["no"], 1, "n")
-        op("v", lambda: v.tensor_scalar(T[on][:], T.no[:].indirect(T.ordn[:, 0:1]), -1.0, None, A.add), ["no", "ordn"], [on], picked(16), "n")
+        ts(T.on[:], T.no[:].indirect(T.ordn[:, 0:1]), -1.0, None, A.add, None, ["no", "ordn"], ["on"], 1, "n", picked(16))
         for h, (c, d) in enumerate(HALF):
-            if ZM[h] == "g":
-                for b in range(4):
-                    op("v", lambda b=b, c=c, d=d: v.tensor_tensor(T.zt[:, 4 * c + b:4 * d:4], T.du[:, 128 * b:128 * b + 128].indirect(T.ok[:, 64 + c // 16:64 + d // 16]),
-                                                                  T.th[:, C * b + c:C * b + d], A.add),
-                       ["du%d" % b, "th%d%d" % (h, b), "ok2"], ["zt%d%d" % (h, b)], 55 + PAR["ttg"] * CYC * (d - c), "z%d" % h)
-            else:
-                ZB = banks(4)
-                for b in range(4):
-                    mm(ZB[b], "efq", "efz", 128 * b, xq, xz, c, d, xk + ["ef%d" % b] + behind, True, False, "R")
-                for i, e in enumerate("eo"):
-                    dq, dz = "a%sq%d" % (e, rd), "a%sz%d" % (e, rd)
-                    off = T.ok[:, 32 * i + c // 16:32 * i + d // 16]
-                    op("v", lambda dq=dq, off=off, c=c, d=d: v.tensor_copy(T[dq][:, c:d].bitcast(dt.uint32), T[uq][:].bitcast(dt.uint32).indirect(off)),
-                       uk + ["ok%d" % i], [dq + str(h)], picked(d - c), "z%d" % h)
-                    op("s", lambda dz=dz, off=off, c=c, d=d: s.activation(T[dz][:, c:d], T[uz][:, 0:128].indirect(off), F.Copy), uk + ["ok%d" % i], [dz + str(h)], picked(d - c), "z%d" % h)
-                    for b in range(4):
-                        mm(ZB[b], "e%sq" % e, "e%sz" % e, 128 * b, dq, dz, c, d, [dq + str(h), dz + str(h), "e%s%d" % (e, b)], False, e == "o", "Z")
-                for b in range(4):
-                    cp("v" if (h, b) in PAR["zv"] else "s", T.zt[:, 4 * c + b:4 * d:4], P[ZB[b]][:, 0:d - c], ["p%d" % ZB[b]], ["zt%d%d" % (h, b)], d - c, 1.0 / 64, "z%d" % h)
+            for b in range(4):
+                tt(T.zt[:, 4 * c + b:4 * d:4], T.du[:, 128 * b:128 * b + 128].indirect(T.ok[:, c // 16:d // 16]), T.th[:, C * b + c:C * b + d], A.add,
+                   ["du%d" % b, "ok", "tr%d%d" % (h, b)] + ["th%d%d" % (i, b) for i in (within(rd - 1, c, d) if rd > 1 else (0,))], ["zt%d%d" % (h, b)],
+                   55 + PAR["ttg"] * CYC * (d - c), "z%d" % h)
             quant("zq", "zz", c, d, T.zt[:, 4 * c:4 * d], ["zt%d%d" % (h, b) for b in range(4)], ["Z%d" % h], "z%d" % h)
         for h, (c, d) in enumerate(HALF):
             for b, bank in enumerate(banks(4)):
                 mm(bank, "efq", "efz", 128 * b, xq, xz, c, d, xk + ["ef%d" % b], True, False, "R")
                 mm(bank, "wq", "wz", 128 * b, "zq", "zz", c, d, ["Z%d" % h, "wq", "wz%d" % (b // 2)], False, True, "W")
-                cp("v" if (h, b) in PAR["xv"] else "s", T.xt[:, 4 * c + b:4 * d:4], P[bank][:, 0:d - c], ["p%d" % bank], ["xt%d%d" % (h, b)], d - c, 1.0 / 32, "x%d" % h)
+                cp("v" if (h, b) in par["xv"] else "s", T.xt[:, 4 * c + b:4 * d:4], P[bank][:, 0:d - c], ["p%d" % bank], ["xt%d%d" % (h, b)], d - c, 1.0 / 32, "x%d" % h)
             quant(nq, nz, c, d, T.xt[:, 4 * c:4 * d], ["xt%d%d" % (h, b) for b in range(4)], [nk[h]], "x%d" % h)
-        for h, (c, d) in enumerate(HALF if PAR["vg"] else ()):
-            for b, bank in enumerate(banks(4)):
-                mm(bank, "efq", "efz", 128 * b, nq, nz, c, d, [nk[h], "ef%d" % b], True, True, "T%d" % h)
-                cp("v" if (h, b) in PAR["uv"] else "s", T.th[:, C * b + c:C * b + d], P[bank][:, 0:d - c], ["p%d" % bank], ["th%d%d" % (h, b)], d - c, 1.0 / 64, "T%d" % h)
-        dst = T.cores[(rank + STEP[rd - 1]) % N]
-        rid, pid, _ = topo.addr(dst)
-        eng = topo.engines(core, dst)
-
-        def far(out, in_, sem, a, b, r, w, late, tag):
-            def f():
-                g.remote_dma(out, in_, T.sem[sem], T.sem["sent"], pid, rid, sum(1 << e for e in eng[a:b]))
-                return b - a
-            op("p", f, r, w, PAR["rq"], tag, late, "far", sem)
-        ne = len(eng)
-        wq, wz, wn, wk = nq, nz, on, nk + nk + [on]
-        if PAR["far"] == "X":
-            wq, wz, wn, wk = "aq%d" % rd, "az%d" % rd, "an%d" % rd, []
-            for h, (c, d) in enumerate(HALF if PAR["xh"] else ((0, C),)):
-                r = [nk[h]] if PAR["xh"] else nk
-                far(T[wq][:, c:d].bitcast(dt.uint8), T[nq][:, c:d].bitcast(dt.uint8), "q%d%d" % (rd, h), 0, ne, r, ["aq%d" % h], PAR["fly"] + 5.0 * (d - c), "F")
-                far(T[wz][:, c:d], T[nz][:, c:d], "z%d%d" % (rd, h), 0, ne, r, ["az%d" % h], PAR["fly"] + 1.5 * (d - c), "F")
-                wk += ["aq%d" % h, "az%d" % h]
-            far(T[wn][:], T[on][:], "rc%d" % rd, 0, ne, [on], ["an"], PAR["fly"], "F")
-            wk = wk + ["an"]
-        if PAR["vg"]:
-            for b in range(4):
-                src = T.th[:, C * b:C * b + C].indirect(T[on][:, 0:8])
-                r = ["th%d%d" % (h, b) for h in range(len(HALF))] + [on]
-                if b in PAR["vv"]:
-                    op("v", lambda b=b, src=src: v.tensor_scalar(T.vt[:, b:512:4], src, 2.0, None, A.mult), r, ["vt%d" % b], picked(128), "V")
-                else:
-                    op("s", lambda b=b, src=src: s.activation(T.vt[:, b:512:4], src, F.Copy, scale=2.0), r, ["vt%d" % b], picked(128), "V")
-        VB = [] if PAR["vg"] else banks(4)
-        for i, e in enumerate("" if PAR["vg"] else "eo"):
-            dq, dz = "v%sq%d" % (e, rd), "v%sz%d" % (e, rd)
-            op("v", lambda dq=dq, i=i: v.tensor_copy(T[dq][:].bitcast(dt.uint32), T[wq][:].bitcast(dt.uint32).indirect(T[wn][:, 8 * i:8 * i + 8])),
-               [k for k in wk if k[:2] != "az"], [dq], picked(128), "V")
-            op("s", lambda dz=dz, i=i: s.activation(T[dz][:], T[wz][:].indirect(T[wn][:, 8 * i:8 * i + 8]), F.Copy), [k for k in wk if k[:2] != "aq"], [dz], picked(128), "V")
-        for i, e in enumerate("" if PAR["vg"] else "eo"):
-            dq, dz = "v%sq%d" % (e, rd), "v%sz%d" % (e, rd)
-            for b in range(4):
-                mm(VB[b], "e%sq" % e, "e%sz" % e, 128 * b, dq, dz, 0, 128, [dq, dz, "e%s%d" % (e, b)], e == "e", e == "o", "V")
-        for b in range(len(VB)):
-            cp("v" if b in PAR["vv"] else "s", T.vt[:, b:512:4], P[VB[b]][:, 0:128], ["p%d" % VB[b]], ["vt%d" % b], 128, 1.0 / 32, "V")
-        if PAR["far"] == "X":
-            quant("uq%d" % rd, "uz%d" % rd, 0, 128, T.vt[:], ["vt%d" % b for b in range(4)], ["U%d" % rd, "Uz%d" % rd], "V")
-        else:
-            quant("sq%d" % rd, "sz%d" % rd, 0, 128, T.vt[:], ["vt%d" % b for b in range(4)], ["out%d" % rd], "V")
-            if PAR["far"] == "V":
-                far(T["uq%d" % rd][:].bitcast(dt.uint8), T["sq%d" % rd][:].bitcast(dt.uint8), "rc%d" % rd, 0, ne // 2, ["out%d" % rd], ["U%d" % rd], PAR["fly"] + 1000, "F")
-                far(T["uz%d" % rd][:, 0:128], T["sz%d" % rd][:, 0:128], "z%d0" % rd, ne // 2, ne, ["out%d" % rd], ["Uz%d" % rd], PAR["fly"] + 500, "F")
+            if ahead:
+                far(STEP[rd - 1], [(u8(T.aq[:, c:d]), u8(T[nq][:, c:d]))], [nk[h]], ["aq%d" % h], 200.0 + 2.5 * (d - c), "F")
+                far(STEP[rd - 1], [(T.az[:, c:d], T[nz][:, c:d])], [nk[h]], ["az%d" % h], 200.0 + 0.8 * (d - c), "F")
+        for h, (c, d) in enumerate(() if rd + 1 != PAR["ahead"] else HALF if PAR["xh"] else ((0, C),)):
+            r = [nk[h]] if PAR["xh"] else nk
+            far(STEP[rd], [(u8(T.hq[:, c:d]), u8(T[nq][:, c:d]))], r, ["hq%d" % h], 200.0 + 2.5 * (d - c), "H")
+            far(STEP[rd], [(T.hz[:, c:d], T[nz][:, c:d])], r, ["hz%d" % h], 200.0 + 0.8 * (d - c), "H")
+        src = "tf" if ahead else "th"
+        for h, (c, d) in enumerate(HALF):
+            if ahead:
+                unpack("tf", "aq", "az", c, d, ["aq%d" % h, "az%d" % h], ["tf%d" % h], banks(4), lambda b: (h, b) in par["wv"], "A%d" % h)
+        for h, (c, d) in enumerate(HALF):
+            unpack("th", nq, nz, c, d, [nk[h]], ["th%d" % h, "tr%d" % h], banks(4), lambda b: (h, b) in par["uv"], "T%d" % h)
+        for b in range(4):
+            win = sl(src, b).indirect(T.on[:, 0:8])
+            r = ["%s%d%d" % (src, h, b) for h in range(len(HALF))] + ["on"]
+            if b in par["vv"]:
+                ts(T.vt[:, b:512:4], win, 2.0, None, A.mult, None, r, ["vt%d" % b], 1, "V", picked(128))
             else:
-                def both():
-                    to = [DstId(rid=rid, pnc=pid)]
-                    g.remote_dma_fused([
-                        RemoteDMATransfer(dst_ids=to, dma_engine_mask=sum(1 << e for e in eng[:ne // 2]), remote_sem=T.sem["rc%d" % rd],
-                                          src=T["sq%d" % rd][:].bitcast(dt.uint8), dst=T["uq%d" % rd][:].bitcast(dt.uint8)),
-                        RemoteDMATransfer(dst_ids=to, dma_engine_mask=sum(1 << e for e in eng[ne // 2:]), remote_sem=T.sem["rc%d" % rd],
-                                          src=T["sz%d" % rd][:], dst=T["uz%d" % rd][:])], local_sem=T.sem["sent"])
-                    return ne
-                op("p", both, ["out%d" % rd] + (["ef0", "ef1", "ef2"], ["ef3", "wz0"], ["wz1", "vq"])[rd - 1], ["U%d" % rd, "Uz%d" % rd], PAR["rq"], "F", PAR["fly"] + PAR["xf"], "far", "rc%d" % rd)
+                act(T.vt[:, b:512:4], win, F.Copy, r, ["vt%d" % b], 1, "V", picked(128), scale=2.0)
+        vk, uq, uz, sq, sz = ["vt%d" % b for b in range(4)], T["uq%d" % rd], T["uz%d" % rd], T["sq%d" % rd], T["sz%d" % rd]
+        if ahead:
+            quant("uq%d" % rd, "uz%d" % rd, 0, 128, T.vt[:], vk, ["U%d" % rd, "Uz%d" % rd], "V")
+        else:
+            quant("sq%d" % rd, "sz%d" % rd, 0, 128, T.vt[:], vk, ["out"], "V")
+            r = ["out"] + (["ef0", "ef1", "ef2"], ["ef3", "wz0"], ["wz1", "vq"])[rd - 1]
+            if rd + 1 == PAR["ahead"]:
+                far(STEP[rd - 1] + STEP[rd], [(u8(T.gq[:]), u8(sq[:])), (T.gz[:], sz[:])], r, ["gq"], PAR["xf"], "G")
+            if PAR["far"] == "W" and not (PAR["ahead"] and rd == 3):
+                far(STEP[rd - 1], [(u8(uq[:]), u8(sq[:])), (uz[:], sz[:])], r, ["U%d" % rd, "Uz%d" % rd], PAR["xf"], "F")
+            else:
+                far(STEP[rd - 1], [(u8(uq[:]), u8(sq[:]))], ["out"], ["U%d" % rd], 450.0, "F")
+                far(STEP[rd - 1], [(uz[:, 0:128], sz[:, 0:128])], ["out"], ["Uz%d" % rd], 300.0, "G")
         return nk, kdk
 
-    quant("vq", "vz", 0, 128, T.vin[:], ["vin"], ["vq"])
     for rd in (1, 2, 3):
         nk, kdk = one_round(rd)
 
-    mm(SS, "vq", "vz", 0, "xq3", "xz3", 0, C, nk + ["vq"], True, True)
-    cp("s", T.yt[:], P[SS][:, 0:C], ["p%d" % SS], ["yt"], C)
+    now[0] = "4"
+    mm(SS, "vq", "vz", 0, "xq3", "xz3", 0, C, nk + ["vq"], True, True, "y")
+    cp("s", T.yt[:], P[SS][:, 0:C], ["p%d" % SS], ["yt"], C, None, "y")
+    dma("s", T.y[:], T.yt[:], ["yt"], [], "outs", "y")
     for h in range(2):
-        ts(T.kf[:, :, h, :], T.kd[:, h, :, 0, :] if twice else T.kd[:, 0, :, h, :], -1.0, T.pf[:, 2 + h:3 + h], A.mult, A.add, kdk + ["pf%d" % (2 + h)], ["kf%d" % h])
-    if PAR["vg"]:
-        ts(T.npg[:], T.nd[:], -1.0, None, A.add, None, ["nd0", "nd1"], ["nop"])
-    else:
-        ts(T.nop[:], T.nd[:, :, 0, :], -1.0, None, A.add, None, ["nd0"], ["nop"])
-    dma("y", T.oc[:], T.xq3[:].bitcast(dt.uint8), nk, [], "outy")
+        ts(T.kf[:, :, h, :], T.kd4[:, h] if by_product[2] else T.kd[:, :, h, :], -1.0, T.pf[:, h:h + 1], A.mult, A.add, kdk + ["pf%d" % h], ["kf%d" % h], 1, "o")
+    ts(T.npg[:], T.nd[:], -1.0, None, A.add, None, ["nd0", "nd1"], ["nop"], 1, "o")
+    dma("y", T.oc[:], u8(T.xq3[:]), nk, [], "outy", "o")
     for k in range(4):
-        dma("y", T.osc[4 * k:4 * k + 4, :], T.xz3[32 * k:32 * k + 4, :], nk, [], "outy")
+        dma("y", T.osc[4 * k:4 * k + 4, :], T.xz3[32 * k:32 * k + 4, :], nk, [], "outy", "o")
     for a in range(4):
         for h in range(2):
-            dma("y", T.op[2 * a + h, 0:C], T.kf[32 * a:32 * a + 12, :, h, :], ["kf%d" % h], [], "outy")
-    dma("s", T.y[:], T.yt[:], ["yt"], [], "outs")
-    for a in range(4):
-        for i in range(2):
-            dma("y", T.op[2 * a + i, C:C + 128], T.npg[32 * a:32 * a + 8:2, :, i, :] if PAR["vg"] else T.nop[32 * a + i:32 * a + 8:2, :, :], ["nop"], [], "outy")
-    dma("s", T.uc[:], T.uq3[:].bitcast(dt.uint8), ["U3"], [], "outs")
+            if by_product[2]:
+                for j in range(3):
+                    dma("y", T.op[2 * a + h, 128 * j:128 * j + 128], T.kf[32 * a + 8 * j:32 * a + 8 * j + 4, :, h, :], ["kf%d" % h], [], "outy", "o")
+            else:
+                dma("y", T.op[2 * a + h, 0:C], T.kf[32 * a:32 * a + 12, :, h, :], ["kf%d" % h], [], "outy", "o")
+            dma("y", T.op[2 * a + h, C:C + 128], T.npg[32 * a:32 * a + 8:2, :, h, :], ["nop"], [], "outy", "o")
+    dma("s", T.uc[:], u8(T.uq3[:]), ["U3"], [], "outs", "u")
     for k in range(4):
-        dma("y" if k % 2 == 0 else "s", T.usc[4 * k:4 * k + 4, :], T.uz3[32 * k:32 * k + 4, 0:128], ["Uz3"], [], "outy" if k % 2 == 0 else "outs")
+        dma("y" if k % 2 == 0 else "s", T.usc[4 * k:4 * k + 4, :], T.uz3[32 * k:32 * k + 4, 0:128], ["Uz3"], [], "outy" if k % 2 == 0 else "outs", "u")
 
     count, seen, nd = {}, {q: {} for q in queues}, [0]
     for i in lay_out(calls):

@@ -5,12 +5,26 @@ N, C, STEP = 4, 384, (1, 2, 3)
 BIG = 1e29
 HW = 388
 PAR = {"ttg": 1.6, "g": 1.56, "dl": 1100.0, "ld": 600.0, "dq": 140.0, "rq": 450.0, "fly": 450.0, "xf": 800.0, "first": 1000.0,
-       "lat": 190.0, "own": 240.0, "tw": 40.0, "tc": 0.55, "far": "W", "ahead": 2, "xh": True, "bias": {}}
+       "lat": 190.0, "own": 240.0, "tw": 40.0, "tc": 0.55, "far": "W", "ahead": 2, "fl": True, "os": True, "kl": 450.0, "xh": True, "bias": {}}
 for _h in (1, 2, 3):
     PAR.update({"av%d" % _h: (), "bv%d" % _h: (), "mv%d" % _h: ("vvps", "psps", "pspp", "vsvs"), "xv%d" % _h: ((0, 1), (0, 2), (1, 1), (1, 2)),
                 "uv%d" % _h: ((0, 0), (1, 0), (1, 1), (1, 2)), "wv%d" % _h: ((1, 0), (1, 1)), "vv%d" % _h: (0, 1), "duv%d" % _h: (), "tv%d" % _h: (),
-                "cut%d" % _h: (256,), "down%d" % _h: "turn", "kq%d" % _h: "yyyy", "gb%d" % _h: (4,), "st%d" % _h: ()})
+                "cut%d" % _h: (256,), "down%d" % _h: "turn", "kq%d" % _h: "yyyy", "gb%d" % _h: (4,), "st%d" % _h: (), "za%d" % _h: (), "vp%d" % _h: 0, "km%d" % _h: "psspsspsspsspssp"})
 PAR.update({'xh': False, 'mv2': ('ssss', 'ssss', 'vvvs', 'vsps'), 'xv2': ((1, 0), (1, 3)), 'uv2': (), 'wv2': ((0, 2), (1, 0), (1, 1)), 'vv2': (0, 3), 'gb2': (), 'st2': (3, 5, 7), 'order': {'v': '0t000q01070u0405080r020c030e0k090s0i0j0d0h0n0o0m0l0g0v060w0p0b0a0f0F0x0G0y0N0H0O0z0I0Q0A0P0J0C0B0T0K0D0U0L0S0E0V0R0M0W190X1a0Z0Y1c1b101f1d1e1g111h1j1i1k121l1m1n14131o15161p171q181r1s1t1u1v1E1w1F1x1G1y1M1H1N1z1O1I1A1B1S1U1R1C1J1D1T1P1Y2f2i2h2g1Q1V2j202k1Z2n2l2m1K2o211X2p1L2q2r25262s1W2827292324222a2t2c2b2d2u2e2v2w2x2y2H2z2I2A2P2J2Q2B2R2K2C2S2L2V2E2D2M2F2W2N2G3y2X2T2O2Y3b2Z3c31303e3d323g3f3h3i333j3l3m3k343n3z2U3o3p35363q38373r393A3s3a3t3u3v3w3x', 's': '0100030402070a080e05090d060i0k0f0b0g0r0j0c0p0l0v0m0x0q0s0h0t0n0o0C0w0D0z0E0y0F0u0B0A0G0I0J0H0L0K0R0N0O0M0P0Z0Q15170S0U0W0T0X0V0Y101i1j1k1l1314111b181n1m121d1c161f191e1a1h1g1o1p1q1r1s1C1B1t1v1u1x1w1y1D1z1E1F1A1I1H1G1M1J1T1K1O1N1Z1V1P1Q1U1W211X26201R271L1Y231S22282924252a2c2d2b2f2e2g2h2k2j2i', 't': '000504070201030a060e0g090c080b0d0k0i0h0f0o0j0m0p0l0n0r0q0t0s0u0v0x0w0y0A0E0B0D0C0z0P0H0L0F0N0J0G0I0K0M0R0T0Q0U0S0O0X0V0W0Y0Z1110121315171814161b1e191f1a1d1h1c1l1j1n1g1p1i1k1r1m1o1v1t1q1s1u1w1y1x1z1A1B1E1C1D1F', 'p': '010002050403080706090a0b0c0e0f0g0h0d0j0l0k0n0m0i0p0o', 'y': '0100040205030q070i0o0c0m0b0n0j0k0p0h0g0a060d090e0f0l080s0r'}})
+PAR.update({'xh': True, 'mv1': ('ppss', 'vsss', 'pppp', 'vsvs'), 'xv1': ((0, 2), (0, 3), (1, 0), (1, 2), (1, 3)), 'uv1': ((0, 0), (1, 0), (1, 1), (1, 2)), 'vv1': (0, 1), 'tv1': (3,), 'down1': 'mm', 'gb1': (3,), 'st1': (4,), 'za1': ((0, 2), (0, 3), (1, 3)),
+            'mv2': ('ssss', 'vvss', 'vpvs', 'vsvs'), 'xv2': ((1, 0),), 'uv2': ((0, 2), (0, 3), (1, 1)), 'wv2': ((0, 2), (1, 1)), 'vv2': (0, 3), 'gb2': (), 'st2': (3, 5, 7), 'za2': ((0, 2), (0, 3), (1, 1), (1, 3)),
+            'mv3': ('ppps', 'psvv', 'spvp', 'vsvs'), 'xv3': ((0, 2), (1, 0), (1, 1), (1, 2)), 'uv3': ((1, 1), (1, 2)), 'vv3': (1, 3), 'cut3': (224,), 'gb3': (), 'st3': (4,), 'za3': ((0, 1), (0, 2), (0, 3), (1, 3)),
+            'order': {'v': '000w0B0x01070k080v0605020d040y0f0c0m0n0p0z0g0i0A0r0q0s0t0l0o0E0D0e0G0P0H0I0Q0F0J0R0K0h030b0X0L0S0Y0j0C0T0Z0a0u0U1117100V18190W0M0N1a130O12141m1l1n1o1r1b1p151q1c1s1d1t1w1u1v1e1x1y1z1A161f1g1B1h1i1C1j1E1k1D1F1H1G091I1J1K1S1L1T1M201U211N1V1P221O1W1Q23261R1X2v242w2x2y1Y2z2D2C28272B2A25292e2E1Z2g2f2F2d2h2c2l2G2n2H2k2m2a2o2j2i2b2p2q2s2r2t2I2u2J2M2N2O2L2K2P2X2Q2Y2R2Z2S35302U2T3736312V3R3Q393f2W32383g3h333e3i3v3j343w3x3y3D3m3k3z3a3A3B3n3C3b3E3F3o3l3G3J3I3H3q3p3d3c3K3s3r3t3S3L3u3M3N3O3P', 's': '000102050403060a0c0e0b0j0809070d0l0r0f0t0g0w0y0D0E0s0k0F0u0m0G0v0n0x0H0p0q0i0A0h0z0I0o0C0B0J0L0K0M0O0N0R0P0S0Q0U100T12170V1k1l0Y1n0X0Z1m111d191p1q1o1r131f1u1s1t1a1418151e1b1g1h0W1c161j1i1w1v1x1y1A1z1F1G1D1B1C1I1H1J1K1E1M1Q1S1L1W292c2b1Y2a1X1N24221Z1O1R2e2d23202f1T26251U2g1P2821271V2h2i2j2l2k2m2n2o2p2q2t2s2r', 't': '0102000403050607090b080a0j0h0f0d0e0c0l0g0k0m0n0i0p0o0r0s0t0u0q0w0v0y0x0A0C0z0B0F0D0E0G0I0L0H0K0J0Q0M0N0O0U0S0R0T0Y0P0V1210130W0X110Z1514161718191b1a1f1c1g1e1d1i1l1k1n1m1h1j1o1s1q1u1r1p1w1y1A1C1t1v1z1x1E1G1F1H1D1B1J1I1L1K1N1M1O1P1Q', 'p': '010200030405060807090b0a0e0c0d0g0h0i0f0k0j0l0o0n0m0q0p', 'y': '010003050708090602040t0j0r0h0n0l0f0a0e0c0g0o0u0i0m0q0d0k0s0p0b0v0w'}})
+PAR.update({'order': {'v': '00010y0v0z060x03080k0B050402070a0f0w0c0o0m0p0A0n0d0r0q0s0t0C0D0b090l0G0E0S0H0I0T0J0F0U0K0M0L0N100V0O0e0i110W0u0j120X1a0g130Y1c1b0Z0P0Q0h1d160R1517141o1p1q1r1u1e1s181f1w1v1g1t1z1x1y1h1A1C1B1D191i1j1E1l1k1F1m1H1n1G1I1K1J1L1M1N1V1O1W1P231X241Q1Y1S251R1Z1T29261U202z2a2y2B2A212C272E2h2G2b2D2F222H282c2i2j2I2g2k2J2f2o2K2q2n2p2d2e2r2m2l2t2s2u2v2w2L2x2M2P2Q2R2O2N2S302T312U322V38333a2X392W342Y3U3T3i2Z353j3b3k3h363l3A3y3c3B3z3m3n373C3G3p3d3E3q3F3D3e3I3H3r3o3J3M3K3L3f3g3s3t3N3v3u3w3O3x3V3P3Q3R3S', 's': '00010204030508070e0a0j09060l0d0r0b0f0w0g0t0y0D0E0s0c0k0F0u0m0v0G0x0n0H0o0p0A0h0i0z0I0q0B0C0J0L0K0M0O0N0Q0R0S0P0U100T12171l1k1m0V1n190W0Z1d111o1p1q1r1f131s1u1t1a140Y181e1b1g1h0X161c151i1j1v1w1x1y1z1A1F1G1B1E1D1C1K1H1I1J1M1Q1S1L1W292a2b1Y1X2c1N221Z1O241R232e2d202f1T251U262g211P27281V2h2i2j2k2l2m2n2o2p2q2s2t2r', 't': '0102000306070504090d0a080b0e0c0f0j0n0l0h0g0m0p0k0i0r0o0s0q0t0u0w0v0y0x0A0z0C0B0F0D0J0H0I0E0G0L0O0N0Q0M0K0U0S0P0R0W0T0Y0V10120Z130X111415161718191a1b1c1e1h1g1f1d1i1n1p1k1j1l1m1o1u1q1s1r1y1A1w1t1C1x1v1z1G1E1F1B1D1H1I1J1K1L1N1M1O1P1Q', 'p': '010200040307080506090b0a0e0c0d0g0h0i0f0k0l0j0n0o0m0q0p', 'y': '010002050308060709040p0f0h0j0t0r0n0l0c0a0d0e0g0b0k0s0i0m0u0o0q0w0v'}})
+PAR.update({'mv1': ('vsvs', 'pppv', 'pppp', 'vsvs'), 'uv1': ((0, 0), (1, 1), (1, 2)), 'duv1': (1,), 'mv2': ('ppss', 'pvvv', 'psps', 'vsps'), 'uv2': ((0, 2), (1, 3)), 'wv2': ((0, 2), (1, 2)), 'mv3': ('ppps', 'pppp', 'pppp', 'vvsv'), 'za3': ((0, 1), (0, 3), (1, 3)),
+            'order': {'v': '0001020b0a09080c0d0e0f0g0h030i0k0x0m0l0y0j0n0z0o0p0F0r0q0A0s050H0G0B0L0w07040C0I0R0D0T060S0N0E0u0t0O0U0v0W0M150V1618171a0P190X1d1c1b1f1e1g0Y0Q0K1h1k1i1j0J100Z1l11121m13141n1o1p1q1r1s1t1u1C1v1D1w1K1E1L1x1F1y1M1z1G1A1Q1N1B1H2e2d2g2f1I2h2k1R2l1Z2j1S2i1T1P2m201O212n1J1Y2o22242p1X2526231U1V1W27282a292q2b2c2r2t2u2v2s2E2w2F2x2M2G2N2y2H2O2z2I2B2A2Q2P2U2C2J2D2V2W2K2T2X2R2Y3c3a3d2Z3b2L3e2S3g3i313f303h3k3j323l3n3m3o3335343p3736383q393r3s3t3u', 's': '00010204030506070d09080b0a0i0c0k0n0p0e0s0u0o0A0z0f0j0q0B0r0l0g0h0t0m0D0w0C0v0E0x0y0F0H0I0J0G0L0K0O0N0M0P0R0W0Q0Y111g1f0S1i0T1h13181j1l1k1m0Z0X1p1o1n1a14100V1219151b1c160U171d1e1q1r1s1t1u1v1C1B1x1A1z1w1y1F1G1D1E1I1M1H1O1R2j2k1J1T1K23221S1W1N1U241V1Y1P25261Q1X271L201Z28212a292c2l2b2d2e2f2g2h2i2n2o2m', 't': '01020003040705090b080a0e0f060d0h0c0j0l0n0k0i0m0g0p0t0o0u0q0r0s0w0v0y0x0z0A0C0B0F0D0J0I0H0G0K0E0O0M0N0L0Q0U0S0P0T0R0Y0V0W100Z0X12131114151617181a191b1d1e1f1g1h1c1i1m1n1k1l1p1j1o1t1v1q1r1x1s1z1u1w1y1B1D1F1C1A1E1G1I1H1K1J1M1L1N1O1P', 'p': '0g0d00070401020f0605030a0b0c09080e0k0l0n0j0i0m0h0o0p0q0t0r0s0v0u0A0B0C0w0y0x0z0E0F0D0M0N0L0K0J0I0G0H0P0O', 'y': '000102050403070609080n0h0l0r0f0t0j0p0e0a0m0u0i0c0o0s0g0k0d0q0b0v0w'}})
+PAR.update({'mv1': ('vsvs', 'pppv', 'ssss', 'vsvs'), 'duv1': (), 'tv1': (2, 3), 'gb1': (), 'mv2': ('ppss', 'psvv', 'ppvv', 'vspv'), 'xv2': ((1, 0), (1, 1)), 'uv2': ((0, 3), (1, 3)), 'down2': 'mm', 'kq2': 'yyss', 'st2': (4, 7), 'mv3': ('vsvs', 'pppp', 'ppps', 'vsvp'), 'xv3': ((0, 3), (1, 0), (1, 3)), 'uv3': ((0, 3), (1, 0), (1, 1)), 'down3': 'mm', 'za3': ((0, 2), (0, 3), (1, 3)),
+            'order': {'v': '000102080a07090b0c0d0e0f030g0h0j0w0i0l0x0k0m0y0p0q0o0n0E0z0r050F0G0A0K060v040B0H0P0C0R0Q0D0s0t0S0O0u0T0L0V150U14171619180M1b0W1c1a1f1d1e0X0I0N1g1h1i1j0J0Y0Z1k11101l12131m1n1o1p1q1s1r1t1v1x1u1w1y1H1z1A1B1C1I1D1P1J1Q1K1R1L1T1S1Z1M1F1E20211Y1G1U222j2i2k2l1N2m2q232n2o2p1O2r241V282s2t292u2a272v252b261W1X2c2d2e2f2g2w2h2x2y2z2A2P2F2B2D2Q2E2G2C2X2R2J2H2K2Y2I2S2L2Z2T3330372U38392V343a363b2N2M2W2O353d3c3n3m3o3p3r3q3e3u3s3t3w3v3f323x3z3y3h3g313A3i3j3B3k3D3l3C3E3F3G', 's': '000102040503070908060d0a0i0b0c0n0k0e0p0x0o0D0C0v0j0q0E0f0l0F0w0m0G0r0u0g0s0z0y0H0t0h0B0A0I0K0L0M0J0O0N0S0R0T0U0Q0P0W0V1113170X190Y1i1j0Z1k1l18121c1m1n1o1p1e1a1q1r1b141d151f1g16101h1s1t1u1v1w1x1F1E1B1y1C1A1z1G1D1L1I1H1Q1J1K1S1V1M1N1X1R1W2127282p2o1Y291Z231T222b1U2a2c1P24252d2e201O262f2g2h2q2i2j2l2k2m2n2s2t2r', 't': '010200030507060408090c0e0b0a0d0f0h0j0n0l0g0m0i0k0p0r0o0q0s0t0u0w0v0y0x0z0C0A0B0F0G0H0D0J0I0K0L0M0O0N0S0E0Q0P0U0R0T0V0W0X100Y121411150Z13161718191a1c1b1d1e1f1g1h1i1j1k1n1l1m1o1p1q1r1t1s1v1u1w1y1A1C1E1D1z1x1B1G1K1H1L1F1I1J1M1N1P1O1R1S1Q1T1U', 'p': '05000107080f0603040a020b0c0d0e090g0i0h0j0l0k0o0m0n0p0q0v0w0x0t0s0r0u0C0E0D0A0y0B0z0F0H0G', 'y': '000104030205060709080a0b0d0c0f0e0p0G0H0q0B0x0u0l0O0L0D0K0F0n0y0N0j0i0g0k0m0h0w0Q0s0r0C0A0E0t0z0v0J0I0o0P0S0M0R'}})
+PAR.update({'av1': (), 'bv1': (), 'mv1': ('ppps', 'sppp', 'ssss', 'ssss'), 'xv1': ((0, 2), (1, 1), (1, 2)), 'uv1': ((0, 3), (1, 1), (1, 2)), 'vv1': (1, 3), 'duv1': (), 'tv1': (1, 3), 'cut1': (224,), 'down1': 'mv', 'gb1': (3,), 'st1': (4,), 'za1': ((0, 1), (0, 3), (1, 3)), 'km1': 'psspssvsppvspssv', 'mv2': ('sppv', 'vppp', 'vspv', 'vspv'), 'xv2': ((1, 2), (1, 3)), 'uv2': ((0, 0), (0, 3)), 'wv2': ((0, 2), (1, 2)), 'vv2': (0, 3), 'cut2': (256,), 'down2': 'mv', 'gb2': (), 'st2': (5, 7), 'za2': ((0, 2), (0, 3), (1, 0), (1, 3)), 'km2': 'ppsssssssvssvssp', 'mv3': ('ppps', 'pppp', 'ppps', 'pvsv'), 'xv3': ((0, 2), (1, 1), (1, 2)), 'uv3': ((0, 3), (1, 1), (1, 2)), 'vv3': (1, 3), 'cut3': (224,), 'down3': 'mv', 'gb3': (), 'st3': (4,), 'za3': ((0, 1), (0, 3), (1, 3)), 'km3': 'psspspssppsspssv',
+            'order': {'v': '0001020907080a030b0c0d0e0f0h0k0n0i0l0o0y0j0p050m0z0s0g0q0A0r0x0G0B060H0t0u0C0v0K0I040P0w0D0J0R0E120Q0M0F0N0S140L11130T0O150U17160V19181b1a0W1c1e1d1f0Y0X1g0Z1h101i1j1k1l1o1m1n1p1s1v1q1t1w1E1u1r1x1F1z1y1M1G1N1A1B1H1O1C1P1D1I2f1J2h1R2g2i1K2j1S1Y2n2k2m2l1Z1T201U2o1L2p211X2q2r251W2s2724261V1Q282322292a2c2b2d2t2e2u2w2x2y2v2N2C2z2F2O2A2D2G2P2E2B2H2V2Q2I2X2W2R2Z2S2Y332J2K2T2L323435372M2U36303k3i3l383j313o3m393a3q3p3n3s3r3b3t3v3u3c3d3w3e3f3x3g3y3h3z3A3B3C', 's': '0001020405030e0f0g0h0i080b0a0d070j060c090l0p0r0k0v0M0N0m0x0D0n0w0q0o0F0O0y0s0P0Q0E0t0R0H0z0A0u0C0B0G0S0T0I0J0L0K0U0V0W0X0Y0Z101c1e1d1f1b131218171915161a11141h1g1l1n1C1i1D1q1j1F1E1s1w1m1H1G1I1J1o1y1L1K1t1p1r1k1x1u1z1A1v1B1N1M1O1Q1P1R1X1Y1T1V1S1W1U292a2d282b2h211Z2620272422252c232m2j2o2e2s2f2y2z2n2i2A2p2k2u2l2t2B2C2P2q2w2D2r2v2E2F2Q2g2x2G2H2R2I2J2K2L2M2N2O2U2T2S', 't': '0102030006070508090a0b0c040e0h0f0d0j0l0g0i0k0m0r0t0p0n0s0o0q0u0w0v0y0x0A0z0B0C0F0G0H0D0J0I0K0L0E0O0Q0P0S0N0M0U0W0T0R0V100X140Y121513110Z171618191b1a1d1c1g1i1j1f1e1h1k1m1n1l1o1q1p1r1y1s1t1w1v1A1u1x1z1B1C1E1D1G1I1K1F1J1H1L1M1N1P1O1R1Q1S1T1U', 'p': '0c0002050401030706080a090b0h0d0f0g0e0i0j0k0m0n0l0o0q0p0t0r0s0w0u0v0x0y0E0F0G0B0z0C0A0D0H0M0I0L0J0K0P0O0N0R0S0Q0T0U0V0W0X0Z0Y', 'y': '0001020304050b0f0n0j0h0l060o0i090e0q080c070a0g0m0d0k0p0s0r'}})
+PAR.update({"smin": 72.0, "gp": 100.0, "lat": 170.0, "own": 228.0, "tw": 35.0, "tc": 0.5, "dl": 1250.0, "ld": 500.0, "fly": 260.0, "kl": 300.0, "ttg": 1.56})
+PAR.update({'mv1': ('sppp', 'vvpv', 'ssss', 'svss'), 'xv1': ((0, 2), (1, 2), (1, 3)), 'uv1': ((0, 0), (0, 3), (1, 1)), 'vv1': (1, 3), 'tv1': (1,), 'cut1': (224,), 'down1': 'mv', 'gb1': (3,), 'st1': (4,), 'za1': ((0, 3), (1, 2), (1, 3)), 'km1': 'sssspsssssvssvsv', 'mv2': ('sppv', 'vpsp', 'vvvv', 'vsps'), 'xv2': ((1, 0), (1, 2), (1, 3)), 'uv2': ((1, 1), (1, 3)), 'wv2': ((0, 2), (1, 2)), 'vv2': (0, 3), 'cut2': (256,), 'down2': 'mv', 'gb2': (), 'st2': (5, 7), 'za2': ((0, 2), (0, 3), (1, 0), (1, 3)), 'km2': 'psssspssvsvssvsv', 'mv3': ('ppps', 'pppp', 'vpvs', 'vvvv'), 'xv3': ((0, 2), (1, 1), (1, 2)), 'uv3': ((0, 3), (1, 1), (1, 2)), 'vv3': (1, 3), 'cut3': (224,), 'down3': 'mv', 'gb3': (), 'st3': (4,), 'za3': ((0, 1), (0, 3), (1, 3)), 'km3': 'pvssvspsssvssssp',
+            'order': {'v': '000102090a07080b0c0d0e0f0g0h0k0n0i0l0o0y0m0j0p030z050q0s0G0r0A0H0x0B0t0u0I060K0C0v0J0S0D0w0T0U0E0L160M0V150N180F170W0O190X1d1b040Y1c1a1f1e0Z1g0Q1i0R1h100P1j12111k131m141l1n1o1p1r1s1q1t1w1z1u1x1A1K1B1y1v1L1F1D1C1E1S1M1T1G1H1N1I1U1O1X1J1V1P2m242n2o2p1Q2q251Y232u262r2t2s20272v1Z1R2w2z2y2d2c2x222e2A2f1W2g29282a2b212h2i2j2B2k2l2C2E2F2D2G2H2X2I2N2K2Y2L2O2Z352P2M2J3630372R2Q2S31383d39323e2T2U332V3c3a3f3h2W343g3y3l3w3b3i3x3C3z3E3m3A3B3D3j3n3F3G3k3H3I3J3r3q3p3o3K3t3s3L3u3M3v3N3O3P3Q', 's': '0001020405030j0k0l0i0m07060b0c0h0e0d08090a0f0n0g0o0p0t0v0y0q0O0r0A0Q0u0P0z0G0I0B0w0C0R0S0H0T0x0D0E0F0K0s0J0V0U0N0L0M0W0X0Y100Z11121f1d1e1g181413151b1a1c1619171i1m1h1o1s1E1F1u1H1j1G1k1x1n1I1J1L1K1v1p1M1z1y1t1q1B1w1A1r1l1C1D1O1N1P1R1Q1S1Y1Z1T1X1V1U1W2c2b2a2d2f2j272e2426252120292322282l2g2o2h2q2u2k2z2p2B2A2r2w2s2m2v2n2C2E2D2y2Q2x2F2G2t2i2H2I2J2S2K2R2L2M2N2O2P2V2U2T', 't': '0102030006070508090c0a0b0e0d0f040j0h0g0i0k0p0l0m0r0n0t0q0u0o0s0w0v0y0x0A0z0C0B0F0G0H0D0I0K0J0E0L0M0O0Q0N0S0P0W0R0T0X0U0V0Y1412151310110Z171618191b1a1c1d1f1e1g1i1h1j1l1k1n1o1m1q1p1r1s1y1A1u1t1w1v1C1G1E1x1z1D1B1I1F1H1J1K1L1M1N1P1O1R1Q1S1T1U', 'p': '010002070b0409060805030c0a0d0e0g0f0h0i0j0k0n0l0m0o0p0q0r0v0w0x0t0s0u0A0y0z0D0B0C0I0G0H0E0F0K0J', 'y': '0001020304050j0a080f0i0e0o0l0b0p0c0h090q0n0k0g0m0d060s070r'}})
 
 
 def _sb(n, d):
@@ -20,19 +34,21 @@ def _sb(n, d):
 CODE, PL, BF, F32, U16, I32 = "float8_e4m3fn_x4", "uint8", "bfloat16", "float32", "uint16", "int32"
 SCRATCH = {
     "xin": _sb(4 * C, BF), "uin": _sb(512, BF), "vin": _sb(512, BF), "wq": _sb(512, CODE), "vq": _sb(128, CODE),
-    "c32": _sb(128, BF), "eye": _sb(128, BF), "pidx": _sb(1, I32), "pi2": _sb(8, I32), "pf": _sb(10, F32),
-    "ef": _sb(520, BF), "efq": _sb(512, CODE), "cz": _sb(1152, PL),
-    "cap": _sb(C, F32), "st": _sb(C, F32), "ex": _sb(C, F32), "nr": _sb(C, BF), "tr": _sb(1024, BF), "nr4": _sb([4, 128], BF), "tr4": _sb([4, 128], BF),
+    "c32": _sb(128, BF), "eye": _sb(128, BF), "tb": _sb(160, F32), "pf": _sb(160, F32), "quad": _sb(1, F32),
+    "ef": _sb(520, BF), "efq": _sb(512, CODE), "cz": _sb(1152, PL), "eh": _sb(520, BF), "ehq": _sb(512, CODE), "ehz": _sb(512, PL), "za": _sb(4 * C, BF),
+    "ee": _sb(520, BF), "eeq": _sb(512, CODE), "eez": _sb(512, PL), "eo": _sb(520, BF), "eoq": _sb(512, CODE), "eoz": _sb(512, PL),
+    "cap": _sb(C, F32), "st": _sb(C, F32), "ex": _sb(C, F32), "nr": _sb(C, BF), "tr": _sb(1024, BF), "nr4": _sb([4, 128], BF), "tr4": _sb([4, 128], BF), "tr3": _sb([3, 128], BF), "km": _sb([32, 2], BF),
     "kd": _sb([2, 2, 16], BF), "kd4": _sb([2, 2, 16], BF), "ko": _sb(64, BF), "ct": _sb(32, BF), "it8": _sb(4, F32), "ordk": _sb(4, U16), "kf": _sb([2, 2, 16], F32),
     "n64": _sb([2, 32], F32), "nd": _sb([2, 2, 16], F32), "no": _sb(64, F32), "npg": _sb([2, 2, 16], F32),
     "cn": _sb(8, F32), "ca": _sb(8, F32), "sg": _sb(8, F32), "ep": _sb(8, F32), "eq": _sb(8, F32), "ob": _sb(8, F32), "one": _sb(8, F32), "zero": _sb(C, BF), "b0": _sb(1, F32), "ordn": _sb(2, U16), "on": _sb(16, U16), "ok": _sb(32, U16),
     "hist": _sb(9 * HW, F32), "ab": _sb(8 * C, BF), "al": _sb(8 * HW, BF), "bl": _sb(8 * C, BF), "bv": _sb(8 * C, BF),
     "th": _sb(4 * C, BF), "tf": _sb(4 * C, BF), "du": _sb(512, BF),
     "zt": _sb(4 * C, BF), "xt": _sb(4 * C, BF), "vt": _sb(512, BF), "yt": _sb(C, F32),
-    "xq0": _sb(512, CODE), "xz0": _sb(512, PL), "hq": _sb(C, CODE), "hz": _sb(C, PL), "gq": _sb(128, CODE), "gz": _sb(512, PL), "aq": _sb(C, CODE), "az": _sb(C, PL),
+    "xq0": _sb(512, CODE), "xz0": _sb(512, PL), "hq": _sb(C, CODE), "hz": _sb(C, PL), "gq": _sb(128, CODE), "gz": _sb(512, PL), "aq": _sb(C, CODE), "az": _sb(C, PL), "bz": _sb(512, PL),
     "zq": _sb(C, CODE), "zz": _sb(C, PL)}
 for _h in (1, 2, 3):
-    SCRATCH.update({"xq%d" % _h: _sb(C, CODE), "xz%d" % _h: _sb(C, PL), "uq%d" % _h: _sb(128, CODE), "uz%d" % _h: _sb(512, PL),
+    SCRATCH.update({"xq%d" % _h: _sb(C, CODE), "xz%d" % _h: _sb(512 if _h == 2 else C, PL), "uq%d" % _h: _sb(128, CODE), "uz%d" % _h: _sb(512, PL),
+                    "veq%d" % _h: _sb(128, CODE), "vez%d" % _h: _sb(128, PL), "voq%d" % _h: _sb(128, CODE), "voz%d" % _h: _sb(128, PL),
                     "sq%d" % _h: _sb(128, CODE), "sz%d" % _h: _sb(512, PL)})
 for _b in range(8):
     SCRATCH["p%d" % _b] = ("psum", [128, 512], F32)
@@ -44,7 +60,7 @@ ABC = "0123456789abcdefghijklmnopqrstuvwxyzABCDEFGHIJKLMNOPQRSTUVWXYZ"
 
 
 def lay_out(calls, ways_only=False):
-    lastw, readers, lastp = {}, {}, {}
+    lastw, readers, lastp, wide = {}, {}, {}, []
     for i, c in enumerate(calls):
         hard, soft = set(), set()
         for k in c["r"]:
@@ -62,6 +78,11 @@ def lay_out(calls, ways_only=False):
                     ahead, mine = mine, []
                 hard.update(ahead)
                 lastp[k] = (c["q"], ahead, mine + [i])
+        if c["q"] == "p" and c["kind"] == "op":
+            if c["tag"][:1] in ("K", "m"):
+                hard.update(wide)
+            else:
+                wide.append(i)
         for k in c["w"]:
             lastw[k], readers[k] = i, []
         for k in c["r"]:
@@ -122,9 +143,13 @@ def rank_program(g, core, T, topo):
     P = [T["p%d" % b] for b in range(8)]
 
     def op(qn, f, r, w, n, tag="", late=0.0, kind="op", sem=None):
+        if kind == "op" and qn in "sp":
+            n = max(n, PAR["smin"]) if qn == "s" else n + PAR["gp"]
         calls.append({"q": qn, "f": f, "r": list(r), "w": list(w), "ns": n, "tag": tag + now[0], "late": late, "kind": kind, "sem": sem})
 
     def plane(z, a, b):
+        if PAR["fl"] and (z in ("vz", "xz2") or z == "az" and a >= 256):
+            return T.xz2[:, 0:128] if z == "vz" else T["xz2" if z == "xz2" else "bz"][:, 128 + a:128 + b]
         if z in ("efz", "wz", "vz"):
             at = {"efz": 0, "wz": 512, "vz": 1024}[z] + a
             if PAR["far"] == "W":
@@ -139,7 +164,7 @@ def rank_program(g, core, T, topo):
         op(qn, lambda: queues[qn].dma_start(out, in_), r, w, PAR["dq"], tag, PAR["dl"] + (0.0 if r else PAR["ld"]), "dma", sem)
 
     def mm(bank, lq, lz, a, rq, rz, c, d, keys, start, stop, tag=""):
-        op("t", lambda: t.matmul_mx(P[bank][:, 0:d - c], T[lq][:, a:a + 128], plane(lz, a, a + 128), T[rq][:, c:d], T[rz][:, c:d], start, stop),
+        op("t", lambda: t.matmul_mx(P[bank][:, 0:d - c], T[lq][:, a:a + 128], plane(lz, a, a + 128), T[rq][:, c:d], plane(rz, c, d), start, stop),
            keys, ["p%d" % bank], (d - c + 16) * PAR["tc"], tag)
 
     def cp(qn, out, in_, r, w, n, scale=None, tag=""):
@@ -201,49 +226,70 @@ def rank_program(g, core, T, topo):
     dma("s", T.xin[:, 0:512], T.x[:, 0:512], [], ["xin0"], None, "L")
     dma("y", T.xin[:, 512:1024], T.x[:, 512:1024], [], ["xin1"], None, "L")
     dma("s", T.xin[:, 1024:1536], T.x[:, 1024:1536], [], ["xin2"], None, "L")
-    dma("y", u8(T.wq[:]), T.wc[:], [], ["wq"])
+    for i in range(4):
+        calls[i]["late"] += 100.0 * i - 150.0
+    first = ["uin", "xin0", "xin1", "xin2"]
+    dma("y", u8(T.wq[:]), T.wc[:], first, ["wq"])
+    calls[-1]["late"] += 1000.0
     for i in range(2):
-        dma("y", plane("wz", 256 * i, 256 * i + 256), T.ws[:, 256 * i:256 * i + 256], [], ["wz%d" % i])
-    dma("y", T.vin[:], T.v[:], [], ["vin"])
+        dma("y", plane("wz", 256 * i, 256 * i + 256), T.ws[:, 256 * i:256 * i + 256], first, ["wz%d" % i])
+    dma("y", T.vin[:], T.v[:], first, ["vin"])
+    calls[-1]["late"] += 1500.0
 
     by_product = [PAR["down%d" % h] == "mm" for h in (1, 2, 3)]
     fill(T.c32[:], 32.0, ["c32"], 64)
     op("p", lambda: g.affine_select(T.eye[:], T.c32[:], [[-1, 128]], A.is_equal, 0.0, 0, 1), ["c32"], ["eye"], 385)
-    op("p", lambda: g.iota(T.pidx[:], [[0, 1]], 0, 1), [], ["pidx"], 135)
-    op("p", lambda: g.iota(T.it8[:], [[8, 4]], 0, 0, allow_small_or_imprecise_dtypes=True), [], ["it8"], 140)
+
+    def count_up(out, pattern, base, step, w, n):
+        op("p", lambda: g.iota(out, pattern, base, step, allow_small_or_imprecise_dtypes=True), [], w, 130 + 2 * CYC * n, "i" + w[0])
+
+    def lowest(out, in_, n, r, w):
+        op("p", lambda: g.affine_select(out, in_, [[0, n]], A.is_gt, -BIG, 0, 0), r, w, 170 + 2 * CYC * n, "i" + w[0])
     fill(T.ef[:], 0.0, ["ef"], 260)
     cp("v", T.ef[:, 3:515:4], T.eye[:], ["eye", "ef"], ["ef"], 64)
-    for i, (b, sh) in enumerate(((96, 0), (112, 0), (1, 0), (6, 0), (8, 0), (15, 1))):
-        if sh:
-            ts(T.pi2[:, i:i + 1], T.pidx[:], b, sh, A.bitwise_and, A.logical_shift_right, ["pidx"], ["i%d" % i])
-        else:
-            ts(T.pi2[:, i:i + 1], T.pidx[:], b, None, A.bitwise_and, None, ["pidx"], ["i%d" % i])
-    for i, (k, m, c) in enumerate(((0, 1.0, 15.0), (0, 1.0, 31.0), (1, 1.0, 15.0), (2, 32.0, 0.0), (4, 0.125, 0.0), (5, 1.0, 0.0), (3, 0.5, 0.0))):
-        if i < 6 or any(by_product):
-            ts(T.pf[:, i:i + 1], T.pi2[:, k:k + 1], m, c, A.mult, A.add, ["i%d" % k], ["pf%d" % i])
-    ts(T.ordn[:, 0:1], T.pi2[:, 3:4], T.pf[:, 3:4], T.pf[:, 4:5], A.add, A.add, ["i3", "pf3", "pf4"], ["ordn"])
-    ts(T.ordk[:, 0:2], T.it8[:, 0:2], T.pf[:, 3:4], T.pf[:, 5:6], A.add, A.add, ["it8", "pf3", "pf5"], ["ordk0"])
+    count_up(T.tb[:, 0:32], [[0, 32]], 0, 1, ["tb0"], 32)
+    count_up(T.tb[:, 32:64], [[16, 2], [0, 16]], 0, 1, ["tb1"], 32)
+    count_up(T.tb[:, 64:96], [[0, 2], [1, 8], [32, 2]], 0, 8, ["tb2"], 32)
+    for i in range(2):
+        count_up(T.tb[:, 96 + 16 * i:112 + 16 * i], [[1, 2], [2, 4], [32, 2]], 0, 0, ["tb%d" % (3 + i)], 16)
+        if any(by_product):
+            count_up(T.tb[:, 128 + 16 * i:144 + 16 * i], [[8, 2], [1, 4], [32, 2]], 0, 16, ["tb%d" % (5 + i)], 16)
+    nt = 160 if any(by_product) else 128
+    turn(T.pf[:, 0:nt], T.tb[:, 0:nt], ["tb%d" % i for i in range(7)], ["pf"], nt, "i")
+    cp("v", T.ordn[:, 0:1], T.pf[:, 96:97], ["pf"], ["ordn"], 1, None, "i")
+    ts(T.quad[:], T.pf[:, 0:1], -8.0, None, A.mult, None, ["pf"], ["quad"], 1, "i")
+    if not all(by_product):
+        ts(T.ordk[:, 0:2], T.pf[:, 64:66], T.quad[:], None, A.add, None, ["pf", "quad"], ["ordk0"], 1, "i")
+    if any(PAR["down%d" % h] == "turn" for h in (1, 2, 3)):
+        count_up(T.tr[:, C + 15:1024:16], [[0, 40]], 0, 0, ["trz"], 40)
+    if any(PAR["down%d" % h] == "mv" for h in (1, 2, 3)):
+        count_up(T.km[:, 12:32, :], [[0, 40]], 0, 0, ["kmz"], 40)
     if any(by_product):
-        ts(T.pf[:, 7:8], T.pi2[:, 4:5], T.pf[:, 3:4], T.pf[:, 6:7], A.add, A.add, ["i4", "pf3", "pf6"], ["pf7"])
-        ts(T.ordk[:, 2:4], T.it8[:, 0:4:2], T.pf[:, 7:8], None, A.add, None, ["it8", "pf7"], ["ordk1"])
-        fill(T.tr4[:, :, 96:128], 0.0, ["tr4z"])
-        fill(T.kd4[:], 0.0, ["kd4z"])
+        ts(T.ordk[:, 2:4], T.pf[:, 128:130], T.quad[:], T.quad[:], A.add, A.add, ["pf", "quad"], ["ordk1"], 1, "i")
+        count_up(T.tr4[:, :, 111:128:16], [[0, 8]], 0, 0, ["tr4z"], 8)
+        count_up(T.kd4[:], [[0, 64]], 0, 0, ["kd4z"], 64)
     act(T.cap[:], T.ef[:, 0:C], F.Copy, ["ef"], ["cap"], C, scale=0.0, bias=BIG)
     act(T.hist[:, 0:HW], T.ef[:, 0:HW], F.Copy, ["ef"], ["h0"], HW, scale=0.0, bias=BIG)
     for b in range(4):
         quant("efq", "efz", 128 * b, 128 * b + 128, T.ef[:, 3 - b:515 - b], ["ef"], ["ef%d" % b], "E")
+    halves = sorted({b for h in (1, 2, 3) for _, b in PAR["za%d" % h]})
+    if halves:
+        act(T.eh[:], T.ef[:], F.Copy, ["ef"], ["eh"], 520, scale=1.0 / 64)
+
+    def halving(rd):
+        for b in halves:
+            if rd == (1 if any(e == b for _, e in PAR["za1"]) else 2):
+                quant("ehq", "ehz", 128 * b, 128 * b + 128, T.eh[:, 3 - b:515 - b], ["eh", "out"], ["eh%d" % b], "E")
     quant("xq0", "xz0", C, C + 128, T.uin[:], ["uin"], ["U0"], "L")
     for i in range(3):
         quant("xq0", "xz0", 128 * i, 128 * i + 128, T.xin[:, 512 * i:512 * i + 512], ["xin%d" % i], ["X0%d" % i], "L")
-    quant("vq", "vz", 0, 128, T.vin[:], ["vin"], ["vq"])
-    fill(T.ex[:, 0:C:128], -BIG, ["exz"])
-    fill(T.tr[:, C + 15:1024:16], 0.0, ["trz"])
-    fill(T.n64[:], 1.0, ["n%d%d" % (G, a) for G in range(4) for a in range(4)])
-    fill(T.hist[:, HW:9 * HW:HW], -BIG, ["hsz"])
-    fill(T.al[:, 1:8 * HW:HW], 1.0, ["alz"])
-    fill(T.cap[:, 0:C:16], -BIG, ["cap"], 1, ["cap"])
+    lowest(T.ex[:, 0:C:128], T.tb[:, 0:3], 3, ["tb0"], ["exz"])
+    lowest(T.hist[:, HW:9 * HW:HW], T.tb[:, 0:8], 8, ["tb0"], ["hsz"])
+    lowest(T.cap[:, 0:C:16], T.tb[:, 0:24], 24, ["tb0", "cap"], ["cap"])
+    count_up(T.n64[:], [[0, 64]], 1, 0, ["n%d%d" % (G, a) for G in range(4) for a in range(4)], 64)
+    count_up(T.al[:, 1:8 * HW:HW], [[0, 8]], 1, 0, ["alz"], 8)
     if any(PAR["st%d" % h] for h in (1, 2, 3)):
-        fill(T.one[:], 1.0, ["one"])
+        count_up(T.one[:], [[0, 8]], 1, 0, ["one"], 8)
         act(T.zero[:], T.ef[:, 0:C], F.Copy, ["ef"], ["zero"], C, scale=0.0)
     SV, SS = 0, 1
     turnb = [0]
@@ -266,7 +312,7 @@ def rank_program(g, core, T, topo):
         return [h for h, (a, b) in enumerate(pieces(rd)) if a < d and c < b]
 
     def unpack(dst, q, z, c, d, r, w, bs, onv, tag):
-        for b in range(4):
+        for b in bs:
             mm(bs[b], "efq", "efz", 128 * b, q, z, c, d, r + ["ef%d" % b], True, True, tag)
             cp("v" if onv(b) else "s", T[dst][:, C * b + c:C * b + d], P[bs[b]][:, 0:d - c], ["p%d" % bs[b]], [k + str(b) for k in w], d - c, 1.0 / 64, tag)
 
@@ -279,17 +325,20 @@ def rank_program(g, core, T, topo):
         uk, nk = ["U%d" % (rd - 1), "Uz%d" % (rd - 1)], ["X%d%d" % (rd, h) for h in range(len(HALF))]
         xk = ["X%d%d" % (rd - 1, h) for h in range(3 if rd == 1 else len(pieces(rd - 1)))]
         ahead = rd == PAR["ahead"]
+        halving(rd)
+        if rd == 2:
+            quant("vq", "vz", 0, 128, T.vin[:], ["vin", "out"], ["vq"], "E")
         if ahead:
-            hk = ["h%s%d" % (e, h) for e in "qz" for h in range(len(pieces(rd - 1)) if PAR["xh"] else 1)]
+            hk = ["hq%d" % h for h in range(len(pieces(rd - 1)) if PAR["xh"] else 1)]
             for b in (SV, SS):
-                mm(b, "gq", "gz", 0, "hq", "hz", 0, C, ["gq"] + hk, True, True, "B")
+                mm(b, "gq", "gz", 0, "hq", "hz", 0, C, ["gq", "gz", "hz"] + hk, True, True, "B")
         mine = SV
-        if par["down"] == "mm":
+        if par["down"] != "turn":
             SB = banks(3)
             if not ahead:
                 mm(SV, uq, uz, ua, xq, xz, 0, C, uk + xk, True, True, "S")
             for j in range(3):
-                mm(SB[j], xq, xz, 128 * j, uq, uz, ua, ua + 128, uk + xk, True, True, "S")
+                mm(SB[j], xq, xz, 128 * j, uq, uz, ua, ua + 128, uk + (xk if rd > 1 else xk[j:j + 1]), True, True, "U")
         else:
             if ahead:
                 mine = banks(1)[0]
@@ -301,14 +350,35 @@ def rank_program(g, core, T, topo):
             for j in range(3):
                 scan(T.ex[:, 128 * j + 1:128 * j + 128], P[SB[j]][:, 0:127], T.cap[:, 1:128], -BIG, A.max, A.min, ["p%d" % SB[j], "cap"], ["ex%d" % j], 128, "k")
                 tt(T.nr4[:, :, 32 * j:32 * j + 32], P[SB[j]][:, 0:128], T.ex[:, 128 * j:128 * j + 128], A.is_le, ["p%d" % SB[j], "ex%d" % j, "exz"], ["nr%d" % j], cy(128), "k")
-            scan(T.tr4[:, :, 0:96], T.nr4[:, :, 0:96], T.nr4[:, :, 0:96], 0.0, A.mult, A.add, ["nr0", "nr1", "nr2"], ["tr"], C / 2, "k")
-            turn(T.ct[:], T.tr4[:, :, 15:128:16], ["tr", "tr4z"], ["ct"], 1, "k")
+            for G in range(4):
+                scan(T.tr4[:, G, 0:96], T.nr4[:, G, 0:96], T.nr4[:, G, 0:96], 0.0, A.mult, A.add, ["nr0", "nr1", "nr2"], ["tq%d" % G], 1, "k")
+            turn(T.ct[:], T.tr4[:, :, 15:128:16], ["tq0", "tq1", "tq2", "tq3", "tr4z"], ["ct"], 1, "k")
             for a in range(4):
                 dma(par["kq"][a], T.kd4[a:128:8], T.ct[32 * a:32 * a + 32, :], ["ct", "kd4z"], ["kd4%d" % a], "m%d4%s" % (rd, par["kq"][a]), "k")
+                calls[-1]["late"] += PAR["kl"]
             kdk = ["kd4%d" % a for a in range(4)]
             for h in range(2):
                 turn(T.ko[:, 32 * h:32 * h + 32], T.kd4[:, :, h, :], kdk, ["ko%d" % h], 1, "k")
             o = 2
+        elif par["down"] == "mv":
+            for j in range(3):
+                nr = T.nr[:, 128 * j:128 * j + 128]
+                scan(T.ex[:, 128 * j + 1:128 * j + 128], P[SB[j]][:, 0:127], T.cap[:, 1:128], -BIG, A.max, A.min, ["p%d" % SB[j], "cap"], ["ex%d" % j], 128, "k")
+                tt(nr, P[SB[j]][:, 0:128], T.ex[:, 128 * j:128 * j + 128], A.is_le, ["p%d" % SB[j], "ex%d" % j, "exz"], ["nr%d" % j], cy(128), "k")
+                scan(T.tr3[:, j, :], nr, nr, 0.0, A.mult, A.add, ["nr%d" % j], ["tq%d" % j], 64, "k")
+            for a in range(4):
+                for G in range(4):
+                    dst, src, q = T.km[32 * G:32 * G + 32, a:12:4, :], T.tr3[32 * a:32 * a + 32, :, 32 * G + 15:32 * G + 32:16], par["km"][4 * a + G]
+                    r, w = ["tq0", "tq1", "tq2", "kmz"], ["km%d%d" % (a, G)]
+                    if q == "p":
+                        op("p", lambda dst=dst, src=src: g.affine_select(dst, src, [[0, 6]], A.is_ge, 0.0, 0, 0), r, w, 180.0, "K")
+                    else:
+                        cp(q, dst, src, r, w, 1, None, "K")
+            for h in range(2):
+                turn(T.kd[:, :, h, :], T.km[:, :, h], ["km%d%d" % (a, G) for a in range(4) for G in range(4)], ["kd%d" % h], 1, "k")
+            kdk = ["kd0", "kd1"]
+            turn(T.ko[:], T.kd[:], kdk, ["ko0", "ko1"], 1, "k")
+            o = 0
         else:
             turn(T.st[:], P[mine][:, 0:C], ["p%d" % mine], ["st"], C, "k")
             scan(T.ex[:, 1:C], T.st[:, 0:C - 1], T.cap[:, 1:C], -BIG, A.max, A.min, ["st", "cap"], ["ex0", "ex1", "ex2", "exw"], C, "k")
@@ -319,12 +389,15 @@ def rank_program(g, core, T, topo):
             kdk = ["kd0", "kd1"]
             turn(T.ko[:], T.kd[:], kdk, ["ko0", "ko1"], 1, "k")
             o = 0
-        ts(T.ok[:], T.ko[:].indirect(T.ordk[:, o:o + 2]), -1.0, T.pf[:, 2:3], A.mult, A.add, ["ko0", "ko1", "pf2", "ordk%d" % (o // 2)], ["ok"], 1, "k", picked(32))
+        ts(T.ok[:], T.ko[:].indirect(T.ordk[:, o:o + 2]), -1.0, T.pf[:, 47:48], A.mult, A.add, ["ko0", "ko1", "pf", "ordk%d" % (o // 2)], ["ok"], 1, "k", picked(32))
         for b, bank in enumerate(banks(4)):
             mm(bank, "efq", "efz", 128 * b, uq, uz, ua, ua + 128, uk + ["ef%d" % b, "S"], True, True, "D")
             cp("v" if b in par["duv"] else "s", T.du[:, 128 * b:128 * b + 128], P[bank][:, 0:128], ["p%d" % bank], ["du%d" % b], 128, 1.0 / 64, "D")
         if rd == 1:
-            unpack("th", xq, xz, 0, C, xk + ["S"], ["th0"], banks(4), lambda b: b in par["tv"], "T")
+            for b in range(4):
+                hs = [h for h in range(len(HALF)) if (h, b) not in par["za"]]
+                if hs:
+                    unpack("th", xq, xz, HALF[hs[0]][0], HALF[hs[-1]][1], xk + ["S"], ["th%d" % h for h in hs], {b: banks(1)[0]}, lambda b: b in par["tv"], "T")
         for k in range(8):
             scan(T.hist[:, HW * (k + 1) + 1:HW * (k + 1) + 1 + C], P[SV][:, 0:C], T.hist[:, HW * k:HW * k + C], -BIG, A.max, A.min,
                  ["p%d" % SV, "h%d" % k, "hsz"], ["h%d" % (k + 1)], C, "M%d" % k)
@@ -378,7 +451,8 @@ def rank_program(g, core, T, topo):
                     act(T.ca[:, k - 1:e], T.cn[:, k - 1:e], F.Abs, r[:e - k + 1], ["ca%d" % G], 1, "m%d" % G)
                     r = ["ca%d" % G] + r[e - k + 1:]
                 for a in range(4):
-                    o, w, q = T.n64[32 * G:32 * G + 32, :, 2 * a], ["n%d%d" % (G, a)], par["mv"][G][a]
+                    o = T.n64[32 * G:32 * G + 32, 0, 2 * a:2 * a + 2] if par["vp"] else T.n64[32 * G:32 * G + 32, :, 2 * a]
+                    w, q = ["n%d%d" % (G, a)], par["mv"][G][a]
                     src = T["ca" if plain else "cn"][32 * a:32 * a + 32, k - 1:k + 1]
                     if q == "p":
                         op("p", lambda o=o, src=src: g.affine_select(o, src, [[0, 2]], A.is_ge, 0.0, 0, 0), r, w, 175.0, "m%d" % G)
@@ -387,13 +461,20 @@ def rank_program(g, core, T, topo):
                     else:
                         act(o, src, F.Abs, r, w, 1, "m%d" % G)
         for i in range(2):
-            turn(T.nd[:, :, i, :], T.n64[:, i, :], ["n%d%d" % (G, a) for G in range(4) for a in range(4)], ["nd%d" % i], 1, "n")
+            turn(T.nd[:, :, i, :], T.n64[:, 0 if par["vp"] else i, :], ["n%d%d" % (G, a) for G in range(4) for a in range(4)], ["nd%d" % i], 1, "n")
         turn(T.no[:], T.nd[:], ["nd0", "nd1"], ["no"], 1, "n")
         ts(T.on[:], T.no[:].indirect(T.ordn[:, 0:1]), -1.0, None, A.add, None, ["no", "ordn"], ["on"], 1, "n", picked(16))
         for h, (c, d) in enumerate(HALF):
             for b in range(4):
-                tt(T.zt[:, 4 * c + b:4 * d:4], T.du[:, 128 * b:128 * b + 128].indirect(T.ok[:, c // 16:d // 16]), T.th[:, C * b + c:C * b + d], A.add,
-                   ["du%d" % b, "ok", "tr%d%d" % (h, b)] + ["th%d%d" % (i, b) for i in (within(rd - 1, c, d) if rd > 1 else (0,))], ["zt%d%d" % (h, b)],
+                win = T.du[:, 128 * b:128 * b + 128].indirect(T.ok[:, c // 16:d // 16])
+                if (h, b) in par["za"]:
+                    bank = banks(1)[0]
+                    mm(bank, "ehq", "ehz", 128 * b, xq, xz, c, d, xk + ["eh%d" % b, "S"], True, True, "Y%d" % h)
+                    act(T.za[:, C * b + c:C * b + d], win, F.Copy, ["du%d" % b, "ok"], ["za%d%d" % (h, b)], 1, "y%d" % h, picked(d - c) + 10)
+                    tt(T.zt[:, 4 * c + b:4 * d:4], P[bank][:, 0:d - c], T.za[:, C * b + c:C * b + d], A.add, ["p%d" % bank, "za%d%d" % (h, b)], ["zt%d%d" % (h, b)], cy(d - c), "z%d" % h)
+                    continue
+                tt(T.zt[:, 4 * c + b:4 * d:4], win, T.th[:, C * b + c:C * b + d], A.add,
+                   ["du%d" % b, "ok", "tr%d%d" % (h, b)] + ["th%d%d" % (i, b) for i in within(max(rd - 1, 1), c, d)], ["zt%d%d" % (h, b)],
                    55 + PAR["ttg"] * CYC * (d - c), "z%d" % h)
             quant("zq", "zz", c, d, T.zt[:, 4 * c:4 * d], ["zt%d%d" % (h, b) for b in range(4)], ["Z%d" % h], "z%d" % h)
         for h, (c, d) in enumerate(HALF):
@@ -403,19 +484,37 @@ def rank_program(g, core, T, topo):
                 cp("v" if (h, b) in par["xv"] else "s", T.xt[:, 4 * c + b:4 * d:4], P[bank][:, 0:d - c], ["p%d" % bank], ["xt%d%d" % (h, b)], d - c, 1.0 / 32, "x%d" % h)
             quant(nq, nz, c, d, T.xt[:, 4 * c:4 * d], ["xt%d%d" % (h, b) for b in range(4)], [nk[h]], "x%d" % h)
             if ahead:
-                far(STEP[rd - 1], [(u8(T.aq[:, c:d]), u8(T[nq][:, c:d]))], [nk[h]], ["aq%d" % h], 200.0 + 2.5 * (d - c), "F")
-                far(STEP[rd - 1], [(T.az[:, c:d], T[nz][:, c:d])], [nk[h]], ["az%d" % h], 200.0 + 0.8 * (d - c), "F")
+                if PAR["fl"] and d == C:
+                    far(STEP[rd - 1], [(u8(T.aq[:, c:d]), u8(T[nq][:, c:d])), (T.bz[:], T.xz2[:])], nk + ["vq"], ["aq%d" % h, "az%d" % h], PAR["xf"], "F")
+                else:
+                    far(STEP[rd - 1], [(u8(T.aq[:, c:d]), u8(T[nq][:, c:d]))], [nk[h]], ["aq%d" % h], 200.0 + 2.5 * (d - c), "F")
+                    far(STEP[rd - 1], [(T.az[:, c:d], plane(nz, c, d))], [nk[h]], ["az%d" % h], 200.0 + 0.8 * (d - c), "F")
         for h, (c, d) in enumerate(() if rd + 1 != PAR["ahead"] else HALF if PAR["xh"] else ((0, C),)):
             r = [nk[h]] if PAR["xh"] else nk
             far(STEP[rd], [(u8(T.hq[:, c:d]), u8(T[nq][:, c:d]))], r, ["hq%d" % h], 200.0 + 2.5 * (d - c), "H")
-            far(STEP[rd], [(T.hz[:, c:d], T[nz][:, c:d])], r, ["hz%d" % h], 200.0 + 0.8 * (d - c), "H")
+            if d == C:
+                far(STEP[rd], [(T.hz[:], T[nz][:, 0:C])], nk, ["hz"], 200.0 + 0.8 * C, "I")
         src = "tf" if ahead else "th"
         for h, (c, d) in enumerate(HALF):
-            if ahead:
-                unpack("tf", "aq", "az", c, d, ["aq%d" % h, "az%d" % h], ["tf%d" % h], banks(4), lambda b: (h, b) in par["wv"], "A%d" % h)
+            if ahead and not par["vp"]:
+                unpack("tf", "aq", "az", c, d, ["aq%d" % h, "az%d" % h], ["tf%d" % h], dict(enumerate(banks(4))), lambda b: (h, b) in par["wv"], "A%d" % h)
+        if par["vp"]:
+            wq, wz = ("aq", "az") if ahead else (nq, nz)
+            VB = banks(4)
+            for i, e in enumerate("eo"):
+                dq, dz, off = "v%sq%d" % (e, rd), "v%sz%d" % (e, rd), T.on[:, 8 * i:8 * i + 8]
+                op("v", lambda dq=dq, off=off: v.tensor_copy(T[dq][:].bitcast(dt.uint32), T[wq][:].bitcast(dt.uint32).indirect(off)),
+                   ["on"] + (["aq%d" % h for h in range(len(HALF))] if ahead else nk), [dq], picked(128), "P")
+                op("s", lambda dz=dz, off=off: s.activation(T[dz][:], T[wz][:].indirect(off), F.Copy),
+                   ["on"] + (["az%d" % h for h in range(len(HALF))] if ahead else nk), [dz], picked(128) + 10, "P")
+                for b in range(4):
+                    mm(VB[b], "e%sq" % e, "e%sz" % e, 128 * b, dq, dz, 0, 128, [dq, dz, "e%s%d" % (e, b)], e == "e", e == "o", "P")
+            for b in range(4):
+                cp("v" if b in par["vv"] else "s", T.vt[:, b:512:4], P[VB[b]][:, 0:128], ["p%d" % VB[b]], ["vt%d" % b], 128, 1.0 / 32, "V")
         for h, (c, d) in enumerate(HALF):
-            unpack("th", nq, nz, c, d, [nk[h]], ["th%d" % h, "tr%d" % h], banks(4), lambda b: (h, b) in par["uv"], "T%d" % h)
-        for b in range(4):
+            bs = [b for b in range(4) if not (ahead or par["vp"]) or rd < 3 and any((i, b) not in PAR["za%d" % (rd + 1)] for i in within(rd + 1, c, d))]
+            unpack("th", nq, nz, c, d, [nk[h]], ["th%d" % h, "tr%d" % h], dict(zip(bs, banks(len(bs)))), lambda b: (h, b) in par["uv"], "T%d" % h)
+        for b in range(0 if par["vp"] else 4):
             win = sl(src, b).indirect(T.on[:, 0:8])
             r = ["%s%d%d" % (src, h, b) for h in range(len(HALF))] + ["on"]
             if b in par["vv"]:
@@ -429,7 +528,11 @@ def rank_program(g, core, T, topo):
             quant("sq%d" % rd, "sz%d" % rd, 0, 128, T.vt[:], vk, ["out"], "V")
             r = ["out"] + (["ef0", "ef1", "ef2"], ["ef3", "wz0"], ["wz1", "vq"])[rd - 1]
             if rd + 1 == PAR["ahead"]:
-                far(STEP[rd - 1] + STEP[rd], [(u8(T.gq[:]), u8(sq[:])), (T.gz[:], sz[:])], r, ["gq"], PAR["xf"], "G")
+                if PAR["fl"]:
+                    far(STEP[rd - 1] + STEP[rd], [(u8(T.gq[:]), u8(sq[:]))], ["out"], ["gq"], 450.0, "G")
+                    far(STEP[rd - 1] + STEP[rd], [(T.gz[:, 0:128], sz[:, 0:128])], ["out"], ["gz"], 300.0, "G")
+                else:
+                    far(STEP[rd - 1] + STEP[rd], [(u8(T.gq[:]), u8(sq[:])), (T.gz[:], sz[:])], r, ["gq", "gz"], PAR["xf"], "G")
             if PAR["far"] == "W" and not (PAR["ahead"] and rd == 3):
                 far(STEP[rd - 1], [(u8(uq[:]), u8(sq[:])), (uz[:], sz[:])], r, ["U%d" % rd, "Uz%d" % rd], PAR["xf"], "F")
             else:
@@ -445,8 +548,15 @@ def rank_program(g, core, T, topo):
     cp("s", T.yt[:], P[SS][:, 0:C], ["p%d" % SS], ["yt"], C, None, "y")
     dma("s", T.y[:], T.yt[:], ["yt"], [], "outs", "y")
     for h in range(2):
-        ts(T.kf[:, :, h, :], T.kd4[:, h] if by_product[2] else T.kd[:, :, h, :], -1.0, T.pf[:, h:h + 1], A.mult, A.add, kdk + ["pf%d" % h], ["kf%d" % h], 1, "o")
-    ts(T.npg[:], T.nd[:], -1.0, None, A.add, None, ["nd0", "nd1"], ["nop"], 1, "o")
+        src, last = T.kd4[:, h] if by_product[2] else T.kd[:, :, h, :], T.pf[:, 15 + 16 * h:16 + 16 * h]
+        if PAR["os"]:
+            act(T.kf[:, :, h, :], src, F.Identity, kdk + ["pf"], ["kf%d" % h], 1, "o", scale=-1.0, bias=last)
+        else:
+            ts(T.kf[:, :, h, :], src, -1.0, last, A.mult, A.add, kdk + ["pf"], ["kf%d" % h], 1, "o")
+    if PAR["os"]:
+        act(T.npg[:], T.nd[:], F.Copy, ["nd0", "nd1"], ["nop"], 1, "q", bias=-1.0)
+    else:
+        ts(T.npg[:], T.nd[:], -1.0, None, A.add, None, ["nd0", "nd1"], ["nop"], 1, "q")
     dma("y", T.oc[:], u8(T.xq3[:]), nk, [], "outy", "o")
     for k in range(4):
         dma("y", T.osc[4 * k:4 * k + 4, :], T.xz3[32 * k:32 * k + 4, :], nk, [], "outy", "o")
@@ -457,7 +567,7 @@ def rank_program(g, core, T, topo):
                     dma("y", T.op[2 * a + h, 128 * j:128 * j + 128], T.kf[32 * a + 8 * j:32 * a + 8 * j + 4, :, h, :], ["kf%d" % h], [], "outy", "o")
             else:
                 dma("y", T.op[2 * a + h, 0:C], T.kf[32 * a:32 * a + 12, :, h, :], ["kf%d" % h], [], "outy", "o")
-            dma("y", T.op[2 * a + h, C:C + 128], T.npg[32 * a:32 * a + 8:2, :, h, :], ["nop"], [], "outy", "o")
+            dma("y", T.op[2 * a + h, C:C + 128], T.npg[32 * a + h:32 * a + 8:2, :, 0, :] if PAR["vp3"] else T.npg[32 * a:32 * a + 8:2, :, h, :], ["nop"], [], "outy", "o")
     dma("s", T.uc[:], u8(T.uq3[:]), ["U3"], [], "outs", "u")
     for k in range(4):
         dma("y" if k % 2 == 0 else "s", T.usc[4 * k:4 * k + 4, :], T.uz3[32 * k:32 * k + 4, 0:128], ["Uz3"], [], "outy" if k % 2 == 0 else "outs", "u")

@@ -1,76 +1,71 @@
+import math
 from concourse.bass import DstId, RemoteDMATransfer
 from concourse.mybir import dt, AluOpType as A, ActivationFunctionType as F
 
 N, C, STEP = 4, 384, (1, 2, 3)
 BIG = 1e29
 HW = 388
-PAR = {"ttg": 1.6, "g": 1.56, "dl": 1100.0, "ld": 600.0, "dq": 140.0, "rq": 450.0, "fly": 450.0, "xf": 800.0, "first": 1000.0,
-       "lat": 190.0, "own": 240.0, "tw": 40.0, "tc": 0.55, "far": "W", "ahead": 2, "fl": True, "os": True, "kl": 450.0, "xh": True, "bias": {}}
+AHEAD = 2
+NS = {"cyc": 0.83, "g": 1.56, "go": 600.0, "dl": 450.0, "row": 15.0, "byte": 0.015, "dq": 140.0, "rq": 450.0, "fly": 70.0, "rr": 31.0, "rb": 0.05, "first": 1400.0,
+      "lat": 183.0, "own": 250.0, "tw": 35.0, "tc": 0.62, "smin": 72.0, "gp": 120.0, "fix": 0.0, "f": 1.03, "slow": 1.42, "gq": 700.0, "gb": 5.0}
+PAR = {"fold": False, "turns": 13000, "seed": 1, "pull": {}, "seeds": (1, 1, 1), "swap": 0.15, "pass": 0.7, "kin": 0.8, "mean": 0.2, "only": (0, 1, 2), "two": False, "give": 25.0, "bias": {},
+       "hc": (128, 256), "zc": (128, 256), "kc": (128, 256), "qa": 0, "ahead": 2}
+PAR.update({"pull": {"k": 0.3, "b": 0.3, "z0": 0.2, "z1": 0.2}, "mean": 0.1, "turns": 9000, "give": 15.0})
+PAR["bias"] = {"i": 5000, "K": 5000, "E": 5000, "c": 3000, "f": 5000, "": 5000}
+for _h in "123":
+    PAR["bias"].update({_k + _h: 1000 for _k in ("ke", "kn", "kt", "k", "K", "U", "D", "y0", "Y0", "y1", "Y1")})
 for _h in (1, 2, 3):
-    PAR.update({"av%d" % _h: (), "bv%d" % _h: (), "mv%d" % _h: ("vvps", "psps", "pspp", "vsvs"), "xv%d" % _h: ((0, 1), (0, 2), (1, 1), (1, 2)),
-                "uv%d" % _h: ((0, 0), (1, 0), (1, 1), (1, 2)), "wv%d" % _h: ((1, 0), (1, 1)), "vv%d" % _h: (0, 1), "duv%d" % _h: (), "tv%d" % _h: (),
-                "cut%d" % _h: (256,), "down%d" % _h: "turn", "kq%d" % _h: "yyyy", "gb%d" % _h: (4,), "st%d" % _h: (), "za%d" % _h: (), "vp%d" % _h: 0, "km%d" % _h: "psspsspsspsspssp"})
-PAR.update({'xh': False, 'mv2': ('ssss', 'ssss', 'vvvs', 'vsps'), 'xv2': ((1, 0), (1, 3)), 'uv2': (), 'wv2': ((0, 2), (1, 0), (1, 1)), 'vv2': (0, 3), 'gb2': (), 'st2': (3, 5, 7), 'order': {'v': '0t000q01070u0405080r020c030e0k090s0i0j0d0h0n0o0m0l0g0v060w0p0b0a0f0F0x0G0y0N0H0O0z0I0Q0A0P0J0C0B0T0K0D0U0L0S0E0V0R0M0W190X1a0Z0Y1c1b101f1d1e1g111h1j1i1k121l1m1n14131o15161p171q181r1s1t1u1v1E1w1F1x1G1y1M1H1N1z1O1I1A1B1S1U1R1C1J1D1T1P1Y2f2i2h2g1Q1V2j202k1Z2n2l2m1K2o211X2p1L2q2r25262s1W2827292324222a2t2c2b2d2u2e2v2w2x2y2H2z2I2A2P2J2Q2B2R2K2C2S2L2V2E2D2M2F2W2N2G3y2X2T2O2Y3b2Z3c31303e3d323g3f3h3i333j3l3m3k343n3z2U3o3p35363q38373r393A3s3a3t3u3v3w3x', 's': '0100030402070a080e05090d060i0k0f0b0g0r0j0c0p0l0v0m0x0q0s0h0t0n0o0C0w0D0z0E0y0F0u0B0A0G0I0J0H0L0K0R0N0O0M0P0Z0Q15170S0U0W0T0X0V0Y101i1j1k1l1314111b181n1m121d1c161f191e1a1h1g1o1p1q1r1s1C1B1t1v1u1x1w1y1D1z1E1F1A1I1H1G1M1J1T1K1O1N1Z1V1P1Q1U1W211X26201R271L1Y231S22282924252a2c2d2b2f2e2g2h2k2j2i', 't': '000504070201030a060e0g090c080b0d0k0i0h0f0o0j0m0p0l0n0r0q0t0s0u0v0x0w0y0A0E0B0D0C0z0P0H0L0F0N0J0G0I0K0M0R0T0Q0U0S0O0X0V0W0Y0Z1110121315171814161b1e191f1a1d1h1c1l1j1n1g1p1i1k1r1m1o1v1t1q1s1u1w1y1x1z1A1B1E1C1D1F', 'p': '010002050403080706090a0b0c0e0f0g0h0d0j0l0k0n0m0i0p0o', 'y': '0100040205030q070i0o0c0m0b0n0j0k0p0h0g0a060d090e0f0l080s0r'}})
-PAR.update({'xh': True, 'mv1': ('ppss', 'vsss', 'pppp', 'vsvs'), 'xv1': ((0, 2), (0, 3), (1, 0), (1, 2), (1, 3)), 'uv1': ((0, 0), (1, 0), (1, 1), (1, 2)), 'vv1': (0, 1), 'tv1': (3,), 'down1': 'mm', 'gb1': (3,), 'st1': (4,), 'za1': ((0, 2), (0, 3), (1, 3)),
-            'mv2': ('ssss', 'vvss', 'vpvs', 'vsvs'), 'xv2': ((1, 0),), 'uv2': ((0, 2), (0, 3), (1, 1)), 'wv2': ((0, 2), (1, 1)), 'vv2': (0, 3), 'gb2': (), 'st2': (3, 5, 7), 'za2': ((0, 2), (0, 3), (1, 1), (1, 3)),
-            'mv3': ('ppps', 'psvv', 'spvp', 'vsvs'), 'xv3': ((0, 2), (1, 0), (1, 1), (1, 2)), 'uv3': ((1, 1), (1, 2)), 'vv3': (1, 3), 'cut3': (224,), 'gb3': (), 'st3': (4,), 'za3': ((0, 1), (0, 2), (0, 3), (1, 3)),
-            'order': {'v': '000w0B0x01070k080v0605020d040y0f0c0m0n0p0z0g0i0A0r0q0s0t0l0o0E0D0e0G0P0H0I0Q0F0J0R0K0h030b0X0L0S0Y0j0C0T0Z0a0u0U1117100V18190W0M0N1a130O12141m1l1n1o1r1b1p151q1c1s1d1t1w1u1v1e1x1y1z1A161f1g1B1h1i1C1j1E1k1D1F1H1G091I1J1K1S1L1T1M201U211N1V1P221O1W1Q23261R1X2v242w2x2y1Y2z2D2C28272B2A25292e2E1Z2g2f2F2d2h2c2l2G2n2H2k2m2a2o2j2i2b2p2q2s2r2t2I2u2J2M2N2O2L2K2P2X2Q2Y2R2Z2S35302U2T3736312V3R3Q393f2W32383g3h333e3i3v3j343w3x3y3D3m3k3z3a3A3B3n3C3b3E3F3o3l3G3J3I3H3q3p3d3c3K3s3r3t3S3L3u3M3N3O3P', 's': '000102050403060a0c0e0b0j0809070d0l0r0f0t0g0w0y0D0E0s0k0F0u0m0G0v0n0x0H0p0q0i0A0h0z0I0o0C0B0J0L0K0M0O0N0R0P0S0Q0U100T12170V1k1l0Y1n0X0Z1m111d191p1q1o1r131f1u1s1t1a1418151e1b1g1h0W1c161j1i1w1v1x1y1A1z1F1G1D1B1C1I1H1J1K1E1M1Q1S1L1W292c2b1Y2a1X1N24221Z1O1R2e2d23202f1T26251U2g1P2821271V2h2i2j2l2k2m2n2o2p2q2t2s2r', 't': '0102000403050607090b080a0j0h0f0d0e0c0l0g0k0m0n0i0p0o0r0s0t0u0q0w0v0y0x0A0C0z0B0F0D0E0G0I0L0H0K0J0Q0M0N0O0U0S0R0T0Y0P0V1210130W0X110Z1514161718191b1a1f1c1g1e1d1i1l1k1n1m1h1j1o1s1q1u1r1p1w1y1A1C1t1v1z1x1E1G1F1H1D1B1J1I1L1K1N1M1O1P1Q', 'p': '010200030405060807090b0a0e0c0d0g0h0i0f0k0j0l0o0n0m0q0p', 'y': '010003050708090602040t0j0r0h0n0l0f0a0e0c0g0o0u0i0m0q0d0k0s0p0b0v0w'}})
-PAR.update({'order': {'v': '00010y0v0z060x03080k0B050402070a0f0w0c0o0m0p0A0n0d0r0q0s0t0C0D0b090l0G0E0S0H0I0T0J0F0U0K0M0L0N100V0O0e0i110W0u0j120X1a0g130Y1c1b0Z0P0Q0h1d160R1517141o1p1q1r1u1e1s181f1w1v1g1t1z1x1y1h1A1C1B1D191i1j1E1l1k1F1m1H1n1G1I1K1J1L1M1N1V1O1W1P231X241Q1Y1S251R1Z1T29261U202z2a2y2B2A212C272E2h2G2b2D2F222H282c2i2j2I2g2k2J2f2o2K2q2n2p2d2e2r2m2l2t2s2u2v2w2L2x2M2P2Q2R2O2N2S302T312U322V38333a2X392W342Y3U3T3i2Z353j3b3k3h363l3A3y3c3B3z3m3n373C3G3p3d3E3q3F3D3e3I3H3r3o3J3M3K3L3f3g3s3t3N3v3u3w3O3x3V3P3Q3R3S', 's': '00010204030508070e0a0j09060l0d0r0b0f0w0g0t0y0D0E0s0c0k0F0u0m0v0G0x0n0H0o0p0A0h0i0z0I0q0B0C0J0L0K0M0O0N0Q0R0S0P0U100T12171l1k1m0V1n190W0Z1d111o1p1q1r1f131s1u1t1a140Y181e1b1g1h0X161c151i1j1v1w1x1y1z1A1F1G1B1E1D1C1K1H1I1J1M1Q1S1L1W292a2b1Y1X2c1N221Z1O241R232e2d202f1T251U262g211P27281V2h2i2j2k2l2m2n2o2p2q2s2t2r', 't': '0102000306070504090d0a080b0e0c0f0j0n0l0h0g0m0p0k0i0r0o0s0q0t0u0w0v0y0x0A0z0C0B0F0D0J0H0I0E0G0L0O0N0Q0M0K0U0S0P0R0W0T0Y0V10120Z130X111415161718191a1b1c1e1h1g1f1d1i1n1p1k1j1l1m1o1u1q1s1r1y1A1w1t1C1x1v1z1G1E1F1B1D1H1I1J1K1L1N1M1O1P1Q', 'p': '010200040307080506090b0a0e0c0d0g0h0i0f0k0l0j0n0o0m0q0p', 'y': '010002050308060709040p0f0h0j0t0r0n0l0c0a0d0e0g0b0k0s0i0m0u0o0q0w0v'}})
-PAR.update({'mv1': ('vsvs', 'pppv', 'pppp', 'vsvs'), 'uv1': ((0, 0), (1, 1), (1, 2)), 'duv1': (1,), 'mv2': ('ppss', 'pvvv', 'psps', 'vsps'), 'uv2': ((0, 2), (1, 3)), 'wv2': ((0, 2), (1, 2)), 'mv3': ('ppps', 'pppp', 'pppp', 'vvsv'), 'za3': ((0, 1), (0, 3), (1, 3)),
-            'order': {'v': '0001020b0a09080c0d0e0f0g0h030i0k0x0m0l0y0j0n0z0o0p0F0r0q0A0s050H0G0B0L0w07040C0I0R0D0T060S0N0E0u0t0O0U0v0W0M150V1618171a0P190X1d1c1b1f1e1g0Y0Q0K1h1k1i1j0J100Z1l11121m13141n1o1p1q1r1s1t1u1C1v1D1w1K1E1L1x1F1y1M1z1G1A1Q1N1B1H2e2d2g2f1I2h2k1R2l1Z2j1S2i1T1P2m201O212n1J1Y2o22242p1X2526231U1V1W27282a292q2b2c2r2t2u2v2s2E2w2F2x2M2G2N2y2H2O2z2I2B2A2Q2P2U2C2J2D2V2W2K2T2X2R2Y3c3a3d2Z3b2L3e2S3g3i313f303h3k3j323l3n3m3o3335343p3736383q393r3s3t3u', 's': '00010204030506070d09080b0a0i0c0k0n0p0e0s0u0o0A0z0f0j0q0B0r0l0g0h0t0m0D0w0C0v0E0x0y0F0H0I0J0G0L0K0O0N0M0P0R0W0Q0Y111g1f0S1i0T1h13181j1l1k1m0Z0X1p1o1n1a14100V1219151b1c160U171d1e1q1r1s1t1u1v1C1B1x1A1z1w1y1F1G1D1E1I1M1H1O1R2j2k1J1T1K23221S1W1N1U241V1Y1P25261Q1X271L201Z28212a292c2l2b2d2e2f2g2h2i2n2o2m', 't': '01020003040705090b080a0e0f060d0h0c0j0l0n0k0i0m0g0p0t0o0u0q0r0s0w0v0y0x0z0A0C0B0F0D0J0I0H0G0K0E0O0M0N0L0Q0U0S0P0T0R0Y0V0W100Z0X12131114151617181a191b1d1e1f1g1h1c1i1m1n1k1l1p1j1o1t1v1q1r1x1s1z1u1w1y1B1D1F1C1A1E1G1I1H1K1J1M1L1N1O1P', 'p': '0g0d00070401020f0605030a0b0c09080e0k0l0n0j0i0m0h0o0p0q0t0r0s0v0u0A0B0C0w0y0x0z0E0F0D0M0N0L0K0J0I0G0H0P0O', 'y': '000102050403070609080n0h0l0r0f0t0j0p0e0a0m0u0i0c0o0s0g0k0d0q0b0v0w'}})
-PAR.update({'mv1': ('vsvs', 'pppv', 'ssss', 'vsvs'), 'duv1': (), 'tv1': (2, 3), 'gb1': (), 'mv2': ('ppss', 'psvv', 'ppvv', 'vspv'), 'xv2': ((1, 0), (1, 1)), 'uv2': ((0, 3), (1, 3)), 'down2': 'mm', 'kq2': 'yyss', 'st2': (4, 7), 'mv3': ('vsvs', 'pppp', 'ppps', 'vsvp'), 'xv3': ((0, 3), (1, 0), (1, 3)), 'uv3': ((0, 3), (1, 0), (1, 1)), 'down3': 'mm', 'za3': ((0, 2), (0, 3), (1, 3)),
-            'order': {'v': '000102080a07090b0c0d0e0f030g0h0j0w0i0l0x0k0m0y0p0q0o0n0E0z0r050F0G0A0K060v040B0H0P0C0R0Q0D0s0t0S0O0u0T0L0V150U14171619180M1b0W1c1a1f1d1e0X0I0N1g1h1i1j0J0Y0Z1k11101l12131m1n1o1p1q1s1r1t1v1x1u1w1y1H1z1A1B1C1I1D1P1J1Q1K1R1L1T1S1Z1M1F1E20211Y1G1U222j2i2k2l1N2m2q232n2o2p1O2r241V282s2t292u2a272v252b261W1X2c2d2e2f2g2w2h2x2y2z2A2P2F2B2D2Q2E2G2C2X2R2J2H2K2Y2I2S2L2Z2T3330372U38392V343a363b2N2M2W2O353d3c3n3m3o3p3r3q3e3u3s3t3w3v3f323x3z3y3h3g313A3i3j3B3k3D3l3C3E3F3G', 's': '000102040503070908060d0a0i0b0c0n0k0e0p0x0o0D0C0v0j0q0E0f0l0F0w0m0G0r0u0g0s0z0y0H0t0h0B0A0I0K0L0M0J0O0N0S0R0T0U0Q0P0W0V1113170X190Y1i1j0Z1k1l18121c1m1n1o1p1e1a1q1r1b141d151f1g16101h1s1t1u1v1w1x1F1E1B1y1C1A1z1G1D1L1I1H1Q1J1K1S1V1M1N1X1R1W2127282p2o1Y291Z231T222b1U2a2c1P24252d2e201O262f2g2h2q2i2j2l2k2m2n2s2t2r', 't': '010200030507060408090c0e0b0a0d0f0h0j0n0l0g0m0i0k0p0r0o0q0s0t0u0w0v0y0x0z0C0A0B0F0G0H0D0J0I0K0L0M0O0N0S0E0Q0P0U0R0T0V0W0X100Y121411150Z13161718191a1c1b1d1e1f1g1h1i1j1k1n1l1m1o1p1q1r1t1s1v1u1w1y1A1C1E1D1z1x1B1G1K1H1L1F1I1J1M1N1P1O1R1S1Q1T1U', 'p': '05000107080f0603040a020b0c0d0e090g0i0h0j0l0k0o0m0n0p0q0v0w0x0t0s0r0u0C0E0D0A0y0B0z0F0H0G', 'y': '000104030205060709080a0b0d0c0f0e0p0G0H0q0B0x0u0l0O0L0D0K0F0n0y0N0j0i0g0k0m0h0w0Q0s0r0C0A0E0t0z0v0J0I0o0P0S0M0R'}})
-PAR.update({'av1': (), 'bv1': (), 'mv1': ('ppps', 'sppp', 'ssss', 'ssss'), 'xv1': ((0, 2), (1, 1), (1, 2)), 'uv1': ((0, 3), (1, 1), (1, 2)), 'vv1': (1, 3), 'duv1': (), 'tv1': (1, 3), 'cut1': (224,), 'down1': 'mv', 'gb1': (3,), 'st1': (4,), 'za1': ((0, 1), (0, 3), (1, 3)), 'km1': 'psspssvsppvspssv', 'mv2': ('sppv', 'vppp', 'vspv', 'vspv'), 'xv2': ((1, 2), (1, 3)), 'uv2': ((0, 0), (0, 3)), 'wv2': ((0, 2), (1, 2)), 'vv2': (0, 3), 'cut2': (256,), 'down2': 'mv', 'gb2': (), 'st2': (5, 7), 'za2': ((0, 2), (0, 3), (1, 0), (1, 3)), 'km2': 'ppsssssssvssvssp', 'mv3': ('ppps', 'pppp', 'ppps', 'pvsv'), 'xv3': ((0, 2), (1, 1), (1, 2)), 'uv3': ((0, 3), (1, 1), (1, 2)), 'vv3': (1, 3), 'cut3': (224,), 'down3': 'mv', 'gb3': (), 'st3': (4,), 'za3': ((0, 1), (0, 3), (1, 3)), 'km3': 'psspspssppsspssv',
-            'order': {'v': '0001020907080a030b0c0d0e0f0h0k0n0i0l0o0y0j0p050m0z0s0g0q0A0r0x0G0B060H0t0u0C0v0K0I040P0w0D0J0R0E120Q0M0F0N0S140L11130T0O150U17160V19181b1a0W1c1e1d1f0Y0X1g0Z1h101i1j1k1l1o1m1n1p1s1v1q1t1w1E1u1r1x1F1z1y1M1G1N1A1B1H1O1C1P1D1I2f1J2h1R2g2i1K2j1S1Y2n2k2m2l1Z1T201U2o1L2p211X2q2r251W2s2724261V1Q282322292a2c2b2d2t2e2u2w2x2y2v2N2C2z2F2O2A2D2G2P2E2B2H2V2Q2I2X2W2R2Z2S2Y332J2K2T2L323435372M2U36303k3i3l383j313o3m393a3q3p3n3s3r3b3t3v3u3c3d3w3e3f3x3g3y3h3z3A3B3C', 's': '0001020405030e0f0g0h0i080b0a0d070j060c090l0p0r0k0v0M0N0m0x0D0n0w0q0o0F0O0y0s0P0Q0E0t0R0H0z0A0u0C0B0G0S0T0I0J0L0K0U0V0W0X0Y0Z101c1e1d1f1b131218171915161a11141h1g1l1n1C1i1D1q1j1F1E1s1w1m1H1G1I1J1o1y1L1K1t1p1r1k1x1u1z1A1v1B1N1M1O1Q1P1R1X1Y1T1V1S1W1U292a2d282b2h211Z2620272422252c232m2j2o2e2s2f2y2z2n2i2A2p2k2u2l2t2B2C2P2q2w2D2r2v2E2F2Q2g2x2G2H2R2I2J2K2L2M2N2O2U2T2S', 't': '0102030006070508090a0b0c040e0h0f0d0j0l0g0i0k0m0r0t0p0n0s0o0q0u0w0v0y0x0A0z0B0C0F0G0H0D0J0I0K0L0E0O0Q0P0S0N0M0U0W0T0R0V100X140Y121513110Z171618191b1a1d1c1g1i1j1f1e1h1k1m1n1l1o1q1p1r1y1s1t1w1v1A1u1x1z1B1C1E1D1G1I1K1F1J1H1L1M1N1P1O1R1Q1S1T1U', 'p': '0c0002050401030706080a090b0h0d0f0g0e0i0j0k0m0n0l0o0q0p0t0r0s0w0u0v0x0y0E0F0G0B0z0C0A0D0H0M0I0L0J0K0P0O0N0R0S0Q0T0U0V0W0X0Z0Y', 'y': '0001020304050b0f0n0j0h0l060o0i090e0q080c070a0g0m0d0k0p0s0r'}})
-PAR.update({"smin": 72.0, "gp": 100.0, "lat": 170.0, "own": 228.0, "tw": 35.0, "tc": 0.5, "dl": 1250.0, "ld": 500.0, "fly": 260.0, "kl": 300.0, "ttg": 1.56})
-PAR.update({'mv1': ('sppp', 'vvpv', 'ssss', 'svss'), 'xv1': ((0, 2), (1, 2), (1, 3)), 'uv1': ((0, 0), (0, 3), (1, 1)), 'vv1': (1, 3), 'tv1': (1,), 'cut1': (224,), 'down1': 'mv', 'gb1': (3,), 'st1': (4,), 'za1': ((0, 3), (1, 2), (1, 3)), 'km1': 'sssspsssssvssvsv', 'mv2': ('sppv', 'vpsp', 'vvvv', 'vsps'), 'xv2': ((1, 0), (1, 2), (1, 3)), 'uv2': ((1, 1), (1, 3)), 'wv2': ((0, 2), (1, 2)), 'vv2': (0, 3), 'cut2': (256,), 'down2': 'mv', 'gb2': (), 'st2': (5, 7), 'za2': ((0, 2), (0, 3), (1, 0), (1, 3)), 'km2': 'psssspssvsvssvsv', 'mv3': ('ppps', 'pppp', 'vpvs', 'vvvv'), 'xv3': ((0, 2), (1, 1), (1, 2)), 'uv3': ((0, 3), (1, 1), (1, 2)), 'vv3': (1, 3), 'cut3': (224,), 'down3': 'mv', 'gb3': (), 'st3': (4,), 'za3': ((0, 1), (0, 3), (1, 3)), 'km3': 'pvssvspsssvssssp',
-            'order': {'v': '000102090a07080b0c0d0e0f0g0h0k0n0i0l0o0y0m0j0p030z050q0s0G0r0A0H0x0B0t0u0I060K0C0v0J0S0D0w0T0U0E0L160M0V150N180F170W0O190X1d1b040Y1c1a1f1e0Z1g0Q1i0R1h100P1j12111k131m141l1n1o1p1r1s1q1t1w1z1u1x1A1K1B1y1v1L1F1D1C1E1S1M1T1G1H1N1I1U1O1X1J1V1P2m242n2o2p1Q2q251Y232u262r2t2s20272v1Z1R2w2z2y2d2c2x222e2A2f1W2g29282a2b212h2i2j2B2k2l2C2E2F2D2G2H2X2I2N2K2Y2L2O2Z352P2M2J3630372R2Q2S31383d39323e2T2U332V3c3a3f3h2W343g3y3l3w3b3i3x3C3z3E3m3A3B3D3j3n3F3G3k3H3I3J3r3q3p3o3K3t3s3L3u3M3v3N3O3P3Q', 's': '0001020405030j0k0l0i0m07060b0c0h0e0d08090a0f0n0g0o0p0t0v0y0q0O0r0A0Q0u0P0z0G0I0B0w0C0R0S0H0T0x0D0E0F0K0s0J0V0U0N0L0M0W0X0Y100Z11121f1d1e1g181413151b1a1c1619171i1m1h1o1s1E1F1u1H1j1G1k1x1n1I1J1L1K1v1p1M1z1y1t1q1B1w1A1r1l1C1D1O1N1P1R1Q1S1Y1Z1T1X1V1U1W2c2b2a2d2f2j272e2426252120292322282l2g2o2h2q2u2k2z2p2B2A2r2w2s2m2v2n2C2E2D2y2Q2x2F2G2t2i2H2I2J2S2K2R2L2M2N2O2P2V2U2T', 't': '0102030006070508090c0a0b0e0d0f040j0h0g0i0k0p0l0m0r0n0t0q0u0o0s0w0v0y0x0A0z0C0B0F0G0H0D0I0K0J0E0L0M0O0Q0N0S0P0W0R0T0X0U0V0Y1412151310110Z171618191b1a1c1d1f1e1g1i1h1j1l1k1n1o1m1q1p1r1s1y1A1u1t1w1v1C1G1E1x1z1D1B1I1F1H1J1K1L1M1N1P1O1R1Q1S1T1U', 'p': '010002070b0409060805030c0a0d0e0g0f0h0i0j0k0n0l0m0o0p0q0r0v0w0x0t0s0u0A0y0z0D0B0C0I0G0H0E0F0K0J', 'y': '0001020304050j0a080f0i0e0o0l0b0p0c0h090q0n0k0g0m0d060s070r'}})
+    PAR.update({"cut%d" % _h: (256,), "nl%d" % _h: 1 - _h % 2, "sent%d" % _h: (256,), "sv%d" % _h: (), "zd%d" % _h: (),
+                "za%d" % _h: ((0, 1), (0, 2), (0, 3), (1, 1), (1, 2), (1, 3)), "vp%d" % _h: 0})
+PAR.update({"za1": tuple((_h, _b) for _h in range(2) for _b in range(4)), "seeds": ((11, 6, 3), (4, 3, 5), (2, 1, 4)), "keep": 0.3, "nl3": 1, "nl1": 1, "turns": 8000,
+            "only": (0, 1, 2), "whole": 0, "warm": 0.3, "za3": ((0, 1), (0, 2), (0, 3), (1, 0), (1, 1), (1, 2), (1, 3)), "wide": 0.9, "spare": 1e9, "hf": True, "both": 0.8, "line": 0.85, "swap": 0.12, "pass": 0.5, "kin": 0.56, "q4": True, "sv1": (128, 256)})
 
 
 def _sb(n, d):
     return ("sbuf", [128] + (n if isinstance(n, list) else [n]), d)
 
 
-CODE, PL, BF, F32, U16, I32 = "float8_e4m3fn_x4", "uint8", "bfloat16", "float32", "uint16", "int32"
+CODE, PL, BF, F16, F32, U16, I32 = "float8_e4m3fn_x4", "uint8", "bfloat16", "float16", "float32", "uint16", "int32"
 SCRATCH = {
-    "xin": _sb(4 * C, BF), "uin": _sb(512, BF), "vin": _sb(512, BF), "wq": _sb(512, CODE), "vq": _sb(128, CODE),
-    "c32": _sb(128, BF), "eye": _sb(128, BF), "tb": _sb(160, F32), "pf": _sb(160, F32), "quad": _sb(1, F32),
-    "ef": _sb(520, BF), "efq": _sb(512, CODE), "cz": _sb(1152, PL), "eh": _sb(520, BF), "ehq": _sb(512, CODE), "ehz": _sb(512, PL), "za": _sb(4 * C, BF),
+    "xin": _sb(4 * C, BF), "uin": _sb(512, BF), "vin": _sb(512, BF), "wq": _sb(512, CODE), "wz": _sb(512, PL), "vq": _sb(128, CODE),
+    "c32": _sb(260, BF), "tb": _sb(224, F32), "pf": _sb(224, F32), "num": _sb(C, F32), "zero": _sb(HW, BF),
+    "ef": _sb(1040, BF), "efq": _sb(512, CODE), "ehq": _sb(512, CODE), "ehz": _sb(512, PL), "za": _sb(4 * C, BF), "zb": _sb(4 * C, BF),
     "ee": _sb(520, BF), "eeq": _sb(512, CODE), "eez": _sb(512, PL), "eo": _sb(520, BF), "eoq": _sb(512, CODE), "eoz": _sb(512, PL),
-    "cap": _sb(C, F32), "st": _sb(C, F32), "ex": _sb(C, F32), "nr": _sb(C, BF), "tr": _sb(1024, BF), "nr4": _sb([4, 128], BF), "tr4": _sb([4, 128], BF), "tr3": _sb([3, 128], BF), "km": _sb([32, 2], BF),
-    "kd": _sb([2, 2, 16], BF), "kd4": _sb([2, 2, 16], BF), "ko": _sb(64, BF), "ct": _sb(32, BF), "it8": _sb(4, F32), "ordk": _sb(4, U16), "kf": _sb([2, 2, 16], F32),
-    "n64": _sb([2, 32], F32), "nd": _sb([2, 2, 16], F32), "no": _sb(64, F32), "npg": _sb([2, 2, 16], F32),
-    "cn": _sb(8, F32), "ca": _sb(8, F32), "sg": _sb(8, F32), "ep": _sb(8, F32), "eq": _sb(8, F32), "ob": _sb(8, F32), "one": _sb(8, F32), "zero": _sb(C, BF), "b0": _sb(1, F32), "ordn": _sb(2, U16), "on": _sb(16, U16), "ok": _sb(32, U16),
-    "hist": _sb(9 * HW, F32), "ab": _sb(8 * C, BF), "al": _sb(8 * HW, BF), "bl": _sb(8 * C, BF), "bv": _sb(8 * C, BF),
+    "cap": _sb(128, F32), "ex": _sb(C, F32), "nr": _sb(C, BF), "tr": _sb([8, 128], BF), "kd": _sb([2, 2, 16], BF), "ko": _sb(64, BF),
+    "ordk": _sb(2, U16), "ordn": _sb(4, U16), "ok": _sb(32, U16), "on": _sb(16, U16), "of": _sb(32, F32), "ot": _sb(32, F32),
+    "hf": _sb(192, F32), "fo": _sb(C, F32), "hist": _sb(9 * HW, F32), "sl": _sb(5 * C, F16), "mk": _sb(5 * C, F16), "zs": _sb(5 * C, F16), "zp": _sb(4 * C + 8, F16), "kh": _sb(9 * HW, F16),
+    "qi": _sb(8, I32), "qa": _sb(8, F32), "qj": _sb(40, F32), "qs": _sb(40, F32), "nb": _sb([4, 8], F32), "nd": _sb([2, 2, 16], F32), "no": _sb(64, F32),
     "th": _sb(4 * C, BF), "tf": _sb(4 * C, BF), "du": _sb(512, BF),
     "zt": _sb(4 * C, BF), "xt": _sb(4 * C, BF), "vt": _sb(512, BF), "yt": _sb(C, F32),
-    "xq0": _sb(512, CODE), "xz0": _sb(512, PL), "hq": _sb(C, CODE), "hz": _sb(C, PL), "gq": _sb(128, CODE), "gz": _sb(512, PL), "aq": _sb(C, CODE), "az": _sb(C, PL), "bz": _sb(512, PL),
+    "xq0": _sb(512, CODE), "xz0": _sb(512, PL), "hq": _sb(C, CODE), "hz": _sb(512, PL), "gq": _sb(128, CODE), "gz": _sb(128, PL), "aq": _sb(C, CODE), "bz": _sb(512, PL),
     "zq": _sb(C, CODE), "zz": _sb(C, PL)}
 for _h in (1, 2, 3):
-    SCRATCH.update({"xq%d" % _h: _sb(C, CODE), "xz%d" % _h: _sb(512 if _h == 2 else C, PL), "uq%d" % _h: _sb(128, CODE), "uz%d" % _h: _sb(512, PL),
+    SCRATCH.update({"xq%d" % _h: _sb(C, CODE), "xz%d" % _h: _sb(512 if _h < 3 else C, PL), "uq%d" % _h: _sb(128, CODE), "uz%d" % _h: _sb(512, PL),
                     "veq%d" % _h: _sb(128, CODE), "vez%d" % _h: _sb(128, PL), "voq%d" % _h: _sb(128, CODE), "voz%d" % _h: _sb(128, PL),
                     "sq%d" % _h: _sb(128, CODE), "sz%d" % _h: _sb(512, PL)})
+SCRATCH["az"] = _sb(C, PL)
 for _b in range(8):
     SCRATCH["p%d" % _b] = ("psum", [128, 512], F32)
 
-SEMAPHORES = (["cv", "cs", "ct", "cp", "sent", "outy", "outs"] + ["d%d" % i for i in range(12)] + ["f%d" % i for i in range(14)]
-              + ["m%d%d%s" % (h, i, q) for h in (1, 2, 3) for i in range(5) for q in "ys"])
-CYC = 0.83
-ABC = "0123456789abcdefghijklmnopqrstuvwxyzABCDEFGHIJKLMNOPQRSTUVWXYZ"
+SEMAPHORES = ["cv", "cs", "ct", "cp", "sent", "outy", "outs"] + ["d%d" % i for i in range(20)] + ["f%d" % i for i in range(14)]
+KEPT = {}
 
 
-def lay_out(calls, ways_only=False):
-    lastw, readers, lastp, wide = {}, {}, {}, []
+def link(calls):
+    lastw, readers, lastp, wide, narrow, first = {}, {}, {}, [], [], []
     for i, c in enumerate(calls):
-        hard, soft = set(), set()
+        hard, soft, war = set(), set(), set()
         for k in c["r"]:
             if k in lastw:
                 hard.add(lastw[k])
         for k in c["w"]:
             if k in lastw:
-                (soft if c["q"] == "t" and calls[lastw[k]]["q"] == "t" else hard).add(lastw[k])
+                (war if c["q"] == "t" and calls[lastw[k]]["q"] == "t" else hard).add(lastw[k])
             for j in readers.get(k, ()):
-                (soft if calls[j]["q"] == c["q"] and not calls[j]["late"] else hard).add(j)
+                hard.add(j)
+        sure = set(hard)
+        for j in war:
+            (soft if calls[j]["q"] == c["q"] else hard).add(j)
         for k in c["r"] + c["w"]:
             if k[0] == "p" and k[1:].isdigit():
                 q, ahead, mine = lastp.get(k, (c["q"], [], []))
@@ -78,103 +73,292 @@ def lay_out(calls, ways_only=False):
                     ahead, mine = mine, []
                 hard.update(ahead)
                 lastp[k] = (c["q"], ahead, mine + [i])
-        if c["q"] == "p" and c["kind"] == "op":
+        if "p" in c["ways"] and c["kind"] == "op":
             if c["tag"][:1] in ("K", "m"):
                 hard.update(wide)
+                sure.update(wide)
+                narrow.append(i)
             else:
+                hard.update(narrow)
+                sure.update(narrow)
                 wide.append(i)
+        if c["kind"] == "far":
+            soft.update(first)
+            war.update(first)
+            first[:] = first or [i]
         for k in c["w"]:
             lastw[k], readers[k] = i, []
         for k in c["r"]:
             readers.setdefault(k, []).append(i)
-        c["hard"], c["soft"], c["next"] = hard, soft - hard, []
-    for i, c in enumerate(calls):
-        for j in c["hard"] | c["soft"]:
-            calls[j]["next"].append(i)
-    for i, c in enumerate(calls):
-        c["gap"] = {}
-        for j in c["next"]:
-            d = calls[j]
-            c["gap"][j] = 0.0 if i not in d["hard"] else (
-                (PAR["own"] if c["q"] == d["q"] and not c["late"] else PAR["lat"] + c["late"]) + (PAR["tw"] if "t" in (c["q"], d["q"]) else 0.0))
-    for i in range(len(calls) - 1, -1, -1):
-        c = calls[i]
-        c["way"] = c["ns"] + max([c["late"]] + [calls[j]["way"] + c["gap"][j] for j in c["next"]])
-    if ways_only:
-        return []
-    if PAR.get("order"):
-        seq, done, order = {}, set(), []
-        for q, e in PAR["order"].items():
-            mine = [i for i, c in enumerate(calls) if c["q"] == q]
-            seq[q] = [mine[62 * ABC.index(e[j]) + ABC.index(e[j + 1])] for j in range(len(e) - 2, -1, -2)]
-        while len(order) < len(calls):
-            q = [q for q in seq if seq[q] and calls[seq[q][-1]]["hard"] | calls[seq[q][-1]]["soft"] <= done][0]
-            done.add(seq[q][-1])
-            order.append(seq[q].pop())
-        return order
-    free, left, order = {}, [len(c["hard"] | c["soft"]) for c in calls], []
-    ready = [i for i in range(len(calls)) if left[i] == 0]
+        c["needs"], c["war"] = (hard, soft - hard), war - sure
+
+
+def gap(d, c, soft, same):
+    if soft:
+        return 0.0
+    return (NS["own"] if same and not d["late"] else NS["lat"] + d["late"]) + (NS["tw"] if "t" in (c["q"], d["q"]) else 0.0)
+
+
+def tie(calls, after):
     for c in calls:
-        c["at"] = 0.0
-    while ready:
-        now = min(max(calls[i]["at"], free.get(calls[i]["q"], 0.0)) for i in ready)
-        can = [i for i in ready if max(calls[i]["at"], free.get(calls[i]["q"], 0.0)) <= now + 1e-6]
-        i = max(can, key=lambda j: (calls[j]["way"] + PAR["bias"].get(calls[j]["tag"], 0.0), -j))
-        c = calls[i]
-        ready.remove(i)
-        order.append(i)
-        free[c["q"]] = now + c["ns"]
-        for j in c["next"]:
+        c["pre"], c["next"] = {}, {}
+    for i, c in enumerate(calls):
+        hard, soft = c["needs"]
+        more = after.get(i, [])
+        c["hard"] = hard | {j for j in more if calls[j]["q"] != "t"}
+        for j in c["hard"] | soft | set(more):
             d = calls[j]
-            d["at"] = max(d["at"], now + c["ns"] + c["gap"][j])
+            c["pre"][j] = d["next"][i] = gap(d, c, j not in c["hard"], c["q"] == d["q"])
+
+
+def place(net, rank, queue, lo, hi, base):
+    ways, tail, pre, nxt, opens, uses, mine = net
+    start, end, todo, holder, free = [list(x) for x in base[:5]]
+    lines, bank, after = {q: (list(a), list(e)) for q, (a, e) in base[5].items()}, dict(base[6]), dict(base[7])
+    left = dict(base[8])
+    ready = sorted([i for i in left if not left[i]], key=lambda j: -rank[j])
+    last = 0.0
+    for _ in range(lo, hi):
+        k = len(ready) - 1
+        while k >= 0 and opens[ready[k]] is not None and min([todo[r] for r in holder]):
+            k -= 1
+        if k < 0:
+            return None
+        i = ready.pop(k)
+        q = queue[i]
+        at, d = 0.0, ways[i][q]
+        for j, same, other in pre[i]:
+            e = end[j] + (same if queue[j] == q else other)
+            if e > at:
+                at = e
+        if opens[i] is not None:
+            b = min([b for b in range(8) if not todo[holder[b]]], key=lambda b: free[b])
+            at = max(at, free[b])
+            after[i] = uses[holder[b]]
+            holder[b], bank[opens[i]] = opens[i], b
+        a, e = lines[q]
+        k = len(a)
+        while k and e[k - 1] > at:
+            k -= 1
+        while k < len(a) and a[k] < at + d:
+            at = e[k]
+            k += 1
+        a.insert(k, at)
+        start[i] = at
+        at += d
+        e.insert(k, at)
+        end[i] = at
+        if at + tail[i] > last:
+            last = at + tail[i]
+        for r in mine[i]:
+            todo[r] -= 1
+            free[bank[r]] = max(free[bank[r]], at + NS["lat"] + NS["tw"])
+        for j in nxt[i]:
             left[j] -= 1
-            if left[j] == 0:
-                ready.append(j)
-    return order
+            if not left[j]:
+                k = len(ready)
+                while k and rank[ready[k - 1]] < rank[j]:
+                    k -= 1
+                ready.insert(k, j)
+    at = over = 0.0
+    for e, i in sorted([(end[i - 1] + pre[i][-1][2], i) for i in base[10]]):
+        at = max(at, e) + ways[i]["e"]
+        over = max(over, at - end[i])
+    slow, busy, far = list(base[11]), dict(base[12]), 0.0
+    more, rest = base[13:]
+    for i in sorted(range(lo, hi), key=lambda i: start[i]):
+        q = queue[i]
+        at = busy[q]
+        for j, same, other in pre[i]:
+            e = slow[j] + (same if queue[j] == q else other) + 25.0
+            if e > at:
+                at = e
+        for j in after.get(i, ()):
+            if slow[j] + 240.0 > at and queue[j] != q:
+                at = slow[j] + 240.0
+        slow[i] = busy[q] = at = at + ways[i][q] * more[i]
+        if at + rest[i] > far:
+            far = at + rest[i]
+    return (last + over + PAR["both"] * far) / (1.0 + PAR["both"]), (start, end, todo, holder, free, lines, bank, after, slow, busy), queue, PAR["mean"] * sum(end[lo:hi]) / (hi - lo) + sum([w * end[i] for i, w in base[9]])
 
 
-def rank_program(g, core, T, topo):
+def holdups(net, got, lo, hi):
+    tail, pre = net[1:3]
+    start, end, after, queue = got[1][0], got[1][1], got[1][7], got[2]
+    ends = {(queue[i], end[i]): i for i in range(lo, hi)}
+    i, out = max(range(lo, hi), key=lambda i: end[i] + tail[i]), []
+    while i >= lo and start[i] > 0.0:
+        by = [j for j, same, other in pre[i] if end[j] + (same if queue[j] == queue[i] else other) > start[i] - 1e-3]
+        if by:
+            i = by[0]
+            continue
+        j = ends.get((queue[i], start[i]))
+        if j is None:
+            j = max(after.get(i) or [-1], key=lambda j: end[j])
+        if j >= lo:
+            out.append((i, j))
+        i = j
+    return out or [(lo, lo)]
+
+
+def lay_out(calls):
+    link(calls)
+    if "order" not in KEPT:
+        n = len(calls)
+        tie(calls, {})
+        way, uses, mine, opens = [0.0] * n, [[] for _ in range(161)], [[] for _ in range(n)], [None] * n
+        for i, c in enumerate(calls):
+            for r in sorted({int(k[1:]) for k in c["r"] + c["w"] if k[0] == "p" and k[1:].isdigit()}):
+                if not uses[r]:
+                    opens[i] = r
+                uses[r].append(i)
+                mine[i].append(r)
+        for i in range(n - 1, -1, -1):
+            c = calls[i]
+            way[i] = c["ns"] + max([c["late"]] + [way[j] + gap for j, gap in c["next"].items()])
+        pre = [[(j, gap(calls[j], c, j in c["war"], True), gap(calls[j], c, False, False)) for j in sorted(c["pre"])] for c in calls]
+        ways, queue = [{q: e[1] for q, e in c["ways"].items()} for c in calls], [c["q"] for c in calls]
+        state = ([0.0] * n, [0.0] * n, [len(u) for u in uses], [160] * 8, [0.0] * 8, {q: ([], []) for q in "vstpye"}, {}, {}, [0.0] * n, {q: 0.0 for q in "vstpye"})
+        more, long = [NS["slow"] if c["kind"] == "op" and c["q"] != "t" else 1.0 for c in calls], [0.0] * n
+        for i in range(n - 1, -1, -1):
+            c = calls[i]
+            long[i] = c["ns"] * more[i] + max([c["late"]] + [long[j] + gap + 25.0 for j, gap in c["next"].items()])
+        cuts = [0] + [min(i for i, c in enumerate(calls) if c["tag"][-1:] == e) for e in "23"] + [n]
+        seed = [PAR["seed"]]
+
+        def draw():
+            seed[0] = (seed[0] * 6364136223846793005 + 1442695040888963407) % 2 ** 64
+            return (seed[0] >> 11) / 2.0 ** 53
+        empty = state
+        for stage, (lo, hi) in enumerate(list(zip(cuts[:-1], cuts[1:])) + [(0, n)] * (3 in PAR["only"])):
+            before, state = state[0], empty if stage == 3 else state
+            tail = [max([c["late"]] + [way[j] + gap for j, gap in c["next"].items() if j >= hi]) for c in calls]
+            net = (ways, tail, pre, [[j for j in c["next"] if j < hi] for c in calls], opens, uses, mine)
+            base = state[:8] + ({i: len([j for j in calls[i]["pre"] if j >= lo]) for i in range(lo, hi)},
+                            list({calls[i]["tag"]: (i, PAR["pull"][calls[i]["tag"][:-1]]) for i in range(lo, hi) if calls[i]["tag"][:-1] in PAR["pull"]}.values()),
+                            [i for i in range(lo, hi) if queue[i] == "e"], state[8], state[9], more,
+                            [max([c["late"]] + [long[j] + gap + 25.0 for j, gap in c["next"].items() if j >= hi]) for c in calls])
+            rank = [-way[i] - PAR["bias"].get(calls[i]["tag"], 0.0) for i in range(n)] if stage < 3 else before
+            best = now = place(net, rank, queue, lo, hi, base)
+            loose, held = [i for i in range(lo, hi) if len(ways[i]) > 1], holdups(net, now, lo, hi)
+            kin = {}
+            for i in range(lo, hi):
+                kin.setdefault(calls[i]["tag"], []).append(i)
+            seeds, fresh, won = PAR["seeds"][stage % 3], now, 0
+            turns = PAR["turns"] if stage < 3 else PAR["whole"]
+            for turn in range(turns * len(seeds) if stage in PAR["only"] else 0):
+                if turn % turns == 0:
+                    seed[0], now = seeds[turn // turns], fresh
+                    held = holdups(net, now, lo, hi)
+                x, rank, queue = [draw() for _ in range(6)], list(now[1][0]), now[2]
+                i, j = held[int(x[1] * len(held))]
+                one = (i, j)[x[2] < 0.5]
+                if x[0] < PAR["swap"]:
+                    i = one if len(ways[one]) > 1 else loose[int(x[3] * len(loose))]
+                    others = [q for q in ways[i] if q != queue[i]]
+                    queue = queue[:i] + [others[int(x[4] * len(others))]] + queue[i + 1:]
+                elif x[0] < PAR["pass"]:
+                    if x[2] < 0.5:
+                        rank[i] = rank[j] - 1.0 - 600.0 * x[3] ** 3
+                    else:
+                        rank[j] = rank[i] + 1.0 + 600.0 * x[3] ** 3
+                elif x[0] < PAR["kin"]:
+                    for k in kin[calls[one if x[3] < 0.5 else lo + int(x[1] * (hi - lo))]["tag"]]:
+                        rank[k] += 1200.0 * (x[4] - 0.5)
+                elif x[0] < PAR["line"]:
+                    k = one if x[3] < 0.6 else lo + int(x[1] * (hi - lo))
+                    todo, seen, at, by = [k], {k}, rank[k], (50.0 + 900.0 * x[4] ** 2) * (1.0 if x[2] < 0.5 else -1.0)
+                    while todo:
+                        k = todo.pop()
+                        for e in (net[3][k] if by > 0.0 else [e[0] for e in pre[k]]):
+                            if e >= lo and e not in seen and abs(rank[e] - at) < 2500.0 * x[3] + 300.0:
+                                seen.add(e)
+                                todo.append(e)
+                    for k in seen:
+                        rank[k] += by
+                else:
+                    at = rank[i] if x[2] < 0.5 else rank[lo + int(x[1] * (hi - lo))]
+                    for k in range(lo, hi):
+                        if abs(rank[k] - at) < 200.0 + 1500.0 * x[3]:
+                            rank[k] += (draw() - 0.5) * (150.0 + 1300.0 * x[4])
+                got = place(net, rank, queue, lo, hi, base)
+                rest = 1.0 - (turn % turns) / turns
+                rest *= PAR["warm"] if stage == 3 else 1.0
+                w = PAR["keep"] + (1.0 - PAR["keep"]) * rest
+                if got and got[0] + w * (got[3] - now[3]) <= now[0] - PAR["give"] * rest * math.log(1.0 - x[5]):
+                    now = got
+                    held = holdups(net, now, lo, hi)
+                    if now[0] + 0.1 * now[3] < best[0] + 0.1 * best[3]:
+                        best, won = now, turn // turns
+            KEPT.setdefault("won", []).append((seeds[won], int(best[0])))
+            state, queue = best[1], best[2]
+            KEPT.setdefault("ends", []).append(int(max(state[1][i] + tail[i] for i in range(lo, hi))))
+        KEPT.update({"order": sorted(range(n), key=lambda i: (state[0][i], i)), "starts": state[0], "end": best[0], "dealt": (state[6], state[7], queue)})
+    for c, q in zip(calls, KEPT["dealt"][2]):
+        c["q"] = q
+        c["f"], c["ns"] = c["ways"][q]
+    link(calls)
+    tie(calls, KEPT["dealt"][1])
+    return KEPT["order"], KEPT["dealt"][0]
+
+
+def write(g, core, T, topo, bank_of):
     rank = T.rank_of(core)
-    if rank is None:
-        return
-    queues = {"v": g.vector, "s": g.scalar, "t": g.tensor, "p": g, "y": g.sync}
+    queues = {"s": g.scalar, "y": g.sync}
     calls, now, nfar = [], [""], [0]
     v, s, t = g.vector, g.scalar, g.tensor
-    P = [T["p%d" % b] for b in range(8)]
+    P = [T["p%d" % bank_of.get(r, 0)] for r in range(160)]
 
     def op(qn, f, r, w, n, tag="", late=0.0, kind="op", sem=None):
         if kind == "op" and qn in "sp":
-            n = max(n, PAR["smin"]) if qn == "s" else n + PAR["gp"]
-        calls.append({"q": qn, "f": f, "r": list(r), "w": list(w), "ns": n, "tag": tag + now[0], "late": late, "kind": kind, "sem": sem})
+            n = max(n, NS["smin"]) if qn == "s" else n + NS["gp"]
+        n = n * (NS["f"] if kind == "op" else 1.0) + NS["fix"]
+        calls.append({"q": qn, "f": f, "r": list(r), "w": list(w), "ns": n, "tag": tag + now[0], "late": late, "kind": kind, "sem": sem, "ways": {qn: (f, n)}})
+
+    def either(k):
+        ways = {c["q"]: (c["f"], c["ns"]) for c in calls[-k:]}
+        calls[-k:] = calls[-k:len(calls) - k + 1]
+        calls[-1]["ways"] = ways
 
     def plane(z, a, b):
-        if PAR["fl"] and (z in ("vz", "xz2") or z == "az" and a >= 256):
-            return T.xz2[:, 0:128] if z == "vz" else T["xz2" if z == "xz2" else "bz"][:, 128 + a:128 + b]
-        if z in ("efz", "wz", "vz"):
-            at = {"efz": 0, "wz": 512, "vz": 1024}[z] + a
-            if PAR["far"] == "W":
-                return T["sz%d" % (1 + at // 384)][:, 128 + at % 384:128 + at % 384 + b - a]
-            return T.cz[:, at:at + b - a]
+        if z == "vz":
+            return T.xz2[:, 0:128]
+        if z == "xz2" or z == "az" and a >= 256:
+            return T["xz2" if z == "xz2" else "bz"][:, 128 + a:128 + b]
+        if z == "efz":
+            return T.sz1[:, 128 + a:128 + b] if a < C else T.sz2[:, 128:256]
+        if z == "ehz" and a != 128:
+            return T.sz2[:, a:b] if a else T.xz1[:, C:512]
         return T[z][:, a:b]
 
     def cy(n):
-        return max(64.0, n) * CYC
+        return max(64.0, n) * NS["cyc"]
 
-    def dma(qn, out, in_, r, w, sem=None, tag=""):
-        op(qn, lambda: queues[qn].dma_start(out, in_), r, w, PAR["dq"], tag, PAR["dl"] + (0.0 if r else PAR["ld"]), "dma", sem)
+    def dma(qn, out, in_, r, w, size, sem=None, tag=""):
+        op(qn, lambda: queues[qn].dma_start(out, in_), r, w, NS["dq"], tag, NS["go"], "dma", sem)
+        under_way(r, w, NS["row"] * size[0] / 16 + NS["byte"] * size[0] * size[1] / 16, NS["dl"])
+
+    def under_way(r, w, n, late):
+        calls[-1]["w"].append("#%d" % len(calls))
+        op("e", len(calls) - 1, list(r) + ["#%d" % len(calls)], w, n, "e", late, "fly")
 
     def mm(bank, lq, lz, a, rq, rz, c, d, keys, start, stop, tag=""):
         op("t", lambda: t.matmul_mx(P[bank][:, 0:d - c], T[lq][:, a:a + 128], plane(lz, a, a + 128), T[rq][:, c:d], plane(rz, c, d), start, stop),
-           keys, ["p%d" % bank], (d - c + 16) * PAR["tc"], tag)
+           keys, ["p%d" % bank], (d - c + 16) * NS["tc"], tag)
 
     def cp(qn, out, in_, r, w, n, scale=None, tag=""):
-        if qn == "v":
-            if scale is None:
-                op("v", lambda: v.tensor_copy(out, in_), r, w, cy(n), tag)
-            else:
-                op("v", lambda: v.tensor_scalar(out, in_, scale, None, A.mult), r, w, cy(n), tag)
-        else:
+        if len(qn) > 1:
+            for q in qn:
+                cp(q, out, in_, r, w, n, scale, tag)
+            either(len(qn))
+        elif qn == "p":
+            op("p", lambda: g.affine_select(out, in_, [[0, n]], A.is_ge, 0.0, 0, 0), r, w, 170 + NS["own"] + 2 * NS["cyc"] * n, tag)
+        elif qn == "s":
             op("s", lambda: s.activation(out, in_, F.Copy, scale=1.0 if scale is None else scale), r, w, cy(n), tag)
+        elif scale is None:
+            op("v", lambda: v.tensor_copy(out, in_), r, w, cy(n), tag)
+        else:
+            op("v", lambda: v.tensor_scalar(out, in_, scale, None, A.mult), r, w, cy(n), tag)
 
     def ts(out, in_, s1, s2, o1, o2, r, w, n=1, tag="", ns=None):
         if o2 is None:
@@ -201,9 +385,9 @@ def rank_program(g, core, T, topo):
         op("s", lambda: s.activation(out, in_, f, **k), r, w, ns or cy(n) + (20 if "accum_out" in k else 0), tag)
 
     def picked(n):
-        return 55 + PAR["g"] * CYC * n
+        return 55 + NS["g"] * NS["cyc"] * n
 
-    def far(step, pairs, r, w, late, tag):
+    def far(step, pairs, r, w, width, tag):
         dst = T.cores[(rank + step) % N]
         rid, pid, _ = topo.addr(dst)
         eng = topo.engines(core, dst)
@@ -216,367 +400,361 @@ def rank_program(g, core, T, topo):
                 g.remote_dma_fused([RemoteDMATransfer(dst_ids=[DstId(rid=rid, pnc=pid)], dma_engine_mask=sum(1 << e for e in eng[k * i:k * i + k]),
                                                       remote_sem=T.sem[sem], src=b, dst=a) for i, (a, b) in enumerate(pairs)], local_sem=T.sem["sent"])
             return len(eng)
-        op("p", f, r, w, PAR["rq"] + (0.0 if nfar[0] else PAR["first"]), tag, PAR["fly"] + late, "far", sem)
+        op("p", f, r, w, NS["rq"] + (0.0 if nfar[0] else NS["first"]), tag, NS["fly"], "far", sem)
+        under_way(r, w, 8 * (NS["rr"] * len(pairs) + NS["rb"] * width), 1.0)
         nfar[0] += 1
 
     def u8(ap):
         return ap.bitcast(dt.uint8)
 
-    dma("y", T.uin[:], T.u[:], [], ["uin"], None, "L")
-    dma("s", T.xin[:, 0:512], T.x[:, 0:512], [], ["xin0"], None, "L")
-    dma("y", T.xin[:, 512:1024], T.x[:, 512:1024], [], ["xin1"], None, "L")
-    dma("s", T.xin[:, 1024:1536], T.x[:, 1024:1536], [], ["xin2"], None, "L")
-    for i in range(4):
-        calls[i]["late"] += 100.0 * i - 150.0
+    def spans(cuts, a=0, b=C):
+        e = [a] + [c for c in cuts if a < c < b] + [b]
+        return list(zip(e[:-1], e[1:]))
+
+    dma("y", T.uin[:], T.u[:], [], ["uin"], (128, 1024), None, "L")
+    dma("s", T.xin[:, 0:512], T.x[:, 0:512], [], ["xin0"], (128, 1024), None, "L")
+    dma("y", T.xin[:, 512:1024], T.x[:, 512:1024], [], ["xin1"], (128, 1024), None, "L")
+    dma("s", T.xin[:, 1024:1536], T.x[:, 1024:1536], [], ["xin2"], (128, 1024), None, "L")
     first = ["uin", "xin0", "xin1", "xin2"]
-    dma("y", u8(T.wq[:]), T.wc[:], first, ["wq"])
-    calls[-1]["late"] += 1000.0
-    for i in range(2):
-        dma("y", plane("wz", 256 * i, 256 * i + 256), T.ws[:, 256 * i:256 * i + 256], first, ["wz%d" % i])
-    dma("y", T.vin[:], T.v[:], first, ["vin"])
-    calls[-1]["late"] += 1500.0
+    dma("y", u8(T.wq[:]), T.wc[:], first, ["wq"], (128, 2048))
+    dma("y", T.wz[:], T.ws[:], first, ["wz"], (128, 512))
+    dma("y", T.vin[:], T.v[:], first, ["vin"], (128, 1024))
 
-    by_product = [PAR["down%d" % h] == "mm" for h in (1, 2, 3)]
-    fill(T.c32[:], 32.0, ["c32"], 64)
-    op("p", lambda: g.affine_select(T.eye[:], T.c32[:], [[-1, 128]], A.is_equal, 0.0, 0, 1), ["c32"], ["eye"], 385)
+    picks = any(PAR["vp%d" % h] for h in (1, 2, 3))
+    for e, a, c in (("ef", 0, 32.0), ("eh", 520, 0.5)):
+        fill(T.ef[:, a:a + 520], 0.0, [e], 260)
+        fill(T.c32[:, a // 4:a // 4 + 128], c, ["c" + e], 64)
+        op("p", lambda a=a: g.affine_select(T.ef[:, a + 3:a + 515:4], T.c32[:, a // 4:a // 4 + 128], [[-1, 128]], A.is_equal, 0.0, 0, 1), ["c" + e, e], [e], 385)
 
-    def count_up(out, pattern, base, step, w, n):
-        op("p", lambda: g.iota(out, pattern, base, step, allow_small_or_imprecise_dtypes=True), [], w, 130 + 2 * CYC * n, "i" + w[0])
+    def count_up(out, pattern, base, step, w, n, tag="i"):
+        op("p", lambda: g.iota(out, pattern, base, step, allow_small_or_imprecise_dtypes=True), [], w, 130 + 2 * NS["cyc"] * n, tag)
 
-    def lowest(out, in_, n, r, w):
-        op("p", lambda: g.affine_select(out, in_, [[0, n]], A.is_gt, -BIG, 0, 0), r, w, 170 + 2 * CYC * n, "i" + w[0])
-    fill(T.ef[:], 0.0, ["ef"], 260)
-    cp("v", T.ef[:, 3:515:4], T.eye[:], ["eye", "ef"], ["ef"], 64)
-    count_up(T.tb[:, 0:32], [[0, 32]], 0, 1, ["tb0"], 32)
-    count_up(T.tb[:, 32:64], [[16, 2], [0, 16]], 0, 1, ["tb1"], 32)
-    count_up(T.tb[:, 64:96], [[0, 2], [1, 8], [32, 2]], 0, 8, ["tb2"], 32)
-    for i in range(2):
-        count_up(T.tb[:, 96 + 16 * i:112 + 16 * i], [[1, 2], [2, 4], [32, 2]], 0, 0, ["tb%d" % (3 + i)], 16)
-        if any(by_product):
-            count_up(T.tb[:, 128 + 16 * i:144 + 16 * i], [[8, 2], [1, 4], [32, 2]], 0, 16, ["tb%d" % (5 + i)], 16)
-    nt = 160 if any(by_product) else 128
-    turn(T.pf[:, 0:nt], T.tb[:, 0:nt], ["tb%d" % i for i in range(7)], ["pf"], nt, "i")
-    cp("v", T.ordn[:, 0:1], T.pf[:, 96:97], ["pf"], ["ordn"], 1, None, "i")
-    ts(T.quad[:], T.pf[:, 0:1], -8.0, None, A.mult, None, ["pf"], ["quad"], 1, "i")
-    if not all(by_product):
-        ts(T.ordk[:, 0:2], T.pf[:, 64:66], T.quad[:], None, A.add, None, ["pf", "quad"], ["ordk0"], 1, "i")
-    if any(PAR["down%d" % h] == "turn" for h in (1, 2, 3)):
-        count_up(T.tr[:, C + 15:1024:16], [[0, 40]], 0, 0, ["trz"], 40)
-    if any(PAR["down%d" % h] == "mv" for h in (1, 2, 3)):
-        count_up(T.km[:, 12:32, :], [[0, 40]], 0, 0, ["kmz"], 40)
-    if any(by_product):
-        ts(T.ordk[:, 2:4], T.pf[:, 128:130], T.quad[:], T.quad[:], A.add, A.add, ["pf", "quad"], ["ordk1"], 1, "i")
-        count_up(T.tr4[:, :, 111:128:16], [[0, 8]], 0, 0, ["tr4z"], 8)
-        count_up(T.kd4[:], [[0, 64]], 0, 0, ["kd4z"], 64)
-    act(T.cap[:], T.ef[:, 0:C], F.Copy, ["ef"], ["cap"], C, scale=0.0, bias=BIG)
-    act(T.hist[:, 0:HW], T.ef[:, 0:HW], F.Copy, ["ef"], ["h0"], HW, scale=0.0, bias=BIG)
+    def const(out, c, w, n):
+        act(out, T.zero[:, 0:n], F.Copy, ["zero"], w, n, "c", scale=0.0, bias=c)
+    fill(T.zero[:], 0.0, ["zero"], HW / 2)
+    count_up(T.tb[:, 0:32], [[16, 2], [0, 16]], 15, 1, ["tb0"], 32)
+    if picks:
+        count_up(T.tb[:, 128:192], [[1, 2], [-1, 2], [0, 16]], 0, 0, ["tb4"], 64)
+    for G in range(4):
+        hi, lo, q = G // 2, G % 2, slice(32 * G, 32 * G + 32)
+        other = (G + 2) % 4 - G
+        count_up(T.tb[q, 32:40], [[12 - 24 * hi, 2], [other * (1 - 2 * lo), 2], [32, 2]], G + 12 * hi + other * lo, 8, ["tk%d" % G], 8, "K")
+    count_up(T.num[:], [[1, C]], 0, 0, ["num"], C)
+    for G in range(4):
+        hi, lo, q = G // 2, G % 2, slice(32 * G, 32 * G + 32)
+        count_up(T.tb[q, 64:72], [[16 - 32 * hi, 2], [8 - 16 * lo, 2], [32, 2]], 10 * G, 0, ["tn%d" % G], 8, "K")
+    tk, tn = ["tk%d" % G for G in range(4)], ["tn%d" % G for G in range(4)]
+    for i in range(1, 4):
+        act(T.tb[:, 32 + 8 * i:40 + 8 * i], T.tb[:, 32:40], F.Copy, tk, ["tk%d" % (3 + i)], 1, "i", bias=4.0 * (i % 2))
+        act(T.tb[:, 64 + 8 * i:72 + 8 * i], T.tb[:, 64:72], F.Copy, tn, ["tn%d" % (3 + i)], 1, "j", bias=1.0 * (i // 2))
+    turn(T.pf[:, 0:64], T.tb[:, 0:64], ["tb0", "tk4", "tk5", "tk6"], ["pf"], 64, "i")
+    turn(T.pf[:, 64:96], T.tb[:, 64:96], ["tn4", "tn5", "tn6"], ["pn"], 32, "j")
+    cp("v", T.ordk[:, 0:2], T.pf[:, 32:34], ["pf"], ["ordk0"], 1, None, "i")
+    cp("v", T.ordn[:, 0:1], T.pf[:, 64:65], ["pn"], ["ordn"], 1, None, "j")
+    if picks:
+        for i in range(2):
+            cp("s", T.tb[:, 96 + 16 * i:104 + 16 * i], T.tb[:, 64:72], tn, ["tp%d" % i], 1, None, "i")
+            cp("s", T.tb[:, 104 + 16 * i:112 + 16 * i], T.tb[:, 80:88], ["tn5"], ["tp%d" % (2 + i)], 1, None, "i")
+        turn(T.pf[:, 96:192], T.tb[:, 96:192], ["tb4"] + ["tp%d" % i for i in range(4)], ["pg"], 96, "i")
+        cp("v", T.ordn[:, 2:3], T.pf[:, 96:97], ["pg"], ["ordp"], 1, None, "i")
+        act(T.tb[:, 192:193], T.pf[:, 128:129], F.Abs, ["pg"], ["odd"], 1, "i")
+        for e, keep, k in (("ee", T.pf[:, 160:161], "pg"), ("eo", T.tb[:, 192:193], "odd")):
+            act(T[e][:], T.ef[:, 0:520], F.Copy, ["ef", k], [e], 520, "E", scale=keep)
+            for b in range(4):
+                quant(e + "q", e + "z", 128 * b, 128 * b + 128, T[e][:, 3 - b:515 - b], [e], [e + str(b)], "E")
     for b in range(4):
         quant("efq", "efz", 128 * b, 128 * b + 128, T.ef[:, 3 - b:515 - b], ["ef"], ["ef%d" % b], "E")
     halves = sorted({b for h in (1, 2, 3) for _, b in PAR["za%d" % h]})
-    if halves:
-        act(T.eh[:], T.ef[:], F.Copy, ["ef"], ["eh"], 520, scale=1.0 / 64)
-
-    def halving(rd):
-        for b in halves:
-            if rd == (1 if any(e == b for _, e in PAR["za1"]) else 2):
-                quant("ehq", "ehz", 128 * b, 128 * b + 128, T.eh[:, 3 - b:515 - b], ["eh", "out"], ["eh%d" % b], "E")
+    for b in halves:
+        quant("ehq", "ehz", 128 * b, 128 * b + 128, T.ef[:, 523 - b:1035 - b], ["eh"], ["eh%d" % b], "E")
     quant("xq0", "xz0", C, C + 128, T.uin[:], ["uin"], ["U0"], "L")
     for i in range(3):
         quant("xq0", "xz0", 128 * i, 128 * i + 128, T.xin[:, 512 * i:512 * i + 512], ["xin%d" % i], ["X0%d" % i], "L")
-    lowest(T.ex[:, 0:C:128], T.tb[:, 0:3], 3, ["tb0"], ["exz"])
-    lowest(T.hist[:, HW:9 * HW:HW], T.tb[:, 0:8], 8, ["tb0"], ["hsz"])
-    lowest(T.cap[:, 0:C:16], T.tb[:, 0:24], 24, ["tb0", "cap"], ["cap"])
-    count_up(T.n64[:], [[0, 64]], 1, 0, ["n%d%d" % (G, a) for G in range(4) for a in range(4)], 64)
-    count_up(T.al[:, 1:8 * HW:HW], [[0, 8]], 1, 0, ["alz"], 8)
-    if any(PAR["st%d" % h] for h in (1, 2, 3)):
-        count_up(T.one[:], [[0, 8]], 1, 0, ["one"], 8)
-        act(T.zero[:], T.ef[:, 0:C], F.Copy, ["ef"], ["zero"], C, scale=0.0)
-    SV, SS = 0, 1
-    turnb = [0]
+    quant("vq", "vz", 0, 128, T.vin[:], ["vin"], ["vq"], "j")
+    const(T.cap[:], BIG, ["cap"], 128)
+    fill(T.cap[:, 0:128:16], -BIG, ["cap"])
+    fill(T.ex[:, 0:C:128], -BIG, ["exz"])
+    fill(T.tr[:, 3:8, 15:128:16], 0.0, ["tr%d%d" % (G, i) for G in range(4) for i in (2, 3)] + ["trz"])
+    fill(T.nb[:], 0.0, ["nb%d%d%s" % (G, x, e) for G in range(4) for x in range(4) for e in "a67"])
+    half = C // 2 if PAR["fold"] else 0
+    const(T.hist[:, 0:HW], BIG, ["h0"], HW)
+    fill(T.hist[:, HW:5 * HW:HW], -BIG, ["hsa"])
+    fill(T.hist[:, 5 * HW + half:9 * HW:HW], -BIG, ["hsb"])
+    const(T.kh[:, 0:HW], -8.0, ["k0"], HW)
+    fill(T.kh[:, HW:9 * HW:HW], 8.0, ["ksa"])
+    if PAR["q4"]:
+        fill(T.qj[:, 4:40:5], 0.0, ["qj4"])
+    wide = max(d - c for c, d in spans(PAR["zc"]))
+    two = PAR["two"]
+    wd = 4 if two else 5
+    for j in range(wd):
+        const(T.mk[:, j:wd * wide:wd], float(min(j, 1)), ["mk%d" % j], wide)
+    cp("s", T.sl[:, wd - 1:wd * C:wd], T.num[:], ["num"], ["sl4"], C, 1.0 / 512, "c")
+    results = [0]
 
     def banks(n):
-        turnb[0] += n
-        return [2 + (turnb[0] - n + i) % 6 for i in range(n)]
+        results[0] += n
+        return list(range(results[0] - n, results[0]))
 
     def hv(k):
         return T.hist[:, HW * (k + 1) + C:HW * (k + 1) + C + 1]
 
-    def sl(name, k):
-        return T[name][:, C * k:C * k + C]
-
     def pieces(rd):
-        e = (0,) + PAR["cut%d" % rd] + (C,)
-        return [(e[i], e[i + 1]) for i in range(len(e) - 1)]
+        return spans(PAR["cut%d" % rd])
 
-    def within(rd, c, d):
-        return [h for h, (a, b) in enumerate(pieces(rd)) if a < d and c < b]
+    def within(cuts, c, d):
+        return [h for h, (a, b) in enumerate(spans(cuts)) if a < d and c < b]
 
-    def unpack(dst, q, z, c, d, r, w, bs, onv, tag):
+    def unpack(dst, q, z, c, d, r, w, bs, tag):
         for b in bs:
             mm(bs[b], "efq", "efz", 128 * b, q, z, c, d, r + ["ef%d" % b], True, True, tag)
-            cp("v" if onv(b) else "s", T[dst][:, C * b + c:C * b + d], P[bs[b]][:, 0:d - c], ["p%d" % bs[b]], [k + str(b) for k in w], d - c, 1.0 / 64, tag)
+            cp("sv", T[dst][:, C * b + c:C * b + d], P[bs[b]][:, 0:d - c], ["p%d" % bs[b]], [k + str(b) for k in w], d - c, 1.0 / 64, tag)
+
+    def histories(H, name, data, key, cuts, lo, first, o0, o1, per, tag):
+        for k in range(1, 9):
+            for c, d in spans(cuts, lo(k)):
+                at, up = HW * k, HW * (k - 1)
+                r = key(c, d) + [name + "sa", name + "sb"] + ([name + "0"] if k == 1 else ["%s%d_%d" % (name, k - 1, a) for a, b in spans(cuts, lo(k - 1)) if a < d - 1 and c - 1 < b])
+                if c > lo(k):
+                    r.append("%s%d_%d" % (name, k, [a for a, b in spans(cuts, lo(k)) if b == c][0]))
+                scan(H[:, at + c + 1:at + d + 1], data(c, d), H[:, up + c:up + d], first if c == lo(k) else H[:, at + c:at + c + 1], o0, o1,
+                     r, ["%s%d_%d" % (name, k, c)], (d - c) * per, tag + str(k))
+        return ["%s%d_%d" % (name, k, spans(cuts, lo(k))[-1][0]) for k in range(1, 9)]
 
     def one_round(rd):
         now[0] = str(rd)
         par = {k[:-1]: x for k, x in PAR.items() if k[-1] == str(rd)}
+        par.update({k: PAR[k] for k in ("hc", "zc", "kc")})
         xq, xz, nq, nz = "xq%d" % (rd - 1), "xz%d" % (rd - 1), "xq%d" % rd, "xz%d" % rd
         uq, uz, ua = ("uq%d" % (rd - 1), "uz%d" % (rd - 1), 0) if rd > 1 else (xq, xz, C)
         HALF = pieces(rd)
         uk, nk = ["U%d" % (rd - 1), "Uz%d" % (rd - 1)], ["X%d%d" % (rd, h) for h in range(len(HALF))]
         xk = ["X%d%d" % (rd - 1, h) for h in range(3 if rd == 1 else len(pieces(rd - 1)))]
         ahead = rd == PAR["ahead"]
-        halving(rd)
-        if rd == 2:
-            quant("vq", "vz", 0, 128, T.vin[:], ["vin", "out"], ["vq"], "E")
-        if ahead:
-            hk = ["hq%d" % h for h in range(len(pieces(rd - 1)) if PAR["xh"] else 1)]
-            for b in (SV, SS):
-                mm(b, "gq", "gz", 0, "hq", "hz", 0, C, ["gq", "gz", "hz"] + hk, True, True, "B")
-        mine = SV
-        if par["down"] != "turn":
-            SB = banks(3)
-            if not ahead:
-                mm(SV, uq, uz, ua, xq, xz, 0, C, uk + xk, True, True, "S")
-            for j in range(3):
-                mm(SB[j], xq, xz, 128 * j, uq, uz, ua, ua + 128, uk + (xk if rd > 1 else xk[j:j + 1]), True, True, "U")
-        else:
+        parts = spans(par["sv"]) + [(0, C)]
+        SP = banks(len(parts))
+        SV, SS = SP[0], SP[-1]
+        for b, (c, d) in zip(SP, parts):
             if ahead:
-                mine = banks(1)[0]
-            mm(mine, uq, uz, ua, xq, xz, 0, C, uk + xk, True, True, "S")
-        calls[-1]["w"].append("S")
-        if not ahead:
-            mm(SS, uq, uz, ua, xq, xz, 0, C, uk + xk, True, True, "S")
-        if par["down"] == "mm":
-            for j in range(3):
-                scan(T.ex[:, 128 * j + 1:128 * j + 128], P[SB[j]][:, 0:127], T.cap[:, 1:128], -BIG, A.max, A.min, ["p%d" % SB[j], "cap"], ["ex%d" % j], 128, "k")
-                tt(T.nr4[:, :, 32 * j:32 * j + 32], P[SB[j]][:, 0:128], T.ex[:, 128 * j:128 * j + 128], A.is_le, ["p%d" % SB[j], "ex%d" % j, "exz"], ["nr%d" % j], cy(128), "k")
-            for G in range(4):
-                scan(T.tr4[:, G, 0:96], T.nr4[:, G, 0:96], T.nr4[:, G, 0:96], 0.0, A.mult, A.add, ["nr0", "nr1", "nr2"], ["tq%d" % G], 1, "k")
-            turn(T.ct[:], T.tr4[:, :, 15:128:16], ["tq0", "tq1", "tq2", "tq3", "tr4z"], ["ct"], 1, "k")
-            for a in range(4):
-                dma(par["kq"][a], T.kd4[a:128:8], T.ct[32 * a:32 * a + 32, :], ["ct", "kd4z"], ["kd4%d" % a], "m%d4%s" % (rd, par["kq"][a]), "k")
-                calls[-1]["late"] += PAR["kl"]
-            kdk = ["kd4%d" % a for a in range(4)]
-            for h in range(2):
-                turn(T.ko[:, 32 * h:32 * h + 32], T.kd4[:, :, h, :], kdk, ["ko%d" % h], 1, "k")
-            o = 2
-        elif par["down"] == "mv":
-            for j in range(3):
-                nr = T.nr[:, 128 * j:128 * j + 128]
-                scan(T.ex[:, 128 * j + 1:128 * j + 128], P[SB[j]][:, 0:127], T.cap[:, 1:128], -BIG, A.max, A.min, ["p%d" % SB[j], "cap"], ["ex%d" % j], 128, "k")
-                tt(nr, P[SB[j]][:, 0:128], T.ex[:, 128 * j:128 * j + 128], A.is_le, ["p%d" % SB[j], "ex%d" % j, "exz"], ["nr%d" % j], cy(128), "k")
-                scan(T.tr3[:, j, :], nr, nr, 0.0, A.mult, A.add, ["nr%d" % j], ["tq%d" % j], 64, "k")
-            for a in range(4):
-                for G in range(4):
-                    dst, src, q = T.km[32 * G:32 * G + 32, a:12:4, :], T.tr3[32 * a:32 * a + 32, :, 32 * G + 15:32 * G + 32:16], par["km"][4 * a + G]
-                    r, w = ["tq0", "tq1", "tq2", "kmz"], ["km%d%d" % (a, G)]
-                    if q == "p":
-                        op("p", lambda dst=dst, src=src: g.affine_select(dst, src, [[0, 6]], A.is_ge, 0.0, 0, 0), r, w, 180.0, "K")
-                    else:
-                        cp(q, dst, src, r, w, 1, None, "K")
-            for h in range(2):
-                turn(T.kd[:, :, h, :], T.km[:, :, h], ["km%d%d" % (a, G) for a in range(4) for G in range(4)], ["kd%d" % h], 1, "k")
-            kdk = ["kd0", "kd1"]
-            turn(T.ko[:], T.kd[:], kdk, ["ko0", "ko1"], 1, "k")
-            o = 0
-        else:
-            turn(T.st[:], P[mine][:, 0:C], ["p%d" % mine], ["st"], C, "k")
-            scan(T.ex[:, 1:C], T.st[:, 0:C - 1], T.cap[:, 1:C], -BIG, A.max, A.min, ["st", "cap"], ["ex0", "ex1", "ex2", "exw"], C, "k")
-            tt(T.nr[:], T.st[:], T.ex[:], A.is_le, ["st", "ex0", "exz"], ["nr"], cy(2 * C), "k")
-            scan(T.tr[:, 0:C], T.nr[:], T.nr[:], 0.0, A.mult, A.add, ["nr"], ["tr"], C / 2, "k")
-            for h in range(2):
-                turn(T.kd[:, :, h, :], T.tr[:, 15 + 16 * h:1024:32], ["tr", "trz"], ["kd%d" % h], 1, "k")
-            kdk = ["kd0", "kd1"]
-            turn(T.ko[:], T.kd[:], kdk, ["ko0", "ko1"], 1, "k")
-            o = 0
-        ts(T.ok[:], T.ko[:].indirect(T.ordk[:, o:o + 2]), -1.0, T.pf[:, 47:48], A.mult, A.add, ["ko0", "ko1", "pf", "ordk%d" % (o // 2)], ["ok"], 1, "k", picked(32))
+                mm(b, "gq", "gz", 0, "hq", "hz", c, d, ["gq", "gz", "hz"] + ["hq0", "hq1", "hq2"], True, True, "S")
+            else:
+                mm(b, uq, uz, ua, xq, xz, c, d, uk + (xk if rd > 1 else xk[c // 128:(d + 127) // 128]), True, True, "S")
+
+        def scores(c, d):
+            i = within(par["sv"], c, d)[0]
+            return P[SP[i]][:, c - parts[i][0]:d - parts[i][0]]
+        SB = banks(3)
+        for j in range(3):
+            mm(SB[j], xq, xz, 128 * j, uq, uz, ua, ua + 128, uk + (xk if rd > 1 else xk[j:j + 1]), True, True, "U")
+        for j in range(3):
+            nr = T.nr[:, 128 * j:128 * j + 128]
+            scan(T.ex[:, 128 * j + 1:128 * j + 128], P[SB[j]][:, 0:127], T.cap[:, 1:128], -BIG, A.max, A.min, ["p%d" % SB[j], "cap"], ["ex%d" % j], 128, "ke")
+            tt(nr, P[SB[j]][:, 0:128], T.ex[:, 128 * j:128 * j + 128], A.is_le, ["p%d" % SB[j], "ex%d" % j, "exz"], ["nr%d" % j], cy(128), "kn")
+            scan(T.tr[:, j, :], nr, nr, 0.0, A.mult, A.add, ["nr%d" % j], ["tq%d" % j], 64, "kt")
+        tq = ["tq0", "tq1", "tq2"]
+        for i in range(2):
+            a, b = 64 * i, 64 - 64 * i
+            cp("svp", T.tr[b:b + 64, 3:6, b + 15:b + 64:16], T.tr[a:a + 64, 0:3, b + 15:b + 64:16], tq + ["tr%d1" % G for G in (2 * i, 2 * i + 1)],
+               ["tr%d2" % G for G in (2 - 2 * i, 3 - 2 * i)], 12, None, "K")
+        for a in range(4):
+            G = a + 1 - 2 * (a % 2)
+            e = 32 * ((G + 2) % 4)
+            cp("svp", T.tr[32 * G:32 * G + 32, 0:6, e + 15:e + 32:16], T.tr[32 * a:32 * a + 32, 0:6, 32 * G + 15:32 * G + 32:16], tq + ["tr%d2" % a],
+               ["tr%d1" % G, "tr%d3" % G], 12, None, "K")
+        for h in range(2):
+            turn(T.kd[:, :, h, :], T.tr[:, :, 15 + 16 * h:128:32], tq + ["trz"] + ["tr%d%d" % (G, i) for G in range(4) for i in (1, 2, 3)], ["kd%d" % h], 1, "k")
+        turn(T.ko[:], T.kd[:], ["kd0", "kd1"], ["ko"], 1, "k")
+        ts(T.ok[:], T.ko[:].indirect(T.ordk[:, 0:2]), -1.0, T.pf[:, 0:1], A.mult, A.add, ["ko", "pf", "ordk0", "ordk1"], ["ok"], 1, "k", picked(32))
         for b, bank in enumerate(banks(4)):
-            mm(bank, "efq", "efz", 128 * b, uq, uz, ua, ua + 128, uk + ["ef%d" % b, "S"], True, True, "D")
-            cp("v" if b in par["duv"] else "s", T.du[:, 128 * b:128 * b + 128], P[bank][:, 0:128], ["p%d" % bank], ["du%d" % b], 128, 1.0 / 64, "D")
+            mm(bank, "efq", "efz", 128 * b, uq, uz, ua, ua + 128, uk + ["ef%d" % b], True, True, "D")
+            cp("sv", T.du[:, 128 * b:128 * b + 128], P[bank][:, 0:128], ["p%d" % bank], ["du%d" % b], 128, 1.0 / 64, "D")
         if rd == 1:
             for b in range(4):
                 hs = [h for h in range(len(HALF)) if (h, b) not in par["za"]]
                 if hs:
-                    unpack("th", xq, xz, HALF[hs[0]][0], HALF[hs[-1]][1], xk + ["S"], ["th%d" % h for h in hs], {b: banks(1)[0]}, lambda b: b in par["tv"], "T")
-        for k in range(8):
-            scan(T.hist[:, HW * (k + 1) + 1:HW * (k + 1) + 1 + C], P[SV][:, 0:C], T.hist[:, HW * k:HW * k + C], -BIG, A.max, A.min,
-                 ["p%d" % SV, "h%d" % k, "hsz"], ["h%d" % (k + 1)], C, "M%d" % k)
-        ts(T.sg[:, 0:1], hv(0), hv(1), -0.5, A.not_equal, A.add, ["h1", "h2"], ["g0"], 1, "g")
-        ts(T.b0[:], hv(0), T.sg[:, 0:1], -1.0, A.mult, A.mult, ["h1", "g0"], ["b0"], 1, "g")
-        for k in range(8):
-            out = sl("bl", k)
-            if k == 0:
-                act(out, T.hist[:, HW:HW + C], F.Sign, ["h1", "g0", "b0"], ["bl0", "c0"], C, "c0",
-                    bias=T.b0[:], scale=T.sg[:, 0:1], accum_out=T.cn[:, 0:1])
-            else:
-                if k in par["gb"]:
-                    tt(T.ep[:, k:k + 3], T.hist[:, HW * (k + 1) + C:HW * (k + 4):HW], T.hist[:, HW * (k + 2) + C:HW * (k + 5):HW], A.is_equal,
-                       ["h%d" % i for i in range(k + 1, k + 5)], ["ep%d" % k], cy(1), "g%d" % k)
-                    ts(T.sg[:, k:k + 3], T.ep[:, k:k + 3], -0.5, None, A.add, None, ["ep%d" % k], ["g%d" % i for i in range(k, k + 3)], 1, "g%d" % k)
-                elif k < 7 and k - 1 not in par["gb"] and k - 2 not in par["gb"] and k + 1 not in par["st"]:
-                    ts(T.sg[:, k:k + 1], hv(k), hv(k + 1), -0.5, A.is_equal, A.add, ["h%d" % (k + 1), "h%d" % (k + 2)], ["g%d" % k], 1, "g%d" % k)
-                if k in par["st"]:
-                    j = max([0] + [i for i in par["st"] if i < k])
-                    tt(T.eq[:, j + 1:k + 1], T.hist[:, HW * (j + 1) + C:HW * (k + 1):HW], T.hist[:, HW * (j + 2) + C:HW * (k + 2):HW], A.is_equal,
-                       ["h%d" % i for i in range(j + 1, k + 2)], ["eq%d" % k], cy(1), "o%d" % k)
-                    scan(T.ob[:, j + 1:k + 1], T.eq[:, j + 1:k + 1], T.one[:, j + 1:k + 1], T.ob[:, j:j + 1] if j else 1.0, A.mult, A.add,
-                         ["eq%d" % k, "one", "ob%d" % j], ["ob%d" % k], 1, "o%d" % k)
-                    if k in par["av"]:
-                        ts(sl("ab", k), P[SV][:, 0:C], hv(k), -1.0, A.is_equal, A.mult, ["p%d" % SV, "h%d" % (k + 1)], ["a%d" % k], C, "a%d" % k)
-                    else:
-                        act(sl("bv", k), P[SS][:, 0:C], F.Sign, ["p%d" % SS, "h%d" % (k + 1)], ["bv%d" % k], C, "a%d" % k, bias=hv(k), scale=-1.0)
-                        ts(sl("ab", k), sl("bv", k), 0.0, -1.0, A.is_equal, A.mult, ["bv%d" % k], ["a%d" % k], C / 2, "b%d" % k)
-                elif k in par["av"]:
-                    ts(sl("ab", k), P[SV][:, 0:C], hv(k), None, A.not_equal, None, ["p%d" % SV, "h%d" % (k + 1)], ["a%d" % k], C, "a%d" % k)
-                else:
-                    act(sl("ab", k), P[SS][:, 0:C], F.Abs, ["p%d" % SS, "h%d" % (k + 1)], ["a%d" % k], C, "a%d" % k, bias=hv(k), scale=-1.0)
-                alive = T.al[:, HW * k + 1:HW * k + 1 + C]
-                bar = "bv" if k in par["bv"] else "bl"
-                if k in par["st"]:
-                    scan(T.al[:, HW * k + 2:HW * k + 2 + C], sl("ab", k), T.zero[:], T.ob[:, k:k + 1], A.add, A.max, ["a%d" % k, "zero", "ob%d" % k], ["l%d" % k], C / 2, "l%d" % k)
-                else:
-                    if bar == "bv":
-                        ts(sl("bv", k - 1), T.al[:, HW * (k - 1) + 1:HW * (k - 1) + 1 + C], T.sg[:, k - 1:k], None, A.mult, None,
-                           ["l%d" % (k - 1), "g%d" % (k - 1), "alz"], ["bv%d" % (k - 1)], C / 2, "b%d" % k)
-                    scan(T.al[:, HW * k + 2:HW * k + 2 + C], sl("ab", k), sl(bar, k - 1), 1.0, A.min, A.max, ["a%d" % k, bar + str(k - 1)], ["l%d" % k], C / 2, "l%d" % k)
-                if k + 1 in par["bv"] or k + 1 in par["st"] or k == 7:
-                    act(out, alive, F.Sign, ["l%d" % k, "alz"], ["bl%d" % k, "c%d" % k], C, "c%d" % k, accum_out=T.cn[:, k:k + 1] if k < 7 else T.ca[:, 7:8])
-                else:
-                    act(out, alive, F.Sign, ["l%d" % k, "g%d" % k, "alz"], ["bl%d" % k, "c%d" % k], C, "c%d" % k, scale=T.sg[:, k:k + 1], accum_out=T.cn[:, k:k + 1])
-            if k % 2:
-                G, r = k // 2, ["c%d" % (k - 1), "c%d" % k]
-                plain = k == 7 or par["mv"][G] != "ssss"
-                if plain:
-                    e = k + 1 if k < 7 else k
-                    act(T.ca[:, k - 1:e], T.cn[:, k - 1:e], F.Abs, r[:e - k + 1], ["ca%d" % G], 1, "m%d" % G)
-                    r = ["ca%d" % G] + r[e - k + 1:]
-                for a in range(4):
-                    o = T.n64[32 * G:32 * G + 32, 0, 2 * a:2 * a + 2] if par["vp"] else T.n64[32 * G:32 * G + 32, :, 2 * a]
-                    w, q = ["n%d%d" % (G, a)], par["mv"][G][a]
-                    src = T["ca" if plain else "cn"][32 * a:32 * a + 32, k - 1:k + 1]
-                    if q == "p":
-                        op("p", lambda o=o, src=src: g.affine_select(o, src, [[0, 2]], A.is_ge, 0.0, 0, 0), r, w, 175.0, "m%d" % G)
-                    elif q == "v":
-                        cp("v", o, src, r, w, 1, None, "m%d" % G)
-                    else:
-                        act(o, src, F.Abs, r, w, 1, "m%d" % G)
+                    unpack("th", xq, xz, HALF[hs[0]][0], HALF[hs[-1]][1], xk, ["th%d" % h for h in hs], {b: banks(1)[0]}, "T")
+        if half:
+            cp("s", T.hf[:], P[SS][:, half:C], ["p%d" % SS], ["hf"], half, None, "M")
+            for i, o in enumerate((A.min, A.max)):
+                tt(T.fo[:, half * i:half * i + half], P[SV][:, 0:half], T.hf[:], o, ["p%d" % SV, "hf"], ["fo%d" % i], cy(half), "M")
+            hk = histories(T.hist, "h", lambda c, d: T.fo[:, c:d], lambda c, d: ["fo%d" % i for i in within((half,), c, d)], par["hc"],
+                           lambda k: 0 if k < 5 else half, -BIG, A.max, A.min, 1.0, "M")
+        else:
+            hk = histories(T.hist, "h", scores, lambda c, d: ["p%d" % SP[within(par["sv"], c, d)[0]]], par["hc"], lambda k: 0, -BIG, A.max, A.min, 1.0, "M")
+        for j in range(4):
+            if two and j == 3:
+                for i, (c, d) in enumerate(spans(par["zc"])):
+                    scan(T.zp[:, 4 * c:4 * d], T.mk[:, 0:4 * (d - c)], T.sl[:, 4 * c:4 * d], 0.0, A.mult, A.add,
+                         ["sl4"] + ["mk%d" % j for j in range(4)] + ["sl%d_%d" % (j, i) for j in range(3)], ["zp%d" % i, "sl3_%d" % i, "sl3_%d" % (i - 1)], 2 * (d - c), "e")
+            for c, d in spans(par["zc"] if j == 3 else ()):
+                out = T.zp[:, 4 * c + 5:4 * d + 5:4] if two and j == 3 else T.sl[:, wd * c + j:wd * d:wd]
+                act(out, P[SS][:, c:d], F.Sign, ["p%d" % SS, hk[2 * j + 1]], ["sl%d_%d" % (j, i) for i in within(par["zc"], c, d)], d - c, "a%d" % j,
+                    bias=hv(2 * j + 1), scale=-1.0)
+        for i, (c, d) in enumerate(spans(par["zc"])):
+            if two:
+                scan(T.zs[:, 2 * c:2 * d], T.mk[:, 0:4 * (d - c):2], T.zp[:, 4 * c + 3:4 * d + 3:2], 0.0, A.mult, A.add, ["sl3_%d" % i], ["zs%d" % i], d - c, "b")
+                continue
+            scan(T.zs[:, 5 * c:5 * d], T.mk[:, 0:5 * (d - c)], T.sl[:, 5 * c:5 * d], 0.0, A.mult, A.add,
+                 ["sl4"] + ["mk%d" % j for j in range(5)] + ["sl%d_%d" % (j, i) for j in range(4)], ["zs%d" % i], 2.5 * (d - c), "b")
+        if PAR["q4"]:
+            for j in range(4):
+                act(T.qj[:, j:40:5], T.hist[:, HW + C:9 * HW:HW], F.Sign, hk, ["qj%d" % j], 1, "q", bias=hv(2 * j + 1), scale=-1.0)
+            scan(T.qs[:], T.mk[:, 0:40], T.qj[:], 0.0, A.mult, A.subtract, ["qj%d" % j for j in range(5)] + ["mk%d" % j for j in range(5)], ["qa%d" % k for k in range(8)], 1, "q")
+        for k in range(8 if PAR["q4"] else PAR["qa"], 8):
+            act(T.qj[:, 4 * k:4 * k + 4], T.hist[:, 2 * HW + C:9 * HW:2 * HW], F.Sign, hk, ["qa%d" % k], 1, "q", bias=hv(k), scale=-1.0, accum_out=T.qa[:, k:k + 1])
+        kk = histories(T.kh, "k", lambda c, d: T.zs[:, 2 * c + 1:2 * d:2] if two else T.zs[:, 5 * c + 4:5 * d:5], lambda c, d: ["zs%d" % i for i in within(par["zc"], c, d)], par["kc"],
+                       lambda k: 0, 8.0, A.min, A.max, 0.5, "N")
+        keys = T.kh[:, HW + C:7 * HW:HW]
+        if PAR["qa"]:
+            ts(T.qi[:, 0:6], keys, -0.375, None, A.add, None, kk[:6], ["qi"], 1, "m")
+            tt(T.nb[:, 0, 0:6], keys, T.qi[:, 0:6], A.subtract, kk[:6] + ["qi"], ["nb%d0a" % G for G in range(4)], cy(1), "m")
+        else:
+            tt(T.nb[:, 0, 0:6], keys, T.qs[:, 4:30:5] if PAR["q4"] else T.qa[:, 0:6], A.add, kk[:6] + ["qa%d" % k for k in range(6)], ["nb%d0a" % G for G in range(4)], cy(1), "m")
         for i in range(2):
-            turn(T.nd[:, :, i, :], T.n64[:, 0 if par["vp"] else i, :], ["n%d%d" % (G, a) for G in range(4) for a in range(4)], ["nd%d" % i], 1, "n")
+            a, b = 64 * i, 64 - 64 * i
+            cp("svp", T.nb[b:b + 64, 2, 0:6], T.nb[a:a + 64, 0, 0:6], ["nb%d0a" % G for G in (2 * i, 2 * i + 1)], ["nb%d2a" % G for G in (2 - 2 * i, 3 - 2 * i)], 6, None, "m")
+        for i, a in enumerate((0, 1, 3)):
+            G = a + 1 - 2 * (a % 2)
+            cp("svp", T.nb[32 * G:32 * G + 32, 1:4:2, 0:6], T.nb[32 * a:32 * a + 32, 0:4:2, 0:6], ["nb%d0a" % a, "nb%d2a" % a], ["nb%d1a" % G, "nb%d3a" % G], 12, None, "m")
+        if par["nl"]:
+            for k in (6, 7):
+                for a in range(4):
+                    q = slice(32 * a, 32 * a + 32)
+                    out, key, lv = T.nb[96:128, 3 - a, k:k + 1], T.kh[q, HW * (k + 1) + C:HW * (k + 1) + C + 1], T.qs[q, 5 * k + 4:5 * k + 5] if PAR["q4"] else T.qa[q, k:k + 1]
+                    r, w = [kk[k], "qa%d" % k], ["nb3%d%d" % (3 - a, k)]
+                    act(out, key, F.Identity, r, w, 1, "l", bias=lv)
+                    ts(out, key, lv, None, A.add, None, r, w, 1, "l")
+                    either(2)
+        else:
+            tt(T.nb[:, 0, 6:8], T.kh[:, 7 * HW + C:9 * HW:HW], T.qa[:, 6:8], A.add, kk[6:] + ["qa6", "qa7"], ["nb%d0%d" % (G, k) for G in range(4) for k in (6, 7)], cy(1), "l")
+            for a in range(3):
+                cp("svp", T.nb[96:128, 3 - a, 6:8], T.nb[32 * a:32 * a + 32, 0, 6:8], ["nb%d06" % a, "nb%d07" % a], ["nb3%d6" % (3 - a), "nb3%d7" % (3 - a)], 2, None, "ml")
+        for i in range(2):
+            turn(T.nd[:, :, i, :], T.nb[:], ["nb%d%d%s" % (G, x, e) for G in range(4) for x in range(4) for e in "a67"], ["nd%d" % i], 1, "n")
         turn(T.no[:], T.nd[:], ["nd0", "nd1"], ["no"], 1, "n")
-        ts(T.on[:], T.no[:].indirect(T.ordn[:, 0:1]), -1.0, None, A.add, None, ["no", "ordn"], ["on"], 1, "n", picked(16))
+        o = 2 if par["vp"] else 0
+        ts(T.on[:], T.no[:].indirect(T.ordn[:, o:o + 1]), 512.0, None, A.mult, None, ["no", "ordp" if o else "ordn"], ["on"], 1, "n", picked(16))
         for h, (c, d) in enumerate(HALF):
             for b in range(4):
                 win = T.du[:, 128 * b:128 * b + 128].indirect(T.ok[:, c // 16:d // 16])
                 if (h, b) in par["za"]:
                     bank = banks(1)[0]
-                    mm(bank, "ehq", "ehz", 128 * b, xq, xz, c, d, xk + ["eh%d" % b, "S"], True, True, "Y%d" % h)
+                    mm(bank, "ehq", "ehz", 128 * b, xq, xz, c, d, xk + ["eh%d" % b], True, True, "Y%d" % h)
                     act(T.za[:, C * b + c:C * b + d], win, F.Copy, ["du%d" % b, "ok"], ["za%d%d" % (h, b)], 1, "y%d" % h, picked(d - c) + 10)
                     tt(T.zt[:, 4 * c + b:4 * d:4], P[bank][:, 0:d - c], T.za[:, C * b + c:C * b + d], A.add, ["p%d" % bank, "za%d%d" % (h, b)], ["zt%d%d" % (h, b)], cy(d - c), "z%d" % h)
                     continue
                 tt(T.zt[:, 4 * c + b:4 * d:4], win, T.th[:, C * b + c:C * b + d], A.add,
-                   ["du%d" % b, "ok", "tr%d%d" % (h, b)] + ["th%d%d" % (i, b) for i in within(max(rd - 1, 1), c, d)], ["zt%d%d" % (h, b)],
-                   55 + PAR["ttg"] * CYC * (d - c), "z%d" % h)
+                   ["du%d" % b, "ok", "tw%d%d" % (h, b)] + ["th%d%d" % (i, b) for i in within(PAR["cut%d" % max(rd - 1, 1)], c, d)], ["zt%d%d" % (h, b)],
+                   picked(d - c), "z%d" % h)
             quant("zq", "zz", c, d, T.zt[:, 4 * c:4 * d], ["zt%d%d" % (h, b) for b in range(4)], ["Z%d" % h], "z%d" % h)
         for h, (c, d) in enumerate(HALF):
             for b, bank in enumerate(banks(4)):
                 mm(bank, "efq", "efz", 128 * b, xq, xz, c, d, xk + ["ef%d" % b], True, False, "R")
-                mm(bank, "wq", "wz", 128 * b, "zq", "zz", c, d, ["Z%d" % h, "wq", "wz%d" % (b // 2)], False, True, "W")
-                cp("v" if (h, b) in par["xv"] else "s", T.xt[:, 4 * c + b:4 * d:4], P[bank][:, 0:d - c], ["p%d" % bank], ["xt%d%d" % (h, b)], d - c, 1.0 / 32, "x%d" % h)
+                mm(bank, "wq", "wz", 128 * b, "zq", "zz", c, d, ["Z%d" % h, "wq", "wz"], False, True, "W")
+                cp("sv", T.xt[:, 4 * c + b:4 * d:4], P[bank][:, 0:d - c], ["p%d" % bank], ["xt%d%d" % (h, b)], d - c, 1.0 / 32, "x%d" % h)
             quant(nq, nz, c, d, T.xt[:, 4 * c:4 * d], ["xt%d%d" % (h, b) for b in range(4)], [nk[h]], "x%d" % h)
+        for h, (c, d) in enumerate(spans(par["sent"])):
+            r = [nk[i] for i in within(par["cut"], c, d)]
             if ahead:
-                if PAR["fl"] and d == C:
-                    far(STEP[rd - 1], [(u8(T.aq[:, c:d]), u8(T[nq][:, c:d])), (T.bz[:], T.xz2[:])], nk + ["vq"], ["aq%d" % h, "az%d" % h], PAR["xf"], "F")
+                if d == C:
+                    far(STEP[rd - 1], [(u8(T.aq[:, c:d]), u8(T[nq][:, c:d])), (T.bz[:], T.xz2[:])], nk + ["vq"], ["aq%d" % h, "az%d" % h], 1024, "F")
                 else:
-                    far(STEP[rd - 1], [(u8(T.aq[:, c:d]), u8(T[nq][:, c:d]))], [nk[h]], ["aq%d" % h], 200.0 + 2.5 * (d - c), "F")
-                    far(STEP[rd - 1], [(T.az[:, c:d], plane(nz, c, d))], [nk[h]], ["az%d" % h], 200.0 + 0.8 * (d - c), "F")
-        for h, (c, d) in enumerate(() if rd + 1 != PAR["ahead"] else HALF if PAR["xh"] else ((0, C),)):
-            r = [nk[h]] if PAR["xh"] else nk
-            far(STEP[rd], [(u8(T.hq[:, c:d]), u8(T[nq][:, c:d]))], r, ["hq%d" % h], 200.0 + 2.5 * (d - c), "H")
-            if d == C:
-                far(STEP[rd], [(T.hz[:], T[nz][:, 0:C])], nk, ["hz"], 200.0 + 0.8 * C, "I")
+                    far(STEP[rd - 1], [(u8(T.aq[:, c:d]), u8(T[nq][:, c:d]))], r, ["aq%d" % h], 4 * (d - c), "F")
+                    if not par["vp"]:
+                        far(STEP[rd - 1], [(T.az[:, c:d], plane(nz, c, d))], r, ["az%d" % h], d - c, "F")
+            if rd + 1 == PAR["ahead"]:
+                if d == C and PAR["hf"]:
+                    far(STEP[rd], [(u8(T.hq[:, c:d]), u8(T[nq][:, c:d])), (T.hz[:], T[nz][:])], nk + ["eh0"], ["hq%d" % h, "hz"], 1024, "I")
+                    continue
+                far(STEP[rd], [(u8(T.hq[:, c:d]), u8(T[nq][:, c:d]))], r, ["hq%d" % h], 4 * (d - c), "H")
+                if d == C:
+                    far(STEP[rd], [(T.hz[:, 0:C], T[nz][:, 0:C])], nk, ["hz"], C, "I")
         src = "tf" if ahead else "th"
-        for h, (c, d) in enumerate(HALF):
+        for h, (c, d) in enumerate(spans(par["sent"])):
             if ahead and not par["vp"]:
-                unpack("tf", "aq", "az", c, d, ["aq%d" % h, "az%d" % h], ["tf%d" % h], dict(enumerate(banks(4))), lambda b: (h, b) in par["wv"], "A%d" % h)
+                unpack("tf", "aq", "az", c, d, ["aq%d" % h, "az%d" % h], ["tf%d" % h], dict(enumerate(banks(4))), "A%d" % h)
         if par["vp"]:
-            wq, wz = ("aq", "az") if ahead else (nq, nz)
+            wq, wz = (T.aq[:], T.bz[:, 128:512]) if ahead else (T[nq][:], T[nz][:])
+            rq, rz = (["aq0", "aq1"], ["az1"]) if ahead else (nk, nk)
             VB = banks(4)
             for i, e in enumerate("eo"):
                 dq, dz, off = "v%sq%d" % (e, rd), "v%sz%d" % (e, rd), T.on[:, 8 * i:8 * i + 8]
-                op("v", lambda dq=dq, off=off: v.tensor_copy(T[dq][:].bitcast(dt.uint32), T[wq][:].bitcast(dt.uint32).indirect(off)),
-                   ["on"] + (["aq%d" % h for h in range(len(HALF))] if ahead else nk), [dq], picked(128), "P")
-                op("s", lambda dz=dz, off=off: s.activation(T[dz][:], T[wz][:].indirect(off), F.Copy),
-                   ["on"] + (["az%d" % h for h in range(len(HALF))] if ahead else nk), [dz], picked(128) + 10, "P")
+                op("v", lambda dq=dq, off=off: v.tensor_copy(T[dq][:].bitcast(dt.uint32), wq.bitcast(dt.uint32).indirect(off)), ["on"] + rq, [dq], picked(128), "P")
+                op("s", lambda dz=dz, off=off: s.activation(T[dz][:], wz.indirect(off), F.Copy), ["on"] + rz, [dz], picked(128) + 10, "P")
                 for b in range(4):
                     mm(VB[b], "e%sq" % e, "e%sz" % e, 128 * b, dq, dz, 0, 128, [dq, dz, "e%s%d" % (e, b)], e == "e", e == "o", "P")
             for b in range(4):
-                cp("v" if b in par["vv"] else "s", T.vt[:, b:512:4], P[VB[b]][:, 0:128], ["p%d" % VB[b]], ["vt%d" % b], 128, 1.0 / 32, "V")
+                cp("sv", T.vt[:, b:512:4], P[VB[b]][:, 0:128], ["p%d" % VB[b]], ["vt%d" % b], 128, 1.0 / 32, "V")
         for h, (c, d) in enumerate(HALF):
-            bs = [b for b in range(4) if not (ahead or par["vp"]) or rd < 3 and any((i, b) not in PAR["za%d" % (rd + 1)] for i in within(rd + 1, c, d))]
-            unpack("th", nq, nz, c, d, [nk[h]], ["th%d" % h, "tr%d" % h], dict(zip(bs, banks(len(bs)))), lambda b: (h, b) in par["uv"], "T%d" % h)
+            bs = [b for b in range(4) if not (ahead or par["vp"]) or rd < 3 and any((i, b) not in PAR["za%d" % (rd + 1)] for i in within(PAR["cut%d" % (rd + 1)], c, d))]
+            unpack("th", nq, nz, c, d, [nk[h]], ["th%d" % h, "tw%d" % h], dict(zip(bs, banks(len(bs)))), "T%d" % h)
         for b in range(0 if par["vp"] else 4):
-            win = sl(src, b).indirect(T.on[:, 0:8])
-            r = ["%s%d%d" % (src, h, b) for h in range(len(HALF))] + ["on"]
-            if b in par["vv"]:
-                ts(T.vt[:, b:512:4], win, 2.0, None, A.mult, None, r, ["vt%d" % b], 1, "V", picked(128))
-            else:
-                act(T.vt[:, b:512:4], win, F.Copy, r, ["vt%d" % b], 1, "V", picked(128), scale=2.0)
+            win = T[src][:, C * b:C * b + C].indirect(T.on[:, 0:8])
+            r = ["%s%d%d" % (src, h, b) for h in range(3)] + ["on"]
+            act(T.vt[:, b:512:4], win, F.Copy, r, ["vt%d" % b], 1, "V", picked(128) + 10, scale=2.0)
+            ts(T.vt[:, b:512:4], win, 2.0, None, A.mult, None, r, ["vt%d" % b], 1, "V", picked(128))
+            either(2)
         vk, uq, uz, sq, sz = ["vt%d" % b for b in range(4)], T["uq%d" % rd], T["uz%d" % rd], T["sq%d" % rd], T["sz%d" % rd]
         if ahead:
             quant("uq%d" % rd, "uz%d" % rd, 0, 128, T.vt[:], vk, ["U%d" % rd, "Uz%d" % rd], "V")
         else:
             quant("sq%d" % rd, "sz%d" % rd, 0, 128, T.vt[:], vk, ["out"], "V")
-            r = ["out"] + (["ef0", "ef1", "ef2"], ["ef3", "wz0"], ["wz1", "vq"])[rd - 1]
-            if rd + 1 == PAR["ahead"]:
-                if PAR["fl"]:
-                    far(STEP[rd - 1] + STEP[rd], [(u8(T.gq[:]), u8(sq[:]))], ["out"], ["gq"], 450.0, "G")
-                    far(STEP[rd - 1] + STEP[rd], [(T.gz[:, 0:128], sz[:, 0:128])], ["out"], ["gz"], 300.0, "G")
-                else:
-                    far(STEP[rd - 1] + STEP[rd], [(u8(T.gq[:]), u8(sq[:])), (T.gz[:], sz[:])], r, ["gq", "gz"], PAR["xf"], "G")
-            if PAR["far"] == "W" and not (PAR["ahead"] and rd == 3):
-                far(STEP[rd - 1], [(u8(uq[:]), u8(sq[:])), (uz[:], sz[:])], r, ["U%d" % rd, "Uz%d" % rd], PAR["xf"], "F")
+            if rd < 3 and rd + 1 != PAR["ahead"]:
+                far(STEP[rd - 1], [(u8(uq[:]), u8(sq[:])), (uz[:], sz[:])], ["out", "ef0", "ef1", "ef2", "ef3", "eh0", "eh1", "eh2", "eh3"], ["U%d" % rd, "Uz%d" % rd], 1024, "F")
+            elif rd + 1 == PAR["ahead"]:
+                far(STEP[rd - 1], [(u8(uq[:]), u8(sq[:])), (uz[:], sz[:])], ["out", "ef0", "ef1", "ef2"], ["U%d" % rd, "Uz%d" % rd], 1024, "F")
+                far(STEP[rd - 1] + STEP[rd], [(u8(T.gq[:]), u8(sq[:]))], ["out"], ["gq"], 512, "G")
+                far(STEP[rd - 1] + STEP[rd], [(T.gz[:], sz[:, 0:128])], ["out"], ["gz"], 128, "G")
             else:
-                far(STEP[rd - 1], [(u8(uq[:]), u8(sq[:]))], ["out"], ["U%d" % rd], 450.0, "F")
-                far(STEP[rd - 1], [(uz[:, 0:128], sz[:, 0:128])], ["out"], ["Uz%d" % rd], 300.0, "G")
-        return nk, kdk
+                far(STEP[rd - 1], [(uz[:, 0:128], sz[:, 0:128])], ["out"], ["Uz%d" % rd], 128, "G")
+                far(STEP[rd - 1], [(u8(uq[:]), u8(sq[:]))], ["out"], ["U%d" % rd], 512, "F")
+        return nk
 
     for rd in (1, 2, 3):
-        nk, kdk = one_round(rd)
+        nk = one_round(rd)
 
     now[0] = "4"
-    mm(SS, "vq", "vz", 0, "xq3", "xz3", 0, C, nk + ["vq"], True, True, "y")
-    cp("s", T.yt[:], P[SS][:, 0:C], ["p%d" % SS], ["yt"], C, None, "y")
-    dma("s", T.y[:], T.yt[:], ["yt"], [], "outs", "y")
-    for h in range(2):
-        src, last = T.kd4[:, h] if by_product[2] else T.kd[:, :, h, :], T.pf[:, 15 + 16 * h:16 + 16 * h]
-        if PAR["os"]:
-            act(T.kf[:, :, h, :], src, F.Identity, kdk + ["pf"], ["kf%d" % h], 1, "o", scale=-1.0, bias=last)
-        else:
-            ts(T.kf[:, :, h, :], src, -1.0, last, A.mult, A.add, kdk + ["pf"], ["kf%d" % h], 1, "o")
-    if PAR["os"]:
-        act(T.npg[:], T.nd[:], F.Copy, ["nd0", "nd1"], ["nop"], 1, "q", bias=-1.0)
+    for h, (c, d) in enumerate(pieces(3)):
+        bank = banks(1)[0]
+        mm(bank, "vq", "vz", 0, "xq3", "xz3", c, d, [nk[h], "vq"], True, True, "y")
+        cp("sv", T.yt[:, c:d], P[bank][:, 0:d - c], ["p%d" % bank], ["yt%d" % h], d - c, None, "y")
+        dma("y", T.y[:, c:d], T.yt[:, c:d], ["yt%d" % h], [], (128, 4 * (d - c)), "outy", "y")
+    cp("v", T.of[:, 0:24], T.ok[:, 0:24], ["ok"], ["of0"], 1, None, "o")
+    if PAR["vp3"]:
+        ts(T.ot[:, 0:16], T.no[:].indirect(T.ordn[:, 0:1]), 512.0, None, A.mult, None, ["no", "ordn"], ["ot"], 1, "o", picked(16))
+        cp("v", T.of[:, 24:32], T.ot[:, 0:8], ["ot"], ["of1"], 1, None, "o")
     else:
-        ts(T.npg[:], T.nd[:], -1.0, None, A.add, None, ["nd0", "nd1"], ["nop"], 1, "q")
-    dma("y", T.oc[:], u8(T.xq3[:]), nk, [], "outy", "o")
+        cp("v", T.of[:, 24:32], T.on[:, 0:8], ["on"], ["of1"], 1, None, "o")
+    turn(T.ot[:], T.of[:], ["of0", "of1"], ["ot"], 1, "o")
+    dma("y", T.oc[:], u8(T.xq3[:]), nk, [], (128, 1536), "outy", "o")
     for k in range(4):
-        dma("y", T.osc[4 * k:4 * k + 4, :], T.xz3[32 * k:32 * k + 4, :], nk, [], "outy", "o")
+        dma("y", T.osc[4 * k:4 * k + 4, :], T.xz3[32 * k:32 * k + 4, :], nk, [], (16, 96), "outy", "o")
     for a in range(4):
         for h in range(2):
-            if by_product[2]:
-                for j in range(3):
-                    dma("y", T.op[2 * a + h, 128 * j:128 * j + 128], T.kf[32 * a + 8 * j:32 * a + 8 * j + 4, :, h, :], ["kf%d" % h], [], "outy", "o")
-            else:
-                dma("y", T.op[2 * a + h, 0:C], T.kf[32 * a:32 * a + 12, :, h, :], ["kf%d" % h], [], "outy", "o")
-            dma("y", T.op[2 * a + h, C:C + 128], T.npg[32 * a + h:32 * a + 8:2, :, 0, :] if PAR["vp3"] else T.npg[32 * a:32 * a + 8:2, :, h, :], ["nop"], [], "outy", "o")
-    dma("s", T.uc[:], u8(T.uq3[:]), ["U3"], [], "outs", "u")
+            dma("y", T.op[2 * a + h, :], T.ot[32 * a:32 * a + 32, 16 * h:16 * h + 16], ["ot"], [], (32, 64), "outy", "o")
+    dma("s", T.uc[:], u8(T.uq3[:]), ["U3"], [], (128, 512), "outs", "u")
     for k in range(4):
-        dma("y" if k % 2 == 0 else "s", T.usc[4 * k:4 * k + 4, :], T.uz3[32 * k:32 * k + 4, 0:128], ["Uz3"], [], "outy" if k % 2 == 0 else "outs", "u")
+        dma("y" if k % 2 == 0 else "s", T.usc[4 * k:4 * k + 4, :], T.uz3[32 * k:32 * k + 4, 0:128], ["Uz3"], [], (16, 32), "outy" if k % 2 == 0 else "outs", "u")
+    return calls
 
-    count, seen, nd = {}, {q: {} for q in queues}, [0]
-    for i in lay_out(calls):
+
+def rank_program(g, core, T, topo):
+    if T.rank_of(core) is None:
+        return
+    queues = {"v": g.vector, "s": g.scalar, "t": g.tensor, "p": g, "y": g.sync}
+    calls = write(g, core, T, topo, lay_out(write(g, core, T, topo, {}))[1])
+    count, seen, nd, moved = {}, {q: {} for q in queues}, [0], []
+    for i in lay_out(calls)[0]:
         c = calls[i]
+        if c["kind"] == "fly":
+            c["tok"], c["know"] = calls[c["f"]]["tok"], calls[c["f"]]["know"]
+            continue
         know = seen[c["q"]]
         need = [calls[j] for j in sorted(c["hard"])]
+        if c["q"] == "p" and len(c["ways"]) > 1:
+            need += moved
+            moved[:] = [c]
+        need = list({d["tok"]: d for d in need}.values())
         for d in need:
             sem, val = d["tok"]
             if know.get(sem, 0) >= val or any(e is not d and e["know"].get(sem, 0) >= val and (e["tok"][0] != sem or e["tok"][1] > val) for e in need):

import math
from concourse.bass import DstId, RemoteDMATransfer
from concourse.mybir import dt, AluOpType as A, ActivationFunctionType as F

N, C, STEP = 4, 384, (1, 2, 3)
BIG = 1e29
HW = 388
AHEAD = 2
NS = {"cyc": 0.83, "g": 1.56, "go": 600.0, "dl": 450.0, "row": 15.0, "byte": 0.015, "dq": 140.0, "rq": 450.0, "fly": 70.0, "rr": 31.0, "rb": 0.05, "first": 1400.0,
      "lat": 183.0, "own": 250.0, "tw": 35.0, "tc": 0.62, "smin": 72.0, "gp": 120.0, "fix": 0.0, "f": 1.03, "slow": 1.42, "gq": 700.0, "gb": 5.0}
PAR = {"fold": False, "turns": 13000, "seed": 1, "pull": {}, "seeds": (1, 1, 1), "swap": 0.15, "pass": 0.7, "kin": 0.8, "mean": 0.2, "only": (0, 1, 2), "two": False, "give": 25.0, "bias": {},
       "hc": (128, 256), "zc": (128, 256), "kc": (128, 256), "qa": 0, "ahead": 2}
PAR.update({"pull": {"k": 0.3, "b": 0.3, "z0": 0.2, "z1": 0.2}, "mean": 0.1, "turns": 9000, "give": 15.0})
PAR["bias"] = {"i": 5000, "K": 5000, "E": 5000, "c": 3000, "f": 5000, "": 5000}
for _h in "123":
    PAR["bias"].update({_k + _h: 1000 for _k in ("ke", "kn", "kt", "k", "K", "U", "D", "y0", "Y0", "y1", "Y1")})
for _h in (1, 2, 3):
    PAR.update({"cut%d" % _h: (256,), "nl%d" % _h: 1 - _h % 2, "sent%d" % _h: (256,), "sv%d" % _h: (), "zd%d" % _h: (),
                "za%d" % _h: ((0, 1), (0, 2), (0, 3), (1, 1), (1, 2), (1, 3)), "vp%d" % _h: 0})
PAR.update({"za1": tuple((_h, _b) for _h in range(2) for _b in range(4)), "seeds": ((11, 6, 3), (4, 3, 5), (2, 1, 4)), "keep": 0.3, "nl3": 1, "nl1": 1, "turns": 8000,
            "only": (0, 1, 2), "whole": 0, "warm": 0.3, "za3": ((0, 1), (0, 2), (0, 3), (1, 0), (1, 1), (1, 2), (1, 3)), "wide": 0.9, "spare": 1e9, "hf": True, "both": 0.8, "line": 0.85, "swap": 0.12, "pass": 0.5, "kin": 0.56, "q4": True, "sv1": (128, 256)})


def _sb(n, d):
    return ("sbuf", [128] + (n if isinstance(n, list) else [n]), d)


CODE, PL, BF, F16, F32, U16, I32 = "float8_e4m3fn_x4", "uint8", "bfloat16", "float16", "float32", "uint16", "int32"
SCRATCH = {
    "xin": _sb(4 * C, BF), "uin": _sb(512, BF), "vin": _sb(512, BF), "wq": _sb(512, CODE), "wz": _sb(512, PL), "vq": _sb(128, CODE),
    "c32": _sb(260, BF), "tb": _sb(224, F32), "pf": _sb(224, F32), "num": _sb(C, F32), "zero": _sb(HW, BF),
    "ef": _sb(1040, BF), "efq": _sb(512, CODE), "ehq": _sb(512, CODE), "ehz": _sb(512, PL), "za": _sb(4 * C, BF), "zb": _sb(4 * C, BF),
    "ee": _sb(520, BF), "eeq": _sb(512, CODE), "eez": _sb(512, PL), "eo": _sb(520, BF), "eoq": _sb(512, CODE), "eoz": _sb(512, PL),
    "cap": _sb(128, F32), "ex": _sb(C, F32), "nr": _sb(C, BF), "tr": _sb([8, 128], BF), "kd": _sb([2, 2, 16], BF), "ko": _sb(64, BF),
    "ordk": _sb(2, U16), "ordn": _sb(4, U16), "ok": _sb(32, U16), "on": _sb(16, U16), "of": _sb(32, F32), "ot": _sb(32, F32),
    "hf": _sb(192, F32), "fo": _sb(C, F32), "hist": _sb(9 * HW, F32), "sl": _sb(5 * C, F16), "mk": _sb(5 * C, F16), "zs": _sb(5 * C, F16), "zp": _sb(4 * C + 8, F16), "kh": _sb(9 * HW, F16),
    "qi": _sb(8, I32), "qa": _sb(8, F32), "qj": _sb(40, F32), "qs": _sb(40, F32), "nb": _sb([4, 8], F32), "nd": _sb([2, 2, 16], F32), "no": _sb(64, F32),
    "th": _sb(4 * C, BF), "tf": _sb(4 * C, BF), "du": _sb(512, BF),
    "zt": _sb(4 * C, BF), "xt": _sb(4 * C, BF), "vt": _sb(512, BF), "yt": _sb(C, F32),
    "xq0": _sb(512, CODE), "xz0": _sb(512, PL), "hq": _sb(C, CODE), "hz": _sb(512, PL), "gq": _sb(128, CODE), "gz": _sb(128, PL), "aq": _sb(C, CODE), "bz": _sb(512, PL),
    "zq": _sb(C, CODE), "zz": _sb(C, PL)}
for _h in (1, 2, 3):
    SCRATCH.update({"xq%d" % _h: _sb(C, CODE), "xz%d" % _h: _sb(512 if _h < 3 else C, PL), "uq%d" % _h: _sb(128, CODE), "uz%d" % _h: _sb(512, PL),
                    "veq%d" % _h: _sb(128, CODE), "vez%d" % _h: _sb(128, PL), "voq%d" % _h: _sb(128, CODE), "voz%d" % _h: _sb(128, PL),
                    "sq%d" % _h: _sb(128, CODE), "sz%d" % _h: _sb(512, PL)})
SCRATCH["az"] = _sb(C, PL)
for _b in range(8):
    SCRATCH["p%d" % _b] = ("psum", [128, 512], F32)

SEMAPHORES = ["cv", "cs", "ct", "cp", "sent", "outy", "outs"] + ["d%d" % i for i in range(20)] + ["f%d" % i for i in range(14)]
KEPT = {}


def link(calls):
    lastw, readers, lastp, wide, narrow, first = {}, {}, {}, [], [], []
    for i, c in enumerate(calls):
        hard, soft, war = set(), set(), set()
        for k in c["r"]:
            if k in lastw:
                hard.add(lastw[k])
        for k in c["w"]:
            if k in lastw:
                (war if c["q"] == "t" and calls[lastw[k]]["q"] == "t" else hard).add(lastw[k])
            for j in readers.get(k, ()):
                hard.add(j)
        sure = set(hard)
        for j in war:
            (soft if calls[j]["q"] == c["q"] else hard).add(j)
        for k in c["r"] + c["w"]:
            if k[0] == "p" and k[1:].isdigit():
                q, ahead, mine = lastp.get(k, (c["q"], [], []))
                if q != c["q"]:
                    ahead, mine = mine, []
                hard.update(ahead)
                lastp[k] = (c["q"], ahead, mine + [i])
        if "p" in c["ways"] and c["kind"] == "op":
            if c["tag"][:1] in ("K", "m"):
                hard.update(wide)
                sure.update(wide)
                narrow.append(i)
            else:
                hard.update(narrow)
                sure.update(narrow)
                wide.append(i)
        if c["kind"] == "far":
            soft.update(first)
            war.update(first)
            first[:] = first or [i]
        for k in c["w"]:
            lastw[k], readers[k] = i, []
        for k in c["r"]:
            readers.setdefault(k, []).append(i)
        c["needs"], c["war"] = (hard, soft - hard), war - sure


def gap(d, c, soft, same):
    if soft:
        return 0.0
    return (NS["own"] if same and not d["late"] else NS["lat"] + d["late"]) + (NS["tw"] if "t" in (c["q"], d["q"]) else 0.0)


def tie(calls, after):
    for c in calls:
        c["pre"], c["next"] = {}, {}
    for i, c in enumerate(calls):
        hard, soft = c["needs"]
        more = after.get(i, [])
        c["hard"] = hard | {j for j in more if calls[j]["q"] != "t"}
        for j in c["hard"] | soft | set(more):
            d = calls[j]
            c["pre"][j] = d["next"][i] = gap(d, c, j not in c["hard"], c["q"] == d["q"])


def place(net, rank, queue, lo, hi, base):
    ways, tail, pre, nxt, opens, uses, mine = net
    start, end, todo, holder, free = [list(x) for x in base[:5]]
    lines, bank, after = {q: (list(a), list(e)) for q, (a, e) in base[5].items()}, dict(base[6]), dict(base[7])
    left = dict(base[8])
    ready = sorted([i for i in left if not left[i]], key=lambda j: -rank[j])
    last = 0.0
    for _ in range(lo, hi):
        k = len(ready) - 1
        while k >= 0 and opens[ready[k]] is not None and min([todo[r] for r in holder]):
            k -= 1
        if k < 0:
            return None
        i = ready.pop(k)
        q = queue[i]
        at, d = 0.0, ways[i][q]
        for j, same, other in pre[i]:
            e = end[j] + (same if queue[j] == q else other)
            if e > at:
                at = e
        if opens[i] is not None:
            b = min([b for b in range(8) if not todo[holder[b]]], key=lambda b: free[b])
            at = max(at, free[b])
            after[i] = uses[holder[b]]
            holder[b], bank[opens[i]] = opens[i], b
        a, e = lines[q]
        k = len(a)
        while k and e[k - 1] > at:
            k -= 1
        while k < len(a) and a[k] < at + d:
            at = e[k]
            k += 1
        a.insert(k, at)
        start[i] = at
        at += d
        e.insert(k, at)
        end[i] = at
        if at + tail[i] > last:
            last = at + tail[i]
        for r in mine[i]:
            todo[r] -= 1
            free[bank[r]] = max(free[bank[r]], at + NS["lat"] + NS["tw"])
        for j in nxt[i]:
            left[j] -= 1
            if not left[j]:
                k = len(ready)
                while k and rank[ready[k - 1]] < rank[j]:
                    k -= 1
                ready.insert(k, j)
    at = over = 0.0
    for e, i in sorted([(end[i - 1] + pre[i][-1][2], i) for i in base[10]]):
        at = max(at, e) + ways[i]["e"]
        over = max(over, at - end[i])
    slow, busy, far = list(base[11]), dict(base[12]), 0.0
    more, rest = base[13:]
    for i in sorted(range(lo, hi), key=lambda i: start[i]):
        q = queue[i]
        at = busy[q]
        for j, same, other in pre[i]:
            e = slow[j] + (same if queue[j] == q else other) + 25.0
            if e > at:
                at = e
        for j in after.get(i, ()):
            if slow[j] + 240.0 > at and queue[j] != q:
                at = slow[j] + 240.0
        slow[i] = busy[q] = at = at + ways[i][q] * more[i]
        if at + rest[i] > far:
            far = at + rest[i]
    return (last + over + PAR["both"] * far) / (1.0 + PAR["both"]), (start, end, todo, holder, free, lines, bank, after, slow, busy), queue, PAR["mean"] * sum(end[lo:hi]) / (hi - lo) + sum([w * end[i] for i, w in base[9]])


def holdups(net, got, lo, hi):
    tail, pre = net[1:3]
    start, end, after, queue = got[1][0], got[1][1], got[1][7], got[2]
    ends = {(queue[i], end[i]): i for i in range(lo, hi)}
    i, out = max(range(lo, hi), key=lambda i: end[i] + tail[i]), []
    while i >= lo and start[i] > 0.0:
        by = [j for j, same, other in pre[i] if end[j] + (same if queue[j] == queue[i] else other) > start[i] - 1e-3]
        if by:
            i = by[0]
            continue
        j = ends.get((queue[i], start[i]))
        if j is None:
            j = max(after.get(i) or [-1], key=lambda j: end[j])
        if j >= lo:
            out.append((i, j))
        i = j
    return out or [(lo, lo)]


def lay_out(calls):
    link(calls)
    if "order" not in KEPT:
        n = len(calls)
        tie(calls, {})
        way, uses, mine, opens = [0.0] * n, [[] for _ in range(161)], [[] for _ in range(n)], [None] * n
        for i, c in enumerate(calls):
            for r in sorted({int(k[1:]) for k in c["r"] + c["w"] if k[0] == "p" and k[1:].isdigit()}):
                if not uses[r]:
                    opens[i] = r
                uses[r].append(i)
                mine[i].append(r)
        for i in range(n - 1, -1, -1):
            c = calls[i]
            way[i] = c["ns"] + max([c["late"]] + [way[j] + gap for j, gap in c["next"].items()])
        pre = [[(j, gap(calls[j], c, j in c["war"], True), gap(calls[j], c, False, False)) for j in sorted(c["pre"])] for c in calls]
        ways, queue = [{q: e[1] for q, e in c["ways"].items()} for c in calls], [c["q"] for c in calls]
        state = ([0.0] * n, [0.0] * n, [len(u) for u in uses], [160] * 8, [0.0] * 8, {q: ([], []) for q in "vstpye"}, {}, {}, [0.0] * n, {q: 0.0 for q in "vstpye"})
        more, long = [NS["slow"] if c["kind"] == "op" and c["q"] != "t" else 1.0 for c in calls], [0.0] * n
        for i in range(n - 1, -1, -1):
            c = calls[i]
            long[i] = c["ns"] * more[i] + max([c["late"]] + [long[j] + gap + 25.0 for j, gap in c["next"].items()])
        cuts = [0] + [min(i for i, c in enumerate(calls) if c["tag"][-1:] == e) for e in "23"] + [n]
        seed = [PAR["seed"]]

        def draw():
            seed[0] = (seed[0] * 6364136223846793005 + 1442695040888963407) % 2 ** 64
            return (seed[0] >> 11) / 2.0 ** 53
        empty = state
        for stage, (lo, hi) in enumerate(list(zip(cuts[:-1], cuts[1:])) + [(0, n)] * (3 in PAR["only"])):
            before, state = state[0], empty if stage == 3 else state
            tail = [max([c["late"]] + [way[j] + gap for j, gap in c["next"].items() if j >= hi]) for c in calls]
            net = (ways, tail, pre, [[j for j in c["next"] if j < hi] for c in calls], opens, uses, mine)
            base = state[:8] + ({i: len([j for j in calls[i]["pre"] if j >= lo]) for i in range(lo, hi)},
                            list({calls[i]["tag"]: (i, PAR["pull"][calls[i]["tag"][:-1]]) for i in range(lo, hi) if calls[i]["tag"][:-1] in PAR["pull"]}.values()),
                            [i for i in range(lo, hi) if queue[i] == "e"], state[8], state[9], more,
                            [max([c["late"]] + [long[j] + gap + 25.0 for j, gap in c["next"].items() if j >= hi]) for c in calls])
            rank = [-way[i] - PAR["bias"].get(calls[i]["tag"], 0.0) for i in range(n)] if stage < 3 else before
            best = now = place(net, rank, queue, lo, hi, base)
            loose, held = [i for i in range(lo, hi) if len(ways[i]) > 1], holdups(net, now, lo, hi)
            kin = {}
            for i in range(lo, hi):
                kin.setdefault(calls[i]["tag"], []).append(i)
            seeds, fresh, won = PAR["seeds"][stage % 3], now, 0
            turns = PAR["turns"] if stage < 3 else PAR["whole"]
            for turn in range(turns * len(seeds) if stage in PAR["only"] else 0):
                if turn % turns == 0:
                    seed[0], now = seeds[turn // turns], fresh
                    held = holdups(net, now, lo, hi)
                x, rank, queue = [draw() for _ in range(6)], list(now[1][0]), now[2]
                i, j = held[int(x[1] * len(held))]
                one = (i, j)[x[2] < 0.5]
                if x[0] < PAR["swap"]:
                    i = one if len(ways[one]) > 1 else loose[int(x[3] * len(loose))]
                    others = [q for q in ways[i] if q != queue[i]]
                    queue = queue[:i] + [others[int(x[4] * len(others))]] + queue[i + 1:]
                elif x[0] < PAR["pass"]:
                    if x[2] < 0.5:
                        rank[i] = rank[j] - 1.0 - 600.0 * x[3] ** 3
                    else:
                        rank[j] = rank[i] + 1.0 + 600.0 * x[3] ** 3
                elif x[0] < PAR["kin"]:
                    for k in kin[calls[one if x[3] < 0.5 else lo + int(x[1] * (hi - lo))]["tag"]]:
                        rank[k] += 1200.0 * (x[4] - 0.5)
                elif x[0] < PAR["line"]:
                    k = one if x[3] < 0.6 else lo + int(x[1] * (hi - lo))
                    todo, seen, at, by = [k], {k}, rank[k], (50.0 + 900.0 * x[4] ** 2) * (1.0 if x[2] < 0.5 else -1.0)
                    while todo:
                        k = todo.pop()
                        for e in (net[3][k] if by > 0.0 else [e[0] for e in pre[k]]):
                            if e >= lo and e not in seen and abs(rank[e] - at) < 2500.0 * x[3] + 300.0:
                                seen.add(e)
                                todo.append(e)
                    for k in seen:
                        rank[k] += by
                else:
                    at = rank[i] if x[2] < 0.5 else rank[lo + int(x[1] * (hi - lo))]
                    for k in range(lo, hi):
                        if abs(rank[k] - at) < 200.0 + 1500.0 * x[3]:
                            rank[k] += (draw() - 0.5) * (150.0 + 1300.0 * x[4])
                got = place(net, rank, queue, lo, hi, base)
                rest = 1.0 - (turn % turns) / turns
                rest *= PAR["warm"] if stage == 3 else 1.0
                w = PAR["keep"] + (1.0 - PAR["keep"]) * rest
                if got and got[0] + w * (got[3] - now[3]) <= now[0] - PAR["give"] * rest * math.log(1.0 - x[5]):
                    now = got
                    held = holdups(net, now, lo, hi)
                    if now[0] + 0.1 * now[3] < best[0] + 0.1 * best[3]:
                        best, won = now, turn // turns
            KEPT.setdefault("won", []).append((seeds[won], int(best[0])))
            state, queue = best[1], best[2]
            KEPT.setdefault("ends", []).append(int(max(state[1][i] + tail[i] for i in range(lo, hi))))
        KEPT.update({"order": sorted(range(n), key=lambda i: (state[0][i], i)), "starts": state[0], "end": best[0], "dealt": (state[6], state[7], queue)})
    for c, q in zip(calls, KEPT["dealt"][2]):
        c["q"] = q
        c["f"], c["ns"] = c["ways"][q]
    link(calls)
    tie(calls, KEPT["dealt"][1])
    return KEPT["order"], KEPT["dealt"][0]


def write(g, core, T, topo, bank_of):
    rank = T.rank_of(core)
    queues = {"s": g.scalar, "y": g.sync}
    calls, now, nfar = [], [""], [0]
    v, s, t = g.vector, g.scalar, g.tensor
    P = [T["p%d" % bank_of.get(r, 0)] for r in range(160)]

    def op(qn, f, r, w, n, tag="", late=0.0, kind="op", sem=None):
        if kind == "op" and qn in "sp":
            n = max(n, NS["smin"]) if qn == "s" else n + NS["gp"]
        n = n * (NS["f"] if kind == "op" else 1.0) + NS["fix"]
        calls.append({"q": qn, "f": f, "r": list(r), "w": list(w), "ns": n, "tag": tag + now[0], "late": late, "kind": kind, "sem": sem, "ways": {qn: (f, n)}})

    def either(k):
        ways = {c["q"]: (c["f"], c["ns"]) for c in calls[-k:]}
        calls[-k:] = calls[-k:len(calls) - k + 1]
        calls[-1]["ways"] = ways

    def plane(z, a, b):
        if z == "vz":
            return T.xz2[:, 0:128]
        if z == "xz2" or z == "az" and a >= 256:
            return T["xz2" if z == "xz2" else "bz"][:, 128 + a:128 + b]
        if z == "efz":
            return T.sz1[:, 128 + a:128 + b] if a < C else T.sz2[:, 128:256]
        if z == "ehz" and a != 128:
            return T.sz2[:, a:b] if a else T.xz1[:, C:512]
        return T[z][:, a:b]

    def cy(n):
        return max(64.0, n) * NS["cyc"]

    def dma(qn, out, in_, r, w, size, sem=None, tag=""):
        op(qn, lambda: queues[qn].dma_start(out, in_), r, w, NS["dq"], tag, NS["go"], "dma", sem)
        under_way(r, w, NS["row"] * size[0] / 16 + NS["byte"] * size[0] * size[1] / 16, NS["dl"])

    def under_way(r, w, n, late):
        calls[-1]["w"].append("#%d" % len(calls))
        op("e", len(calls) - 1, list(r) + ["#%d" % len(calls)], w, n, "e", late, "fly")

    def mm(bank, lq, lz, a, rq, rz, c, d, keys, start, stop, tag=""):
        op("t", lambda: t.matmul_mx(P[bank][:, 0:d - c], T[lq][:, a:a + 128], plane(lz, a, a + 128), T[rq][:, c:d], plane(rz, c, d), start, stop),
           keys, ["p%d" % bank], (d - c + 16) * NS["tc"], tag)

    def cp(qn, out, in_, r, w, n, scale=None, tag=""):
        if len(qn) > 1:
            for q in qn:
                cp(q, out, in_, r, w, n, scale, tag)
            either(len(qn))
        elif qn == "p":
            op("p", lambda: g.affine_select(out, in_, [[0, n]], A.is_ge, 0.0, 0, 0), r, w, 170 + NS["own"] + 2 * NS["cyc"] * n, tag)
        elif qn == "s":
            op("s", lambda: s.activation(out, in_, F.Copy, scale=1.0 if scale is None else scale), r, w, cy(n), tag)
        elif scale is None:
            op("v", lambda: v.tensor_copy(out, in_), r, w, cy(n), tag)
        else:
            op("v", lambda: v.tensor_scalar(out, in_, scale, None, A.mult), r, w, cy(n), tag)

    def ts(out, in_, s1, s2, o1, o2, r, w, n=1, tag="", ns=None):
        if o2 is None:
            op("v", lambda: v.tensor_scalar(out, in_, s1, None, o1), r, w, ns or cy(n), tag)
        else:
            op("v", lambda: v.tensor_scalar(out, in_, s1, s2, o1, o2), r, w, ns or cy(n), tag)

    def tt(out, in0, in1, o, r, w, ns, tag):
        op("v", lambda: v.tensor_tensor(out, in0, in1, o), r, w, ns, tag)

    def fill(ap, c, w, n=1, r=()):
        op("v", lambda: v.memset(ap, c), r, w, cy(n), "f")

    def quant(q, z, a, b, src, r, w, tag=""):
        op("v", lambda: v.quantize_mx(T[q][:, a:b], plane(z, a, b), src), r, w, 12 + 0.88 * (b - a), tag)

    def scan(out, d0, d1, first, o0, o1, r, w, n, tag=""):
        op("v", lambda: v.tensor_tensor_scan(out, d0, d1, first, o0, o1), r, w, cy(n), tag)

    def turn(out, in_, r, w, n=1, tag=""):
        op("v", lambda: v.transpose(out, in_), r, w, cy(n), tag)

    def act(out, in_, f, r, w, n, tag="", ns=None, **k):
        op("s", lambda: s.activation(out, in_, f, **k), r, w, ns or cy(n) + (20 if "accum_out" in k else 0), tag)

    def picked(n):
        return 55 + NS["g"] * NS["cyc"] * n

    def far(step, pairs, r, w, width, tag):
        dst = T.cores[(rank + step) % N]
        rid, pid, _ = topo.addr(dst)
        eng = topo.engines(core, dst)
        sem, k = "f%d" % nfar[0], len(eng) // len(pairs)

        def f():
            if len(pairs) == 1:
                g.remote_dma(pairs[0][0], pairs[0][1], T.sem[sem], T.sem["sent"], pid, rid, sum(1 << e for e in eng))
            else:
                g.remote_dma_fused([RemoteDMATransfer(dst_ids=[DstId(rid=rid, pnc=pid)], dma_engine_mask=sum(1 << e for e in eng[k * i:k * i + k]),
                                                      remote_sem=T.sem[sem], src=b, dst=a) for i, (a, b) in enumerate(pairs)], local_sem=T.sem["sent"])
            return len(eng)
        op("p", f, r, w, NS["rq"] + (0.0 if nfar[0] else NS["first"]), tag, NS["fly"], "far", sem)
        under_way(r, w, 8 * (NS["rr"] * len(pairs) + NS["rb"] * width), 1.0)
        nfar[0] += 1

    def u8(ap):
        return ap.bitcast(dt.uint8)

    def spans(cuts, a=0, b=C):
        e = [a] + [c for c in cuts if a < c < b] + [b]
        return list(zip(e[:-1], e[1:]))

    dma("y", T.uin[:], T.u[:], [], ["uin"], (128, 1024), None, "L")
    dma("s", T.xin[:, 0:512], T.x[:, 0:512], [], ["xin0"], (128, 1024), None, "L")
    dma("y", T.xin[:, 512:1024], T.x[:, 512:1024], [], ["xin1"], (128, 1024), None, "L")
    dma("s", T.xin[:, 1024:1536], T.x[:, 1024:1536], [], ["xin2"], (128, 1024), None, "L")
    first = ["uin", "xin0", "xin1", "xin2"]
    dma("y", u8(T.wq[:]), T.wc[:], first, ["wq"], (128, 2048))
    dma("y", T.wz[:], T.ws[:], first, ["wz"], (128, 512))
    dma("y", T.vin[:], T.v[:], first, ["vin"], (128, 1024))

    picks = any(PAR["vp%d" % h] for h in (1, 2, 3))
    for e, a, c in (("ef", 0, 32.0), ("eh", 520, 0.5)):
        fill(T.ef[:, a:a + 520], 0.0, [e], 260)
        fill(T.c32[:, a // 4:a // 4 + 128], c, ["c" + e], 64)
        op("p", lambda a=a: g.affine_select(T.ef[:, a + 3:a + 515:4], T.c32[:, a // 4:a // 4 + 128], [[-1, 128]], A.is_equal, 0.0, 0, 1), ["c" + e, e], [e], 385)

    def count_up(out, pattern, base, step, w, n, tag="i"):
        op("p", lambda: g.iota(out, pattern, base, step, allow_small_or_imprecise_dtypes=True), [], w, 130 + 2 * NS["cyc"] * n, tag)

    def const(out, c, w, n):
        act(out, T.zero[:, 0:n], F.Copy, ["zero"], w, n, "c", scale=0.0, bias=c)
    fill(T.zero[:], 0.0, ["zero"], HW / 2)
    count_up(T.tb[:, 0:32], [[16, 2], [0, 16]], 15, 1, ["tb0"], 32)
    if picks:
        count_up(T.tb[:, 128:192], [[1, 2], [-1, 2], [0, 16]], 0, 0, ["tb4"], 64)
    for G in range(4):
        hi, lo, q = G // 2, G % 2, slice(32 * G, 32 * G + 32)
        other = (G + 2) % 4 - G
        count_up(T.tb[q, 32:40], [[12 - 24 * hi, 2], [other * (1 - 2 * lo), 2], [32, 2]], G + 12 * hi + other * lo, 8, ["tk%d" % G], 8, "K")
    count_up(T.num[:], [[1, C]], 0, 0, ["num"], C)
    for G in range(4):
        hi, lo, q = G // 2, G % 2, slice(32 * G, 32 * G + 32)
        count_up(T.tb[q, 64:72], [[16 - 32 * hi, 2], [8 - 16 * lo, 2], [32, 2]], 10 * G, 0, ["tn%d" % G], 8, "K")
    tk, tn = ["tk%d" % G for G in range(4)], ["tn%d" % G for G in range(4)]
    for i in range(1, 4):
        act(T.tb[:, 32 + 8 * i:40 + 8 * i], T.tb[:, 32:40], F.Copy, tk, ["tk%d" % (3 + i)], 1, "i", bias=4.0 * (i % 2))
        act(T.tb[:, 64 + 8 * i:72 + 8 * i], T.tb[:, 64:72], F.Copy, tn, ["tn%d" % (3 + i)], 1, "j", bias=1.0 * (i // 2))
    turn(T.pf[:, 0:64], T.tb[:, 0:64], ["tb0", "tk4", "tk5", "tk6"], ["pf"], 64, "i")
    turn(T.pf[:, 64:96], T.tb[:, 64:96], ["tn4", "tn5", "tn6"], ["pn"], 32, "j")
    cp("v", T.ordk[:, 0:2], T.pf[:, 32:34], ["pf"], ["ordk0"], 1, None, "i")
    cp("v", T.ordn[:, 0:1], T.pf[:, 64:65], ["pn"], ["ordn"], 1, None, "j")
    if picks:
        for i in range(2):
            cp("s", T.tb[:, 96 + 16 * i:104 + 16 * i], T.tb[:, 64:72], tn, ["tp%d" % i], 1, None, "i")
            cp("s", T.tb[:, 104 + 16 * i:112 + 16 * i], T.tb[:, 80:88], ["tn5"], ["tp%d" % (2 + i)], 1, None, "i")
        turn(T.pf[:, 96:192], T.tb[:, 96:192], ["tb4"] + ["tp%d" % i for i in range(4)], ["pg"], 96, "i")
        cp("v", T.ordn[:, 2:3], T.pf[:, 96:97], ["pg"], ["ordp"], 1, None, "i")
        act(T.tb[:, 192:193], T.pf[:, 128:129], F.Abs, ["pg"], ["odd"], 1, "i")
        for e, keep, k in (("ee", T.pf[:, 160:161], "pg"), ("eo", T.tb[:, 192:193], "odd")):
            act(T[e][:], T.ef[:, 0:520], F.Copy, ["ef", k], [e], 520, "E", scale=keep)
            for b in range(4):
                quant(e + "q", e + "z", 128 * b, 128 * b + 128, T[e][:, 3 - b:515 - b], [e], [e + str(b)], "E")
    for b in range(4):
        quant("efq", "efz", 128 * b, 128 * b + 128, T.ef[:, 3 - b:515 - b], ["ef"], ["ef%d" % b], "E")
    halves = sorted({b for h in (1, 2, 3) for _, b in PAR["za%d" % h]})
    for b in halves:
        quant("ehq", "ehz", 128 * b, 128 * b + 128, T.ef[:, 523 - b:1035 - b], ["eh"], ["eh%d" % b], "E")
    quant("xq0", "xz0", C, C + 128, T.uin[:], ["uin"], ["U0"], "L")
    for i in range(3):
        quant("xq0", "xz0", 128 * i, 128 * i + 128, T.xin[:, 512 * i:512 * i + 512], ["xin%d" % i], ["X0%d" % i], "L")
    quant("vq", "vz", 0, 128, T.vin[:], ["vin"], ["vq"], "j")
    const(T.cap[:], BIG, ["cap"], 128)
    fill(T.cap[:, 0:128:16], -BIG, ["cap"])
    fill(T.ex[:, 0:C:128], -BIG, ["exz"])
    fill(T.tr[:, 3:8, 15:128:16], 0.0, ["tr%d%d" % (G, i) for G in range(4) for i in (2, 3)] + ["trz"])
    fill(T.nb[:], 0.0, ["nb%d%d%s" % (G, x, e) for G in range(4) for x in range(4) for e in "a67"])
    half = C // 2 if PAR["fold"] else 0
    const(T.hist[:, 0:HW], BIG, ["h0"], HW)
    fill(T.hist[:, HW:5 * HW:HW], -BIG, ["hsa"])
    fill(T.hist[:, 5 * HW + half:9 * HW:HW], -BIG, ["hsb"])
    const(T.kh[:, 0:HW], -8.0, ["k0"], HW)
    fill(T.kh[:, HW:9 * HW:HW], 8.0, ["ksa"])
    if PAR["q4"]:
        fill(T.qj[:, 4:40:5], 0.0, ["qj4"])
    wide = max(d - c for c, d in spans(PAR["zc"]))
    two = PAR["two"]
    wd = 4 if two else 5
    for j in range(wd):
        const(T.mk[:, j:wd * wide:wd], float(min(j, 1)), ["mk%d" % j], wide)
    cp("s", T.sl[:, wd - 1:wd * C:wd], T.num[:], ["num"], ["sl4"], C, 1.0 / 512, "c")
    results = [0]

    def banks(n):
        results[0] += n
        return list(range(results[0] - n, results[0]))

    def hv(k):
        return T.hist[:, HW * (k + 1) + C:HW * (k + 1) + C + 1]

    def pieces(rd):
        return spans(PAR["cut%d" % rd])

    def within(cuts, c, d):
        return [h for h, (a, b) in enumerate(spans(cuts)) if a < d and c < b]

    def unpack(dst, q, z, c, d, r, w, bs, tag):
        for b in bs:
            mm(bs[b], "efq", "efz", 128 * b, q, z, c, d, r + ["ef%d" % b], True, True, tag)
            cp("sv", T[dst][:, C * b + c:C * b + d], P[bs[b]][:, 0:d - c], ["p%d" % bs[b]], [k + str(b) for k in w], d - c, 1.0 / 64, tag)

    def histories(H, name, data, key, cuts, lo, first, o0, o1, per, tag):
        for k in range(1, 9):
            for c, d in spans(cuts, lo(k)):
                at, up = HW * k, HW * (k - 1)
                r = key(c, d) + [name + "sa", name + "sb"] + ([name + "0"] if k == 1 else ["%s%d_%d" % (name, k - 1, a) for a, b in spans(cuts, lo(k - 1)) if a < d - 1 and c - 1 < b])
                if c > lo(k):
                    r.append("%s%d_%d" % (name, k, [a for a, b in spans(cuts, lo(k)) if b == c][0]))
                scan(H[:, at + c + 1:at + d + 1], data(c, d), H[:, up + c:up + d], first if c == lo(k) else H[:, at + c:at + c + 1], o0, o1,
                     r, ["%s%d_%d" % (name, k, c)], (d - c) * per, tag + str(k))
        return ["%s%d_%d" % (name, k, spans(cuts, lo(k))[-1][0]) for k in range(1, 9)]

    def one_round(rd):
        now[0] = str(rd)
        par = {k[:-1]: x for k, x in PAR.items() if k[-1] == str(rd)}
        par.update({k: PAR[k] for k in ("hc", "zc", "kc")})
        xq, xz, nq, nz = "xq%d" % (rd - 1), "xz%d" % (rd - 1), "xq%d" % rd, "xz%d" % rd
        uq, uz, ua = ("uq%d" % (rd - 1), "uz%d" % (rd - 1), 0) if rd > 1 else (xq, xz, C)
        HALF = pieces(rd)
        uk, nk = ["U%d" % (rd - 1), "Uz%d" % (rd - 1)], ["X%d%d" % (rd, h) for h in range(len(HALF))]
        xk = ["X%d%d" % (rd - 1, h) for h in range(3 if rd == 1 else len(pieces(rd - 1)))]
        ahead = rd == PAR["ahead"]
        parts = spans(par["sv"]) + [(0, C)]
        SP = banks(len(parts))
        SV, SS = SP[0], SP[-1]
        for b, (c, d) in zip(SP, parts):
            if ahead:
                mm(b, "gq", "gz", 0, "hq", "hz", c, d, ["gq", "gz", "hz"] + ["hq0", "hq1", "hq2"], True, True, "S")
            else:
                mm(b, uq, uz, ua, xq, xz, c, d, uk + (xk if rd > 1 else xk[c // 128:(d + 127) // 128]), True, True, "S")

        def scores(c, d):
            i = within(par["sv"], c, d)[0]
            return P[SP[i]][:, c - parts[i][0]:d - parts[i][0]]
        SB = banks(3)
        for j in range(3):
            mm(SB[j], xq, xz, 128 * j, uq, uz, ua, ua + 128, uk + (xk if rd > 1 else xk[j:j + 1]), True, True, "U")
        for j in range(3):
            nr = T.nr[:, 128 * j:128 * j + 128]
            scan(T.ex[:, 128 * j + 1:128 * j + 128], P[SB[j]][:, 0:127], T.cap[:, 1:128], -BIG, A.max, A.min, ["p%d" % SB[j], "cap"], ["ex%d" % j], 128, "ke")
            tt(nr, P[SB[j]][:, 0:128], T.ex[:, 128 * j:128 * j + 128], A.is_le, ["p%d" % SB[j], "ex%d" % j, "exz"], ["nr%d" % j], cy(128), "kn")
            scan(T.tr[:, j, :], nr, nr, 0.0, A.mult, A.add, ["nr%d" % j], ["tq%d" % j], 64, "kt")
        tq = ["tq0", "tq1", "tq2"]
        for i in range(2):
            a, b = 64 * i, 64 - 64 * i
            cp("svp", T.tr[b:b + 64, 3:6, b + 15:b + 64:16], T.tr[a:a + 64, 0:3, b + 15:b + 64:16], tq + ["tr%d1" % G for G in (2 * i, 2 * i + 1)],
               ["tr%d2" % G for G in (2 - 2 * i, 3 - 2 * i)], 12, None, "K")
        for a in range(4):
            G = a + 1 - 2 * (a % 2)
            e = 32 * ((G + 2) % 4)
            cp("svp", T.tr[32 * G:32 * G + 32, 0:6, e + 15:e + 32:16], T.tr[32 * a:32 * a + 32, 0:6, 32 * G + 15:32 * G + 32:16], tq + ["tr%d2" % a],
               ["tr%d1" % G, "tr%d3" % G], 12, None, "K")
        for h in range(2):
            turn(T.kd[:, :, h, :], T.tr[:, :, 15 + 16 * h:128:32], tq + ["trz"] + ["tr%d%d" % (G, i) for G in range(4) for i in (1, 2, 3)], ["kd%d" % h], 1, "k")
        turn(T.ko[:], T.kd[:], ["kd0", "kd1"], ["ko"], 1, "k")
        ts(T.ok[:], T.ko[:].indirect(T.ordk[:, 0:2]), -1.0, T.pf[:, 0:1], A.mult, A.add, ["ko", "pf", "ordk0", "ordk1"], ["ok"], 1, "k", picked(32))
        for b, bank in enumerate(banks(4)):
            mm(bank, "efq", "efz", 128 * b, uq, uz, ua, ua + 128, uk + ["ef%d" % b], True, True, "D")
            cp("sv", T.du[:, 128 * b:128 * b + 128], P[bank][:, 0:128], ["p%d" % bank], ["du%d" % b], 128, 1.0 / 64, "D")
        if rd == 1:
            for b in range(4):
                hs = [h for h in range(len(HALF)) if (h, b) not in par["za"]]
                if hs:
                    unpack("th", xq, xz, HALF[hs[0]][0], HALF[hs[-1]][1], xk, ["th%d" % h for h in hs], {b: banks(1)[0]}, "T")
        if half:
            cp("s", T.hf[:], P[SS][:, half:C], ["p%d" % SS], ["hf"], half, None, "M")
            for i, o in enumerate((A.min, A.max)):
                tt(T.fo[:, half * i:half * i + half], P[SV][:, 0:half], T.hf[:], o, ["p%d" % SV, "hf"], ["fo%d" % i], cy(half), "M")
            hk = histories(T.hist, "h", lambda c, d: T.fo[:, c:d], lambda c, d: ["fo%d" % i for i in within((half,), c, d)], par["hc"],
                           lambda k: 0 if k < 5 else half, -BIG, A.max, A.min, 1.0, "M")
        else:
            hk = histories(T.hist, "h", scores, lambda c, d: ["p%d" % SP[within(par["sv"], c, d)[0]]], par["hc"], lambda k: 0, -BIG, A.max, A.min, 1.0, "M")
        for j in range(4):
            if two and j == 3:
                for i, (c, d) in enumerate(spans(par["zc"])):
                    scan(T.zp[:, 4 * c:4 * d], T.mk[:, 0:4 * (d - c)], T.sl[:, 4 * c:4 * d], 0.0, A.mult, A.add,
                         ["sl4"] + ["mk%d" % j for j in range(4)] + ["sl%d_%d" % (j, i) for j in range(3)], ["zp%d" % i, "sl3_%d" % i, "sl3_%d" % (i - 1)], 2 * (d - c), "e")
            for c, d in spans(par["zc"] if j == 3 else ()):
                out = T.zp[:, 4 * c + 5:4 * d + 5:4] if two and j == 3 else T.sl[:, wd * c + j:wd * d:wd]
                act(out, P[SS][:, c:d], F.Sign, ["p%d" % SS, hk[2 * j + 1]], ["sl%d_%d" % (j, i) for i in within(par["zc"], c, d)], d - c, "a%d" % j,
                    bias=hv(2 * j + 1), scale=-1.0)
        for i, (c, d) in enumerate(spans(par["zc"])):
            if two:
                scan(T.zs[:, 2 * c:2 * d], T.mk[:, 0:4 * (d - c):2], T.zp[:, 4 * c + 3:4 * d + 3:2], 0.0, A.mult, A.add, ["sl3_%d" % i], ["zs%d" % i], d - c, "b")
                continue
            scan(T.zs[:, 5 * c:5 * d], T.mk[:, 0:5 * (d - c)], T.sl[:, 5 * c:5 * d], 0.0, A.mult, A.add,
                 ["sl4"] + ["mk%d" % j for j in range(5)] + ["sl%d_%d" % (j, i) for j in range(4)], ["zs%d" % i], 2.5 * (d - c), "b")
        if PAR["q4"]:
            for j in range(4):
                act(T.qj[:, j:40:5], T.hist[:, HW + C:9 * HW:HW], F.Sign, hk, ["qj%d" % j], 1, "q", bias=hv(2 * j + 1), scale=-1.0)
            scan(T.qs[:], T.mk[:, 0:40], T.qj[:], 0.0, A.mult, A.subtract, ["qj%d" % j for j in range(5)] + ["mk%d" % j for j in range(5)], ["qa%d" % k for k in range(8)], 1, "q")
        for k in range(8 if PAR["q4"] else PAR["qa"], 8):
            act(T.qj[:, 4 * k:4 * k + 4], T.hist[:, 2 * HW + C:9 * HW:2 * HW], F.Sign, hk, ["qa%d" % k], 1, "q", bias=hv(k), scale=-1.0, accum_out=T.qa[:, k:k + 1])
        kk = histories(T.kh, "k", lambda c, d: T.zs[:, 2 * c + 1:2 * d:2] if two else T.zs[:, 5 * c + 4:5 * d:5], lambda c, d: ["zs%d" % i for i in within(par["zc"], c, d)], par["kc"],
                       lambda k: 0, 8.0, A.min, A.max, 0.5, "N")
        keys = T.kh[:, HW + C:7 * HW:HW]
        if PAR["qa"]:
            ts(T.qi[:, 0:6], keys, -0.375, None, A.add, None, kk[:6], ["qi"], 1, "m")
            tt(T.nb[:, 0, 0:6], keys, T.qi[:, 0:6], A.subtract, kk[:6] + ["qi"], ["nb%d0a" % G for G in range(4)], cy(1), "m")
        else:
            tt(T.nb[:, 0, 0:6], keys, T.qs[:, 4:30:5] if PAR["q4"] else T.qa[:, 0:6], A.add, kk[:6] + ["qa%d" % k for k in range(6)], ["nb%d0a" % G for G in range(4)], cy(1), "m")
        for i in range(2):
            a, b = 64 * i, 64 - 64 * i
            cp("svp", T.nb[b:b + 64, 2, 0:6], T.nb[a:a + 64, 0, 0:6], ["nb%d0a" % G for G in (2 * i, 2 * i + 1)], ["nb%d2a" % G for G in (2 - 2 * i, 3 - 2 * i)], 6, None, "m")
        for i, a in enumerate((0, 1, 3)):
            G = a + 1 - 2 * (a % 2)
            cp("svp", T.nb[32 * G:32 * G + 32, 1:4:2, 0:6], T.nb[32 * a:32 * a + 32, 0:4:2, 0:6], ["nb%d0a" % a, "nb%d2a" % a], ["nb%d1a" % G, "nb%d3a" % G], 12, None, "m")
        if par["nl"]:
            for k in (6, 7):
                for a in range(4):
                    q = slice(32 * a, 32 * a + 32)
                    out, key, lv = T.nb[96:128, 3 - a, k:k + 1], T.kh[q, HW * (k + 1) + C:HW * (k + 1) + C + 1], T.qs[q, 5 * k + 4:5 * k + 5] if PAR["q4"] else T.qa[q, k:k + 1]
                    r, w = [kk[k], "qa%d" % k], ["nb3%d%d" % (3 - a, k)]
                    act(out, key, F.Identity, r, w, 1, "l", bias=lv)
                    ts(out, key, lv, None, A.add, None, r, w, 1, "l")
                    either(2)
        else:
            tt(T.nb[:, 0, 6:8], T.kh[:, 7 * HW + C:9 * HW:HW], T.qa[:, 6:8], A.add, kk[6:] + ["qa6", "qa7"], ["nb%d0%d" % (G, k) for G in range(4) for k in (6, 7)], cy(1), "l")
            for a in range(3):
                cp("svp", T.nb[96:128, 3 - a, 6:8], T.nb[32 * a:32 * a + 32, 0, 6:8], ["nb%d06" % a, "nb%d07" % a], ["nb3%d6" % (3 - a), "nb3%d7" % (3 - a)], 2, None, "ml")
        for i in range(2):
            turn(T.nd[:, :, i, :], T.nb[:], ["nb%d%d%s" % (G, x, e) for G in range(4) for x in range(4) for e in "a67"], ["nd%d" % i], 1, "n")
        turn(T.no[:], T.nd[:], ["nd0", "nd1"], ["no"], 1, "n")
        o = 2 if par["vp"] else 0
        ts(T.on[:], T.no[:].indirect(T.ordn[:, o:o + 1]), 512.0, None, A.mult, None, ["no", "ordp" if o else "ordn"], ["on"], 1, "n", picked(16))
        for h, (c, d) in enumerate(HALF):
            for b in range(4):
                win = T.du[:, 128 * b:128 * b + 128].indirect(T.ok[:, c // 16:d // 16])
                if (h, b) in par["za"]:
                    bank = banks(1)[0]
                    mm(bank, "ehq", "ehz", 128 * b, xq, xz, c, d, xk + ["eh%d" % b], True, True, "Y%d" % h)
                    act(T.za[:, C * b + c:C * b + d], win, F.Copy, ["du%d" % b, "ok"], ["za%d%d" % (h, b)], 1, "y%d" % h, picked(d - c) + 10)
                    tt(T.zt[:, 4 * c + b:4 * d:4], P[bank][:, 0:d - c], T.za[:, C * b + c:C * b + d], A.add, ["p%d" % bank, "za%d%d" % (h, b)], ["zt%d%d" % (h, b)], cy(d - c), "z%d" % h)
                    continue
                tt(T.zt[:, 4 * c + b:4 * d:4], win, T.th[:, C * b + c:C * b + d], A.add,
                   ["du%d" % b, "ok", "tw%d%d" % (h, b)] + ["th%d%d" % (i, b) for i in within(PAR["cut%d" % max(rd - 1, 1)], c, d)], ["zt%d%d" % (h, b)],
                   picked(d - c), "z%d" % h)
            quant("zq", "zz", c, d, T.zt[:, 4 * c:4 * d], ["zt%d%d" % (h, b) for b in range(4)], ["Z%d" % h], "z%d" % h)
        for h, (c, d) in enumerate(HALF):
            for b, bank in enumerate(banks(4)):
                mm(bank, "efq", "efz", 128 * b, xq, xz, c, d, xk + ["ef%d" % b], True, False, "R")
                mm(bank, "wq", "wz", 128 * b, "zq", "zz", c, d, ["Z%d" % h, "wq", "wz"], False, True, "W")
                cp("sv", T.xt[:, 4 * c + b:4 * d:4], P[bank][:, 0:d - c], ["p%d" % bank], ["xt%d%d" % (h, b)], d - c, 1.0 / 32, "x%d" % h)
            quant(nq, nz, c, d, T.xt[:, 4 * c:4 * d], ["xt%d%d" % (h, b) for b in range(4)], [nk[h]], "x%d" % h)
        for h, (c, d) in enumerate(spans(par["sent"])):
            r = [nk[i] for i in within(par["cut"], c, d)]
            if ahead:
                if d == C:
                    far(STEP[rd - 1], [(u8(T.aq[:, c:d]), u8(T[nq][:, c:d])), (T.bz[:], T.xz2[:])], nk + ["vq"], ["aq%d" % h, "az%d" % h], 1024, "F")
                else:
                    far(STEP[rd - 1], [(u8(T.aq[:, c:d]), u8(T[nq][:, c:d]))], r, ["aq%d" % h], 4 * (d - c), "F")
                    if not par["vp"]:
                        far(STEP[rd - 1], [(T.az[:, c:d], plane(nz, c, d))], r, ["az%d" % h], d - c, "F")
            if rd + 1 == PAR["ahead"]:
                if d == C and PAR["hf"]:
                    far(STEP[rd], [(u8(T.hq[:, c:d]), u8(T[nq][:, c:d])), (T.hz[:], T[nz][:])], nk + ["eh0"], ["hq%d" % h, "hz"], 1024, "I")
                    continue
                far(STEP[rd], [(u8(T.hq[:, c:d]), u8(T[nq][:, c:d]))], r, ["hq%d" % h], 4 * (d - c), "H")
                if d == C:
                    far(STEP[rd], [(T.hz[:, 0:C], T[nz][:, 0:C])], nk, ["hz"], C, "I")
        src = "tf" if ahead else "th"
        for h, (c, d) in enumerate(spans(par["sent"])):
            if ahead and not par["vp"]:
                unpack("tf", "aq", "az", c, d, ["aq%d" % h, "az%d" % h], ["tf%d" % h], dict(enumerate(banks(4))), "A%d" % h)
        if par["vp"]:
            wq, wz = (T.aq[:], T.bz[:, 128:512]) if ahead else (T[nq][:], T[nz][:])
            rq, rz = (["aq0", "aq1"], ["az1"]) if ahead else (nk, nk)
            VB = banks(4)
            for i, e in enumerate("eo"):
                dq, dz, off = "v%sq%d" % (e, rd), "v%sz%d" % (e, rd), T.on[:, 8 * i:8 * i + 8]
                op("v", lambda dq=dq, off=off: v.tensor_copy(T[dq][:].bitcast(dt.uint32), wq.bitcast(dt.uint32).indirect(off)), ["on"] + rq, [dq], picked(128), "P")
                op("s", lambda dz=dz, off=off: s.activation(T[dz][:], wz.indirect(off), F.Copy), ["on"] + rz, [dz], picked(128) + 10, "P")
                for b in range(4):
                    mm(VB[b], "e%sq" % e, "e%sz" % e, 128 * b, dq, dz, 0, 128, [dq, dz, "e%s%d" % (e, b)], e == "e", e == "o", "P")
            for b in range(4):
                cp("sv", T.vt[:, b:512:4], P[VB[b]][:, 0:128], ["p%d" % VB[b]], ["vt%d" % b], 128, 1.0 / 32, "V")
        for h, (c, d) in enumerate(HALF):
            bs = [b for b in range(4) if not (ahead or par["vp"]) or rd < 3 and any((i, b) not in PAR["za%d" % (rd + 1)] for i in within(PAR["cut%d" % (rd + 1)], c, d))]
            unpack("th", nq, nz, c, d, [nk[h]], ["th%d" % h, "tw%d" % h], dict(zip(bs, banks(len(bs)))), "T%d" % h)
        for b in range(0 if par["vp"] else 4):
            win = T[src][:, C * b:C * b + C].indirect(T.on[:, 0:8])
            r = ["%s%d%d" % (src, h, b) for h in range(3)] + ["on"]
            act(T.vt[:, b:512:4], win, F.Copy, r, ["vt%d" % b], 1, "V", picked(128) + 10, scale=2.0)
            ts(T.vt[:, b:512:4], win, 2.0, None, A.mult, None, r, ["vt%d" % b], 1, "V", picked(128))
            either(2)
        vk, uq, uz, sq, sz = ["vt%d" % b for b in range(4)], T["uq%d" % rd], T["uz%d" % rd], T["sq%d" % rd], T["sz%d" % rd]
        if ahead:
            quant("uq%d" % rd, "uz%d" % rd, 0, 128, T.vt[:], vk, ["U%d" % rd, "Uz%d" % rd], "V")
        else:
            quant("sq%d" % rd, "sz%d" % rd, 0, 128, T.vt[:], vk, ["out"], "V")
            if rd < 3 and rd + 1 != PAR["ahead"]:
                far(STEP[rd - 1], [(u8(uq[:]), u8(sq[:])), (uz[:], sz[:])], ["out", "ef0", "ef1", "ef2", "ef3", "eh0", "eh1", "eh2", "eh3"], ["U%d" % rd, "Uz%d" % rd], 1024, "F")
            elif rd + 1 == PAR["ahead"]:
                far(STEP[rd - 1], [(u8(uq[:]), u8(sq[:])), (uz[:], sz[:])], ["out", "ef0", "ef1", "ef2"], ["U%d" % rd, "Uz%d" % rd], 1024, "F")
                far(STEP[rd - 1] + STEP[rd], [(u8(T.gq[:]), u8(sq[:]))], ["out"], ["gq"], 512, "G")
                far(STEP[rd - 1] + STEP[rd], [(T.gz[:], sz[:, 0:128])], ["out"], ["gz"], 128, "G")
            else:
                far(STEP[rd - 1], [(uz[:, 0:128], sz[:, 0:128])], ["out"], ["Uz%d" % rd], 128, "G")
                far(STEP[rd - 1], [(u8(uq[:]), u8(sq[:]))], ["out"], ["U%d" % rd], 512, "F")
        return nk

    for rd in (1, 2, 3):
        nk = one_round(rd)

    now[0] = "4"
    for h, (c, d) in enumerate(pieces(3)):
        bank = banks(1)[0]
        mm(bank, "vq", "vz", 0, "xq3", "xz3", c, d, [nk[h], "vq"], True, True, "y")
        cp("sv", T.yt[:, c:d], P[bank][:, 0:d - c], ["p%d" % bank], ["yt%d" % h], d - c, None, "y")
        dma("y", T.y[:, c:d], T.yt[:, c:d], ["yt%d" % h], [], (128, 4 * (d - c)), "outy", "y")
    cp("v", T.of[:, 0:24], T.ok[:, 0:24], ["ok"], ["of0"], 1, None, "o")
    if PAR["vp3"]:
        ts(T.ot[:, 0:16], T.no[:].indirect(T.ordn[:, 0:1]), 512.0, None, A.mult, None, ["no", "ordn"], ["ot"], 1, "o", picked(16))
        cp("v", T.of[:, 24:32], T.ot[:, 0:8], ["ot"], ["of1"], 1, None, "o")
    else:
        cp("v", T.of[:, 24:32], T.on[:, 0:8], ["on"], ["of1"], 1, None, "o")
    turn(T.ot[:], T.of[:], ["of0", "of1"], ["ot"], 1, "o")
    dma("y", T.oc[:], u8(T.xq3[:]), nk, [], (128, 1536), "outy", "o")
    for k in range(4):
        dma("y", T.osc[4 * k:4 * k + 4, :], T.xz3[32 * k:32 * k + 4, :], nk, [], (16, 96), "outy", "o")
    for a in range(4):
        for h in range(2):
            dma("y", T.op[2 * a + h, :], T.ot[32 * a:32 * a + 32, 16 * h:16 * h + 16], ["ot"], [], (32, 64), "outy", "o")
    dma("s", T.uc[:], u8(T.uq3[:]), ["U3"], [], (128, 512), "outs", "u")
    for k in range(4):
        dma("y" if k % 2 == 0 else "s", T.usc[4 * k:4 * k + 4, :], T.uz3[32 * k:32 * k + 4, 0:128], ["Uz3"], [], (16, 32), "outy" if k % 2 == 0 else "outs", "u")
    return calls


def rank_program(g, core, T, topo):
    if T.rank_of(core) is None:
        return
    queues = {"v": g.vector, "s": g.scalar, "t": g.tensor, "p": g, "y": g.sync}
    calls = write(g, core, T, topo, lay_out(write(g, core, T, topo, {}))[1])
    count, seen, nd, moved = {}, {q: {} for q in queues}, [0], []
    for i in lay_out(calls)[0]:
        c = calls[i]
        if c["kind"] == "fly":
            c["tok"], c["know"] = calls[c["f"]]["tok"], calls[c["f"]]["know"]
            continue
        know = seen[c["q"]]
        need = [calls[j] for j in sorted(c["hard"])]
        if c["q"] == "p" and len(c["ways"]) > 1:
            need += moved
            moved[:] = [c]
        need = list({d["tok"]: d for d in need}.values())
        for d in need:
            sem, val = d["tok"]
            if know.get(sem, 0) >= val or any(e is not d and e["know"].get(sem, 0) >= val and (e["tok"][0] != sem or e["tok"][1] > val) for e in need):
                continue
            queues[c["q"]].wait_ge(T.sem[sem], val)
        for d in need:
            for sem, val in d["know"].items():
                know[sem] = max(know.get(sem, 0), val)
        if c["kind"] == "far":
            n = c["f"]()
            count["sent"] = count.get("sent", 0) + n
            count[c["sem"]] = n
            c["tok"] = (c["sem"], n)
            c["know"] = {c["sem"]: n}
            continue
        sem, n = c["sem"], 16
        if c["kind"] == "op":
            sem, n = "c" + c["q"], 1
        elif sem is None:
            sem = "d%d" % nd[0]
            nd[0] += 1
        count[sem] = count.get(sem, 0) + n
        c["f"]().then_inc(T.sem[sem], n)
        c["tok"] = (sem, count[sem])
        c["know"] = dict(know)
        c["know"][sem] = count[sem]
    for sem in sorted(count):
        g.wait_ge(T.sem[sem], count[sem])
